import numpy as np, ml_dtypes
CORES = [40,64,80,88,96,104,120,144]
N = 8
BF = ml_dtypes.bfloat16
def gentries(a):
    return np.ascontiguousarray(a.reshape(8, 16, -1).transpose(0, 2, 1)).reshape(8, -1)
def gtable(e):
    e = np.asarray(e); return np.ascontiguousarray(e.reshape(8, -1, 16).transpose(0, 2, 1)).reshape(128, -1).astype(np.int32)
V, L, ST, RO, CAP = 1024, 128, 2, 2, 32
W = V + RO * ST * L
E = 4095
VOID = 2 ** 20
def pack(a, c, x, t, h):
    return {"a0": np.ascontiguousarray(a.reshape(N, 128, V)).astype(np.float32).astype(BF), "kids": np.ascontiguousarray(c.reshape(N, 128, V)).astype(np.int32),
            "x0": np.ascontiguousarray(x.reshape(N, 128, L)).astype(np.float32).astype(BF), "tops": np.stack([gtable(u) for u in t]), "th": np.ascontiguousarray(h).astype(np.int32)}
def near(rng, p, n):
    k = rng.integers(0, 24, (N, 8, 1, n)); z = rng.integers(1, 25, (N, 8, 1, n))
    v = np.take_along_axis(np.broadcast_to(p, (N, 8, 16, 24)), np.broadcast_to(k, (N, 8, 16, n)), 3)
    return np.clip(v + np.rint(z * rng.standard_normal((N, 8, 16, n))), 0, 255).astype(np.int64)
def parts(rng):
    p = rng.integers(0, 256, (8, 16, 24)); p[..., ::3] = rng.integers(0, 40, (8, 16, 8))
    fill = rng.choice(np.array([0.2, 0.5, 0.8, 1.0]), (N, 8, 1, V))
    c = np.where(rng.random((N, 8, 16, V)) < fill, rng.integers(0, V, (N, 8, 16, V)), E)
    hot = np.take_along_axis(rng.integers(0, V, (N, 8, 8)), rng.integers(0, 8, (N, 8, L)), 2)
    t = np.where(rng.random((N, 8, L)) < 0.2, hot, rng.integers(0, V, (N, 8, L)))
    h = np.minimum(rng.choice(np.array([60, 200, 500, 900, 4000]), (N, 8, L)) + rng.integers(0, 100, (N, 8, L)), 4080)
    return near(rng, p, V), c, near(rng, p, L), t, h
def setup_inputs(rng):
    return pack(*parts(rng))
def setup_inputs_spread(rng):
    a = np.minimum(np.exp2(8 * rng.random((N, 8, 1, V))) * rng.random((N, 8, 16, V)), 255).astype(np.int64)
    x = np.minimum(np.exp2(8 * rng.random((N, 8, 1, L))) * rng.random((N, 8, 16, L)), 255).astype(np.int64)
    fill = np.minimum(1.25 * rng.random((N, 8, 1, V)), 1.0)
    c = np.where(rng.random((N, 8, 16, V)) < fill, np.minimum((V * rng.random((N, 8, 16, V)) ** 2).astype(np.int64), V - 1), E)
    t = np.minimum((V * rng.random((N, 8, L)) ** 3).astype(np.int64), V - 1)
    h = np.minimum(np.exp2(12 * rng.random((N, 8, L))).astype(np.int64) - 1, 4080)
    return pack(a, c, x, t, h)
def setup_inputs_ends(rng):
    def both(n):
        k = rng.integers(0, 4, (N, 8, 1, n)); m = 255 * rng.integers(0, 2, (N, 8, 16, n))
        return np.where(k == 0, 0, np.where(k == 1, 255, m))
    a, x = both(V), both(L); a[..., 0] = 255 * rng.integers(0, 2, (N, 8, 16))
    h = 4080 * rng.integers(0, 2, (N, 8, L)); s = (N, 8, 16, V)
    c = np.where(rng.random(s) < 0.5, 0, np.where(rng.random(s) < 0.3, V - 1, rng.integers(0, V, s)))
    c = np.where(rng.random(s) < rng.choice(np.array([0.1, 0.4, 0.6, 1.0]), (N, 8, 1, V)), c, E)
    m = np.argsort(rng.random((N, 8, L)), axis=2) < (2 * L) // 3
    t = np.where(m, (V - 1) * rng.integers(0, 2, (N, 8, L)), rng.integers(1, V - 5, (N, 8, L)))
    t[:, 7] = np.where(m[:, 7], t[:, 7], rng.integers(1, V - 6 - (CAP + 2), (N, L)))
    a[..., V - 1] = 255; a[..., V - 2] = 255; c[..., V - 1] = E; c[..., V - 2] = E
    c[:, :, 2, V - 1] = V - 2; c[:, :, 15, V - 1] = V - 1; c[:, :, 15, V - 2] = V - 1
    a[..., V - 5] = 0; c[..., V - 5] = E; c[:, :, 0, V - 5] = V - 5; c[..., V - 4] = V - 5
    o = t[:, 1::2]; o[o == V - 1] = 0
    for q in range(N):
        i = np.nonzero(~m[q, 7, :L - 2])[0][-(CAP + 2):]; u = V - 6 - np.arange(CAP + 2)
        c[q, 7][:, u] = V - 5; x[q, 7][:, i] = 255; h[q, 7, i] = 0; t[q, 7, i] = u
    x[..., L - 1] = 0; h[..., L - 1] = 4080; t[..., L - 1] = V - 1
    x[..., L - 2] = 255; h[..., L - 2] = 0; t[..., L - 2] = V - 4
    return pack(a, c, x, t, h)
def setup_inputs_corners(rng):
    a = rng.integers(0, 201, (N, 8, 16, V)); x = rng.integers(201, 256, (N, 8, 16, L)); s = (N, 8, 16, V)
    c = np.where(rng.random(s) < rng.choice(np.array([0.1, 0.5, 0.9]), (N, 8, 1, V)), rng.integers(0, V, s), E)
    t = np.zeros((N, 8, L), np.int64); h = np.zeros((N, 8, L), np.int64)
    case = np.array([0, 1, CAP - 1, CAP, CAP + 1, L])[rng.integers(0, 6, (N, 8))]
    case[0] = (CAP, CAP + 1, L, CAP - 1, 1, 0, CAP, CAP + 1); case[1] = (0, L, 1, 0, CAP, CAP + 1, CAP - 1, 0); case[N - 1, 7] = CAP
    for q in range(N):
        for g in range(8):
            n = int(case[q, g]); o = rng.permutation(V); full, leaf, one, more = o[:L], o[L:L + 64], o[L + 64:L + 128], o[L + 128:]; k = c[q, g]
            k[:, full] = rng.integers(0, V, (16, L)); k[:, leaf] = E; k[:, one] = E; k[rng.integers(0, 16, 64), one] = rng.integers(0, V, 64)
            if n == 0: k[15, np.all(k == E, axis=0)] = V - 1
            w = rng.integers(0, 4, L); again = rng.choice(full[:n] if n else one, L)
            u = np.where(w == 0, again, np.where(w == 1, rng.choice(leaf, L), np.where(w == 2, rng.choice(one, L), rng.choice(more, L))))
            y = np.where((w == 0) & (n > 0), 0, 4080); i = rng.permutation(L)[:n]; u[i] = full[:n]; y[i] = 0
            t[q, g] = u; h[q, g] = y
    return pack(a, c, x, t, h)
def half(rng, who, n):
    return np.where(rng.random((16, n)) < 0.5, rng.choice(who, (16, n)), E)
def late(rng, A, C, X, T, H):
    u = rng.permutation(V)[:L // 2]; A[:] = rng.integers(0, 201, (16, V)); X[:] = rng.integers(201, 256, (16, L))
    C[:, u] = rng.integers(0, V, (16, L // 2)); C[rng.integers(0, 16, L // 2), u] = E
    T[:] = np.repeat(u, 2); H[:] = 0
def splits(rng, A, C, X, T, H):
    o = rng.permutation(V); s, b, d, far = o[:L], o[L:L + 16], o[L + 16:L + 32], o[L + 32:]
    A[:, far] = rng.integers(240, 256, (16, far.size)); A[:, b] = rng.integers(200, 211, (16, 16)); A[:, d] = rng.integers(100, 121, (16, 16))
    kb = rng.integers(0, 16, 16); kd = (kb + rng.integers(1, 16, 16)) & 15; w = rng.integers(0, 16, L)
    C[:] = E; C[:, far] = half(rng, far, far.size); C[:, b] = half(rng, far, 16); C[kb, b] = E; C[kd, b] = d
    C[:, s] = half(rng, far, L); C[kd[w], s] = rng.choice(far, L); C[kb[w], s] = b[w]
    X[:] = A[:, d[w]] + rng.integers(0, 3, (16, L)); T[:] = s; H[:] = rng.integers(400, 600, L)
def hosts(rng, A, C, X, T, H):
    o = rng.permutation(V); s, b, far = o[:L], o[L:2 * L], o[2 * L:]
    X[:] = rng.integers(100, 121, (16, L)); A[:, far] = rng.integers(240, 256, (16, far.size)); A[:, b] = X + rng.integers(5, 13, (16, L))
    C[:] = E; C[:, far] = half(rng, far, far.size); C[:, b] = half(rng, far, L); C[:, s] = half(rng, far, L); C[rng.integers(0, 16, L), s] = b
    T[:] = s; H[:] = rng.integers(900, 1100, L)
def made(rng, A, C, X, T, H):
    k = L // 8; o = rng.permutation(V); v, b, s, far = o[:k], o[k:2 * k], o[2 * k:3 * k], o[3 * k:]
    i = rng.permutation(L); pz = np.sort(i[:2 * k].reshape(k, 2), axis=1); p, z, r = pz[:, 0], pz[:, 1], i[2 * k:3 * k]
    n = rng.integers(12, 41, k); m = np.argsort(rng.random((16, k)), axis=0) < 8
    w = np.argsort(rng.random((16, k)), axis=0)[:3]; w[:2] = np.sort(w[:2], axis=0)
    A[:, far] = rng.integers(240, 256, (16, far.size)); A[:, b] = np.where(m, n, 0); A[:, s] = np.where(m, n, 2 * n)
    C[:] = E; C[:, far] = half(rng, far, far.size); C[w[0], v] = b; C[w[1], v] = s
    C[:, b] = rng.choice(far, (16, k)); C[w[2], b] = E
    T[:] = rng.choice(far, L); T[p] = v; T[z] = v; T[r] = b
    y = np.where(m, 2 * n, n); X[:, p] = y; X[:, z] = n; X[:, r] = y + rng.integers(1, 4, (16, k))
    H[p] = 12 * n; H[z] = 0; H[r] = 0
def setup_inputs_ties(rng):
    a = 100 * (rng.random((N, 8, 1, V)) < 0.6) + rng.integers(0, 3, (N, 8, 16, V)) * (rng.random((N, 8, 1, V)) < 0.8)
    x = 100 + rng.integers(0, 3, (N, 8, 16, L)) * (rng.random((N, 8, 1, L)) < 0.8); s = (N, 8, 16, V)
    c = np.where(rng.random(s) < 0.5, rng.integers(0, 64, s), rng.integers(0, V, s))
    c = np.where(rng.random(s) < rng.choice(np.array([0.2, 0.6, 0.9, 1.0]), (N, 8, 1, V)), c, E)
    h = np.where(rng.random((N, 8, L)) < 0.8, rng.integers(0, 20, (N, 8, L)), 1600)
    t = rng.integers(0, V, (N, 8, L))
    for q in range(N):
        for g, fn in ((1, late), (2, splits), (4, hosts), (6, made)):
            if g == 1 or q % 2 == 0: fn(rng, a[q, g], c[q, g], x[q, g], t[q, g], h[q, g])
    return pack(a, c, x, t, h)
def setup_inputs_alike(rng):
    a, c, x, t, h = parts(rng)
    c[:, 0] = rng.integers(0, V, (N, 1, V)); c[:, 1] = np.where(c[:, 1] == E, E, np.arange(V))
    t[:, 2] = rng.integers(0, V, (N, 1)); t[:, 3] = np.where(rng.random((N, L)) < 0.5, rng.integers(0, V, (N, 1)), V - 1)
    c[:, 4] = np.where(c[:, 4] == E, E, rng.choice(np.array([0, 5, V - 1]), (N, 16, V)))
    a[:, 5] = np.minimum(a[:, 5], 200); c[:, 5] = rng.integers(0, V, (N, 16, V)); t[:, 5] = np.arange(L) % CAP
    x[:, 5] = rng.integers(201, 256, (N, 16, L)); h[:, 5] = 0
    x[:, 6] = x[:, 6, :, :1]
    c[:, 7] = rng.integers(0, V, (N, 16, V))
    return pack(a, c, x, t, h)
def check_inputs(d):
    bad = []
    for k, lo, hi in (("a0", 0, 255), ("kids", 0, E), ("x0", 0, 255), ("tops", 0, V - 1), ("th", 0, 4080)):
        v = np.asarray(d[k]).astype(np.float64)
        if not (np.min(v) >= lo and np.max(v) <= hi) or np.any(v != np.floor(v)): bad.append("range of " + k)
        elif k == "kids" and np.any((v >= V) & (v != E)): bad.append("range of " + k)
    return bad
def first(key, on):
    k = np.where(on, key, 8192 + np.arange(L)); o = np.argsort(k, axis=1, kind="stable"); s = np.take_along_axis(k, o, 1)
    m = np.ones(k.shape, bool); m[:, 1:] = s[:, 1:] != s[:, :-1]
    r = np.zeros(k.shape, bool); np.put_along_axis(r, o, m, 1)
    return r & on
def pick(t, i):
    return t[np.arange(t.shape[0]).reshape((-1,) + (1,) * (i.ndim - 1)), i]
def at(t, k):
    return np.take_along_axis(t, k[..., None], 2)[..., 0]
def reference(a0, kids, x0, tops, th):
    B = 8 * N
    A = np.zeros((B, W, 16), np.int32); A[:, :V] = a0.astype(np.float32).astype(np.int32).reshape(B, 16, V).transpose(0, 2, 1)
    C = np.full((B, W, 16), E, np.int32); C[:, :V] = kids.reshape(B, 16, V).transpose(0, 2, 1)
    x = np.ascontiguousarray(x0.astype(np.float32).astype(np.int32).reshape(B, 16, L).transpose(0, 2, 1))
    top = np.stack([gentries(u) for u in tops]).astype(np.int64).reshape(B, L); lim = th.reshape(B, L).astype(np.int32)
    for rnd in range(RO):
        v = top.copy(); rest = np.zeros((B, L), bool)
        come = np.zeros((N, 8, ST * CAP, 16), np.int32); ok = np.zeros((N, 8, ST * CAP), bool)
        for j in range(ST):
            sg = rnd * ST + j; act = first(v, ~rest)
            c = pick(C, v); filled = c != E
            e = np.where(filled, np.add.reduce(np.abs(x[:, :, None] - pick(A, np.where(filled, c, 0))), axis=3), VOID)
            kb = np.argmin(e, axis=2); eb = at(e, kb); e2 = e.copy(); np.put_along_axis(e2, kb[..., None], VOID, 2)
            kq = np.argmin(e2, axis=2); eq = at(e2, kq)
            b = np.where(eb < VOID, at(c, kb), 0); q = np.where(eq < VOID, at(c, kq), 0)
            ab = pick(A, b); mid = (ab + pick(A, q)) >> 1
            em = np.where(eq < VOID, np.add.reduce(np.abs(x - mid), axis=2), VOID)
            d = np.where((eb < VOID)[..., None], pick(C, b), E)
            f = np.where(d != E, np.add.reduce(np.abs(x[:, :, None] - pick(A, np.where(d != E, d, 0))), axis=3), VOID)
            w = np.argmin(np.stack([eb, em, np.min(f, axis=2), lim], axis=2), axis=2)
            host, merge, split, new = [act & (w == u) for u in range(4)]
            empty = ~filled; room = np.any(empty, axis=2); k0 = np.argmax(empty, axis=2); over = new & ~room
            n = V + L * sg + np.arange(L)
            g, i = np.nonzero(host & first(b, host))
            A[g, b[g, i]] = ab[g, i] + np.clip(x[g, i] - ab[g, i], -4, 4)
            g, i = np.nonzero(merge)
            A[g, n[i]] = mid[g, i]; C[g, n[i], kb[g, i]] = b[g, i]; C[g, n[i], kq[g, i]] = q[g, i]
            C[g, v[g, i], kb[g, i]] = n[i]; C[g, v[g, i], kq[g, i]] = E
            g, i = np.nonzero(split)
            t = c[g, i]; t[np.arange(len(g)), kb[g, i]] = E; C[g, v[g, i]] = np.where(t == E, d[g, i], t)
            g, i = np.nonzero(new & room)
            A[g, n[i]] = x[g, i]; C[g, v[g, i], k0[g, i]] = n[i]
            v = np.where(host, b, np.where(merge, n, v)); rest = rest | new
            pl = np.add.accumulate(over.astype(np.int64), axis=1) - 1; g, i = np.nonzero(over & (pl < CAP))
            to = (g // 8 + 1 + sg % (N - 1)) % N
            come[to, g % 8, j * CAP + pl[g, i]] = x[g, i]; ok[to, g % 8, j * CAP + pl[g, i]] = True
        ok = ok.reshape(B, ST * CAP); come = pick(come.reshape(B, ST * CAP, 16), np.argsort(~ok, axis=1, kind="stable"))
        cnt = np.add.reduce(ok.astype(np.int64), axis=1)[:, None]; nr = np.add.accumulate(rest.astype(np.int64), axis=1) - 1
        got = rest & (nr < cnt)
        x = np.where(got[..., None], pick(come, np.clip(nr, 0, ST * CAP - 1)), np.abs(x - pick(A, v)))
    return {"ya": np.ascontiguousarray(A.transpose(0, 2, 1)).reshape(N, 128, W).astype(np.float32).astype(BF),
            "yc": np.ascontiguousarray(C.transpose(0, 2, 1)).reshape(N, 128, W).astype(np.float32),
            "yx": np.ascontiguousarray(x.transpose(0, 2, 1)).reshape(N, 128, L).astype(np.float32).astype(BF)}

@@ -1,0 +1,672 @@
+from concourse.mybir import AluOpType as OP, ActivationFunctionType as AF, AxisListType
+
+V0, L, ST, RO, CAP, NR = 1024, 128, 2, 2, 32, 8
+W = V0 + RO * ST * L
+E1 = W
+WIN = W + 8
+DUMP = WIN
+FAR = 2048
+BIG = float(2 ** 30)
+MAGIC = float(2 ** 23)
+PIECES = [(0, 32), (32, 32), (64, 32), (96, 16), (112, 16)]
+
+SLOT = {}
+SIZE = {"F": 0, "B": 0, "I": 0, "U": 0}
+
+
+def _s(kind, **kw):
+    for n, w in kw.items():
+        SLOT[n] = ("ar" + kind, SIZE[kind], w)
+        SIZE[kind] += (w + 15) // 16 * 16
+
+
+_s("B", A=1680, xrep=2048, df=2048, ag=2048, ab2=2048, xb=128, xT=128, R=2048, onesb=512, zb=512, idb=128, ipb=136,
+   hc=272, f16p=136, selb=8, sel2=8, bk=16, sb=32, tri=128, trib=512, kcb=408, rmask=384, Di=128, I128=128, GN=640, GE=256,
+   m1c=128, bb=143, bs=1664, EE=128, Tb=1664, h8=128, Fm=128, cod=128, codE=128, codO=128, bod=128, bodE=128, bodO=128,
+   eqa=1024, eqb=1024, ex=256, ex2=256, oh=384, gx=256, gm=384, exS=128, exU=128, exH=128, exP=128, exN=128, absM=128, Mb=128,
+   An=128, hv=128, hF=8, ov=8, nov=8, rest=8, rest2=8, nonr=8, nonr2=8, one8=8, nF=8)
+_s("F", CW=FAR + 1680, idf=136, zf=272, RM=272, RM2=128, kcf=408, kcg=408, kpat=384, iGL=8, dmp=8, dmp16=8, lim=8, lim1=8, thf=128, topf=16,
+   r=128, y=128, cvf=128, dvf=128, m1=272, m2=272, cand=272, k0s=136, abm=128, sm=128, ym=128, xs=128, xp=128, dM=128,
+   hm=8, he=8, nn=8, T0=8, Tt=8, act0=8, an=8, ah0=8, k1=8, k2=8, wal=128, ral=128, w3=128, f3=128, t3=128, v16=8, nv=8,
+   rsp=128, c0=128, cb=128, t1=128, t2=128, X3=24, g3=24, gm3=32, Dv=16, q1=16, vf=16, fsm=128, Sf=8, anr0=8, nrm=8, h1=8,
+   oA=8, pos=8, nrs=8, am4=128, ap4=128, nGL=32, ge=8, idx=8, msk=32, n0=1, cd=1, ad=128, mE=1, mO=1, bd=8, p128=1, m128=1)
+_s("I", KI=1024, tp=8, thi=128, ci=128, rmi=384, pin=8, pr=8, m16=8, cio=13, bt=143, m1e=16, dec=16, eb=8, kk=24, m2e=16,
+   dec2=16, kq=8, hx=128, xi=128, iv=8)
+_s("U", bl=128, tu=8, cvu=128, dvu=128, bu=8, qu=8, uvu=8, vu2=16, oAu=8, posu=8, iu=8)
+SLOT["C"] = ("arF", SLOT["CW"][1] + FAR, 1680)
+
+SCRATCH = {"arF": ("sbuf", [128, SIZE["F"]], "float32"), "arB": ("sbuf", [128, SIZE["B"]], "bfloat16"),
+           "arI": ("sbuf", [128, SIZE["I"]], "int32"), "arU": ("sbuf", [128, SIZE["U"]], "uint16")}
+for _k in range(8):
+    SCRATCH["pb%d" % _k] = ("psum", [128, 512], "float32")
+for _k in range(4):
+    SCRATCH["msg%d" % _k] = ("sbuf", [128, 256], "float32")
+    SCRATCH["rl%d" % _k] = ("sbuf", [128, 32], "float32")
+for _k in range(2):
+    SCRATCH["come%d" % _k] = ("sbuf", [128, 80], "float32")
+SEMAPHORES = (["qv", "qs", "qt", "qg"] + ["in%d" % k for k in range(4)] + ["rr%d" % k for k in range(4)] + ["ls%d" % k for k in range(4)]
+              + ["ld%d" % k for k in range(8)])
+
+
+def emask(topo, src, dst, n):
+    m = 0
+    for e in topo.engines(src, dst)[:n]:
+        m |= 1 << e
+    return m
+
+
+NE_ON, NE_OFF = 16, 8
+
+
+def hops(T, topo, rank, s):
+    src, dst = T.cores[rank], T.cores[(rank + 1 + s % (NR - 1)) % NR]
+    if s > 0 and topo.may_write(src, dst):
+        return [src, dst]
+    ways = [c for c in topo.cores_of(src) if c != src and all(topo.may_write(c, d) for d in T.cores if d not in topo.cores_of(src))]
+    ways.sort(key=lambda c: topo.die(c) != topo.die(src))
+    return [src, ways[0], dst]
+
+
+def engines_of(topo, a, b):
+    return NE_ON if b in topo.cores_of(a) else NE_OFF
+
+
+def relay(g, core, T, topo):
+    for s in range(ST * RO):
+        for rank in range(NR):
+            h = hops(T, topo, rank, s)
+            if len(h) == 3 and h[1] == core:
+                n = engines_of(topo, h[1], h[2])
+                g.wait_ge(T.sem["rr%d" % s], engines_of(topo, h[0], core))
+                rid, pid = topo.addr(h[2], core)
+                g.remote_dma(T["come%d" % (s // ST)][:, CAP * (s % ST):CAP * (s % ST) + CAP], T["rl%d" % s][:, 0:CAP], T.sem["in%d" % s],
+                             T.sem["ls%d" % s], pid, rid, emask(topo, core, h[2], n))
+    for s in range(ST * RO):
+        for rank in range(NR):
+            h = hops(T, topo, rank, s)
+            if len(h) == 3 and h[1] == core:
+                g.wait_ge(T.sem["ls%d" % s], engines_of(topo, h[1], h[2]))
+
+
+def rank_program(g, core, T, topo):
+    rank = T.rank_of(core)
+    if rank is None:
+        relay(g, core, T, topo)
+        return
+    eng = {"v": g.vector, "s": g.scalar, "t": g.tensor, "g": g, "y": g.sync}
+    own = {"v": "qv", "s": "qs", "t": "qt", "g": "qg"}
+    cnt = {"qv": 0, "qs": 0, "qt": 0, "qg": 0}
+    know = {q: {} for q in eng}
+    wr, rd = {}, {}
+
+    def need(q, R, Wk, dma=False):
+        deps = []
+        for k in R:
+            if k in wr:
+                deps.append(wr[k])
+            if k[:2] == "pb":
+                deps += [d for d in rd.get(k, []) if d[0] != q]
+        for k in Wk:
+            if k in wr and (wr[k][0] != q or dma):
+                deps.append(wr[k])
+            deps += [d for d in rd.get(k, []) if d[0] != q or dma or k[:2] == "pb"]
+        deps = sorted(deps, key=lambda d: -d[2])
+        for d in deps:
+            if know[q].get(d[1], 0) < d[2]:
+                eng[q].wait_ge(T.sem[d[1]], d[2])
+                for n, v in d[3].items():
+                    know[q][n] = max(know[q].get(n, 0), v)
+
+    def note(tag, sem, val, snap, R, Wk):
+        snap = dict(snap)
+        snap[sem] = val
+        d = (tag, sem, val, snap)
+        for k in R:
+            rd.setdefault(k, []).append(d)
+            rd[k] = [e for e in rd[k] if e is d or e[0] != tag or e[1] != sem]
+        for k in Wk:
+            wr[k] = d
+            rd[k] = []
+
+    def op(q, call, R, Wk):
+        need(q, R, Wk)
+        s = own[q]
+        cnt[s] += 1
+        call(eng[q]).then_inc(T.sem[s], 1)
+        note(q, s, cnt[s], know[q], R, Wk)
+
+    def dma(q, sem, out, in_, R, Wk):
+        need(q, R, Wk, True)
+        eng[q].dma_start(out, in_).then_inc(T.sem[sem], 16)
+        cnt[sem] = 16
+        note("dma" + sem, sem, 16, know[q], R, Wk)
+
+    def b(name, c0=0, c1=None, st=1, p0=0, p1=128, key=None):
+        if name in SLOT:
+            buf, o, w = SLOT[name]
+        else:
+            buf, o, w = name, 0, SCRATCH[name][1][1]
+        c1 = w if c1 is None else c1
+        return (T[buf][p0:p1, o + c0:o + c1:st] if st != 1 else T[buf][p0:p1, o + c0:o + c1], key if isinstance(key, list) else [key or name])
+
+    def ind(win, off):
+        return (win[0].indirect(off[0]), win[1] + off[1])
+
+    def ks(*refs):
+        return [k for r in refs if isinstance(r, tuple) for k in r[1]]
+
+    def ap(x):
+        return x[0] if isinstance(x, tuple) else x
+
+    def tt(o, a, c, f):
+        op("v", lambda e: e.tensor_tensor(o[0], a[0], c[0], f), ks(a, c), ks(o))
+
+    def ts(o, a, s1, f0, s2=None, f1=None):
+        if f1 is None:
+            op("v", lambda e: e.tensor_scalar(o[0], a[0], ap(s1), None, f0), ks(a, s1), ks(o))
+        else:
+            op("v", lambda e: e.tensor_scalar(o[0], a[0], ap(s1), ap(s2), f0, f1), ks(a, s1, s2), ks(o))
+
+    def cp(o, a):
+        op("v", lambda e: e.tensor_copy(o[0], a[0]), ks(a), ks(o))
+
+    def scatter(win, off, a):
+        op("v", lambda e: e.tensor_copy(win[0].indirect(off[0]), a[0]), ks(a, off), ks(win))
+
+    def ms(o, v):
+        op("v", lambda e: e.memset(o[0], v), [], ks(o))
+
+    def scan(o, a, c, f0, f1):
+        op("v", lambda e: e.tensor_tensor_scan(o[0], a[0], c[0], BIG, f0, f1), ks(a, c), ks(o))
+
+    def act(o, a, f, bias=0.0, scale=1.0):
+        op("s", lambda e: e.activation(o[0], a[0], f, bias=ap(bias), scale=ap(scale)), ks(a, scale, bias), ks(o))
+
+    def mm(o, l, r, start=True, stop=True):
+        op("t", lambda e: e.matmul(o[0], l[0], r[0], start, stop), ks(l, r), ks(o))
+
+    def io(o, pat, base, cm, flag=False):
+        if flag:
+            op("g", lambda e: e.iota(o[0], pat, base, cm, allow_small_or_imprecise_dtypes=True), [], ks(o))
+        else:
+            op("g", lambda e: e.iota(o[0], pat, base, cm), [], ks(o))
+
+    def asel(o, a, pat, f, fill, base, cm):
+        op("g", lambda e: e.affine_select(o[0], a[0], pat, f, fill, base, cm), ks(a), ks(o))
+
+    bl = lambda n, c0=0: b("bl", c0, c0 + n)
+    one = b("onesb", 0, 128, 1, 0, 1)
+
+    dma("y", "ld0", b("tp")[0], T.tops[:], [], ["tp"])
+    dma("y", "ld1", b("xb")[0], T.x0[:], [], ["xb"])
+    dma("y", "ld2", b("KI")[0], T.kids[:], [], ["KI"])
+    dma("s", "ld4", b("thi", 0, 128, 1, 0, 8)[0], T.th[:], [], ["thi"])
+    ms(b("A", V0, W), 0.0)
+    ms(b("A", W, WIN), 4096.0)
+    dma("y", "ld3", b("A", 0, V0)[0], T.a0[:], [], ["A"])
+    ms(b("onesb"), 1.0)
+    ms(b("zf"), 0.0)
+    ms(b("zb"), 0.0)
+    for k in range(2):
+        ms(b("come%d" % k, 64, 80, key="come%dz" % k), 0.0)
+    for k in range(4):
+        ms(b("msg%d" % k, 0, CAP), 0.0)
+    io(b("cio"), [[128, 13]], 0, 1)
+    io(b("ci"), [[1, 128]], 0, 0)
+    asel(b("idb"), b("onesb", 0, 128), [[-1, 128]], OP.is_equal, 0.0, 0, 1)
+    asel(b("EE", p1=16), b("onesb", 0, 128, 1, 0, 16), [[0, 8], [-1, 16]], OP.is_equal, 0.0, 0, 1)
+    asel(b("ipb"), b("onesb", 0, 136), [[-16, 8], [-1, 17]], OP.is_equal, 0.0, 1, 1)
+    io(b("kcf", 0, 136, key="kcf0"), [[0, 8], [128, 17]], 64, 0, True)
+    io(b("kcf", 136, 272, key="kcf1"), [[0, 8], [128, 17]], 0, 0, True)
+    io(b("kcf", 272, 408, key="kcf2"), [[0, 8], [1, 17]], 0, 0, True)
+    asel(b("kcg"), b("kcf", key=["kcf0", "kcf1", "kcf2"]), [[0, 24], [1, 17]], OP.not_equal, BIG, 0, 0)
+    asel(b("sel2"), b("onesb", 0, 8), [[-16, 8]], OP.is_ge, 0.0, 0, 1)
+    asel(b("selb"), b("sel2"), [[16, 8]], OP.is_ge, 0.0, 15, -1)
+    io(b("pin"), [[0, 8]], 0, 1)
+    io(b("m16"), [[16, 8]], 0, 0)
+    asel(b("RM"), b("zf"), [[0, 16], [1, 17]], OP.not_equal, BIG, 0, 0)
+    io(b("rmi"), [[0, 24], [-1, 16]], 16, 1)
+    asel(b("trib"), b("zb"), [[0, 4], [1, 128]], OP.is_gt, -32.0, 0, -1)
+    io(b("kpat"), [[0, 24], [1, 16]], 1, 0, True)
+    asel(b("tri"), b("onesb", 0, 128), [[1, 128]], OP.is_gt, 0.0, 0, -1)
+    asel(b("RM2"), b("zf", 0, 128), [[0, 8], [1, 16]], OP.not_equal, BIG, 0, 0)
+
+    ms(b("C", V0, WIN), 4095.0)
+    for k in range(11):
+        ts(b("bt", 13 * k, 13 * k + 13, key="bt"), b("cio"), k, OP.logical_shift_right, 1, OP.bitwise_and)
+    ts(b("bb"), b("bt"), 2.0, OP.mult, -1.0, OP.add)
+    cp(b("bl"), b("ci"))
+    cp(b("tu"), b("tp"))
+    cp(b("topf", 0, 8, key="topf"), b("tp"))
+    for k in range(16):
+        cp(b("xrep", k, 2048, 16, key="xr"), b("xb"))
+    for k in range(16):
+        act(b("R", k, 2048, 16, key="R"), b("idb"), AF.Copy, 0.0, -1.0)
+    for q in range(13):
+        mm(b("pb%d" % (4 + q // 4), 128 * (q % 4), 128 * (q % 4) + 128, 1, 0, 11), b("bb", q, 143, 13), b("idb"))
+    for h in range(4):
+        n = 512 if h < 3 else 128
+        act(b("bs", 512 * h, 512 * h + n, 1, 0, 11, key="bs%d" % h), b("pb%d" % (4 + h), 0, n, 1, 0, 11), AF.Copy)
+
+    def table(h):
+        n = 512 if h < 3 else 128
+        mm(b("pb%d" % (4 + h), 0, n), b("EE", p1=11), b("bs", 512 * h, 512 * h + n, 1, 0, 11, key="bs%d" % h))
+        act(b("Tb", 512 * h, 512 * h + n), b("pb%d" % (4 + h), 0, n), AF.Copy)
+
+    def consts_a():
+        cp(b("idf"), b("ipb"))
+        ts(b("hc", 0, 136, key="hc0"), b("ipb"), -16.0, OP.mult)
+        cp(b("hc", 136, 272, key="hc1"), b("ipb"))
+        ts(b("f16p"), b("ipb"), 16.0, OP.mult)
+        cp(b("kcb"), b("kcg"))
+        ts(b("bk", 0, 8, key="bk0"), b("selb"), 4096.0, OP.mult)
+        ts(b("bk", 8, 16, key="bk1"), b("selb"), 4096.0, OP.mult)
+
+    def consts_b():
+        ts(b("iv"), b("pin"), 4, OP.logical_shift_right, 1, OP.bitwise_and)
+        for j, m in enumerate((-1.0, -16.0, 1.0, float(FAR))):
+            ts(b("sb", 8 * j, 8 * j + 8, key="sb%d" % j), b("selb"), m, OP.mult)
+        ts(b("rmi"), b("rmi"), 15, OP.bitwise_and)
+        cp(b("mO"), b("iv", 0, 1))
+        ts(b("mE"), b("iv", 0, 1), -1.0, OP.mult, 1.0, OP.add)
+        ts(b("rmask"), b("rmi"), 0.0, OP.is_equal)
+        ts(b("pr"), b("pin"), 15, OP.bitwise_and)
+        ms(b("one8"), 1.0)
+        ms(b("Dv", 8, 16, key="Dv1"), 1.0)
+        tt(b("iGL"), b("pr"), b("m16"), OP.add)
+        ts(b("p128"), b("pin", 0, 1), 128.0, OP.add)
+        ts(b("m128"), b("pin", 0, 1), -1.0, OP.mult, -128.0, OP.add)
+        ts(b("dmp"), b("iGL"), float(DUMP), OP.add)
+        ts(b("dmp16"), b("iGL"), float(DUMP - 1600), OP.add)
+        for k in range(4):
+            ts(b("nGL", 8 * k, 8 * k + 8, key="nGL%d" % k), b("iGL"), float(V0 + L * k), OP.add)
+
+    def consts_c():
+        cp(b("thf", 0, 128, 1, 0, 8), b("thi", 0, 128, 1, 0, 8))
+        mm(b("pb3", 0, 8), b("thf", 0, 128, 1, 0, 8), b("idf", 1, 9, 1, 0, 8))
+        cp(b("lim"), b("pb3", 0, 8))
+        ts(b("lim1"), b("lim"), 1.0, OP.add)
+
+    def consts_d():
+        tt(b("Di"), b("idb"), b("ci"), OP.mult)
+        ts(b("I128"), b("idb"), 128.0, OP.mult)
+        for s in range(4):
+            ts(b("GN", 128 + 128 * s, 256 + 128 * s, key="GN%d" % s), b("idb"), float(128 * (s - 24)), OP.mult)
+        ts(b("GE", 128, 256, key="GE1"), b("idb"), 4096.0, OP.mult)
+        ts(b("m1c"), b("idb"), -1.0, OP.mult)
+
+    def x_forms(src):
+        act(b("xs"), src, AF.Identity, MAGIC)
+        act(b("xp"), src, AF.Identity, 256.0)
+
+    def turn_x():
+        mm(b("pb3", 0, 128), b("xb"), b("idb"))
+        mm(b("pb1", 384, 512), b("idb"), b("xb"))
+        act(b("xT"), b("pb3", 0, 128), AF.Copy)
+
+    def preload_x(cs):
+        for c in cs:
+            mm(b("pb%d" % (4 + c)), b("xT"), b("R", 512 * c, 512 * c + 512), True, False)
+
+    def codes_masked(d):
+        for m in "EO":
+            if d == "cod":
+                ts(b(d + m), b(d), b("m" + m), OP.mult)
+            else:
+                act(b(d + m), b(d), AF.Copy, 0.0, b("m" + m))
+
+    def equal(d, bank, h):
+        mm(b(bank), b("idb"), b("trib"), True, False)
+        for j in range(4):
+            w = 4 * h + j
+            p = w // 2 * 32
+            if j == 2:
+                need("t", [bank], [])
+            mm(b(bank, 128 * j, 128 * j + 128), b(d, 0, 128, 1, p, p + 32), b(d + ("O" if w % 2 else "E"), 0, 128, 1, p, p + 32),
+               False, j == 3)
+
+    def count(eq, mask, o):
+        for w in range(8):
+            mm(b(o[0], o[1] + w, o[1] + w + 1), b(eq, 128 * w, 128 * w + 128, key=eq + str(w // 4)), b(mask, w, w + 1))
+
+    def to_lists(ex, n, o, scales):
+        for j in range(n):
+            mm(b(o[0], o[1] + 8 * j, o[1] + 8 * j + 8), b(ex, 128 * j, 128 * j + 128), b("sb", 8 * scales[j], 8 * scales[j] + 8, key="sb%d" % scales[j]))
+
+    def expand(ex, src, n):
+        tt(b(ex, 0, 128 * n), ind(src, bl(8 * n)), b("rmask", 0, 128 * n), OP.mult)
+
+    def front_v(s, vu):
+        ts(b("cvu"), ind(b("KI") if s == 0 else b("C", 0, WIN), vu), float(E1), OP.min)
+
+    def front(s, vu):
+        act(b("r"), ind(b("C", 0, WIN), vu), AF.Relu, float(E1), -1.0)
+        act(b("y"), b("r"), AF.Identity, MAGIC, 1.0 / 127.95)
+        act(b("h8"), b("y"), AF.Identity, -8 * MAGIC, 8.0)
+        act(b("Fm"), b("r"), AF.Sign)
+        mm(b("pb0", 272, 408), one, b("kcb", 272, 408, 1, 0, 1), True, False)
+        mm(b("pb0", 272, 408), b("Fm"), b("f16p"), False, True)
+        mm(b("pb0", 0, 272), one, b("kcb", 0, 272, 1, 0, 1), True, False)
+        mm(b("pb0", 0, 136), b("r"), b("idf"), False, False)
+        mm(b("pb0", 0, 272), b("h8"), b("hc", key=["hc0", "hc1"]), False, False)
+
+    def gather(c):
+        act(b("ag", 512 * c, 512 * c + 512, key="ag%d" % c), ind(b("A", 0, WIN), b("dvu", 32 * c, 32 * c + 32)), AF.Copy)
+
+    def less_x(c):
+        mm(b("pb%d" % (4 + c)), b("idb"), b("ag", 512 * c, 512 * c + 512, key="ag%d" % c), False, True)
+
+    def away(c):
+        act(b("ab2", 512 * c, 512 * c + 512, key="ab2%d" % c), b("pb%d" % (4 + c)), AF.Abs)
+
+    def sums2(l0, l1, cs):
+        for k in range(16):
+            mm(b("pb0", k, 128, 16, l0, l1), b("ab2", 16 * l0 + k, 16 * l1, 16, key=["ab2%d" % c for c in cs]), b("selb"))
+
+    def step(s, vu, tv):
+        t = s % ST
+        n0 = V0 + L * s
+        vf = b(tv, 0, 8)
+        if s == 0:
+            front_v(0, vu)
+            for h in range(4):
+                table(h)
+            cp(b("C", 0, V0), b("KI"))
+            consts_a()
+        if s != 2:
+            front(s, vu)
+        if s == 0:
+            turn_x()
+        if s != 2:
+            preload_x((0, 1, 2, 3))
+        for j, (l0, n) in enumerate(PIECES):
+            c0, c1 = 16 * l0, 16 * (l0 + n)
+            dj = b("df", c0, c1, key="df%d" % j)
+            if s == 2:
+                tt(dj, ind(b("xi"), bl(n, l0)), b("ag", c0, c1, key="ag%d" % (l0 // 32)), OP.subtract)
+                if j == 0:
+                    cp(b("xb"), b("xi"))
+            else:
+                tt(dj, ind(b("A", 0, WIN), b("cvu", l0, l0 + n)), b("xrep", c0, c1, key="xr"), OP.subtract)
+            act(dj, dj, AF.Abs)
+            if s == 2 and j == 0:
+                turn_x()
+        if s != 2:
+            act(b("cod"), ind(b("Tb", 0, WIN), vu), AF.Copy)
+            act(b("cvf"), ind(b("C", 0, WIN), vu), AF.Copy)
+        for l0, l1, js in ((0, 64, (0, 1)), (64, 96, (2,)), (96, 128, (3, 4))):
+            for k in range(16):
+                mm(b("pb0", 1 + k, 272, 17, l0, l1), b("df", 16 * l0 + k, 16 * l1, 16, key=["df%d" % j for j in js]),
+                   b("bk", key=["bk0", "bk1"]), False, k == 15)
+        if t == 1:
+            tt(b("rest"), b("Sf"), b("an"), OP.is_lt)
+            tt(b("ov"), b("Sf"), b("anr0"), OP.is_lt)
+            act(b("nonr"), b("rest"), AF.Identity, 1.0, -1.0)
+            act(b("nov"), b("ov"), AF.Identity, b("p128"), b("m128"))
+            mm(b("pb1", 96, 104), b("tri"), b("ov"))
+        if s == 0:
+            consts_b()
+        if s in (0, 2):
+            x_forms(b("xb"))
+        if s == 2:
+            for k in range(16):
+                cp(b("xrep", k, 2048, 16, key="xr"), b("xb"))
+        tt(b("X3", 8, 16, key="X3c"), vf, b("dmp"), OP.subtract)
+        tt(b("X3", 16, 24, key="X3b"), b("nGL", 8 * s, 8 * s + 8, key="nGL%d" % s), vf, OP.subtract)
+        act(b("v16"), vf, AF.Identity, -1600.0)
+        scan(b("m1"), b("RM"), b("pb0", 0, 272), OP.max, OP.min)
+        cp(b("m1e"), b("m1", 16, 272, 17))
+        ts(b("dec"), b("m1e"), 127, OP.bitwise_and)
+        expand("ex", b("dec"), 2)
+        if s == 2:
+            preload_x((0, 1))
+        to_b = b("pb1", 0, 8)
+        mm(to_b, b("ex", 0, 128), b("sb", 0, 8, key="sb0"), True, False)
+        mm(to_b, b("ex", 128, 256), b("sb", 8, 16, key="sb1"), False, True)
+        if s == 2:
+            preload_x((2, 3))
+        else:
+            codes_masked("cod")
+            equal("cod", "pb2", 0)
+            equal("cod", "pb3", 1)
+        tt(b("cand", 1, 272), b("m1", 0, 271), b("pb0", 1, 272), OP.max)
+        ts(b("bu"), to_b, 1600.0, OP.add)
+        ts(b("dvu"), ind(b("C", 0, WIN), b("bu")), float(E1), OP.min)
+        tt(b("X3", 0, 8, key="X3a"), to_b, b("v16"), OP.subtract)
+        tt(b("bd"), to_b, b("dmp16"), OP.subtract)
+        act(b("abm"), ind(b("A", 0, WIN), b("bu")), AF.Identity, -0.5)
+        act(b("am4"), b("abm"), AF.Identity, -3.5)
+        act(b("ap4"), b("abm"), AF.Identity, 4.5)
+        gather(0)
+        if s != 2:
+            act(b("eqa", 0, 512, key="eqa0"), b("pb2"), AF.Relu, -10.0)
+            act(b("eqa", 512, 1024, key="eqa1"), b("pb3"), AF.Relu, -10.0)
+        scan(b("m2", 1, 272), b("RM", 1, 272), b("cand", 1, 272), OP.max, OP.min)
+        cp(b("m2e"), b("m2", 16, 272, 17))
+        ts(b("dec2"), b("m2e"), 127, OP.bitwise_and)
+        expand("ex2", b("dec2"), 2)
+        ts(b("eb"), b("m1e", 0, 8), 12, OP.logical_shift_right)
+        ts(b("kk", 0, 8, key="kk0"), b("m1e", 0, 8), 7, OP.logical_shift_right, 31, OP.bitwise_and)
+        ts(b("kq"), b("m2e", 0, 8), 7, OP.logical_shift_right, 31, OP.bitwise_and)
+        to_q = b("pb1", 8, 16)
+        mm(to_q, b("ex2", 0, 128), b("sb", 0, 8, key="sb0"), True, False)
+        mm(to_q, b("ex2", 128, 256), b("sb", 8, 16, key="sb1"), False, True)
+        scan(b("k0s"), b("RM", 0, 136), b("pb0", 272, 408), OP.max, OP.min)
+        ts(b("qu"), to_q, 1600.0, OP.add)
+        if s != 2:
+            count("eqa", "nonr" if t == 1 else "one8", ("pb1", 16))
+        tt(b("sm"), ind(b("A", 0, WIN), b("qu")), b("abm"), OP.add)
+        if s == 0:
+            consts_c()
+        ym = b("pb2", 384, 512)
+        ts(ym, b("sm"), 0.5, OP.mult, MAGIC, OP.add)
+        tt(b("dM"), b("xs"), ym, OP.subtract)
+        tt(b("pb1", 256, 384), b("pb1", 384, 512), b("am4"), OP.max)
+        tt(b("hv"), b("pb1", 256, 384), b("ap4"), OP.min)
+
+        less_x(0)
+        act(b("bod"), ind(b("Tb", 0, WIN), b("bu")), AF.Copy)
+        act(b("nrm"), b("k0s", 16, 136, 17), AF.Relu, -16.0)
+        codes_masked("bod")
+        act(b("absM"), b("dM"), AF.Abs)
+        mm(b("pb1", 24, 32), b("absM"), b("selb"))
+        gather(1)
+        less_x(1)
+        equal("bod", "pb3", 0)
+        away(0)
+        if s != 2:
+            equal("bod", "pb4", 1)
+        gather(2)
+        act(b("Mb"), ym, AF.Identity, -MAGIC)
+        away(1)
+        gather(3)
+        act(b("dvf"), ind(b("C", 0, WIN), b("bu")), AF.Copy)
+
+        ac = b("gm3", 8, 16, key="ac")
+        if s == 2:
+            cp(ac, b("act0"))
+        else:
+            tt(ac, b("pb1", 16, 24), b("one8" if s == 0 else "nonr"), OP.is_lt)
+        em = b("pb1", 24, 32)
+        ah, am = b("gm3", 0, 8, key="ah"), b("gm3", 16, 24, key="am")
+        tt(b("hm"), em, b("eb"), OP.min)
+        tt(b("he"), em, b("eb"), OP.is_ge)
+        tt(b("nn"), b("lim"), b("hm"), OP.is_lt)
+        tt(b("T0"), b("lim1"), b("hm"), OP.min)
+        tt(b("an"), b("nn"), ac, OP.mult)
+        tt(b("Tt"), b("T0"), ac, OP.mult)
+        tt(b("ah0"), ac, b("an"), OP.subtract)
+        tt(b("k2"), b("an"), b("k0s", 16, 136, 17), OP.mult)
+        tt(ah, b("ah0"), b("he"), OP.mult)
+        tt(b("anr0"), b("an"), b("nrm"), OP.mult)
+        tt(am, b("ah0"), ah, OP.subtract)
+        if s == 0:
+            cp(b("act0"), ac)
+        tt(b("k1"), am, b("kk", 0, 8, key="kk0"), OP.mult)
+        tt(b("kk", 16, 24, key="kk2"), am, b("kq"), OP.mult)
+        tt(b("kk", 8, 16, key="kk1"), b("k1"), b("k2"), OP.add)
+        tt(b("gm3", 24, 32, key="ax"), b("an"), b("anr0"), OP.subtract)
+        tt(b("oh"), ind(b("kk", key=["kk0", "kk1", "kk2"]), bl(24)), b("kpat"), OP.is_equal)
+        if s == 0:
+            consts_d()
+        ohb, ohn, ohe = b("oh", 0, 128), b("oh", 128, 256), b("oh", 256, 384)
+        i8 = b("GE", 128, 256, key="GE1")
+        mm(b("pb2", 256, 384), ohb, i8)
+        mm(b("pb2", 0, 128), ohn, i8, True, False)
+        mm(b("pb2", 0, 128), ohe, i8, False, True)
+        mm(b("pb2", 128, 256), ohn, b("GN", 128 + 128 * s, 256 + 128 * s, key="GN%d" % s), True, False)
+        mm(b("pb2", 128, 256), ohn, b("Di"), False, False)
+        mm(b("pb2", 128, 256), ohe, b("m1c"), False, True)
+        less_x(2)
+        act(b("gx"), ind(b("gm3", 16, 32, key=["am", "ax"]), bl(16)), AF.Copy)
+        away(2)
+        if t == 1:
+            send_rank()
+        tt(b("gm"), ind(b("gm3", 0, 24, key=["ah", "ac", "am"]), bl(24)), b("rmask"), OP.mult)
+        to_lists("gm", 3, ("pb1", 32), (2, 2, 2))
+        if t == 1:
+            to_lists("exP", 1, ("pb1", 80), (2,))
+        mm(b("pb5", 0, 128), b("gx", 0, 128), b("idb"))
+        mm(b("pb5", 128, 256), b("gx", 128, 256), b("idb"))
+        less_x(3)
+        sums2(0, 96, (0, 1, 2))
+        away(3)
+        sums2(96, 128, (3,))
+        if s == 2:
+            equal("bod", "pb4", 1)
+        tt(b("w3"), b("cvf"), b("pb2", 256, 384), OP.max)
+        tt(b("wal"), b("cvf"), b("pb2", 0, 128), OP.max)
+        act(b("pb6", 0, 128), b("w3"), AF.Relu, 8 * 4095.0, -8.0)
+        tt(b("ral"), b("wal"), b("pb2", 128, 256), OP.add)
+        act(b("pb7", 0, 128), b("pb2", 0, 128), AF.Relu, 4095.0, -1.0)
+        act(b("eqb", 0, 512, key="eqb0"), b("pb3"), AF.Relu, -10.0)
+        act(b("eqb", 512, 1024, key="eqb1"), b("pb4"), AF.Relu, -10.0)
+        tt(b("g3"), b("pb1", 32, 56), b("X3", key=["X3a", "X3b", "X3c"]), OP.mult)
+        tt(b("pb5", 256, 384), b("pb5", 0, 128), b("Mb"), OP.mult)
+        tt(b(tv, 8, 16, key=tv + "u"), b("g3", 8, 16), b("dmp"), OP.add)
+        tt(b("t2"), b("pb5", 128, 256), b("xb"), OP.mult)
+        cp(b("uvu"), b(tv, 8, 16, key=tv + "u"))
+        tt(b("Dv", 0, 8, key="Dv0"), b("g3", 0, 8), b("g3", 16, 24), OP.add)
+        scatter(b("C"), b("uvu"), b("ral"))
+        if t == 1:
+            send_list(s - 1)
+        tt(b("pb5", 384, 512), b("pb6", 0, 128), b("dvf"), OP.add)
+        tt(b("rsp"), b("w3"), b("pb5", 384, 512), OP.min)
+
+        scan(b("fsm"), b("RM2"), b("pb0", 0, 128), OP.max, OP.min)
+        tt(b("Sf"), b("fsm", 15, 128, 16), b("Tt"), OP.is_lt)
+        act(b("exU"), ind(b("Sf"), bl(8)), AF.Copy)
+        if t == 1:
+            tt(b("ov"), b("Sf"), b("anr0"), OP.is_lt)
+            ts(b("nov"), b("ov"), 0.0, OP.is_equal, b("p128"), OP.mult)
+            mm(b("pb3", 8, 16), b("tri"), b("ov"))
+        expand("exS", b("Sf"), 1)
+        if t == 1:
+            tt(b("pos"), b("pb3", 8, 16), b("nov"), OP.max)
+            expand("exP", b("pos"), 1)
+        tt(b("hF"), b("Sf"), ah, OP.is_lt)
+        mm(b("pb1", 56, 64), one, b("onesb", 0, 8, 1, 0, 1), True, False)
+        mm(b("pb1", 56, 64), b("exS"), b("sb", 0, 8, key="sb0"), False, True)
+        mm(b("pb1", 64, 72), b("exS"), b("sb", 24, 32, key="sb3"))
+        if t == 1:
+            to_lists("exP", 1, ("pb1", 80), (2,))
+            tt(b("An"), b("pb5", 256, 384), b("t2"), OP.add)
+            tt(b("cb"), b("pb7", 0, 128), b("cvf"), OP.max)
+            send_list(s)
+        count("eqb", "hF", ("pb3", 0))
+        if t == 0:
+            tt(b("An"), b("pb5", 256, 384), b("t2"), OP.add)
+            tt(b("cb"), b("pb7", 0, 128), b("cvf"), OP.max)
+        tt(b("q1"), b("pb1", 56, 72), b("Dv", key=["Dv0", "Dv1"]), OP.mult)
+        tt(b("vf", 0, 16, key="vf"), b("q1"), b(tv, 0, 16, key=[tv, tv + "u"]), OP.add)
+        cp(b("vu2"), b("vf", 0, 16, key="vf"))
+        scatter(b("CW", key="C"), b("vu2", 8, 16), b("rsp"))
+        mm(b("pb2", 128, 256), b("exU"), b("GE", 128, 256, key="GE1"), True, False)
+        mm(b("pb2", 128, 256), b("exU"), b("m1c"), False, True)
+        mm(b("pb2", 0, 128), one, one, True, False)
+        mm(b("pb2", 0, 128), b("exU"), b("m1c"), False, True)
+        tt(b("h1"), b("pb3", 0, 8), b("hF"), OP.is_lt)
+        expand("exH", b("h1"), 1)
+        tt(b("C", n0, n0 + L), b("pb2", 128, 256), b("cb"), OP.max)
+        to_lists("exH", 1, ("pb1", 72), (2,))
+        if s == 3:
+            dma("y", "ld5", T.yc[:], b("C", 0, W)[0], ["C"], ["yc"])
+        tt(b("A", n0, n0 + L), b("pb2", 0, 128), b("An"), OP.mult)
+        tt(b("oA"), b("pb1", 72, 80), b("bd"), OP.mult)
+        if s < 3:
+            front_v(s + 1, b("tu") if s == 1 else b("vu2", 0, 8))
+        tt(b("oA"), b("oA"), b("dmp"), OP.add)
+        if t == 1:
+            tt(b("nF"), b("Sf"), b("an"), OP.is_lt)
+        cp(b("oAu"), b("oA"))
+        scatter(b("A"), b("oAu"), b("hv"))
+        if s == 3:
+            dma("y", "ld6", T.ya[:], b("A", 0, W)[0], ["A"], ["ya"])
+        if t == 1:
+            tt(b("rest2"), b("rest"), b("nF"), OP.add)
+            act(b("nonr2"), b("rest2"), AF.Identity, 1.0, -1.0)
+
+    def send_rank():
+        tt(b("pos"), b("pb1", 96, 104), b("nov"), OP.max)
+        expand("exP", b("pos"), 1)
+
+    def send_list(s):
+        h = hops(T, topo, rank, s)
+        m = "msg%d" % s
+        cp(b("posu"), b("pb1", 80, 88))
+        scatter(b(m), b("posu"), b("xp"))
+        need("g", [m], [])
+        n = engines_of(topo, core, h[1])
+        rid, pid = topo.addr(h[1], core)
+        if len(h) == 3:
+            to, sem = T["rl%d" % s][:, 0:CAP], T.sem["rr%d" % s]
+        else:
+            to, sem = T["come%d" % (s // ST)][:, CAP * (s % ST):CAP * (s % ST) + CAP], T.sem["in%d" % s]
+        g.remote_dma(to, T[m][:, 0:CAP], sem, T.sem["ls%d" % s], pid, rid, emask(topo, core, h[1], n))
+
+    for s in range(ST * RO):
+        h = hops(T, topo, (rank - 1 - s % (NR - 1)) % NR, s)
+        n = engines_of(topo, h[-2], h[-1])
+        wr["come%d_%d" % (s // ST, s % ST)] = ("remote", "in%d" % s, n, {"in%d" % s: n})
+        cnt["in%d" % s] = n
+
+    def round_end(s):
+        cm = "come%d" % (s // ST)
+        mm(b("pb3", 16, 24), b("tri"), b("rest2"), True, False)
+        mm(b("pb3", 16, 24), b("I128"), b("nonr2"), False, True)
+        tt(b("dM"), ind(b("A", 0, WIN), b("vu2", 0, 8)), b("xb"), OP.subtract)
+        act(b("ad"), b("dM"), AF.Abs)
+        cp(b("nrs"), b("pb3", 16, 24))
+        expand("exN", b("nrs"), 1)
+        to_lists("exN", 1, ("pb1", 88), (2,))
+        if s == 1:
+            front(2, b("tu"))
+            act(b("cvf"), ind(b("C", 0, WIN), b("tu")), AF.Copy)
+            for c in range(4):
+                o, a = b("ag", 512 * c, 512 * c + 512, key="ag%d" % c), ind(b("A", 0, WIN), b("cvu", 32 * c, 32 * c + 32))
+                if c < 3:
+                    act(o, a, AF.Copy)
+                else:
+                    cp(o, a)
+        ts(b("msk"), b(cm, 0, CAP, key=cm + "_0"), 0.5, OP.is_gt)
+        op("v", lambda e: e.tensor_reduce(b("n0")[0], b("msk")[0], AxisListType.X, OP.add), ["msk"], ["n0"])
+        ts(b("cd"), b("n0"), -1.0, OP.mult, float(CAP), OP.add)
+        ts(b("ge"), b("pb1", 88, 96), b("n0"), OP.is_ge, b("cd"), OP.mult)
+        tt(b("idx"), b("pb1", 88, 96), b("ge"), OP.add)
+        ts(b("iu"), b("idx"), 64.0, OP.min)
+        tt(b("hx"), ind(b(cm, key=[cm + "_0", cm + "_1", cm + "z"]), b("iu")), b("ad"), OP.max)
+        ts(b("xi"), b("hx"), 255, OP.bitwise_and)
+
+    for s in range(4):
+        if s % ST == 0:
+            step(s, b("tu"), "topf")
+        else:
+            step(s, b("vu2", 0, 8), "vf")
+            round_end(s)
+    cp(b("xb"), b("xi"))
+    dma("y", "ld7", T.yx[:], b("xb")[0], ["xb"], ["yx"])
+    for n in sorted(cnt):
+        if cnt[n] and know["g"].get(n, 0) < cnt[n]:
+            g.wait_ge(T.sem[n], cnt[n])
+    for s in range(4):
+        g.wait_ge(T.sem["ls%d" % s], engines_of(topo, core, hops(T, topo, rank, s)[1]))

@@ -4,11 +4,13 @@ V0, L, ST, RO, CAP, NR = 1024, 128, 2, 2, 32, 8
 W = V0 + RO * ST * L
 E1 = W
 WIN = W + 8
-DUMP = WIN
-FAR = 2048
 BIG = float(2 ** 30)
-MAGIC = float(2 ** 23)
-PIECES = [(0, 32), (32, 32), (64, 32), (96, 16), (112, 16)]
+MAGIC = float(3 * 2 ** 22)
+M = 2048.0
+P1 = [4, 4, 4, 2, 1, 1]
+P2S = [(0, "pb7"), (4, "pb0")]
+P2V = [4, 2, 1, 1]
+WAKE, GAT, SCA = 220.0, 1.5, 3.0
 
 SLOT = {}
 SIZE = {"F": 0, "B": 0, "I": 0, "U": 0}
@@ -20,20 +22,21 @@ def _s(kind, **kw):
         SIZE[kind] += (w + 15) // 16 * 16
 
 
-_s("B", A=1680, xrep=2048, df=2048, ag=2048, ab2=2048, xb=128, xT=128, R=2048, onesb=512, zb=512, idb=128, ipb=136,
-   hc=272, f16p=136, selb=8, sel2=8, bk=16, sb=32, tri=128, trib=512, kcb=408, rmask=384, Di=128, I128=128, GN=640, GE=256,
-   m1c=128, bb=143, bs=1664, EE=128, Tb=1664, h8=128, Fm=128, cod=128, codE=128, codO=128, bod=128, bodE=128, bodO=128,
-   eqa=1024, eqb=1024, ex=256, ex2=256, oh=384, gx=256, gm=384, exS=128, exU=128, exH=128, exP=128, exN=128, absM=128, Mb=128,
-   An=128, hv=128, hF=8, ov=8, nov=8, rest=8, rest2=8, nonr=8, nonr2=8, one8=8, nF=8)
-_s("F", CW=FAR + 1680, idf=136, zf=272, RM=272, RM2=128, kcf=408, kcg=408, kpat=384, iGL=8, dmp=8, dmp16=8, lim=8, lim1=8, thf=128, topf=16,
-   r=128, y=128, cvf=128, dvf=128, m1=272, m2=272, cand=272, k0s=136, abm=128, sm=128, ym=128, xs=128, xp=128, dM=128,
-   hm=8, he=8, nn=8, T0=8, Tt=8, act0=8, an=8, ah0=8, k1=8, k2=8, wal=128, ral=128, w3=128, f3=128, t3=128, v16=8, nv=8,
-   rsp=128, c0=128, cb=128, t1=128, t2=128, X3=24, g3=24, gm3=32, Dv=16, q1=16, vf=16, fsm=128, Sf=8, anr0=8, nrm=8, h1=8,
-   oA=8, pos=8, nrs=8, am4=128, ap4=128, nGL=32, ge=8, idx=8, msk=32, n0=1, cd=1, ad=128, mE=1, mO=1, bd=8, p128=1, m128=1)
-_s("I", KI=1024, tp=8, thi=128, ci=128, rmi=384, pin=8, pr=8, m16=8, cio=13, bt=143, m1e=16, dec=16, eb=8, kk=24, m2e=16,
-   dec2=16, kq=8, hx=128, xi=128, iv=8)
-_s("U", bl=128, tu=8, cvu=128, dvu=128, bu=8, qu=8, uvu=8, vu2=16, oAu=8, posu=8, iu=8)
-SLOT["C"] = ("arF", SLOT["CW"][1] + FAR, 1680)
+_s("B", AW=128 + WIN, xrep=2048, D=2048, Dab=2048, ag=2048, AN=272, xP=128, ones=144, B=144, sel2=8, selb=8, bones=128, lo=128, lt=128,
+   ld=128, nl8=128, I=128, nI=128, I63=128, nI63=128, nI128=128, nI8=128, IM=128, sh=128, cr=1536, cnt0=136, emc=128, tab=128,
+   emp=128, oh=256, dd=256, cl=128, absM=128, hv=128, E=1088, fl0=32, fl1=32, rest2=8)
+_s("F", CW=128 + WIN, iot=WIN, RW=416, CN=272, idf=128, dm=128, RM=128, RM2=128, tr=288, dl=128, rr=272, r0=128, e=128, cand=128, pay=128,
+   row=144, r17=144, clv=136, clb=136, zv=136, zb=136, w3=128, w4=128, rsp=128, rpre=128, dvf=128, es=128, fs=128, xm=128, xp=128,
+   dM=128, ad=128, thf=128, thx=128, lim=8, lim1=8, jL=8, cj=8, topf=8, nL=32, acB0=32, acB1=32, nac0=8, nac1=8, rB=16, W4=32, G1=16, G2=16,
+   UU=32, U1=8, U4=32, Tt4=32, FL=40, nfl=32, TH=32, coef=48, prod=48, d0=64, d1=64, s2=48, sp=8, nonr=8, one8=8, hf=8, pz=8, nrs=8, ge=8,
+   idx=8, msk=32, n0=1, cd=1, r7=1, hi=1, p128=1, pf=1, tmp=16, tmp2=16, tmp3=16)
+_s("I", KI=WIN, tp=8, thi=128, pin=16, pa=16, pb=16, ci=128, ri=128, dec=16, dk=16, hx=128, xi=128)
+_s("U", tu=8, tu2=16, cvu=128, dvu=128, bu=8, bu2=16, du=16, ku=16, uvu0=8, uvu1=8, lu=24, vu2=16, spu=8, oAu=8, posu=8, iu=8,
+   plist=128, lperm=8, l17=10, lend=8, lsel=8, lF=2, lr=2, lz=2, lg=2, lfl=4)
+SLOT["C"] = ("arF", SLOT["CW"][1] + 128, WIN)
+SLOT["A"] = ("arB", SLOT["AW"][1] + 128, WIN)
+SLOT["cvf"] = ("arF", SLOT["RW"][1] + 16, 128)
+SLOT["xb"] = ("arB", SLOT["AN"][1] + 128, 128)
 
 SCRATCH = {"arF": ("sbuf", [128, SIZE["F"]], "float32"), "arB": ("sbuf", [128, SIZE["B"]], "bfloat16"),
            "arI": ("sbuf", [128, SIZE["I"]], "int32"), "arU": ("sbuf", [128, SIZE["U"]], "uint16")}
@@ -46,6 +49,7 @@ for _k in range(2):
     SCRATCH["come%d" % _k] = ("sbuf", [128, 80], "float32")
 SEMAPHORES = (["qv", "qs", "qt", "qg"] + ["in%d" % k for k in range(4)] + ["rr%d" % k for k in range(4)] + ["ls%d" % k for k in range(4)]
               + ["ld%d" % k for k in range(8)])
+ORDER = {}
 
 
 def emask(topo, src, dst, n):
@@ -88,18 +92,518 @@ def relay(g, core, T, topo):
                 g.wait_ge(T.sem["ls%d" % s], engines_of(topo, h[1], h[2]))
 
 
+def order_calls(ops):
+    n = len(ops)
+    wr, rd, pre = {}, {}, []
+    for i, o in enumerate(ops):
+        d = {}
+        for k in o["R"]:
+            if k in wr:
+                d[wr[k]] = WAKE
+            if k[:2] == "pb":
+                for j in rd.get(k, []):
+                    d[j] = max(d.get(j, 0.0), WAKE if ops[j]["q"] != o["q"] else 0.0)
+        for k in o["W"]:
+            for j in rd.get(k, []) + ([wr[k]] if k in wr else []):
+                near = ops[j]["q"] == o["q"] == "t" and j == wr.get(k)
+                d[j] = max(d.get(j, 0.0), 0.0 if near else WAKE)
+        for k in o["R"]:
+            rd.setdefault(k, []).append(i)
+        for k in o["W"]:
+            wr[k] = i
+            rd[k] = []
+        d.pop(i, None)
+        pre.append(d)
+    way = [0.0] * n
+    for i in range(n - 1, -1, -1):
+        way[i] += ops[i]["c"] + ops[i]["lag"]
+        for j, w in pre[i].items():
+            way[j] = max(way[j], way[i] + w)
+    busy, start, end = {}, [0.0] * n, [0.0] * n
+    for i in sorted(range(n), key=lambda i: (-way[i], i)):
+        t = max([end[j] + w for j, w in pre[i].items()] + [0.0])
+        c, row = ops[i]["c"], busy.setdefault(ops[i]["q"], [])
+        at = len(row)
+        for m, (a, z) in enumerate(row):
+            if z <= t:
+                continue
+            if t + c <= a:
+                at = m
+                break
+            t = z
+        row.insert(at, (t, t + c))
+        start[i], end[i] = t, t + c + ops[i]["lag"]
+    return sorted(range(n), key=lambda i: (start[i], i))
+
+
 def rank_program(g, core, T, topo):
     rank = T.rank_of(core)
     if rank is None:
         relay(g, core, T, topo)
         return
     eng = {"v": g.vector, "s": g.scalar, "t": g.tensor, "g": g, "y": g.sync}
+    ops = []
+
+    def op(q, call, R, Wk, c, lag=0.0, dma=None):
+        ops.append({"q": q, "call": call, "R": R, "W": Wk, "c": c * 0.83, "lag": lag, "dma": dma})
+
+    def dma(q, sem, out, in_, R, Wk, lag):
+        op(q, lambda e: e.dma_start(out, in_), R, Wk, 60, lag, sem)
+
+    def b(name, c0=0, c1=None, st=1, p1=128, key=None):
+        if name in SLOT:
+            buf, o, w = SLOT[name]
+        else:
+            buf, o, w = name, 0, SCRATCH[name][1][1]
+        c1 = w if c1 is None else c1
+        a = T[buf][0:p1, o + c0:o + c1:st] if st != 1 else T[buf][0:p1, o + c0:o + c1]
+        return (a, key if isinstance(key, list) else [key or name], (c1 - c0 + st - 1) // st, buf[:3])
+
+    def ind(win, off):
+        return (win[0].indirect(off[0]), win[1] + off[1], 16 * off[2], "ind")
+
+    def ks(*refs):
+        return [k for r in refs if isinstance(r, tuple) for k in r[1]]
+
+    def ap(x):
+        return x[0] if isinstance(x, tuple) else x
+
+    def cyc(o, a, f=1.0):
+        if a[3] == "ind":
+            return 70 + GAT * a[2]
+        return max(64, a[2] * (f / 2 if o[3] in ("arB", "arU") and a[3] in ("arB", "arU") and f == 1.0 else f))
+
+    def tt(o, a, c, f):
+        op("v", lambda e: e.tensor_tensor(o[0], a[0], c[0], f), ks(a, c), ks(o), cyc(o, a, 1.01 if "p" in (a[3][0], c[3][0]) else 2))
+
+    def ts(o, a, s1, f0, s2=None, f1=None):
+        if f1 is None:
+            op("v", lambda e: e.tensor_scalar(o[0], a[0], ap(s1), None, f0), ks(a, s1), ks(o), cyc(o, a))
+        else:
+            op("v", lambda e: e.tensor_scalar(o[0], a[0], ap(s1), ap(s2), f0, f1), ks(a, s1, s2), ks(o), cyc(o, a))
+
+    def cp(o, a):
+        op("v", lambda e: e.tensor_copy(o[0], a[0]), ks(a), ks(o), cyc(o, a))
+
+    def scatter(win, off, a):
+        op("v", lambda e: e.tensor_copy(win[0].indirect(off[0]), a[0]), ks(a, off), ks(win), 60 + SCA * a[2])
+
+    def ms(o, v):
+        op("v", lambda e: e.memset(o[0], v), [], ks(o), cyc(o, o))
+
+    def scan(o, a, c, f0, f1):
+        op("v", lambda e: e.tensor_tensor_scan(o[0], a[0], c[0], 0.0, f0, f1), ks(a, c), ks(o), cyc(o, a, 1.01))
+
+    def turn(o, a):
+        op("v", lambda e: e.transpose(o[0], a[0]), ks(a), ks(o), cyc(o, a, 1.01))
+
+    def act(o, a, f, bias=0.0, scale=1.0):
+        op("s", lambda e: e.activation(o[0], a[0], f, bias=ap(bias), scale=ap(scale)), ks(a, scale, bias), ks(o), cyc(o, a, 1.01))
+
+    def mm(o, l, r, start=True, stop=True):
+        op("t", lambda e: e.matmul(o[0], l[0], r[0], start, stop), ks(l, r), ks(o), max(min(64, l[2]), r[2]) * (4 if l[3] == "arF" else 1))
+
+    def mms(o, pairs):
+        for j, (l, r) in enumerate(pairs):
+            mm(o, l, r, j == 0, j == len(pairs) - 1)
+
+    def io(o, pat, base, cm):
+        if o[3] == "arI":
+            op("g", lambda e: e.iota(o[0], pat, base, cm), [], ks(o), 160 + 2 * o[2])
+        else:
+            op("g", lambda e: e.iota(o[0], pat, base, cm, allow_small_or_imprecise_dtypes=True), [], ks(o), 160 + 2 * o[2])
+
+    def asel(o, a, pat, f, fill, base, cm):
+        op("g", lambda e: e.affine_select(o[0], a[0], pat, f, fill, base, cm), ks(a), ks(o), 200 + 2 * o[2])
+
+    def row(j, n=128):
+        return b("cr", 144 * j, 144 * j + n, 1, 1, key="cr%d" % j)
+
+    ONE, JROW, R63, R65, R128, RH, R127, NROW = row(0), row(1), row(2), row(3), row(4), row(5), row(6), 0
+    blocks = lambda t, n: ["%sb%d" % (t, k) for k in range(n)]
+    Cw = lambda s: b("KI", key=["KI", "KIe"]) if s == 0 else b("C", key=["C", "Ce"] + blocks("C", 4))
+    Aw = b("A", key=["A", "Ae"] + blocks("A", 4))
+    lhs = lambda p: b("B", 15 - p, 143 - p)
+
+    dma("y", "ld0", b("tp")[0], T.tops[:], [], ["tp"], 1500)
+    dma("y", "ld2", b("KI", 0, V0)[0], T.kids[:], [], ["KI"], 4000)
+    dma("s", "ld3", b("A", 0, V0)[0], T.a0[:], [], ["A"], 4000)
+    dma("y", "ld1", b("xb")[0], T.x0[:], [], ["xb"], 2000)
+    dma("s", "ld4", b("thi", p1=8)[0], T.th[:], [], ["thi"], 2000)
+    ms(b("KI", V0, WIN, key="KIe"), 4095)
+    ms(b("C", V0, WIN, key=["Ce"] + blocks("C", 4)), 4095.0)
+    ms(b("A", V0, W, key=blocks("A", 4)), 0.0)
+    ms(b("A", W, WIN, key="Ae"), 4096.0)
+    ms(b("ones"), 1.0)
+    ms(b("one8"), 1.0)
+    ms(b("AN", 256, 272, key="ANz"), 0.0)
+    ms(b("CN", 128, 272, key="CNz"), 4095.0)
+    ms(b("RW", 0, 16, key="RWa"), 0.0)
+    ms(b("RW", 144, 160, key="rowM"), 0.0)
+    ms(b("row", 128, 144, key="rowz"), -1.0)
+    ms(b("rr", 0, 16, key="rra"), -1.0)
+    ms(b("d0", key=["d0", "d0a", "d0b"]), 0.0)
+    ms(b("d1", key=["d1a", "d1b", "d1c", "d1s"]), 256.0)
+    ms(b("B"), 0.0)
+    for j, v in ((0, 1.0), (2, 63.0), (3, 65.0), (4, 128.0), (5, -0.5), (6, 127.0)):
+        ms(row(j, 144), v)
+    for s in range(4):
+        ms(b("cr", 1008 + 128 * s, 1136 + 128 * s, 1, 1, key="n%d" % s), 8320.0 + V0 + L * s)
+    for nm in ("RM", "RM2"):
+        ms(b(nm), 0.0)
+        ms(b(nm, 0, 128, 16), BIG)
+    ms(b("RM2", 1, 128, 16), BIG)
+    for nm in ("clv", "clb"):
+        ms(b(nm, key=[nm, nm + "t"]), BIG)
+        ms(b(nm, 0, 136, 17), -BIG)
+    for k in range(2):
+        ms(b("come%d" % k, 64, 80, key="come%dz" % k), 0.0)
+    for k in range(4):
+        ms(b("msg%d" % k, 0, CAP), 0.0)
+    ms(b("coef", 16, 24, key="coefc"), 128.0)
+    ms(b("coef", 40, 48, key="coeff"), 256.0)
+
+    asel(b("sel2"), b("ones", 0, 8), [[-16, 8]], OP.is_ge, 0.0, 0, 1)
+    asel(b("selb"), b("sel2"), [[16, 8]], OP.is_ge, 0.0, 15, -1)
+    ts(b("B", 15, 143, 16), b("selb"), 128.0, OP.mult)
+    io(b("pin"), [[0, 16]], 0, 1)
+    io(b("ci"), [[1, 128]], 0, 0)
+    io(b("ri"), [[1, 16], [16, 8]], 0, 0)
+    cp(b("plist"), b("ri"))
+    cp(row(1), b("ci", p1=1))
+    asel(b("I"), b("ones", 0, 128), [[-1, 128]], OP.is_equal, 0.0, 0, 1)
+    for nm, v in (("nI", -1.0), ("I63", 63.0), ("nI63", -63.0), ("nI128", -128.0), ("nI8", -8320.0), ("IM", 256 * M), ("idf", 1.0)):
+        act(b(nm), b("I"), AF.Copy, 0.0, v)
+    ts(b("pa"), b("pin"), 15, OP.bitwise_and)
+    cp(b("pf"), b("pa", 0, 1))
+    ts(b("p128"), b("pa", 0, 1), 128.0, OP.mult)
+    ts(b("pb", 0, 2), b("pin", 0, 2), 7, OP.bitwise_and)
+    cp(b("r7"), b("pb", 0, 1))
+    ts(b("pb", 2, 4, key="pb_"), b("pin", 0, 2), 3, OP.logical_shift_right, 1, OP.bitwise_and)
+    cp(b("hi"), b("pb", 2, 3, key="pb_"))
+    ts(b("jL"), b("ci", 0, 128, 16), b("pf"), OP.add)
+    ts(b("cj"), b("jL"), -M, OP.mult, 129 * M, OP.add)
+    for s in range(4):
+        ts(b("nL", 8 * s, 8 * s + 8, key="nL%d" % s), b("jL"), float(V0 + L * s), OP.add)
+    ts(b("coef", 8, 16, key="coefb"), b("jL"), -256.0, OP.add)
+    ts(b("coef", 32, 40, key="coefe"), b("jL"), -128.0, OP.add)
+    ts(b("lend"), b("ci", 0, 128, 16), 15.0, OP.add)
+    ts(b("lF"), b("pb", 0, 2), 16.0, OP.mult, 15.0, OP.add)
+    ts(b("lz"), b("pb", 0, 2), 17.0, OP.mult, 15.0, OP.add)
+    cp(b("lr"), b("pb", 0, 2))
+    ts(b("tmp", 0, 1, key="tmpa"), b("hi"), 8.0, OP.mult, b("r7"), OP.add)
+    ts(b("tmp", 1, 2, key="tmpb"), b("r7"), 8.0, OP.add)
+    cp(b("lg"), b("tmp", 0, 2, key=["tmpa", "tmpb"]))
+    for j, (u, v) in enumerate(((0, 32), (32, 32), (24, 16), (0, 0))):
+        ts(b("tmp", 4 + j, 5 + j, key="tmp%d" % j), b("hi"), float(v - u), OP.mult, float(u), OP.add)
+    ts(b("lfl"), b("tmp", 4, 8, key=["tmp%d" % j for j in range(4)]), b("r7"), OP.add)
+    ts(b("tmp2", 0, 1, key="tmp2a"), b("r7"), 16.0, OP.mult, b("hi"), OP.add)
+    ts(b("lperm"), b("ci", 0, 16, 2), b("tmp2", 0, 1, key="tmp2a"), OP.add)
+    ts(b("tmp3", 0, 10), b("ci", 0, 10), b("pf"), OP.is_gt, b("pf"), OP.add)
+    ts(b("tmp2", 2, 12, key="tmp2b"), b("ci", 0, 10), -1.0, OP.add, b("pf"), OP.is_equal)
+    ts(b("tmp2", 2, 12, key="tmp2b"), b("tmp2", 2, 12, key="tmp2b"), 128.0, OP.mult)
+    tt(b("tmp3", 0, 10), b("tmp3", 0, 10), b("tmp2", 2, 12, key="tmp2b"), OP.add)
+    ts(b("tmp2", 2, 12, key="tmp2b"), b("ci", 0, 10), 15.0, OP.mult)
+    tt(b("tmp3", 0, 10), b("tmp3", 0, 10), b("tmp2", 2, 12, key="tmp2b"), OP.add)
+    ts(b("l17"), b("tmp3", 0, 10), 128.0, OP.min)
+    ts(b("dec", 0, 8), b("pin", 0, 8), 4, OP.logical_shift_right)
+    tt(b("dec", 0, 8), b("dec", 0, 8), b("ci", 0, 8), OP.add)
+    ts(b("dec", 0, 8), b("dec", 0, 8), 1, OP.bitwise_and)
+    ts(b("tmp", 8, 16, key="tmpz"), b("dec", 0, 8), 144.0, OP.mult)
+    tt(b("tmp", 8, 16, key="tmpz"), b("tmp", 8, 16, key="tmpz"), b("jL"), OP.add)
+    cp(b("lsel"), b("tmp", 8, 16, key="tmpz"))
+    asel(b("lt"), b("ones", 0, 128), [[-16, 8], [0, 16]], OP.is_ge, 0.0, 0, 1)
+    asel(b("bones"), b("lt"), [[16, 8], [0, 16]], OP.is_ge, 0.0, 15, -1)
+    act(b("lo"), b("bones"), AF.Copy, 0.0, -M)
+    asel(b("lt"), b("lo"), [[1, 128]], OP.is_ge, 0.0, 0, -1)
+    asel(b("ld"), b("lt"), [[1, 128]], OP.not_equal, M, 0, -1)
+    act(b("nl8"), b("ld"), AF.Copy, 0.0, -8320.0 / M)
+    asel(b("sh"), b("bones"), [[-1, 128]], OP.is_equal, 0.0, -1, 1)
+    tt(b("dm"), b("I"), b("sh"), OP.subtract)
+    act(b("bones"), b("bones"), AF.Copy, 0.0, 128.0)
+    io(b("hx"), [[0, 8], [-1, 16]], 16, 1)
+    ts(b("hx"), b("hx"), 15, OP.bitwise_and)
+    ts(b("tab"), b("hx"), 0.0, OP.is_equal, 65.0, OP.mult)
+    ts(b("emc"), b("hx"), 0.0, OP.not_equal, float(2 ** 26), OP.mult)
+    ts(b("emc"), b("emc"), 127.0, OP.max)
+    for c in range(8):
+        ts(b("cnt0", 17 * c, 17 * c + 16), b("hx", 0, 16), 0.0, OP.not_equal, -float(2 ** 20), OP.mult)
+    cp(b("cnt0", 16, 136, 17), b("jL"))
+    io(b("iot"), [[1, WIN]], 0, 0)
+    cp(b("tu"), b("tp"))
+    cp(b("tu2", 0, 16, 2), b("tp"))
+    cp(b("topf"), b("tp"))
+    for h in range(4):
+        cp(b("C", 256 * h, 256 * h + 256), b("KI", 256 * h, 256 * h + 256))
+    cp(b("thf", p1=8), b("thi", p1=8))
+    asel(b("thx", p1=8), b("ones", 0, 128, 1, 8), [[1, 128]], OP.is_ge, 0.0, 0, -16)
+    asel(b("es", p1=8), b("thx", p1=8), [[-1, 128]], OP.is_ge, 0.0, 15, 16)
+    act(b("es", p1=8), b("es", p1=8), AF.Copy, 0.0, 128.0)
+    mms(b("pb6", 384, 512), [(b("I"), b("emc")), (b("es", p1=8), b("thf", p1=8))])
+    scan(b("thx"), b("RM"), b("pb6", 384, 512), OP.max, OP.min)
+    cp(b("lim"), b("thx", 15, 128, 16))
+    ts(b("lim1"), b("thx", 15, 128, 16), 1.0, OP.add)
+
+    def x_forms(src, s):
+        if s == 2:
+            cp(b("xb"), src)
+        act(b("xP"), ind(b("xb"), b("lperm")), AF.Copy)
+        for k in range(16):
+            o = b("xrep", k, 2048, 16, key="xr%d" % k)
+            if k % 3 == 2:
+                act(o, b("xP"), AF.Copy)
+            else:
+                cp(o, b("xP"))
+        act(b("xm"), b("xb"), AF.Identity, -MAGIC)
+        act(b("xp"), b("xb"), AF.Identity, 256.0)
+
+    XR = ["xr%d" % k for k in range(16)]
+
+    def children(out, s, lst):
+        for c in range(8):
+            ts(b(out, c, 128, 8, key="%s%d" % (out, c)), ind(Cw(s), b(lst, 2 * c, 2 * c + 1)), float(E1), OP.min)
+
+    def rows(out, s, lst):
+        if s == 0:
+            cp(out, ind(Cw(s), lst))
+        else:
+            act(out, ind(Cw(s), lst), AF.Copy)
+
+    def lst(name, p0, n):
+        return b(name, 8 * p0, 8 * (p0 + n), key=["%s%d" % (name, c) for c in range(8)])
+
+    def sums(bank, p0, n, last):
+        for p in range(p0, p0 + n):
+            mm(b(bank, 0, 128), lhs(p), b("Dab", 128 * p, 128 * p + 128, key="Dab%d" % p), False, last and p == p0 + n - 1)
+
+    pk = lambda nm, p0, n: ["%s%d" % (nm, p) for p in range(p0, p0 + n)]
+
+    def firsts(lists, node, on, bank, cl, z):
+        act(b("row", 0, 128), ind(b("iot"), lists), AF.Copy)
+        act(b("r17"), ind(b("row", key=["row", "rowz"]), b("l17", 0, 9)), AF.Copy)
+        mm(b(bank, 0, 136), b("I"), b("cnt0"), True, False)
+        for c in range(8):
+            e0 = 136 * c
+            ts(b("E", e0 + 17 * c, e0 + 136, key="E%d" % c), b("r17", 17 * c, 136), node(c), OP.is_equal, on(c), OP.mult)
+            mm(b(bank, 17 * c, 17 * c + 17), b("ld"), b("E", e0 + 17 * c, e0 + 17 * c + 17, key="E%d" % c), False, c == 7)
+            if c < 7:
+                mm(b(bank, 17 * c + 17, 136), b("lo"), b("E", e0 + 17 * c + 17, e0 + 136, key="E%d" % c), False, False)
+        scan(b(z), b(cl, key=[cl, cl + "t"]), b(bank, 0, 136), OP.min, OP.max)
+
+    def prefix(o0, f):
+        mm(b("pb2", o0, o0 + 8), b("ld"), f(0, 8), True, False)
+        for d in range(1, 8):
+            mm(b("pb2", o0 + d, o0 + 8), b("lo"), f(0, 8 - d), False, False)
+        mm(b("pb2", o0, o0 + 8), b("IM"), f(0, 8), False, True)
+
+    def send(s):
+        h = hops(T, topo, rank, s)
+        m = "msg%d" % s
+        fl = "fl%d" % (s % ST)
+        prefix(176, lambda a, z: b(fl, 8 + a, 8 + z))
+        tt(b("pz"), b("pb2", 176, 184), b("cj"), OP.max)
+        ts(b("posu"), b("pz"), -1.0 / M, OP.mult, 257.0, OP.add)
+        scatter(b(m), b("posu"), b("xp"))
+        n = engines_of(topo, core, h[1])
+        rid, pid = topo.addr(h[1], core)
+        if len(h) == 3:
+            to, sem = T["rl%d" % s][:, 0:CAP], T.sem["rr%d" % s]
+        else:
+            to, sem = T["come%d" % (s // ST)][:, CAP * (s % ST):CAP * (s % ST) + CAP], T.sem["in%d" % s]
+        op("g", lambda e: e.remote_dma(to, T[m][:, 0:CAP], sem, T.sem["ls%d" % s], pid, rid, emask(topo, core, h[1], n)),
+           [m], ["come%d_%d" % (s // ST, s % ST)], 120, 3500, "remote%d" % s)
+
+    def front(s):
+        t = s % ST
+        vu, vu2 = (b("tu"), "tu2") if t == 0 else (b("lu", 8, 16), "vu2")
+        vf = (lambda a, z: b("topf", a, z)) if t == 0 else (lambda a, z: b("s2", 17 + 2 * a, 17 + 2 * z, 2))
+        children("cvu", s, vu2)
+        rows(b("cvf"), s, vu)
+        mm(b("pb2", 0, 160), b("dm"), b("RW", 0, 160, key=["RWa", "cvf", "rowM"]))
+        turn(b("tr", 0, 128, key="tra"), b("pb2", 16, 144))
+        turn(b("tr", 128, 288, key="trb"), b("pb2", 0, 160))
+        act(b("dl"), ind(b("tr", key=["tra", "trb"]), b("lsel")), AF.Copy)
+        act(b("emp"), b("cvf"), AF.Relu, -4094.0)
+        for p in range(16):
+            mm(b("pb2", 160, 168), lhs(p), b("emp", p, 128, 16), p == 0, p == 15)
+        act(b("rB", 0, 8, key="rBa"), b("pb2", 160, 168), AF.Copy, 0.0, BIG / 128)
+        act(b("rB", 8, 16, key="rBb"), b("pb2", 160, 168), AF.Relu, BIG, -BIG / 128)
+        nrow = (ONE, b("cr", 1008 + 128 * s, 1136 + 128 * s, 1, 1, key="n%d" % s))
+        mms(b("pb3", 144, 272), [(ONE, JROW), nrow, (b("nl8"), b("emp"))])
+        tt(b("RW", 272, 400, key="rowN"), b("cvf"), b("pb3", 144, 272), OP.min)
+        if s != 2:
+            ts(b("clv", 16, 136, 17, key="clvt"), vf(0, 8), 128.0, OP.add)
+            firsts(vu, lambda c: vf(c, c + 1), lambda c: b("one8" if t == 0 else "nonr", c, c + 1), "pb3", "clv", "zv")
+            cp(b("uvu%d" % t), b("zv", 16, 136, 17))
+            act(b("acB%d" % t), ind(b("zv"), b("lz")), AF.Relu, 0.0, BIG / M)
+            act(b("nac%d" % t), b("acB%d" % t, 0, 8), AF.Identity, BIG, -1.0)
+        tt(b("W4", 16, 24, key="W4c"), b("lim1"), b("nac%d" % t), OP.max)
+        tt(b("W4", 8, 16, key="W4b"), b("W4", 16, 24, key="W4c"), b("rB", 0, 8, key="rBa"), OP.max)
+        tt(b("W4", 24, 32, key="W4d"), b("W4", 16, 24, key="W4c"), b("rB", 8, 16, key="rBb"), OP.max)
+        tt(b("coef", 24, 32, key="coefd"), b("nL", 8 * s, 8 * s + 8, key="nL%d" % s), vf(0, 8), OP.subtract)
+        ts(b("d1", 1, 16, 2, key="d1a"), vf(0, 8), 128.0, OP.add)
+        cp(b("d1", 17, 32, 2, key="d1b"), vf(0, 8))
+        tt(b("d0", 1, 16, 2, key="d0a"), b("jL"), b("d1", 1, 16, 2, key="d1a"), OP.subtract)
+        return nrow
+
+    def step(s, nrow):
+        t = s % ST
+        n0 = V0 + L * s
+        pos, neg = (b("nI"), b("I")) if s == 2 else (b("I"), b("nI"))
+        v0 = b("d1", 17, 32, 2, key="d1b")
+        mm(b("pb0", 0, 128), ONE, JROW, True, False)
+        p0 = 0
+        for n in P1:
+            c0, c1 = 128 * p0, 128 * (p0 + n)
+            d = b("D", c0, c1, key=pk("D", p0, n))
+            if s == 2:
+                tt(d, ind(b("xi"), b("plist", 8 * p0, 8 * (p0 + n))), b("ag", c0, c1, key=pk("ag", p0, n)), OP.subtract)
+            else:
+                tt(d, ind(Aw, lst("cvu", p0, n)), b("xrep", c0, c1, key=XR), OP.subtract)
+            act(b("Dab", c0, c1, key=pk("Dab", p0, n)), d, AF.Abs)
+            sums("pb0", p0, n, p0 + n == 16)
+            p0 += n
+        r = b("rr", 16, 144, key="r1")
+        rs = b("rr", 15, 143, key=["r1", "rra"])
+        scan(r, b("RM"), b("pb0", 0, 128), OP.max, OP.min)
+        scan(b("r0"), b("RM"), b("pb0", 0, 128), OP.max, OP.min)
+        tt(b("e"), ind(b("r0"), b("lend")), rs, OP.is_equal)
+        scan(b("pay"), b("e"), b("dl"), OP.mult, OP.add)
+        bf = lambda a, z: b("pay", 15 + 16 * a, 16 * z, 16)
+        ts(b("bu2", 0, 16, 2), bf(0, 8), float(E1), OP.min)
+        ts(b("bu"), bf(0, 8), float(E1), OP.min)
+        children("dvu", s, "bu2")
+        rows(b("dvf"), s, b("bu"))
+        tt(b("cand"), rs, b("pb0", 0, 128), OP.max)
+        scan(b("rr", 144, 272, key="r2"), b("RM2"), b("cand"), OP.max, OP.min)
+        cp(b("dec"), b("rr", 31, 272, 16, key=["r1", "r2"]))
+        ts(b("dk"), b("dec"), 127, OP.bitwise_and)
+        ts(b("du"), b("dk"), b("p128"), OP.add)
+        cp(b("ku"), b("dk"))
+        act(b("dd"), ind(b("D", key=pk("D", 0, 16)), b("du")), AF.Copy)
+        act(b("oh"), ind(b("tab"), b("ku")), AF.Copy)
+        db, dq, ohb, ohq = b("dd", 0, 128), b("dd", 128, 256), b("oh", 0, 128), b("oh", 128, 256)
+        mms(b("pb6", 0, 128), [(ONE, RH), (pos, db), (pos, dq)])
+        act(b("pb6", 128, 256), b("pb6", 0, 128), AF.Identity, MAGIC, 0.5)
+        act(b("absM"), b("pb6", 128, 256), AF.Abs, -MAGIC)
+        tt(b("AN", 0, 128, key="Mb"), b("xm"), b("pb6", 128, 256), OP.add)
+        mms(b("pb4", 256, 384), [(b("I"), b("emc")), (b("bones"), b("absM"))])
+        scan(b("es"), b("RM"), b("pb4", 256, 384), OP.max, OP.min)
+        ts(b("cl"), db, -4.0, OP.max, 4.0, OP.min)
+        mms(b("pb6", 256, 384), [(b("I"), b("xb")), (pos, db), (neg, b("cl"))])
+        act(b("hv"), b("pb6", 256, 384), AF.Copy)
+        mm(b("pb1", 0, 128), ONE, R127, True, False)
+        for p0, bank in P2S:
+            c0, c1 = 128 * p0, 128 * p0 + 512
+            a = b("ag", c0, c1, key=pk("ag", p0, 4))
+            act(a, ind(Aw, lst("dvu", p0, 4)), AF.Copy)
+            mms(b(bank), [(b("nI"), b("xrep", c0, c1, key=XR)), (b("I"), a)])
+            act(b("Dab", c0, c1, key=pk("Dab", p0, 4)), b(bank), AF.Abs)
+            sums("pb1", p0, 4, False)
+        p0 = 4 * len(P2S)
+        for n in P2V:
+            c0, c1 = 128 * p0, 128 * (p0 + n)
+            d = b("ag", c0, c1, key=pk("ag", p0, n))
+            tt(d, ind(Aw, lst("dvu", p0, n)), b("xrep", c0, c1, key=XR), OP.subtract)
+            act(b("Dab", c0, c1, key=pk("Dab", p0, n)), d, AF.Abs)
+            sums("pb1", p0, n, p0 + n == 16)
+            p0 += n
+        mb = b("rr", 31, 144, 16, key="r1")
+        tt(b("W4", 0, 8, key="W4a"), mb, b("nac%d" % t), OP.max)
+        tt(b("G1", 0, 8, key="G1a"), mb, b("lim"), OP.is_gt)
+        tt(b("G1", 8, 16, key="G1b"), mb, b("lim"), OP.is_le)
+        ts(b("G2"), b("G1", key=["G1a", "G1b"]), BIG, OP.mult)
+        tt(b("UU"), ind(b("G2"), b("lg")), b("W4", key=["W4a", "W4b", "W4c", "W4d"]), OP.max)
+        tt(b("U1"), mb, b("lim1"), OP.min)
+        tt(b("U4"), ind(b("U1"), b("lr")), b("acB%d" % t), OP.min)
+        tt(b("coef", 0, 8, key="coefa"), bf(0, 8), v0, OP.subtract)
+        ts(b("clb", 16, 136, 17, key="clbt"), bf(0, 8), 128.0, OP.add)
+        tt(b("FL", 0, 32), ind(b("es"), b("lF")), b("UU"), OP.is_ge)
+        tt(b("FL", 32, 40, key="am"), b("es", 15, 128, 16), b("U4", 0, 8), OP.is_lt)
+        tt(b("Tt4"), ind(b("es"), b("lF")), b("U4"), OP.min)
+        ts(b("nfl"), b("FL", 0, 32), -BIG, OP.mult, BIG, OP.add)
+        tt(b("TH"), b("Tt4"), b("nfl"), OP.max)
+        tt(b("prod"), ind(b("FL", key=["FL", "am"]), b("lfl", 0, 3)), b("coef", key=["coef" + k for k in "abcdef"]), OP.mult)
+        tt(b("d0", 17, 64, 2, key="d0b"), b("prod", 0, 24), b("prod", 24, 48), OP.add)
+        tt(b("sp"), b("d0", 49, 64, 2, key="d0b"), b("jL"), OP.add)
+        cp(b("spu"), b("sp"))
+        mms(b("pb5", 0, 128), [(b("I63"), ohb)])
+        mms(b("pb5", 128, 256), [(b("I63"), ohb), (b("I63"), ohq)])
+        mms(b("pb5", 256, 384), [(ONE, JROW), nrow, (b("nI128"), ohb)])
+        mms(b("pb5", 384, 512), [(R63, R65), (b("nI63"), ohb), (b("nI63"), ohq)])
+        mms(b("pb3", 272, 400), [(R128, R65), (b("nI8"), b("emp")), (b("nI128"), ohb), (b("idf"), b("dvf"))])
+        tt(b("w3"), b("cvf"), b("pb5", 0, 128), OP.max)
+        tt(b("w4"), b("cvf"), b("pb5", 128, 256), OP.max)
+        tt(b("CN", 0, 128), b("cvf"), b("pb5", 384, 512), OP.max)
+        tt(b("RW", 144, 272, key="rowM"), b("w4"), b("pb5", 256, 384), OP.min)
+        tt(b("rsp"), b("w3"), b("pb3", 272, 400), OP.min)
+        act(b("rpre"), ind(b("RW", 16, 400, key=["cvf", "rowM", "rowN"]), b("spu")), AF.Copy)
+        Cs = b("CW", 0, 128 + n0, key=["C"] + blocks("C", s))
+        scatter(Cs, b("uvu%d" % t), b("rpre"))
+        fl = "fl%d" % t
+        scan(b("fs"), b("RM"), b("pb1", 0, 128), OP.max, OP.min)
+        tt(b("hf"), b("fs", 15, 128, 16), b("TH", 0, 8), OP.is_ge)
+        tt(b(fl, 8, 24), ind(b("fs"), b("lF", 0, 1)), b("TH", 8, 24), OP.is_ge)
+        tt(b("d1", 0, 64, 2, key="d1s"), ind(b("fs"), b("lF")), b("Tt4"), OP.is_ge)
+        scan(b("s2"), b("d0", 0, 48, key=["d0", "d0a", "d0b"]), b("d1", 0, 48, key=["d1a", "d1b", "d1c", "d1s"]), OP.mult, OP.add)
+        cp(b("lu"), b("s2", 1, 48, 2))
+        if t == 0:
+            cp(b("vu2", 0, 16, 2), b("s2", 17, 32, 2))
+            act(b("nonr"), b(fl, 16, 24), AF.Identity, 1.0, -1.0)
+        scatter(Cs, b("lu", 0, 8), b("rsp"))
+        act(b("C", n0, n0 + L, key="Cb%d" % s), ind(b("CN", key=["CN", "CNz"]), b("lu", 16, 24)), AF.Copy)
+        act(b("A", n0, n0 + L, key="Ab%d" % s), ind(b("AN", key=["Mb", "xb", "ANz"]), b("lu", 16, 24)), AF.Copy)
+        firsts(b("bu"), lambda c: bf(c, c + 1), lambda c: b("hf", c, c + 1), "pb4", "clb", "zb")
+        cp(b("oAu"), b("zb", 16, 136, 17))
+        scatter(b("AW", 0, 128 + n0, key=["A"] + blocks("A", s)), b("oAu"), b("hv"))
+        send(s)
+
+    def round_end(s):
+        cm = "come%d" % (s // ST)
+        tt(b("rest2"), b("fl0", 16, 24), b("fl1", 16, 24), OP.add)
+        prefix(192, lambda a, z: b("rest2", a, z))
+        ts(b("nrs"), b("pb2", 192, 200), -1.0 / M, OP.mult, 257.0, OP.add)
+        tt(b("dM"), ind(Aw, b("lu", 8, 16)), b("xb"), OP.subtract)
+        act(b("ad"), b("dM"), AF.Abs)
+        ts(b("msk"), b(cm, 0, CAP, key=cm + "_0"), 0.5, OP.is_gt)
+        op("v", lambda e: e.tensor_reduce(b("n0")[0], b("msk")[0], AxisListType.X, OP.add), ["msk"], ["n0"], 64)
+        ts(b("cd"), b("n0"), -1.0, OP.mult, float(CAP), OP.add)
+        ts(b("ge"), b("nrs"), b("n0"), OP.is_ge, b("cd"), OP.mult)
+        tt(b("idx"), b("nrs"), b("ge"), OP.add)
+        ts(b("iu"), b("idx"), 64.0, OP.min)
+        tt(b("hx"), ind(b(cm, key=[cm + "_0", cm + "_1", cm + "z"]), b("iu")), b("ad"), OP.max)
+        ts(b("xi"), b("hx"), 255, OP.bitwise_and)
+
+    x_forms(b("xb"), 0)
+    nrow = front(0)
+    for s in range(4):
+        step(s, nrow)
+        if s == 3:
+            dma("y", "ld5", T.yc[:], b("C", 0, W)[0], ["C"] + blocks("C", 4), ["yc"], 5000)
+            dma("s", "ld6", T.ya[:], b("A", 0, W)[0], ["A"] + blocks("A", 4), ["ya"], 3500)
+        if s % ST == 1:
+            round_end(s)
+        if s < 3:
+            nrow = front(s + 1)
+        if s == 1:
+            for j in range(8):
+                o, a = b("ag", 256 * j, 256 * j + 256, key=pk("ag", 2 * j, 2)), ind(Aw, lst("cvu", 2 * j, 2))
+                if j % 2:
+                    act(o, a, AF.Copy)
+                else:
+                    cp(o, a)
+            x_forms(b("xi"), 2)
+    cp(b("xb"), b("xi"))
+    dma("y", "ld7", T.yx[:], b("xb")[0], ["xb"], ["yx"], 1500)
+
+    if "o" not in ORDER:
+        ORDER["o"] = order_calls(ops)
     own = {"v": "qv", "s": "qs", "t": "qt", "g": "qg"}
     cnt = {"qv": 0, "qs": 0, "qt": 0, "qg": 0}
     know = {q: {} for q in eng}
     wr, rd = {}, {}
 
-    def need(q, R, Wk, dma=False):
+    def need(q, R, Wk, isdma):
         deps = []
         for k in R:
             if k in wr:
@@ -107,11 +611,10 @@ def rank_program(g, core, T, topo):
             if k[:2] == "pb":
                 deps += [d for d in rd.get(k, []) if d[0] != q]
         for k in Wk:
-            if k in wr and (wr[k][0] != q or dma):
+            if k in wr and (wr[k][0] != q or q != "t"):
                 deps.append(wr[k])
-            deps += [d for d in rd.get(k, []) if d[0] != q or dma or k[:2] == "pb"]
-        deps = sorted(deps, key=lambda d: -d[2])
-        for d in deps:
+            deps += rd.get(k, [])
+        for d in sorted(deps, key=lambda d: -d[2]):
             if know[q].get(d[1], 0) < d[2]:
                 eng[q].wait_ge(T.sem[d[1]], d[2])
                 for n, v in d[3].items():
@@ -128,543 +631,27 @@ def rank_program(g, core, T, topo):
             wr[k] = d
             rd[k] = []
 
-    def op(q, call, R, Wk):
-        need(q, R, Wk)
-        s = own[q]
-        cnt[s] += 1
-        call(eng[q]).then_inc(T.sem[s], 1)
-        note(q, s, cnt[s], know[q], R, Wk)
-
-    def dma(q, sem, out, in_, R, Wk):
-        need(q, R, Wk, True)
-        eng[q].dma_start(out, in_).then_inc(T.sem[sem], 16)
-        cnt[sem] = 16
-        note("dma" + sem, sem, 16, know[q], R, Wk)
-
-    def b(name, c0=0, c1=None, st=1, p0=0, p1=128, key=None):
-        if name in SLOT:
-            buf, o, w = SLOT[name]
+    for i in ORDER["o"]:
+        o = ops[i]
+        q, kind = o["q"], o["dma"]
+        if kind is None:
+            need(q, o["R"], o["W"], False)
+            cnt[own[q]] += 1
+            o["call"](eng[q]).then_inc(T.sem[own[q]], 1)
+            note(q, own[q], cnt[own[q]], know[q], o["R"], o["W"])
+        elif kind[:6] == "remote":
+            s = int(kind[6:])
+            need(q, o["R"], [], True)
+            o["call"](g)
+            h = hops(T, topo, (rank - 1 - s % (NR - 1)) % NR, s)
+            n = engines_of(topo, h[-2], h[-1])
+            wr[o["W"][0]] = ("remote", "in%d" % s, n, {"in%d" % s: n})
+            cnt["in%d" % s] = n
         else:
-            buf, o, w = name, 0, SCRATCH[name][1][1]
-        c1 = w if c1 is None else c1
-        return (T[buf][p0:p1, o + c0:o + c1:st] if st != 1 else T[buf][p0:p1, o + c0:o + c1], key if isinstance(key, list) else [key or name])
-
-    def ind(win, off):
-        return (win[0].indirect(off[0]), win[1] + off[1])
-
-    def ks(*refs):
-        return [k for r in refs if isinstance(r, tuple) for k in r[1]]
-
-    def ap(x):
-        return x[0] if isinstance(x, tuple) else x
-
-    def tt(o, a, c, f):
-        op("v", lambda e: e.tensor_tensor(o[0], a[0], c[0], f), ks(a, c), ks(o))
-
-    def ts(o, a, s1, f0, s2=None, f1=None):
-        if f1 is None:
-            op("v", lambda e: e.tensor_scalar(o[0], a[0], ap(s1), None, f0), ks(a, s1), ks(o))
-        else:
-            op("v", lambda e: e.tensor_scalar(o[0], a[0], ap(s1), ap(s2), f0, f1), ks(a, s1, s2), ks(o))
-
-    def cp(o, a):
-        op("v", lambda e: e.tensor_copy(o[0], a[0]), ks(a), ks(o))
-
-    def scatter(win, off, a):
-        op("v", lambda e: e.tensor_copy(win[0].indirect(off[0]), a[0]), ks(a, off), ks(win))
-
-    def ms(o, v):
-        op("v", lambda e: e.memset(o[0], v), [], ks(o))
-
-    def scan(o, a, c, f0, f1):
-        op("v", lambda e: e.tensor_tensor_scan(o[0], a[0], c[0], BIG, f0, f1), ks(a, c), ks(o))
-
-    def act(o, a, f, bias=0.0, scale=1.0):
-        op("s", lambda e: e.activation(o[0], a[0], f, bias=ap(bias), scale=ap(scale)), ks(a, scale, bias), ks(o))
-
-    def mm(o, l, r, start=True, stop=True):
-        op("t", lambda e: e.matmul(o[0], l[0], r[0], start, stop), ks(l, r), ks(o))
-
-    def io(o, pat, base, cm, flag=False):
-        if flag:
-            op("g", lambda e: e.iota(o[0], pat, base, cm, allow_small_or_imprecise_dtypes=True), [], ks(o))
-        else:
-            op("g", lambda e: e.iota(o[0], pat, base, cm), [], ks(o))
-
-    def asel(o, a, pat, f, fill, base, cm):
-        op("g", lambda e: e.affine_select(o[0], a[0], pat, f, fill, base, cm), ks(a), ks(o))
-
-    bl = lambda n, c0=0: b("bl", c0, c0 + n)
-    one = b("onesb", 0, 128, 1, 0, 1)
-
-    dma("y", "ld0", b("tp")[0], T.tops[:], [], ["tp"])
-    dma("y", "ld1", b("xb")[0], T.x0[:], [], ["xb"])
-    dma("y", "ld2", b("KI")[0], T.kids[:], [], ["KI"])
-    dma("s", "ld4", b("thi", 0, 128, 1, 0, 8)[0], T.th[:], [], ["thi"])
-    ms(b("A", V0, W), 0.0)
-    ms(b("A", W, WIN), 4096.0)
-    dma("y", "ld3", b("A", 0, V0)[0], T.a0[:], [], ["A"])
-    ms(b("onesb"), 1.0)
-    ms(b("zf"), 0.0)
-    ms(b("zb"), 0.0)
-    for k in range(2):
-        ms(b("come%d" % k, 64, 80, key="come%dz" % k), 0.0)
-    for k in range(4):
-        ms(b("msg%d" % k, 0, CAP), 0.0)
-    io(b("cio"), [[128, 13]], 0, 1)
-    io(b("ci"), [[1, 128]], 0, 0)
-    asel(b("idb"), b("onesb", 0, 128), [[-1, 128]], OP.is_equal, 0.0, 0, 1)
-    asel(b("EE", p1=16), b("onesb", 0, 128, 1, 0, 16), [[0, 8], [-1, 16]], OP.is_equal, 0.0, 0, 1)
-    asel(b("ipb"), b("onesb", 0, 136), [[-16, 8], [-1, 17]], OP.is_equal, 0.0, 1, 1)
-    io(b("kcf", 0, 136, key="kcf0"), [[0, 8], [128, 17]], 64, 0, True)
-    io(b("kcf", 136, 272, key="kcf1"), [[0, 8], [128, 17]], 0, 0, True)
-    io(b("kcf", 272, 408, key="kcf2"), [[0, 8], [1, 17]], 0, 0, True)
-    asel(b("kcg"), b("kcf", key=["kcf0", "kcf1", "kcf2"]), [[0, 24], [1, 17]], OP.not_equal, BIG, 0, 0)
-    asel(b("sel2"), b("onesb", 0, 8), [[-16, 8]], OP.is_ge, 0.0, 0, 1)
-    asel(b("selb"), b("sel2"), [[16, 8]], OP.is_ge, 0.0, 15, -1)
-    io(b("pin"), [[0, 8]], 0, 1)
-    io(b("m16"), [[16, 8]], 0, 0)
-    asel(b("RM"), b("zf"), [[0, 16], [1, 17]], OP.not_equal, BIG, 0, 0)
-    io(b("rmi"), [[0, 24], [-1, 16]], 16, 1)
-    asel(b("trib"), b("zb"), [[0, 4], [1, 128]], OP.is_gt, -32.0, 0, -1)
-    io(b("kpat"), [[0, 24], [1, 16]], 1, 0, True)
-    asel(b("tri"), b("onesb", 0, 128), [[1, 128]], OP.is_gt, 0.0, 0, -1)
-    asel(b("RM2"), b("zf", 0, 128), [[0, 8], [1, 16]], OP.not_equal, BIG, 0, 0)
-
-    ms(b("C", V0, WIN), 4095.0)
-    for k in range(11):
-        ts(b("bt", 13 * k, 13 * k + 13, key="bt"), b("cio"), k, OP.logical_shift_right, 1, OP.bitwise_and)
-    ts(b("bb"), b("bt"), 2.0, OP.mult, -1.0, OP.add)
-    cp(b("bl"), b("ci"))
-    cp(b("tu"), b("tp"))
-    cp(b("topf", 0, 8, key="topf"), b("tp"))
-    for k in range(16):
-        cp(b("xrep", k, 2048, 16, key="xr"), b("xb"))
-    for k in range(16):
-        act(b("R", k, 2048, 16, key="R"), b("idb"), AF.Copy, 0.0, -1.0)
-    for q in range(13):
-        mm(b("pb%d" % (4 + q // 4), 128 * (q % 4), 128 * (q % 4) + 128, 1, 0, 11), b("bb", q, 143, 13), b("idb"))
-    for h in range(4):
-        n = 512 if h < 3 else 128
-        act(b("bs", 512 * h, 512 * h + n, 1, 0, 11, key="bs%d" % h), b("pb%d" % (4 + h), 0, n, 1, 0, 11), AF.Copy)
-
-    def table(h):
-        n = 512 if h < 3 else 128
-        mm(b("pb%d" % (4 + h), 0, n), b("EE", p1=11), b("bs", 512 * h, 512 * h + n, 1, 0, 11, key="bs%d" % h))
-        act(b("Tb", 512 * h, 512 * h + n), b("pb%d" % (4 + h), 0, n), AF.Copy)
-
-    def consts_a():
-        cp(b("idf"), b("ipb"))
-        ts(b("hc", 0, 136, key="hc0"), b("ipb"), -16.0, OP.mult)
-        cp(b("hc", 136, 272, key="hc1"), b("ipb"))
-        ts(b("f16p"), b("ipb"), 16.0, OP.mult)
-        cp(b("kcb"), b("kcg"))
-        ts(b("bk", 0, 8, key="bk0"), b("selb"), 4096.0, OP.mult)
-        ts(b("bk", 8, 16, key="bk1"), b("selb"), 4096.0, OP.mult)
-
-    def consts_b():
-        ts(b("iv"), b("pin"), 4, OP.logical_shift_right, 1, OP.bitwise_and)
-        for j, m in enumerate((-1.0, -16.0, 1.0, float(FAR))):
-            ts(b("sb", 8 * j, 8 * j + 8, key="sb%d" % j), b("selb"), m, OP.mult)
-        ts(b("rmi"), b("rmi"), 15, OP.bitwise_and)
-        cp(b("mO"), b("iv", 0, 1))
-        ts(b("mE"), b("iv", 0, 1), -1.0, OP.mult, 1.0, OP.add)
-        ts(b("rmask"), b("rmi"), 0.0, OP.is_equal)
-        ts(b("pr"), b("pin"), 15, OP.bitwise_and)
-        ms(b("one8"), 1.0)
-        ms(b("Dv", 8, 16, key="Dv1"), 1.0)
-        tt(b("iGL"), b("pr"), b("m16"), OP.add)
-        ts(b("p128"), b("pin", 0, 1), 128.0, OP.add)
-        ts(b("m128"), b("pin", 0, 1), -1.0, OP.mult, -128.0, OP.add)
-        ts(b("dmp"), b("iGL"), float(DUMP), OP.add)
-        ts(b("dmp16"), b("iGL"), float(DUMP - 1600), OP.add)
-        for k in range(4):
-            ts(b("nGL", 8 * k, 8 * k + 8, key="nGL%d" % k), b("iGL"), float(V0 + L * k), OP.add)
-
-    def consts_c():
-        cp(b("thf", 0, 128, 1, 0, 8), b("thi", 0, 128, 1, 0, 8))
-        mm(b("pb3", 0, 8), b("thf", 0, 128, 1, 0, 8), b("idf", 1, 9, 1, 0, 8))
-        cp(b("lim"), b("pb3", 0, 8))
-        ts(b("lim1"), b("lim"), 1.0, OP.add)
-
-    def consts_d():
-        tt(b("Di"), b("idb"), b("ci"), OP.mult)
-        ts(b("I128"), b("idb"), 128.0, OP.mult)
-        for s in range(4):
-            ts(b("GN", 128 + 128 * s, 256 + 128 * s, key="GN%d" % s), b("idb"), float(128 * (s - 24)), OP.mult)
-        ts(b("GE", 128, 256, key="GE1"), b("idb"), 4096.0, OP.mult)
-        ts(b("m1c"), b("idb"), -1.0, OP.mult)
-
-    def x_forms(src):
-        act(b("xs"), src, AF.Identity, MAGIC)
-        act(b("xp"), src, AF.Identity, 256.0)
-
-    def turn_x():
-        mm(b("pb3", 0, 128), b("xb"), b("idb"))
-        mm(b("pb1", 384, 512), b("idb"), b("xb"))
-        act(b("xT"), b("pb3", 0, 128), AF.Copy)
-
-    def preload_x(cs):
-        for c in cs:
-            mm(b("pb%d" % (4 + c)), b("xT"), b("R", 512 * c, 512 * c + 512), True, False)
-
-    def codes_masked(d):
-        for m in "EO":
-            if d == "cod":
-                ts(b(d + m), b(d), b("m" + m), OP.mult)
-            else:
-                act(b(d + m), b(d), AF.Copy, 0.0, b("m" + m))
-
-    def equal(d, bank, h):
-        mm(b(bank), b("idb"), b("trib"), True, False)
-        for j in range(4):
-            w = 4 * h + j
-            p = w // 2 * 32
-            if j == 2:
-                need("t", [bank], [])
-            mm(b(bank, 128 * j, 128 * j + 128), b(d, 0, 128, 1, p, p + 32), b(d + ("O" if w % 2 else "E"), 0, 128, 1, p, p + 32),
-               False, j == 3)
-
-    def count(eq, mask, o):
-        for w in range(8):
-            mm(b(o[0], o[1] + w, o[1] + w + 1), b(eq, 128 * w, 128 * w + 128, key=eq + str(w // 4)), b(mask, w, w + 1))
-
-    def to_lists(ex, n, o, scales):
-        for j in range(n):
-            mm(b(o[0], o[1] + 8 * j, o[1] + 8 * j + 8), b(ex, 128 * j, 128 * j + 128), b("sb", 8 * scales[j], 8 * scales[j] + 8, key="sb%d" % scales[j]))
-
-    def expand(ex, src, n):
-        tt(b(ex, 0, 128 * n), ind(src, bl(8 * n)), b("rmask", 0, 128 * n), OP.mult)
-
-    def front_v(s, vu):
-        ts(b("cvu"), ind(b("KI") if s == 0 else b("C", 0, WIN), vu), float(E1), OP.min)
-
-    def front(s, vu):
-        act(b("r"), ind(b("C", 0, WIN), vu), AF.Relu, float(E1), -1.0)
-        act(b("y"), b("r"), AF.Identity, MAGIC, 1.0 / 127.95)
-        act(b("h8"), b("y"), AF.Identity, -8 * MAGIC, 8.0)
-        act(b("Fm"), b("r"), AF.Sign)
-        mm(b("pb0", 272, 408), one, b("kcb", 272, 408, 1, 0, 1), True, False)
-        mm(b("pb0", 272, 408), b("Fm"), b("f16p"), False, True)
-        mm(b("pb0", 0, 272), one, b("kcb", 0, 272, 1, 0, 1), True, False)
-        mm(b("pb0", 0, 136), b("r"), b("idf"), False, False)
-        mm(b("pb0", 0, 272), b("h8"), b("hc", key=["hc0", "hc1"]), False, False)
-
-    def gather(c):
-        act(b("ag", 512 * c, 512 * c + 512, key="ag%d" % c), ind(b("A", 0, WIN), b("dvu", 32 * c, 32 * c + 32)), AF.Copy)
-
-    def less_x(c):
-        mm(b("pb%d" % (4 + c)), b("idb"), b("ag", 512 * c, 512 * c + 512, key="ag%d" % c), False, True)
-
-    def away(c):
-        act(b("ab2", 512 * c, 512 * c + 512, key="ab2%d" % c), b("pb%d" % (4 + c)), AF.Abs)
-
-    def sums2(l0, l1, cs):
-        for k in range(16):
-            mm(b("pb0", k, 128, 16, l0, l1), b("ab2", 16 * l0 + k, 16 * l1, 16, key=["ab2%d" % c for c in cs]), b("selb"))
-
-    def step(s, vu, tv):
-        t = s % ST
-        n0 = V0 + L * s
-        vf = b(tv, 0, 8)
-        if s == 0:
-            front_v(0, vu)
-            for h in range(4):
-                table(h)
-            cp(b("C", 0, V0), b("KI"))
-            consts_a()
-        if s != 2:
-            front(s, vu)
-        if s == 0:
-            turn_x()
-        if s != 2:
-            preload_x((0, 1, 2, 3))
-        for j, (l0, n) in enumerate(PIECES):
-            c0, c1 = 16 * l0, 16 * (l0 + n)
-            dj = b("df", c0, c1, key="df%d" % j)
-            if s == 2:
-                tt(dj, ind(b("xi"), bl(n, l0)), b("ag", c0, c1, key="ag%d" % (l0 // 32)), OP.subtract)
-                if j == 0:
-                    cp(b("xb"), b("xi"))
-            else:
-                tt(dj, ind(b("A", 0, WIN), b("cvu", l0, l0 + n)), b("xrep", c0, c1, key="xr"), OP.subtract)
-            act(dj, dj, AF.Abs)
-            if s == 2 and j == 0:
-                turn_x()
-        if s != 2:
-            act(b("cod"), ind(b("Tb", 0, WIN), vu), AF.Copy)
-            act(b("cvf"), ind(b("C", 0, WIN), vu), AF.Copy)
-        for l0, l1, js in ((0, 64, (0, 1)), (64, 96, (2,)), (96, 128, (3, 4))):
-            for k in range(16):
-                mm(b("pb0", 1 + k, 272, 17, l0, l1), b("df", 16 * l0 + k, 16 * l1, 16, key=["df%d" % j for j in js]),
-                   b("bk", key=["bk0", "bk1"]), False, k == 15)
-        if t == 1:
-            tt(b("rest"), b("Sf"), b("an"), OP.is_lt)
-            tt(b("ov"), b("Sf"), b("anr0"), OP.is_lt)
-            act(b("nonr"), b("rest"), AF.Identity, 1.0, -1.0)
-            act(b("nov"), b("ov"), AF.Identity, b("p128"), b("m128"))
-            mm(b("pb1", 96, 104), b("tri"), b("ov"))
-        if s == 0:
-            consts_b()
-        if s in (0, 2):
-            x_forms(b("xb"))
-        if s == 2:
-            for k in range(16):
-                cp(b("xrep", k, 2048, 16, key="xr"), b("xb"))
-        tt(b("X3", 8, 16, key="X3c"), vf, b("dmp"), OP.subtract)
-        tt(b("X3", 16, 24, key="X3b"), b("nGL", 8 * s, 8 * s + 8, key="nGL%d" % s), vf, OP.subtract)
-        act(b("v16"), vf, AF.Identity, -1600.0)
-        scan(b("m1"), b("RM"), b("pb0", 0, 272), OP.max, OP.min)
-        cp(b("m1e"), b("m1", 16, 272, 17))
-        ts(b("dec"), b("m1e"), 127, OP.bitwise_and)
-        expand("ex", b("dec"), 2)
-        if s == 2:
-            preload_x((0, 1))
-        to_b = b("pb1", 0, 8)
-        mm(to_b, b("ex", 0, 128), b("sb", 0, 8, key="sb0"), True, False)
-        mm(to_b, b("ex", 128, 256), b("sb", 8, 16, key="sb1"), False, True)
-        if s == 2:
-            preload_x((2, 3))
-        else:
-            codes_masked("cod")
-            equal("cod", "pb2", 0)
-            equal("cod", "pb3", 1)
-        tt(b("cand", 1, 272), b("m1", 0, 271), b("pb0", 1, 272), OP.max)
-        ts(b("bu"), to_b, 1600.0, OP.add)
-        ts(b("dvu"), ind(b("C", 0, WIN), b("bu")), float(E1), OP.min)
-        tt(b("X3", 0, 8, key="X3a"), to_b, b("v16"), OP.subtract)
-        tt(b("bd"), to_b, b("dmp16"), OP.subtract)
-        act(b("abm"), ind(b("A", 0, WIN), b("bu")), AF.Identity, -0.5)
-        act(b("am4"), b("abm"), AF.Identity, -3.5)
-        act(b("ap4"), b("abm"), AF.Identity, 4.5)
-        gather(0)
-        if s != 2:
-            act(b("eqa", 0, 512, key="eqa0"), b("pb2"), AF.Relu, -10.0)
-            act(b("eqa", 512, 1024, key="eqa1"), b("pb3"), AF.Relu, -10.0)
-        scan(b("m2", 1, 272), b("RM", 1, 272), b("cand", 1, 272), OP.max, OP.min)
-        cp(b("m2e"), b("m2", 16, 272, 17))
-        ts(b("dec2"), b("m2e"), 127, OP.bitwise_and)
-        expand("ex2", b("dec2"), 2)
-        ts(b("eb"), b("m1e", 0, 8), 12, OP.logical_shift_right)
-        ts(b("kk", 0, 8, key="kk0"), b("m1e", 0, 8), 7, OP.logical_shift_right, 31, OP.bitwise_and)
-        ts(b("kq"), b("m2e", 0, 8), 7, OP.logical_shift_right, 31, OP.bitwise_and)
-        to_q = b("pb1", 8, 16)
-        mm(to_q, b("ex2", 0, 128), b("sb", 0, 8, key="sb0"), True, False)
-        mm(to_q, b("ex2", 128, 256), b("sb", 8, 16, key="sb1"), False, True)
-        scan(b("k0s"), b("RM", 0, 136), b("pb0", 272, 408), OP.max, OP.min)
-        ts(b("qu"), to_q, 1600.0, OP.add)
-        if s != 2:
-            count("eqa", "nonr" if t == 1 else "one8", ("pb1", 16))
-        tt(b("sm"), ind(b("A", 0, WIN), b("qu")), b("abm"), OP.add)
-        if s == 0:
-            consts_c()
-        ym = b("pb2", 384, 512)
-        ts(ym, b("sm"), 0.5, OP.mult, MAGIC, OP.add)
-        tt(b("dM"), b("xs"), ym, OP.subtract)
-        tt(b("pb1", 256, 384), b("pb1", 384, 512), b("am4"), OP.max)
-        tt(b("hv"), b("pb1", 256, 384), b("ap4"), OP.min)
-
-        less_x(0)
-        act(b("bod"), ind(b("Tb", 0, WIN), b("bu")), AF.Copy)
-        act(b("nrm"), b("k0s", 16, 136, 17), AF.Relu, -16.0)
-        codes_masked("bod")
-        act(b("absM"), b("dM"), AF.Abs)
-        mm(b("pb1", 24, 32), b("absM"), b("selb"))
-        gather(1)
-        less_x(1)
-        equal("bod", "pb3", 0)
-        away(0)
-        if s != 2:
-            equal("bod", "pb4", 1)
-        gather(2)
-        act(b("Mb"), ym, AF.Identity, -MAGIC)
-        away(1)
-        gather(3)
-        act(b("dvf"), ind(b("C", 0, WIN), b("bu")), AF.Copy)
-
-        ac = b("gm3", 8, 16, key="ac")
-        if s == 2:
-            cp(ac, b("act0"))
-        else:
-            tt(ac, b("pb1", 16, 24), b("one8" if s == 0 else "nonr"), OP.is_lt)
-        em = b("pb1", 24, 32)
-        ah, am = b("gm3", 0, 8, key="ah"), b("gm3", 16, 24, key="am")
-        tt(b("hm"), em, b("eb"), OP.min)
-        tt(b("he"), em, b("eb"), OP.is_ge)
-        tt(b("nn"), b("lim"), b("hm"), OP.is_lt)
-        tt(b("T0"), b("lim1"), b("hm"), OP.min)
-        tt(b("an"), b("nn"), ac, OP.mult)
-        tt(b("Tt"), b("T0"), ac, OP.mult)
-        tt(b("ah0"), ac, b("an"), OP.subtract)
-        tt(b("k2"), b("an"), b("k0s", 16, 136, 17), OP.mult)
-        tt(ah, b("ah0"), b("he"), OP.mult)
-        tt(b("anr0"), b("an"), b("nrm"), OP.mult)
-        tt(am, b("ah0"), ah, OP.subtract)
-        if s == 0:
-            cp(b("act0"), ac)
-        tt(b("k1"), am, b("kk", 0, 8, key="kk0"), OP.mult)
-        tt(b("kk", 16, 24, key="kk2"), am, b("kq"), OP.mult)
-        tt(b("kk", 8, 16, key="kk1"), b("k1"), b("k2"), OP.add)
-        tt(b("gm3", 24, 32, key="ax"), b("an"), b("anr0"), OP.subtract)
-        tt(b("oh"), ind(b("kk", key=["kk0", "kk1", "kk2"]), bl(24)), b("kpat"), OP.is_equal)
-        if s == 0:
-            consts_d()
-        ohb, ohn, ohe = b("oh", 0, 128), b("oh", 128, 256), b("oh", 256, 384)
-        i8 = b("GE", 128, 256, key="GE1")
-        mm(b("pb2", 256, 384), ohb, i8)
-        mm(b("pb2", 0, 128), ohn, i8, True, False)
-        mm(b("pb2", 0, 128), ohe, i8, False, True)
-        mm(b("pb2", 128, 256), ohn, b("GN", 128 + 128 * s, 256 + 128 * s, key="GN%d" % s), True, False)
-        mm(b("pb2", 128, 256), ohn, b("Di"), False, False)
-        mm(b("pb2", 128, 256), ohe, b("m1c"), False, True)
-        less_x(2)
-        act(b("gx"), ind(b("gm3", 16, 32, key=["am", "ax"]), bl(16)), AF.Copy)
-        away(2)
-        if t == 1:
-            send_rank()
-        tt(b("gm"), ind(b("gm3", 0, 24, key=["ah", "ac", "am"]), bl(24)), b("rmask"), OP.mult)
-        to_lists("gm", 3, ("pb1", 32), (2, 2, 2))
-        if t == 1:
-            to_lists("exP", 1, ("pb1", 80), (2,))
-        mm(b("pb5", 0, 128), b("gx", 0, 128), b("idb"))
-        mm(b("pb5", 128, 256), b("gx", 128, 256), b("idb"))
-        less_x(3)
-        sums2(0, 96, (0, 1, 2))
-        away(3)
-        sums2(96, 128, (3,))
-        if s == 2:
-            equal("bod", "pb4", 1)
-        tt(b("w3"), b("cvf"), b("pb2", 256, 384), OP.max)
-        tt(b("wal"), b("cvf"), b("pb2", 0, 128), OP.max)
-        act(b("pb6", 0, 128), b("w3"), AF.Relu, 8 * 4095.0, -8.0)
-        tt(b("ral"), b("wal"), b("pb2", 128, 256), OP.add)
-        act(b("pb7", 0, 128), b("pb2", 0, 128), AF.Relu, 4095.0, -1.0)
-        act(b("eqb", 0, 512, key="eqb0"), b("pb3"), AF.Relu, -10.0)
-        act(b("eqb", 512, 1024, key="eqb1"), b("pb4"), AF.Relu, -10.0)
-        tt(b("g3"), b("pb1", 32, 56), b("X3", key=["X3a", "X3b", "X3c"]), OP.mult)
-        tt(b("pb5", 256, 384), b("pb5", 0, 128), b("Mb"), OP.mult)
-        tt(b(tv, 8, 16, key=tv + "u"), b("g3", 8, 16), b("dmp"), OP.add)
-        tt(b("t2"), b("pb5", 128, 256), b("xb"), OP.mult)
-        cp(b("uvu"), b(tv, 8, 16, key=tv + "u"))
-        tt(b("Dv", 0, 8, key="Dv0"), b("g3", 0, 8), b("g3", 16, 24), OP.add)
-        scatter(b("C"), b("uvu"), b("ral"))
-        if t == 1:
-            send_list(s - 1)
-        tt(b("pb5", 384, 512), b("pb6", 0, 128), b("dvf"), OP.add)
-        tt(b("rsp"), b("w3"), b("pb5", 384, 512), OP.min)
-
-        scan(b("fsm"), b("RM2"), b("pb0", 0, 128), OP.max, OP.min)
-        tt(b("Sf"), b("fsm", 15, 128, 16), b("Tt"), OP.is_lt)
-        act(b("exU"), ind(b("Sf"), bl(8)), AF.Copy)
-        if t == 1:
-            tt(b("ov"), b("Sf"), b("anr0"), OP.is_lt)
-            ts(b("nov"), b("ov"), 0.0, OP.is_equal, b("p128"), OP.mult)
-            mm(b("pb3", 8, 16), b("tri"), b("ov"))
-        expand("exS", b("Sf"), 1)
-        if t == 1:
-            tt(b("pos"), b("pb3", 8, 16), b("nov"), OP.max)
-            expand("exP", b("pos"), 1)
-        tt(b("hF"), b("Sf"), ah, OP.is_lt)
-        mm(b("pb1", 56, 64), one, b("onesb", 0, 8, 1, 0, 1), True, False)
-        mm(b("pb1", 56, 64), b("exS"), b("sb", 0, 8, key="sb0"), False, True)
-        mm(b("pb1", 64, 72), b("exS"), b("sb", 24, 32, key="sb3"))
-        if t == 1:
-            to_lists("exP", 1, ("pb1", 80), (2,))
-            tt(b("An"), b("pb5", 256, 384), b("t2"), OP.add)
-            tt(b("cb"), b("pb7", 0, 128), b("cvf"), OP.max)
-            send_list(s)
-        count("eqb", "hF", ("pb3", 0))
-        if t == 0:
-            tt(b("An"), b("pb5", 256, 384), b("t2"), OP.add)
-            tt(b("cb"), b("pb7", 0, 128), b("cvf"), OP.max)
-        tt(b("q1"), b("pb1", 56, 72), b("Dv", key=["Dv0", "Dv1"]), OP.mult)
-        tt(b("vf", 0, 16, key="vf"), b("q1"), b(tv, 0, 16, key=[tv, tv + "u"]), OP.add)
-        cp(b("vu2"), b("vf", 0, 16, key="vf"))
-        scatter(b("CW", key="C"), b("vu2", 8, 16), b("rsp"))
-        mm(b("pb2", 128, 256), b("exU"), b("GE", 128, 256, key="GE1"), True, False)
-        mm(b("pb2", 128, 256), b("exU"), b("m1c"), False, True)
-        mm(b("pb2", 0, 128), one, one, True, False)
-        mm(b("pb2", 0, 128), b("exU"), b("m1c"), False, True)
-        tt(b("h1"), b("pb3", 0, 8), b("hF"), OP.is_lt)
-        expand("exH", b("h1"), 1)
-        tt(b("C", n0, n0 + L), b("pb2", 128, 256), b("cb"), OP.max)
-        to_lists("exH", 1, ("pb1", 72), (2,))
-        if s == 3:
-            dma("y", "ld5", T.yc[:], b("C", 0, W)[0], ["C"], ["yc"])
-        tt(b("A", n0, n0 + L), b("pb2", 0, 128), b("An"), OP.mult)
-        tt(b("oA"), b("pb1", 72, 80), b("bd"), OP.mult)
-        if s < 3:
-            front_v(s + 1, b("tu") if s == 1 else b("vu2", 0, 8))
-        tt(b("oA"), b("oA"), b("dmp"), OP.add)
-        if t == 1:
-            tt(b("nF"), b("Sf"), b("an"), OP.is_lt)
-        cp(b("oAu"), b("oA"))
-        scatter(b("A"), b("oAu"), b("hv"))
-        if s == 3:
-            dma("y", "ld6", T.ya[:], b("A", 0, W)[0], ["A"], ["ya"])
-        if t == 1:
-            tt(b("rest2"), b("rest"), b("nF"), OP.add)
-            act(b("nonr2"), b("rest2"), AF.Identity, 1.0, -1.0)
-
-    def send_rank():
-        tt(b("pos"), b("pb1", 96, 104), b("nov"), OP.max)
-        expand("exP", b("pos"), 1)
-
-    def send_list(s):
-        h = hops(T, topo, rank, s)
-        m = "msg%d" % s
-        cp(b("posu"), b("pb1", 80, 88))
-        scatter(b(m), b("posu"), b("xp"))
-        need("g", [m], [])
-        n = engines_of(topo, core, h[1])
-        rid, pid = topo.addr(h[1], core)
-        if len(h) == 3:
-            to, sem = T["rl%d" % s][:, 0:CAP], T.sem["rr%d" % s]
-        else:
-            to, sem = T["come%d" % (s // ST)][:, CAP * (s % ST):CAP * (s % ST) + CAP], T.sem["in%d" % s]
-        g.remote_dma(to, T[m][:, 0:CAP], sem, T.sem["ls%d" % s], pid, rid, emask(topo, core, h[1], n))
-
-    for s in range(ST * RO):
-        h = hops(T, topo, (rank - 1 - s % (NR - 1)) % NR, s)
-        n = engines_of(topo, h[-2], h[-1])
-        wr["come%d_%d" % (s // ST, s % ST)] = ("remote", "in%d" % s, n, {"in%d" % s: n})
-        cnt["in%d" % s] = n
-
-    def round_end(s):
-        cm = "come%d" % (s // ST)
-        mm(b("pb3", 16, 24), b("tri"), b("rest2"), True, False)
-        mm(b("pb3", 16, 24), b("I128"), b("nonr2"), False, True)
-        tt(b("dM"), ind(b("A", 0, WIN), b("vu2", 0, 8)), b("xb"), OP.subtract)
-        act(b("ad"), b("dM"), AF.Abs)
-        cp(b("nrs"), b("pb3", 16, 24))
-        expand("exN", b("nrs"), 1)
-        to_lists("exN", 1, ("pb1", 88), (2,))
-        if s == 1:
-            front(2, b("tu"))
-            act(b("cvf"), ind(b("C", 0, WIN), b("tu")), AF.Copy)
-            for c in range(4):
-                o, a = b("ag", 512 * c, 512 * c + 512, key="ag%d" % c), ind(b("A", 0, WIN), b("cvu", 32 * c, 32 * c + 32))
-                if c < 3:
-                    act(o, a, AF.Copy)
-                else:
-                    cp(o, a)
-        ts(b("msk"), b(cm, 0, CAP, key=cm + "_0"), 0.5, OP.is_gt)
-        op("v", lambda e: e.tensor_reduce(b("n0")[0], b("msk")[0], AxisListType.X, OP.add), ["msk"], ["n0"])
-        ts(b("cd"), b("n0"), -1.0, OP.mult, float(CAP), OP.add)
-        ts(b("ge"), b("pb1", 88, 96), b("n0"), OP.is_ge, b("cd"), OP.mult)
-        tt(b("idx"), b("pb1", 88, 96), b("ge"), OP.add)
-        ts(b("iu"), b("idx"), 64.0, OP.min)
-        tt(b("hx"), ind(b(cm, key=[cm + "_0", cm + "_1", cm + "z"]), b("iu")), b("ad"), OP.max)
-        ts(b("xi"), b("hx"), 255, OP.bitwise_and)
-
-    for s in range(4):
-        if s % ST == 0:
-            step(s, b("tu"), "topf")
-        else:
-            step(s, b("vu2", 0, 8), "vf")
-            round_end(s)
-    cp(b("xb"), b("xi"))
-    dma("y", "ld7", T.yx[:], b("xb")[0], ["xb"], ["yx"])
+            need(q, o["R"], o["W"], True)
+            o["call"](eng[q]).then_inc(T.sem[kind], 16)
+            cnt[kind] = 16
+            note("dma" + kind, kind, 16, know[q], o["R"], o["W"])
     for n in sorted(cnt):
         if cnt[n] and know["g"].get(n, 0) < cnt[n]:
             g.wait_ge(T.sem[n], cnt[n])

@@ -7,9 +7,10 @@ WIN = W + 8
 BIG = float(2 ** 30)
 MAGIC = float(3 * 2 ** 22)
 M = 2048.0
-P1 = [4, 4, 4, 2, 1, 1]
-P2S = [(0, "pb7"), (4, "pb0")]
-P2V = [4, 2, 1, 1]
+P1 = [(2, None), (3, None), (4, "pb7"), (3, None), (2, None), (2, None)]
+P1X = [(2, None), (3, None), (3, "pb7"), (3, None), (3, "pb1"), (2, None)]
+P2 = [(2, None), (3, None), (3, "pb7"), (3, None), (3, None), (2, None)]
+ROUNDS = 6
 WAKE, GAT, SCA = 220.0, 1.5, 3.0
 
 SLOT = {}
@@ -22,17 +23,17 @@ def _s(kind, **kw):
         SIZE[kind] += (w + 15) // 16 * 16
 
 
-_s("B", AW=128 + WIN, xrep=2048, D=2048, Dab=2048, ag=2048, AN=272, xP=128, ones=144, B=144, sel2=8, selb=8, bones=128, lo=128, lt=128,
-   ld=128, nl8=128, I=128, nI=128, I63=128, nI63=128, nI128=128, nI8=128, IM=128, sh=128, cr=1536, cnt0=136, emc=128, tab=128,
-   emp=128, oh=256, dd=256, cl=128, absM=128, hv=128, E=1088, fl0=32, fl1=32, rest2=8)
-_s("F", CW=128 + WIN, iot=WIN, RW=416, CN=272, idf=128, dm=128, RM=128, RM2=128, tr=288, dl=128, rr=272, r0=128, e=128, cand=128, pay=128,
-   row=144, r17=144, clv=136, clb=136, zv=136, zb=136, w3=128, w4=128, rsp=128, rpre=128, dvf=128, es=128, fs=128, xm=128, xp=128,
-   dM=128, ad=128, thf=128, thx=128, lim=8, lim1=8, jL=8, cj=8, topf=8, nL=32, acB0=32, acB1=32, nac0=8, nac1=8, rB=16, W4=32, G1=16, G2=16,
-   UU=32, U1=8, U4=32, Tt4=32, FL=40, nfl=32, TH=32, coef=48, prod=48, d0=64, d1=64, s2=48, sp=8, nonr=8, one8=8, hf=8, pz=8, nrs=8, ge=8,
-   idx=8, msk=32, n0=1, cd=1, r7=1, hi=1, p128=1, pf=1, tmp=16, tmp2=16, tmp3=16)
-_s("I", KI=WIN, tp=8, thi=128, pin=16, pa=16, pb=16, ci=128, ri=128, dec=16, dk=16, hx=128, xi=128)
-_s("U", tu=8, tu2=16, cvu=128, dvu=128, bu=8, bu2=16, du=16, ku=16, uvu0=8, uvu1=8, lu=24, vu2=16, spu=8, oAu=8, posu=8, iu=8,
-   plist=128, lperm=8, l17=10, lend=8, lsel=8, lF=2, lr=2, lz=2, lg=2, lfl=4)
+_s("B", AW=128 + WIN, xrep=2048, D=2048, Dab=2048, ag=2048, AN=272, xP=128, xd=128, nr2=640, ones=144, B=144, B2=144, nB=144, pw=128,
+   bones=128, lo=128, lt=128, ld=128, nl8=128, I=128, nI=128, nI2=128, I63=128, nI63=128, nI128=128, nI8=128, IM=128, sh=128, cr=1024,
+   cnt0=136, emc=128, tab=144, emp=128, oh=256, dd=256, cl=256, absM=128, hv=128, E=1088, fl0=32, fl1=32, rest2=8, msk=32)
+_s("F", CW=128 + WIN, iot=WIN, RW=544, CN=272, idf=128, dm=128, RM=128, RM2=128, tr=288, dl=128, rr=272, r0=128, e=128, cand=128, pay=128,
+   row=144, r17=144, clv=136, clb=136, zv=136, zb=136, w3=128, w4=128, rpre=128, dvf=128, es=128, fs=128, xm=128, xp=128,
+   ad=128, thf=128, thx=128, lim=8, lim1=8, jL=8, cj=8, topf=8, nL=32, acB0=32, acB1=32, nac0=8, nac1=8, rB=16, W4=32, G2=16,
+   UU=32, U1=8, U4=32, Tt4=32, FL=40, nfl=32, TH=32, coef=48, prod=56, d0=64, d1=64, s2=48, df=8, mbx=8, nonr=8, one8=8, hf=8, pz=8,
+   nrs=8, ge=8, idx=8, n0=1, cd=1, r7=1, hi=1, p128=1, pf=1, pP=1, pG=1, pQ=1, tmp=16, tmp2=16, tmp3=16)
+_s("I", KI=WIN, tp=8, thi=128, pin=16, pa=16, pc=16, ci=128, ri=128, dec=16, dk=16, hx=128, xi=128)
+_s("U", tu=8, cvu=128, dvu=128, bu=8, du=16, ku=16, uvu0=8, uvu1=8, lu=24, oAu=8, posu=8, iu=8,
+   plist=128, lperm=8, l17=10, lend=8, lsel=8, lF=2, lr=2, lz=2, lg=2, lfl=4, lxd=8)
 SLOT["C"] = ("arF", SLOT["CW"][1] + 128, WIN)
 SLOT["A"] = ("arB", SLOT["AW"][1] + 128, WIN)
 SLOT["cvf"] = ("arF", SLOT["RW"][1] + 16, 128)
@@ -94,9 +95,15 @@ def relay(g, core, T, topo):
 
 def order_calls(ops):
     n = len(ops)
-    wr, rd, pre = {}, {}, []
+    wr, rd, pre, adds = {}, {}, [], {}
     for i, o in enumerate(ops):
         d = {}
+        for k in o["R"] + o["W"]:
+            if not o["adds"]:
+                for j in adds.get(k, []):
+                    d[j] = 0.0 if o["q"] == "t" else WAKE
+        if o["adds"]:
+            adds.setdefault(o["W"][0], []).append(i)
         for k in o["R"]:
             if k in wr:
                 d[wr[k]] = WAKE
@@ -110,30 +117,56 @@ def order_calls(ops):
         for k in o["R"]:
             rd.setdefault(k, []).append(i)
         for k in o["W"]:
-            wr[k] = i
-            rd[k] = []
+            if not o["adds"]:
+                wr[k] = i
+                rd[k] = []
+                adds[k] = []
         d.pop(i, None)
         pre.append(d)
-    way = [0.0] * n
+    post = [{} for _ in range(n)]
+    for i in range(n):
+        for j, w in pre[i].items():
+            post[j][i] = w
+
+    def place(rank, before, back):
+        busy, start, end = {}, [0.0] * n, [0.0] * n
+        for i in rank:
+            c, lag, row = ops[i]["c"], ops[i]["lag"], busy.setdefault(ops[i]["q"], [])
+            t = max([end[j] + w for j, w in before[i].items()] + [0.0]) + (lag if back else 0.0)
+            at = len(row)
+            for m, (a, z) in enumerate(row):
+                if z <= t:
+                    continue
+                if t + c <= a:
+                    at = m
+                    break
+                t = z
+            row.insert(at, (t, t + c))
+            start[i], end[i] = t, t + c + (0.0 if back else lag)
+        return start, end
+
+    way, behind = [0.0] * n, {}
     for i in range(n - 1, -1, -1):
+        k = ops[i]["adds"]
+        if k:
+            way[i] = max(way[i], behind.get(k, 0.0))
         way[i] += ops[i]["c"] + ops[i]["lag"]
+        behind[k] = way[i]
         for j, w in pre[i].items():
             way[j] = max(way[j], way[i] + w)
-    busy, start, end = {}, [0.0] * n, [0.0] * n
-    for i in sorted(range(n), key=lambda i: (-way[i], i)):
-        t = max([end[j] + w for j, w in pre[i].items()] + [0.0])
-        c, row = ops[i]["c"], busy.setdefault(ops[i]["q"], [])
-        at = len(row)
-        for m, (a, z) in enumerate(row):
-            if z <= t:
-                continue
-            if t + c <= a:
-                at = m
-                break
-            t = z
-        row.insert(at, (t, t + c))
-        start[i], end[i] = t, t + c + ops[i]["lag"]
-    return sorted(range(n), key=lambda i: (start[i], i))
+    ORDER["dag"] = (ops, pre, post, list(way))
+    best = None
+    for _ in range(ROUNDS):
+        start, end = place(sorted(range(n), key=lambda i: (-way[i], i)), pre, False)
+        if best is None or max(end) < best[0]:
+            best = (max(end), start)
+        way = place(sorted(range(n), key=lambda i: (-end[i], -i)), post, True)[1]
+    return sorted(range(n), key=lambda i: (best[1][i], i))
+
+
+def parts(pieces, scalar):
+    return [p for j, (n, bank) in enumerate(pieces) if bool(bank) == scalar
+            for p in range(sum(q[0] for q in pieces[:j]), sum(q[0] for q in pieces[:j + 1]))]
 
 
 def rank_program(g, core, T, topo):
@@ -144,8 +177,8 @@ def rank_program(g, core, T, topo):
     eng = {"v": g.vector, "s": g.scalar, "t": g.tensor, "g": g, "y": g.sync}
     ops = []
 
-    def op(q, call, R, Wk, c, lag=0.0, dma=None):
-        ops.append({"q": q, "call": call, "R": R, "W": Wk, "c": c * 0.83, "lag": lag, "dma": dma})
+    def op(q, call, R, Wk, c, lag=0.0, dma=None, adds=None):
+        ops.append({"q": q, "call": call, "R": R, "W": Wk, "c": c * 0.83, "lag": lag, "dma": dma, "adds": adds})
 
     def dma(q, sem, out, in_, R, Wk, lag):
         op(q, lambda e: e.dma_start(out, in_), R, Wk, 60, lag, sem)
@@ -203,9 +236,28 @@ def rank_program(g, core, T, topo):
     def mm(o, l, r, start=True, stop=True):
         op("t", lambda e: e.matmul(o[0], l[0], r[0], start, stop), ks(l, r), ks(o), max(min(64, l[2]), r[2]) * (4 if l[3] == "arF" else 1))
 
+    left, opened = {}, {}
+
+    def begin(o, l, r):
+        opened[o[1][0]] = len(ops)
+        mm(o, l, r, True, False)
+
+    def add(o, l, r):
+        k = (o[1][0], opened[o[1][0]])
+        left[k] = left.get(k, 0) + 1
+
+        def call(e):
+            left[k] -= 1
+            return e.matmul(o[0], l[0], r[0], False, left[k] == 0)
+        op("t", call, ks(l, r), ks(o), max(min(64, l[2]), r[2]) * (4 if l[3] == "arF" else 1), adds=k)
+
     def mms(o, pairs):
-        for j, (l, r) in enumerate(pairs):
-            mm(o, l, r, j == 0, j == len(pairs) - 1)
+        if len(pairs) == 1:
+            mm(o, *pairs[0])
+        else:
+            begin(o, *pairs[0])
+            for l, r in pairs[1:]:
+                add(o, l, r)
 
     def io(o, pat, base, cm):
         if o[3] == "arI":
@@ -213,89 +265,93 @@ def rank_program(g, core, T, topo):
         else:
             op("g", lambda e: e.iota(o[0], pat, base, cm, allow_small_or_imprecise_dtypes=True), [], ks(o), 160 + 2 * o[2])
 
-    def asel(o, a, pat, f, fill, base, cm):
-        op("g", lambda e: e.affine_select(o[0], a[0], pat, f, fill, base, cm), ks(a), ks(o), 200 + 2 * o[2])
+    def fill(o, v):
+        io(o, [[0, o[2]]], int(v), 0)
 
-    def row(j, n=128):
-        return b("cr", 144 * j, 144 * j + n, 1, 1, key="cr%d" % j)
+    def asel(o, a, pat, f, other, base, cm):
+        op("g", lambda e: e.affine_select(o[0], a[0], pat, f, other, base, cm), ks(a), ks(o), 200 + 2 * o[2])
 
-    ONE, JROW, R63, R65, R128, RH, R127, NROW = row(0), row(1), row(2), row(3), row(4), row(5), row(6), 0
+    def row(j):
+        return b("cr", 128 * j, 128 * j + 128, 1, 1, key="cr%d" % j)
+
+    ONE, JROW, R63, R65, R128, RH, R127 = [row(j) for j in range(7)]
     blocks = lambda t, n: ["%sb%d" % (t, k) for k in range(n)]
     Cw = lambda s: b("KI", key=["KI", "KIe"]) if s == 0 else b("C", key=["C", "Ce"] + blocks("C", 4))
     Aw = b("A", key=["A", "Ae"] + blocks("A", 4))
-    lhs = lambda p: b("B", 15 - p, 143 - p)
+    lhs = lambda p, m="B": b(m, 15 - p, 143 - p)
 
     dma("y", "ld0", b("tp")[0], T.tops[:], [], ["tp"], 1500)
     dma("y", "ld2", b("KI", 0, V0)[0], T.kids[:], [], ["KI"], 4000)
-    dma("s", "ld3", b("A", 0, V0)[0], T.a0[:], [], ["A"], 4000)
-    dma("y", "ld1", b("xb")[0], T.x0[:], [], ["xb"], 2000)
+    dma("y", "ld3", b("A", 0, V0)[0], T.a0[:], [], ["A"], 3900)
+    dma("s", "ld1", b("xb")[0], T.x0[:], [], ["xb"], 2000)
     dma("s", "ld4", b("thi", p1=8)[0], T.th[:], [], ["thi"], 2000)
-    ms(b("KI", V0, WIN, key="KIe"), 4095)
-    ms(b("C", V0, WIN, key=["Ce"] + blocks("C", 4)), 4095.0)
+    fill(b("KI", V0, WIN, key="KIe"), 4095)
+    fill(b("C", V0, WIN, key=["Ce"] + blocks("C", 4)), 4095)
     ms(b("A", V0, W, key=blocks("A", 4)), 0.0)
     ms(b("A", W, WIN, key="Ae"), 4096.0)
     ms(b("ones"), 1.0)
     ms(b("one8"), 1.0)
-    ms(b("AN", 256, 272, key="ANz"), 0.0)
-    ms(b("CN", 128, 272, key="CNz"), 4095.0)
+    fill(b("AN", 256, 272, key="ANz"), 0)
+    fill(b("AN", 0, 128, key="Mb"), 0)
+    fill(b("CN", 128, 272, key="CNz"), 4095)
     ms(b("RW", 0, 16, key="RWa"), 0.0)
     ms(b("RW", 144, 160, key="rowM"), 0.0)
     ms(b("row", 128, 144, key="rowz"), -1.0)
     ms(b("rr", 0, 16, key="rra"), -1.0)
-    ms(b("d0", key=["d0", "d0a", "d0b"]), 0.0)
-    ms(b("d1", key=["d1a", "d1b", "d1c", "d1s"]), 256.0)
+    fill(b("d0", key=["d0", "d0b"]), 0)
+    fill(b("d1", key=["d1a", "d1b", "d1c", "d1s"]), 256)
     ms(b("B"), 0.0)
     for j, v in ((0, 1.0), (2, 63.0), (3, 65.0), (4, 128.0), (5, -0.5), (6, 127.0)):
-        ms(row(j, 144), v)
-    for s in range(4):
-        ms(b("cr", 1008 + 128 * s, 1136 + 128 * s, 1, 1, key="n%d" % s), 8320.0 + V0 + L * s)
+        (fill if j in (2, 3, 4, 6) else ms)(row(j), v)
     for nm in ("RM", "RM2"):
         ms(b(nm), 0.0)
         ms(b(nm, 0, 128, 16), BIG)
     ms(b("RM2", 1, 128, 16), BIG)
     for nm in ("clv", "clb"):
-        ms(b(nm, key=[nm, nm + "t"]), BIG)
-        ms(b(nm, 0, 136, 17), -BIG)
+        fill(b(nm, key=[nm, nm + "t"]), 2 ** 23)
+        fill(b(nm, 0, 136, 17), -2 ** 23)
     for k in range(2):
-        ms(b("come%d" % k, 64, 80, key="come%dz" % k), 0.0)
+        fill(b("come%d" % k, 64, 80, key="come%dz" % k), 0)
     for k in range(4):
-        ms(b("msg%d" % k, 0, CAP), 0.0)
-    ms(b("coef", 16, 24, key="coefc"), 128.0)
-    ms(b("coef", 40, 48, key="coeff"), 256.0)
+        fill(b("msg%d" % k, 0, CAP), 0)
+    fill(b("coef", 16, 24, key="coefc"), 128)
+    fill(b("coef", 40, 48, key="coeff"), 0)
 
-    asel(b("sel2"), b("ones", 0, 8), [[-16, 8]], OP.is_ge, 0.0, 0, 1)
-    asel(b("selb"), b("sel2"), [[16, 8]], OP.is_ge, 0.0, 15, -1)
-    ts(b("B", 15, 143, 16), b("selb"), 128.0, OP.mult)
     io(b("pin"), [[0, 16]], 0, 1)
     io(b("ci"), [[1, 128]], 0, 0)
     io(b("ri"), [[1, 16], [16, 8]], 0, 0)
     cp(b("plist"), b("ri"))
-    cp(row(1), b("ci", p1=1))
-    asel(b("I"), b("ones", 0, 128), [[-1, 128]], OP.is_equal, 0.0, 0, 1)
-    for nm, v in (("nI", -1.0), ("I63", 63.0), ("nI63", -63.0), ("nI128", -128.0), ("nI8", -8320.0), ("IM", 256 * M), ("idf", 1.0)):
+    cp(JROW, b("ci", p1=1))
+    cp(b("pP"), b("pin", 0, 1))
+    ts(b("I"), b("ci"), b("pP"), OP.is_equal)
+    cp(b("iot", 0, 128, key="iot0"), b("ci"))
+    for k in range(1, 13):
+        act(b("iot", 128 * k, min(WIN, 128 * k + 128), key="iot%d" % k), b("iot", 0, min(128, WIN - 128 * k), key="iot0"), AF.Identity, 128.0 * k)
+    for nm, v in (("nI", -1.0), ("nI2", -2.0), ("I63", 63.0), ("nI63", -63.0), ("nI128", -128.0), ("nI8", -8320.0), ("IM", 256 * M), ("idf", 1.0)):
         act(b(nm), b("I"), AF.Copy, 0.0, v)
-    ts(b("pa"), b("pin"), 15, OP.bitwise_and)
+    ts(b("pa", 0, 2), b("pin", 0, 2), 15, OP.bitwise_and)
     cp(b("pf"), b("pa", 0, 1))
     ts(b("p128"), b("pa", 0, 1), 128.0, OP.mult)
-    ts(b("pb", 0, 2), b("pin", 0, 2), 7, OP.bitwise_and)
-    cp(b("r7"), b("pb", 0, 1))
-    ts(b("pb", 2, 4, key="pb_"), b("pin", 0, 2), 3, OP.logical_shift_right, 1, OP.bitwise_and)
-    cp(b("hi"), b("pb", 2, 3, key="pb_"))
+    ts(b("pc", 0, 2), b("pin", 0, 2), 7, OP.bitwise_and)
+    cp(b("r7"), b("pc", 0, 1))
+    ts(b("pc", 2, 4, key="pc_"), b("pin", 0, 2), 3, OP.logical_shift_right, 1, OP.bitwise_and)
+    cp(b("hi"), b("pc", 2, 3, key="pc_"))
     ts(b("jL"), b("ci", 0, 128, 16), b("pf"), OP.add)
-    ts(b("cj"), b("jL"), -M, OP.mult, 129 * M, OP.add)
+    act(b("cj"), b("jL"), AF.Identity, 129 * M, -M)
     for s in range(4):
-        ts(b("nL", 8 * s, 8 * s + 8, key="nL%d" % s), b("jL"), float(V0 + L * s), OP.add)
-    ts(b("coef", 8, 16, key="coefb"), b("jL"), -256.0, OP.add)
-    ts(b("coef", 32, 40, key="coefe"), b("jL"), -128.0, OP.add)
+        act(b("nL", 8 * s, 8 * s + 8, key="nL%d" % s), b("jL"), AF.Identity, float(V0 + L * s))
+    act(b("coef", 8, 16, key="coefb"), b("jL"), AF.Identity, -256.0)
+    act(b("coef", 32, 40, key="coefe"), b("jL"), AF.Identity, -128.0)
+    act(b("d1", 1, 16, 2, key="d1a"), b("jL"), AF.Identity, 384.0)
     ts(b("lend"), b("ci", 0, 128, 16), 15.0, OP.add)
-    ts(b("lF"), b("pb", 0, 2), 16.0, OP.mult, 15.0, OP.add)
-    ts(b("lz"), b("pb", 0, 2), 17.0, OP.mult, 15.0, OP.add)
-    cp(b("lr"), b("pb", 0, 2))
+    ts(b("lF"), b("pc", 0, 2), 16.0, OP.mult, 15.0, OP.add)
+    ts(b("lz"), b("pc", 0, 2), 17.0, OP.mult, 15.0, OP.add)
+    cp(b("lr"), b("pc", 0, 2))
     ts(b("tmp", 0, 1, key="tmpa"), b("hi"), 8.0, OP.mult, b("r7"), OP.add)
     ts(b("tmp", 1, 2, key="tmpb"), b("r7"), 8.0, OP.add)
     cp(b("lg"), b("tmp", 0, 2, key=["tmpa", "tmpb"]))
-    for j, (u, v) in enumerate(((0, 32), (32, 32), (24, 16), (0, 0))):
-        ts(b("tmp", 4 + j, 5 + j, key="tmp%d" % j), b("hi"), float(v - u), OP.mult, float(u), OP.add)
+    for j, (u, v) in enumerate(((0, 32), (32, 32), (24, 24), (0, 0))):
+        act(b("tmp", 4 + j, 5 + j, key="tmp%d" % j), b("hi"), AF.Identity, float(u), float(v - u))
     ts(b("lfl"), b("tmp", 4, 8, key=["tmp%d" % j for j in range(4)]), b("r7"), OP.add)
     ts(b("tmp2", 0, 1, key="tmp2a"), b("r7"), 16.0, OP.mult, b("hi"), OP.add)
     ts(b("lperm"), b("ci", 0, 16, 2), b("tmp2", 0, 1, key="tmp2a"), OP.add)
@@ -312,26 +368,41 @@ def rank_program(g, core, T, topo):
     ts(b("tmp", 8, 16, key="tmpz"), b("dec", 0, 8), 144.0, OP.mult)
     tt(b("tmp", 8, 16, key="tmpz"), b("tmp", 8, 16, key="tmpz"), b("jL"), OP.add)
     cp(b("lsel"), b("tmp", 8, 16, key="tmpz"))
-    asel(b("lt"), b("ones", 0, 128), [[-16, 8], [0, 16]], OP.is_ge, 0.0, 0, 1)
-    asel(b("bones"), b("lt"), [[16, 8], [0, 16]], OP.is_ge, 0.0, 15, -1)
-    act(b("lo"), b("bones"), AF.Copy, 0.0, -M)
-    asel(b("lt"), b("lo"), [[1, 128]], OP.is_ge, 0.0, 0, -1)
-    asel(b("ld"), b("lt"), [[1, 128]], OP.not_equal, M, 0, -1)
+    raw = parts(P1, True)
+    ts(b("tmp3", 12, 13, key="tmp3c"), b("pf"), float(raw[0]), OP.is_ge)
+    ts(b("tmp3", 11, 12, key="tmp3b"), b("pf"), float(raw[-1]), OP.is_le, b("tmp3", 12, 13, key="tmp3c"), OP.mult)
+    ts(b("tmp2", 2, 10, key="tmp2b"), b("jL"), -128.0, OP.add, b("tmp3", 11, 12, key="tmp3b"), OP.mult)
+    ts(b("lxd"), b("tmp2", 2, 10, key="tmp2b"), 256.0, OP.add)
+    ts(b("pa", 2, 4, key="pa_"), b("pin", 0, 2), 4, OP.logical_shift_right)
+    cp(b("pG"), b("pa", 2, 3, key="pa_"))
+    ts(b("xi"), b("ci"), 4, OP.logical_shift_right)
+    ts(b("bones"), b("xi"), b("pG"), OP.is_equal, 128.0, OP.mult)
+    cp(b("B", 15, 143, 16), b("bones", 0, 128, 16))
+    act(b("B2"), b("B"), AF.Copy, 0.0, 2.0)
+    act(b("nB"), b("B"), AF.Copy, 0.0, -1.0)
+    act(b("lo"), b("bones"), AF.Copy, 0.0, -M / 128)
+    ts(b("lt"), b("ci"), b("pP"), OP.is_gt)
+    tt(b("lt"), b("lt"), b("lo"), OP.mult)
+    act(b("sh"), b("I"), AF.Copy, 0.0, M)
+    tt(b("ld"), b("lt"), b("sh"), OP.add)
     act(b("nl8"), b("ld"), AF.Copy, 0.0, -8320.0 / M)
-    asel(b("sh"), b("bones"), [[-1, 128]], OP.is_equal, 0.0, -1, 1)
-    tt(b("dm"), b("I"), b("sh"), OP.subtract)
-    act(b("bones"), b("bones"), AF.Copy, 0.0, 128.0)
-    io(b("hx"), [[0, 8], [-1, 16]], 16, 1)
-    ts(b("hx"), b("hx"), 15, OP.bitwise_and)
-    ts(b("tab"), b("hx"), 0.0, OP.is_equal, 65.0, OP.mult)
-    ts(b("emc"), b("hx"), 0.0, OP.not_equal, float(2 ** 26), OP.mult)
-    ts(b("emc"), b("emc"), 127.0, OP.max)
-    for c in range(8):
-        ts(b("cnt0", 17 * c, 17 * c + 16), b("hx", 0, 16), 0.0, OP.not_equal, -float(2 ** 20), OP.mult)
-    cp(b("cnt0", 16, 136, 17), b("jL"))
-    io(b("iot"), [[1, WIN]], 0, 0)
+    ts(b("pQ"), b("pin", 0, 1), -1.0, OP.add)
+    ts(b("pw"), b("ci"), b("pQ"), OP.is_equal, 1.0 / 128, OP.mult)
+    tt(b("pw"), b("pw"), b("bones"), OP.mult)
+    tt(b("dm"), b("I"), b("pw"), OP.subtract)
+    ts(b("nr2", 512, 640, 1, 2, key="jr2"), b("ci", p1=2), b("p128", p1=2), OP.add)
+    ts(b("sh", p1=2), b("ones", 0, 128, 1, 2), b("pf", p1=2), OP.mult)
+    for s in range(4):
+        act(b("nr2", 128 * s, 128 * s + 128, 1, 2, key="n%d" % s), b("sh", p1=2), AF.Identity, -72.0 - s, 145.0 + 2 * s)
+    ts(b("hx"), b("ci"), 15, OP.bitwise_and)
+    ts(b("tab", 0, 128), b("hx"), b("pf"), OP.is_equal, 65.0, OP.mult)
+    ms(b("tab", 128, 144, key="tabz"), 65.0)
+    act(b("hv"), b("tab", 0, 128), AF.Relu, float(2 ** 26), -float(2 ** 26))
+    ts(b("emc"), b("hv"), 127.0, OP.max)
+    act(b("E", 0, 144, key="E0"), ind(b("tab", key=["tab", "tabz"]), b("l17", 0, 9)), AF.Relu, float(2 ** 20), -float(2 ** 20))
+    act(b("cnt0"), b("E", 0, 136, key="E0"), AF.Copy, 0.0, -1.0)
+    act(b("cnt0", 16, 136, 17), b("jL"), AF.Copy)
     cp(b("tu"), b("tp"))
-    cp(b("tu2", 0, 16, 2), b("tp"))
     cp(b("topf"), b("tp"))
     for h in range(4):
         cp(b("C", 256 * h, 256 * h + 256), b("KI", 256 * h, 256 * h + 256))
@@ -341,8 +412,8 @@ def rank_program(g, core, T, topo):
     act(b("es", p1=8), b("es", p1=8), AF.Copy, 0.0, 128.0)
     mms(b("pb6", 384, 512), [(b("I"), b("emc")), (b("es", p1=8), b("thf", p1=8))])
     scan(b("thx"), b("RM"), b("pb6", 384, 512), OP.max, OP.min)
-    cp(b("lim"), b("thx", 15, 128, 16))
-    ts(b("lim1"), b("thx", 15, 128, 16), 1.0, OP.add)
+    act(b("lim"), b("thx", 15, 128, 16), AF.Copy)
+    act(b("lim1"), b("thx", 15, 128, 16), AF.Identity, 1.0)
 
     def x_forms(src, s):
         if s == 2:
@@ -350,44 +421,78 @@ def rank_program(g, core, T, topo):
         act(b("xP"), ind(b("xb"), b("lperm")), AF.Copy)
         for k in range(16):
             o = b("xrep", k, 2048, 16, key="xr%d" % k)
-            if k % 3 == 2:
+            if k % 2:
                 act(o, b("xP"), AF.Copy)
             else:
                 cp(o, b("xP"))
+        act(b("xd"), ind(b("AN", key=["Mb", "xb", "ANz"]), b("lxd")), AF.Copy)
         act(b("xm"), b("xb"), AF.Identity, -MAGIC)
         act(b("xp"), b("xb"), AF.Identity, 256.0)
 
     XR = ["xr%d" % k for k in range(16)]
-
-    def children(out, s, lst):
-        for c in range(8):
-            ts(b(out, c, 128, 8, key="%s%d" % (out, c)), ind(Cw(s), b(lst, 2 * c, 2 * c + 1)), float(E1), OP.min)
-
-    def rows(out, s, lst):
-        if s == 0:
-            cp(out, ind(Cw(s), lst))
-        else:
-            act(out, ind(Cw(s), lst), AF.Copy)
-
-    def lst(name, p0, n):
-        return b(name, 8 * p0, 8 * (p0 + n), key=["%s%d" % (name, c) for c in range(8)])
-
-    def sums(bank, p0, n, last):
-        for p in range(p0, p0 + n):
-            mm(b(bank, 0, 128), lhs(p), b("Dab", 128 * p, 128 * p + 128, key="Dab%d" % p), False, last and p == p0 + n - 1)
-
     pk = lambda nm, p0, n: ["%s%d" % (nm, p) for p in range(p0, p0 + n)]
 
+    def children(out, nodes):
+        ts(b(out), ind(nodes, b("lperm")), float(E1), OP.min)
+
+    def rows(out, s, nodes):
+        if s == 0:
+            cp(out, ind(Cw(s), nodes))
+        else:
+            act(out, ind(Cw(s), nodes), AF.Copy)
+
+    def lst(name, p0, n):
+        return b(name, 8 * p0, 8 * (p0 + n))
+
+    def sums(bank, p0, n, m="B", of="Dab"):
+        for p in range(p0, p0 + n):
+            add(b(bank, 0, 128), lhs(p, m), b(of, 128 * p, 128 * p + 128, key="%s%d" % (of, p)))
+
+    def sweep(pieces, lists, into, keys):
+        p0 = 0
+        for n, bank in pieces:
+            c0, c1 = 128 * p0, 128 * (p0 + n)
+            d, x = b(into, c0, c1, key=pk(into, p0, n)), b("xrep", c0, c1, key=XR)
+            if bank:
+                act(d, ind(Aw, lst(lists, p0, n)), AF.Copy)
+                mms(b(bank, 0, c1 - c0), [(b("nI"), x), (b("I"), d)])
+                d = b(bank, 0, c1 - c0)
+            else:
+                tt(d, ind(Aw, lst(lists, p0, n)), x, OP.subtract)
+            act(b("Dab", c0, c1, key=pk("Dab", p0, n)), d, AF.Abs)
+            sums(keys, p0, n)
+            p0 += n
+
+    def sweep_arrived():
+        p0 = 0
+        for n, bank in P1X:
+            c0, c1 = 128 * p0, 128 * (p0 + n)
+            a, o, l = b("ag", c0, c1, key=pk("ag", p0, n)), b("Dab", c0, c1, key=pk("Dab", p0, n)), b("plist", 8 * p0, 8 * (p0 + n))
+            if bank:
+                x = b("D", c0, c1, key=pk("D", p0, n))
+                act(x, ind(b("xb"), l), AF.Copy)
+                mms(b(bank, 0, c1 - c0), [(b("I"), a), (b("nI"), x)])
+                act(o, b(bank, 0, c1 - c0), AF.Abs)
+                sums("pb0", p0, n)
+            else:
+                tt(o, ind(b("xi"), l), a, OP.max)
+                sums("pb0", p0, n, "nB", "ag")
+                sums("pb0", p0, n, "B2")
+            p0 += n
+        ps = parts(P1X, False)
+        for p in ps:
+            mm(b("pb2", 168, 176), lhs(p), b("xb", p, 128, 16), p == ps[0], p == ps[-1])
+
     def firsts(lists, node, on, bank, cl, z):
-        act(b("row", 0, 128), ind(b("iot"), lists), AF.Copy)
+        act(b("row", 0, 128), ind(b("iot", key=["iot%d" % k for k in range(13)]), lists), AF.Copy)
         act(b("r17"), ind(b("row", key=["row", "rowz"]), b("l17", 0, 9)), AF.Copy)
-        mm(b(bank, 0, 136), b("I"), b("cnt0"), True, False)
+        begin(b(bank, 0, 136), b("I"), b("cnt0"))
         for c in range(8):
             e0 = 136 * c
             ts(b("E", e0 + 17 * c, e0 + 136, key="E%d" % c), b("r17", 17 * c, 136), node(c), OP.is_equal, on(c), OP.mult)
-            mm(b(bank, 17 * c, 17 * c + 17), b("ld"), b("E", e0 + 17 * c, e0 + 17 * c + 17, key="E%d" % c), False, c == 7)
+            add(b(bank, 17 * c, 17 * c + 17), b("ld"), b("E", e0 + 17 * c, e0 + 17 * c + 17, key="E%d" % c))
             if c < 7:
-                mm(b(bank, 17 * c + 17, 136), b("lo"), b("E", e0 + 17 * c + 17, e0 + 136, key="E%d" % c), False, False)
+                add(b(bank, 17 * c + 17, 136), b("lo"), b("E", e0 + 17 * c + 17, e0 + 136, key="E%d" % c))
         scan(b(z), b(cl, key=[cl, cl + "t"]), b(bank, 0, 136), OP.min, OP.max)
 
     def prefix(o0, f):
@@ -415,10 +520,10 @@ def rank_program(g, core, T, topo):
 
     def front(s):
         t = s % ST
-        vu, vu2 = (b("tu"), "tu2") if t == 0 else (b("lu", 8, 16), "vu2")
+        vu = b("tu") if t == 0 else b("lu", 8, 16)
         vf = (lambda a, z: b("topf", a, z)) if t == 0 else (lambda a, z: b("s2", 17 + 2 * a, 17 + 2 * z, 2))
-        children("cvu", s, vu2)
         rows(b("cvf"), s, vu)
+        children("cvu", b("cvf"))
         mm(b("pb2", 0, 160), b("dm"), b("RW", 0, 160, key=["RWa", "cvf", "rowM"]))
         turn(b("tr", 0, 128, key="tra"), b("pb2", 16, 144))
         turn(b("tr", 128, 288, key="trb"), b("pb2", 0, 160))
@@ -428,11 +533,11 @@ def rank_program(g, core, T, topo):
             mm(b("pb2", 160, 168), lhs(p), b("emp", p, 128, 16), p == 0, p == 15)
         act(b("rB", 0, 8, key="rBa"), b("pb2", 160, 168), AF.Copy, 0.0, BIG / 128)
         act(b("rB", 8, 16, key="rBb"), b("pb2", 160, 168), AF.Relu, BIG, -BIG / 128)
-        nrow = (ONE, b("cr", 1008 + 128 * s, 1136 + 128 * s, 1, 1, key="n%d" % s))
-        mms(b("pb3", 144, 272), [(ONE, JROW), nrow, (b("nl8"), b("emp"))])
+        nrow = (b("nr2", 128 * s, 128 * s + 128, 1, 2, key="n%d" % s), b("nr2", 512, 640, 1, 2, key="jr2"))
+        mms(b("pb3", 144, 272), [nrow, (b("nl8"), b("emp"))])
         tt(b("RW", 272, 400, key="rowN"), b("cvf"), b("pb3", 144, 272), OP.min)
         if s != 2:
-            ts(b("clv", 16, 136, 17, key="clvt"), vf(0, 8), 128.0, OP.add)
+            act(b("clv", 16, 136, 17, key="clvt"), vf(0, 8), AF.Identity, 128.0)
             firsts(vu, lambda c: vf(c, c + 1), lambda c: b("one8" if t == 0 else "nonr", c, c + 1), "pb3", "clv", "zv")
             cp(b("uvu%d" % t), b("zv", 16, 136, 17))
             act(b("acB%d" % t), ind(b("zv"), b("lz")), AF.Relu, 0.0, BIG / M)
@@ -441,28 +546,18 @@ def rank_program(g, core, T, topo):
         tt(b("W4", 8, 16, key="W4b"), b("W4", 16, 24, key="W4c"), b("rB", 0, 8, key="rBa"), OP.max)
         tt(b("W4", 24, 32, key="W4d"), b("W4", 16, 24, key="W4c"), b("rB", 8, 16, key="rBb"), OP.max)
         tt(b("coef", 24, 32, key="coefd"), b("nL", 8 * s, 8 * s + 8, key="nL%d" % s), vf(0, 8), OP.subtract)
-        ts(b("d1", 1, 16, 2, key="d1a"), vf(0, 8), 128.0, OP.add)
-        cp(b("d1", 17, 32, 2, key="d1b"), vf(0, 8))
-        tt(b("d0", 1, 16, 2, key="d0a"), b("jL"), b("d1", 1, 16, 2, key="d1a"), OP.subtract)
+        act(b("d1", 17, 32, 2, key="d1b"), vf(0, 8), AF.Copy)
         return nrow
 
     def step(s, nrow):
         t = s % ST
         n0 = V0 + L * s
-        pos, neg = (b("nI"), b("I")) if s == 2 else (b("I"), b("nI"))
         v0 = b("d1", 17, 32, 2, key="d1b")
-        mm(b("pb0", 0, 128), ONE, JROW, True, False)
-        p0 = 0
-        for n in P1:
-            c0, c1 = 128 * p0, 128 * (p0 + n)
-            d = b("D", c0, c1, key=pk("D", p0, n))
-            if s == 2:
-                tt(d, ind(b("xi"), b("plist", 8 * p0, 8 * (p0 + n))), b("ag", c0, c1, key=pk("ag", p0, n)), OP.subtract)
-            else:
-                tt(d, ind(Aw, lst("cvu", p0, n)), b("xrep", c0, c1, key=XR), OP.subtract)
-            act(b("Dab", c0, c1, key=pk("Dab", p0, n)), d, AF.Abs)
-            sums("pb0", p0, n, p0 + n == 16)
-            p0 += n
+        begin(b("pb0", 0, 128), ONE, JROW)
+        if s == 2:
+            sweep_arrived()
+        else:
+            sweep(P1, "cvu", "D", "pb0")
         r = b("rr", 16, 144, key="r1")
         rs = b("rr", 15, 143, key=["r1", "rra"])
         scan(r, b("RM"), b("pb0", 0, 128), OP.max, OP.min)
@@ -470,87 +565,75 @@ def rank_program(g, core, T, topo):
         tt(b("e"), ind(b("r0"), b("lend")), rs, OP.is_equal)
         scan(b("pay"), b("e"), b("dl"), OP.mult, OP.add)
         bf = lambda a, z: b("pay", 15 + 16 * a, 16 * z, 16)
-        ts(b("bu2", 0, 16, 2), bf(0, 8), float(E1), OP.min)
         ts(b("bu"), bf(0, 8), float(E1), OP.min)
-        children("dvu", s, "bu2")
         rows(b("dvf"), s, b("bu"))
+        children("dvu", b("dvf"))
         tt(b("cand"), rs, b("pb0", 0, 128), OP.max)
         scan(b("rr", 144, 272, key="r2"), b("RM2"), b("cand"), OP.max, OP.min)
         cp(b("dec"), b("rr", 31, 272, 16, key=["r1", "r2"]))
         ts(b("dk"), b("dec"), 127, OP.bitwise_and)
         ts(b("du"), b("dk"), b("p128"), OP.add)
         cp(b("ku"), b("dk"))
-        act(b("dd"), ind(b("D", key=pk("D", 0, 16)), b("du")), AF.Copy)
-        act(b("oh"), ind(b("tab"), b("ku")), AF.Copy)
+        bare = "ag" if s == 2 else "D"
+        act(b("dd"), ind(b(bare, key=pk(bare, 0, 16)), b("du")), AF.Copy)
+        act(b("oh"), ind(b("tab", 0, 128), b("ku")), AF.Copy)
         db, dq, ohb, ohq = b("dd", 0, 128), b("dd", 128, 256), b("oh", 0, 128), b("oh", 128, 256)
-        mms(b("pb6", 0, 128), [(ONE, RH), (pos, db), (pos, dq)])
+        xd = b("xb" if s == 2 else "xd")
+        mms(b("pb6", 0, 128), [(ONE, RH), (b("nI2"), xd), (b("I"), db), (b("I"), dq)])
         act(b("pb6", 128, 256), b("pb6", 0, 128), AF.Identity, MAGIC, 0.5)
         act(b("absM"), b("pb6", 128, 256), AF.Abs, -MAGIC)
         tt(b("AN", 0, 128, key="Mb"), b("xm"), b("pb6", 128, 256), OP.add)
         mms(b("pb4", 256, 384), [(b("I"), b("emc")), (b("bones"), b("absM"))])
         scan(b("es"), b("RM"), b("pb4", 256, 384), OP.max, OP.min)
-        ts(b("cl"), db, -4.0, OP.max, 4.0, OP.min)
-        mms(b("pb6", 256, 384), [(b("I"), b("xb")), (pos, db), (neg, b("cl"))])
+        mms(b("pb4", 384, 512), [(b("nI"), xd), (b("I"), db)])
+        act(b("cl", 0, 128, key="cla"), b("pb4", 384, 512), AF.Relu, -4.0)
+        act(b("cl", 128, 256, key="clz"), b("pb4", 384, 512), AF.Relu, -4.0, -1.0)
+        mms(b("pb6", 256, 384), [(b("I"), b("xb")), (b("I"), b("cl", 0, 128, key="cla")), (b("nI"), b("cl", 128, 256, key="clz"))])
         act(b("hv"), b("pb6", 256, 384), AF.Copy)
-        mm(b("pb1", 0, 128), ONE, R127, True, False)
-        for p0, bank in P2S:
-            c0, c1 = 128 * p0, 128 * p0 + 512
-            a = b("ag", c0, c1, key=pk("ag", p0, 4))
-            act(a, ind(Aw, lst("dvu", p0, 4)), AF.Copy)
-            mms(b(bank), [(b("nI"), b("xrep", c0, c1, key=XR)), (b("I"), a)])
-            act(b("Dab", c0, c1, key=pk("Dab", p0, 4)), b(bank), AF.Abs)
-            sums("pb1", p0, 4, False)
-        p0 = 4 * len(P2S)
-        for n in P2V:
-            c0, c1 = 128 * p0, 128 * (p0 + n)
-            d = b("ag", c0, c1, key=pk("ag", p0, n))
-            tt(d, ind(Aw, lst("dvu", p0, n)), b("xrep", c0, c1, key=XR), OP.subtract)
-            act(b("Dab", c0, c1, key=pk("Dab", p0, n)), d, AF.Abs)
-            sums("pb1", p0, n, p0 + n == 16)
-            p0 += n
+        begin(b("pb1", 0, 128), ONE, R127)
+        sweep(P2, "dvu", "D" if s == 2 else "ag", "pb1")
         mb = b("rr", 31, 144, 16, key="r1")
+        if s == 2:
+            tt(b("mbx"), mb, b("pb2", 168, 176), OP.subtract)
+            mb = b("mbx")
         tt(b("W4", 0, 8, key="W4a"), mb, b("nac%d" % t), OP.max)
-        tt(b("G1", 0, 8, key="G1a"), mb, b("lim"), OP.is_gt)
-        tt(b("G1", 8, 16, key="G1b"), mb, b("lim"), OP.is_le)
-        ts(b("G2"), b("G1", key=["G1a", "G1b"]), BIG, OP.mult)
-        tt(b("UU"), ind(b("G2"), b("lg")), b("W4", key=["W4a", "W4b", "W4c", "W4d"]), OP.max)
+        tt(b("df"), mb, b("lim"), OP.subtract)
+        act(b("G2", 0, 8, key="G2a"), b("df"), AF.Relu, 0.0, BIG)
+        act(b("G2", 8, 16, key="G2b"), b("df"), AF.Relu, BIG, -BIG)
+        tt(b("UU"), ind(b("G2", key=["G2a", "G2b"]), b("lg")), b("W4", key=["W4a", "W4b", "W4c", "W4d"]), OP.max)
         tt(b("U1"), mb, b("lim1"), OP.min)
         tt(b("U4"), ind(b("U1"), b("lr")), b("acB%d" % t), OP.min)
         tt(b("coef", 0, 8, key="coefa"), bf(0, 8), v0, OP.subtract)
-        ts(b("clb", 16, 136, 17, key="clbt"), bf(0, 8), 128.0, OP.add)
+        act(b("clb", 16, 136, 17, key="clbt"), bf(0, 8), AF.Identity, 128.0)
         tt(b("FL", 0, 32), ind(b("es"), b("lF")), b("UU"), OP.is_ge)
         tt(b("FL", 32, 40, key="am"), b("es", 15, 128, 16), b("U4", 0, 8), OP.is_lt)
         tt(b("Tt4"), ind(b("es"), b("lF")), b("U4"), OP.min)
-        ts(b("nfl"), b("FL", 0, 32), -BIG, OP.mult, BIG, OP.add)
-        tt(b("TH"), b("Tt4"), b("nfl"), OP.max)
-        tt(b("prod"), ind(b("FL", key=["FL", "am"]), b("lfl", 0, 3)), b("coef", key=["coef" + k for k in "abcdef"]), OP.mult)
-        tt(b("d0", 17, 64, 2, key="d0b"), b("prod", 0, 24), b("prod", 24, 48), OP.add)
-        tt(b("sp"), b("d0", 49, 64, 2, key="d0b"), b("jL"), OP.add)
-        cp(b("spu"), b("sp"))
+        act(b("nfl"), b("FL", 0, 32), AF.Identity, BIG, -BIG)
+        tt(b("TH"), b("U4"), b("nfl"), OP.max)
+        tt(b("prod", 8, 56), ind(b("FL", key=["FL", "am"]), b("lfl", 0, 3)), b("coef", key=["coef" + k for k in "abcdef"]), OP.mult)
+        act(b("prod", 0, 8, key="proda"), b("FL", 16, 24), AF.Identity, -384.0, 256.0)
+        tt(b("d0", 1, 48, 2, key="d0b"), b("prod", 0, 24, key=["prod", "proda"]), b("prod", 24, 48), OP.add)
         mms(b("pb5", 0, 128), [(b("I63"), ohb)])
         mms(b("pb5", 128, 256), [(b("I63"), ohb), (b("I63"), ohq)])
-        mms(b("pb5", 256, 384), [(ONE, JROW), nrow, (b("nI128"), ohb)])
+        mms(b("pb5", 256, 384), [nrow, (b("nI128"), ohb)])
         mms(b("pb5", 384, 512), [(R63, R65), (b("nI63"), ohb), (b("nI63"), ohq)])
         mms(b("pb3", 272, 400), [(R128, R65), (b("nI8"), b("emp")), (b("nI128"), ohb), (b("idf"), b("dvf"))])
         tt(b("w3"), b("cvf"), b("pb5", 0, 128), OP.max)
         tt(b("w4"), b("cvf"), b("pb5", 128, 256), OP.max)
         tt(b("CN", 0, 128), b("cvf"), b("pb5", 384, 512), OP.max)
         tt(b("RW", 144, 272, key="rowM"), b("w4"), b("pb5", 256, 384), OP.min)
-        tt(b("rsp"), b("w3"), b("pb3", 272, 400), OP.min)
-        act(b("rpre"), ind(b("RW", 16, 400, key=["cvf", "rowM", "rowN"]), b("spu")), AF.Copy)
-        Cs = b("CW", 0, 128 + n0, key=["C"] + blocks("C", s))
-        scatter(Cs, b("uvu%d" % t), b("rpre"))
+        tt(b("RW", 400, 528, key="rsp"), b("w3"), b("pb3", 272, 400), OP.min)
         fl = "fl%d" % t
         scan(b("fs"), b("RM"), b("pb1", 0, 128), OP.max, OP.min)
         tt(b("hf"), b("fs", 15, 128, 16), b("TH", 0, 8), OP.is_ge)
         tt(b(fl, 8, 24), ind(b("fs"), b("lF", 0, 1)), b("TH", 8, 24), OP.is_ge)
         tt(b("d1", 0, 64, 2, key="d1s"), ind(b("fs"), b("lF")), b("Tt4"), OP.is_ge)
-        scan(b("s2"), b("d0", 0, 48, key=["d0", "d0a", "d0b"]), b("d1", 0, 48, key=["d1a", "d1b", "d1c", "d1s"]), OP.mult, OP.add)
+        scan(b("s2"), b("d0", 0, 48, key=["d0", "d0b"]), b("d1", 0, 48, key=["d1a", "d1b", "d1c", "d1s"]), OP.mult, OP.add)
         cp(b("lu"), b("s2", 1, 48, 2))
         if t == 0:
-            cp(b("vu2", 0, 16, 2), b("s2", 17, 32, 2))
             act(b("nonr"), b(fl, 16, 24), AF.Identity, 1.0, -1.0)
-        scatter(Cs, b("lu", 0, 8), b("rsp"))
+        act(b("rpre"), ind(b("RW", 16, 528, key=["cvf", "rowM", "rowN", "rsp"]), b("lu", 0, 8)), AF.Copy)
+        scatter(b("CW", 0, 128 + n0, key=["C"] + blocks("C", s)), b("uvu%d" % t), b("rpre"))
         act(b("C", n0, n0 + L, key="Cb%d" % s), ind(b("CN", key=["CN", "CNz"]), b("lu", 16, 24)), AF.Copy)
         act(b("A", n0, n0 + L, key="Ab%d" % s), ind(b("AN", key=["Mb", "xb", "ANz"]), b("lu", 16, 24)), AF.Copy)
         firsts(b("bu"), lambda c: bf(c, c + 1), lambda c: b("hf", c, c + 1), "pb4", "clb", "zb")
@@ -562,12 +645,13 @@ def rank_program(g, core, T, topo):
         cm = "come%d" % (s // ST)
         tt(b("rest2"), b("fl0", 16, 24), b("fl1", 16, 24), OP.add)
         prefix(192, lambda a, z: b("rest2", a, z))
-        ts(b("nrs"), b("pb2", 192, 200), -1.0 / M, OP.mult, 257.0, OP.add)
-        tt(b("dM"), ind(Aw, b("lu", 8, 16)), b("xb"), OP.subtract)
-        act(b("ad"), b("dM"), AF.Abs)
-        ts(b("msk"), b(cm, 0, CAP, key=cm + "_0"), 0.5, OP.is_gt)
-        op("v", lambda e: e.tensor_reduce(b("n0")[0], b("msk")[0], AxisListType.X, OP.add), ["msk"], ["n0"], 64)
-        ts(b("cd"), b("n0"), -1.0, OP.mult, float(CAP), OP.add)
+        act(b("nrs"), b("pb2", 192, 200), AF.Identity, 257.0, -1.0 / M)
+        act(b("absM"), ind(Aw, b("lu", 8, 16)), AF.Copy)
+        mms(b("pb6", 0, 128), [(b("nI"), b("xb")), (b("I"), b("absM"))])
+        act(b("ad"), b("pb6", 0, 128), AF.Abs)
+        first = b(cm, 0, CAP, key=cm + "_0")
+        op("s", lambda e: e.activation(b("msk")[0], first[0], AF.Sign, accum_out=b("n0")[0]), first[1], ["msk", "n0"], 90)
+        act(b("cd"), b("n0"), AF.Identity, float(CAP), -1.0)
         ts(b("ge"), b("nrs"), b("n0"), OP.is_ge, b("cd"), OP.mult)
         tt(b("idx"), b("nrs"), b("ge"), OP.add)
         ts(b("iu"), b("idx"), 64.0, OP.min)
@@ -603,7 +687,7 @@ def rank_program(g, core, T, topo):
     know = {q: {} for q in eng}
     wr, rd = {}, {}
 
-    def need(q, R, Wk, isdma):
+    def need(q, R, Wk):
         deps = []
         for k in R:
             if k in wr:
@@ -635,20 +719,20 @@ def rank_program(g, core, T, topo):
         o = ops[i]
         q, kind = o["q"], o["dma"]
         if kind is None:
-            need(q, o["R"], o["W"], False)
+            need(q, o["R"], o["W"])
             cnt[own[q]] += 1
             o["call"](eng[q]).then_inc(T.sem[own[q]], 1)
             note(q, own[q], cnt[own[q]], know[q], o["R"], o["W"])
         elif kind[:6] == "remote":
             s = int(kind[6:])
-            need(q, o["R"], [], True)
+            need(q, o["R"], [])
             o["call"](g)
             h = hops(T, topo, (rank - 1 - s % (NR - 1)) % NR, s)
             n = engines_of(topo, h[-2], h[-1])
             wr[o["W"][0]] = ("remote", "in%d" % s, n, {"in%d" % s: n})
             cnt["in%d" % s] = n
         else:
-            need(q, o["R"], o["W"], True)
+            need(q, o["R"], o["W"])
             o["call"](eng[q]).then_inc(T.sem[kind], 16)
             cnt[kind] = 16
             note("dma" + kind, kind, 16, know[q], o["R"], o["W"])

@@ -1,4 +1,4 @@
-from concourse.mybir import AluOpType as OP, ActivationFunctionType as AF, AxisListType
+from concourse.mybir import AluOpType as OP, ActivationFunctionType as AF
 
 V0, L, ST, RO, CAP, NR = 1024, 128, 2, 2, 32, 8
 W = V0 + RO * ST * L
@@ -6,12 +6,16 @@ E1 = W
 WIN = W + 8
 BIG = float(2 ** 30)
 MAGIC = float(3 * 2 ** 22)
+NONE = 1000
 M = 2048.0
-P1 = [(2, None), (3, None), (4, "pb7"), (3, None), (2, None), (2, None)]
-P1X = [(2, None), (3, None), (3, "pb7"), (3, None), (3, "pb1"), (2, None)]
-P2 = [(2, None), (3, None), (3, "pb7"), (3, None), (3, None), (2, None)]
-ROUNDS = 6
-WAKE, GAT, SCA = 220.0, 1.5, 3.0
+P1 = [[(4, None), (4, bank), (5, None), (3, None)] for bank in ("pb7", "pb4")]
+P1X = [[(5, None), (2, bank), (5, None), (4, None)] for bank in ("pb7", "pb4")]
+P2 = P1
+ROUNDS, TRIES, SLACK = 6, (5000, 3000, 2000), 60.0
+CYCLE, GAT, SCA = 0.83, 1.5, 3.2
+START, KIB = 1000.0, 3.9
+TRIP = (10000, 3900, 7000, 3900)
+WAKE = 220.0
 
 SLOT = {}
 SIZE = {"F": 0, "B": 0, "I": 0, "U": 0}
@@ -23,17 +27,17 @@ def _s(kind, **kw):
         SIZE[kind] += (w + 15) // 16 * 16
 
 
-_s("B", AW=128 + WIN, xrep=2048, D=2048, Dab=2048, ag=2048, AN=272, xP=128, xd=128, nr2=640, ones=144, B=144, B2=144, nB=144, pw=128,
-   bones=128, lo=128, lt=128, ld=128, nl8=128, I=128, nI=128, nI2=128, I63=128, nI63=128, nI128=128, nI8=128, IM=128, sh=128, cr=1024,
-   cnt0=136, emc=128, tab=144, emp=128, oh=256, dd=256, cl=256, absM=128, hv=128, E=1088, fl0=32, fl1=32, rest2=8, msk=32)
-_s("F", CW=128 + WIN, iot=WIN, RW=544, CN=272, idf=128, dm=128, RM=128, RM2=128, tr=288, dl=128, rr=272, r0=128, e=128, cand=128, pay=128,
-   row=144, r17=144, clv=136, clb=136, zv=136, zb=136, w3=128, w4=128, rpre=128, dvf=128, es=128, fs=128, xm=128, xp=128,
-   ad=128, thf=128, thx=128, lim=8, lim1=8, jL=8, cj=8, topf=8, nL=32, acB0=32, acB1=32, nac0=8, nac1=8, rB=16, W4=32, G2=16,
-   UU=32, U1=8, U4=32, Tt4=32, FL=40, nfl=32, TH=32, coef=48, prod=56, d0=64, d1=64, s2=48, df=8, mbx=8, nonr=8, one8=8, hf=8, pz=8,
-   nrs=8, ge=8, idx=8, n0=1, cd=1, r7=1, hi=1, p128=1, pf=1, pP=1, pG=1, pQ=1, tmp=16, tmp2=16, tmp3=16)
+_s("B", AW=128 + WIN, xrep=2048, D=2048, Dab=2048, ag=2048, AN=272, xP=128, xd=128, xn=128, hz=128, nr2=640, ones=144, B=144, B2=144, nB=144, pw=128,
+   bones=128, lo=128, lt=128, ld=128, lp=128, nl8=128, I=128, nI=128, nI2=128, I63=128, nI128=128, nI8=128, sh=128, cr=1024,
+   cnt0=136, emc=128, tab=144, emp=128, oh=256, dd=256, cl=256, absM=128, hv=128, E=1088, fl0=32, fl1=32, rest2=8, cum=8, cj=8, fw=8, msk=32)
+_s("F", CW=128 + WIN, iot=WIN, RW=544, CN=272, idf=128, dm=128, RM=128, RM2=64, tr=288, dl=128, rr=272, e=128, cand=128, pay=128,
+   row=144, r17=144, clv=136, clb=136, zv=136, zb=136, w3=128, w4=128, rpre=128, dvf=128, es=128, fs=128, xm=128,
+   ad=128, thf=128, thx=128, lim=8, lim1=8, jL=8, topf=8, nL=32, acB0=32, acB1=32, nac0=8, nac1=8, W4=32, G2=16, G4=32,
+   UU=32, U1=8, Uac=8, U4=32, TT=56, FL=40, nfl=32, coef=48, prod=56, d0=48, d1=64, s2=48, df=8, mbt=8, mbx=8, nonr=8, one8=8,
+   nrs=8, ge=8, idx=8, na=1, n0=1, cd=1, r7=1, hi=1, p64=1, p64b=1, pf=1, pG=1, tmp=16, tmp2=16, tmp3=16)
 _s("I", KI=WIN, tp=8, thi=128, pin=16, pa=16, pc=16, ci=128, ri=128, dec=16, dk=16, hx=128, xi=128)
 _s("U", tu=8, cvu=128, dvu=128, bu=8, du=16, ku=16, uvu0=8, uvu1=8, lu=24, oAu=8, posu=8, iu=8,
-   plist=128, lperm=8, l17=10, lend=8, lsel=8, lF=2, lr=2, lz=2, lg=2, lfl=4, lxd=8)
+   plist=128, lperm=8, l17=10, lsel=8, lF=2, lr=2, lz=2, lg=2, lfl=4, lxd=8)
 SLOT["C"] = ("arF", SLOT["CW"][1] + 128, WIN)
 SLOT["A"] = ("arB", SLOT["AW"][1] + 128, WIN)
 SLOT["cvf"] = ("arF", SLOT["RW"][1] + 16, 128)
@@ -44,10 +48,10 @@ SCRATCH = {"arF": ("sbuf", [128, SIZE["F"]], "float32"), "arB": ("sbuf", [128, S
 for _k in range(8):
     SCRATCH["pb%d" % _k] = ("psum", [128, 512], "float32")
 for _k in range(4):
-    SCRATCH["msg%d" % _k] = ("sbuf", [128, 256], "float32")
-    SCRATCH["rl%d" % _k] = ("sbuf", [128, 32], "float32")
+    SCRATCH["msg%d" % _k] = ("sbuf", [128, 384], "bfloat16")
+    SCRATCH["rl%d" % _k] = ("sbuf", [128, 32], "bfloat16")
 for _k in range(2):
-    SCRATCH["come%d" % _k] = ("sbuf", [128, 80], "float32")
+    SCRATCH["come%d" % _k] = ("sbuf", [128, 80], "bfloat16")
 SEMAPHORES = (["qv", "qs", "qt", "qg"] + ["in%d" % k for k in range(4)] + ["rr%d" % k for k in range(4)] + ["ls%d" % k for k in range(4)]
               + ["ld%d" % k for k in range(8)])
 ORDER = {}
@@ -161,7 +165,61 @@ def order_calls(ops):
         if best is None or max(end) < best[0]:
             best = (max(end), start)
         way = place(sorted(range(n), key=lambda i: (-end[i], -i)), post, True)[1]
-    return sorted(range(n), key=lambda i: (best[1][i], i))
+    need = [list(d.items()) for d in pre]
+    time, lag, queue = [o["c"] for o in ops], [o["lag"] for o in ops], [o["q"] for o in ops]
+
+    def run(order):
+        end, why, free = [0.0] * n, [-1] * n, {q: (0.0, 0) for q in queue}
+        for i in order:
+            t, y = free[queue[i]]
+            y = -2 - y if t else -1
+            for j, w in need[i]:
+                if end[j] + w >= t:
+                    t, y = end[j] + w, j
+            free[queue[i]], end[i], why[i] = (t + time[i], i), t + time[i] + lag[i], y
+        return max(end), end, why
+
+    def exchange(order, tries, seed):
+        last, end, why = run(order)
+        good = (last, order, end)
+        for _ in range(tries):
+            seed = (seed * 1103515245 + 12345) % 2 ** 31
+            i, pairs = end.index(last), []
+            while i >= 0:
+                if why[i] <= -2:
+                    pairs.append((-2 - why[i], i))
+                i = why[i] if why[i] >= -1 else -2 - why[i]
+            u, v = pairs[(seed >> 8) % len(pairs)]
+            a, z, early = order.index(u), order.index(v), seed >> 5 & 1
+            for _ in range((0, 0, 0, 1, 2, 4)[(seed >> 20) % 6]):
+                if early:
+                    a = max([m for m in range(max(0, a - 60), a) if queue[order[m]] == queue[u]] or [a])
+                else:
+                    z = min([m for m in range(z + 1, min(n, z + 60)) if queue[order[m]] == queue[u]] or [z])
+            part, tied = order[a:z + 1], {v if early else u}
+            for x in (reversed(part) if early else part):
+                if early and x in tied:
+                    tied.update(pre[x])
+                elif not early and any(j in tied for j in pre[x]):
+                    tied.add(x)
+            if order[a if early else z] in tied:
+                continue
+            new = order[:a] + [x for x in part if (x in tied) == early] + [x for x in part if (x in tied) != early] + order[z + 1:]
+            now = run(new)
+            if now[0] <= last + SLACK * (seed >> 3 & 3) / 3 * (seed >> 12 & 3) / 3:
+                order, (last, end, why) = new, now
+                if last < good[0]:
+                    good = (last, order, end)
+        return good
+
+    order = sorted(range(n), key=lambda i: (best[1][i], i))
+    for k, tries in enumerate(TRIES):
+        last, order, end = exchange(order, tries, k + 1)
+        way = place(sorted(range(n), key=lambda i: (-end[i], -i)), post, True)[1]
+        start, end = place(sorted(range(n), key=lambda i: (-way[i], i)), pre, False)
+        if max(end) < last:
+            order = sorted(range(n), key=lambda i: (start[i], i))
+    return order
 
 
 def parts(pieces, scalar):
@@ -178,10 +236,10 @@ def rank_program(g, core, T, topo):
     ops = []
 
     def op(q, call, R, Wk, c, lag=0.0, dma=None, adds=None):
-        ops.append({"q": q, "call": call, "R": R, "W": Wk, "c": c * 0.83, "lag": lag, "dma": dma, "adds": adds})
+        ops.append({"q": q, "call": call, "R": R, "W": Wk, "c": c * CYCLE, "lag": lag, "dma": dma, "adds": adds})
 
-    def dma(q, sem, out, in_, R, Wk, lag):
-        op(q, lambda e: e.dma_start(out, in_), R, Wk, 60, lag, sem)
+    def dma(sem, out, in_, R, Wk, kib):
+        op("y", lambda e: e.dma_start(out, in_), R, Wk, 60 + kib * KIB / CYCLE, START, sem)
 
     def b(name, c0=0, c1=None, st=1, p1=128, key=None):
         if name in SLOT:
@@ -271,104 +329,110 @@ def rank_program(g, core, T, topo):
     def asel(o, a, pat, f, other, base, cm):
         op("g", lambda e: e.affine_select(o[0], a[0], pat, f, other, base, cm), ks(a), ks(o), 200 + 2 * o[2])
 
-    def row(j):
-        return b("cr", 128 * j, 128 * j + 128, 1, 1, key="cr%d" % j)
+    def row(j, c0=0, c1=128):
+        return b("cr", 128 * j + c0, 128 * j + c1, 1, 1, key="cr%d" % j)
 
-    ONE, JROW, R63, R65, R128, RH, R127 = [row(j) for j in range(7)]
+    ONE, JROW, R65, R128, RH, R127 = range(6)
     blocks = lambda t, n: ["%sb%d" % (t, k) for k in range(n)]
+    pk = lambda nm, p0, n: ["%s%d" % (nm, p) for p in range(p0, p0 + n)]
     Cw = lambda s: b("KI", key=["KI", "KIe"]) if s == 0 else b("C", key=["C", "Ce"] + blocks("C", 4))
     Aw = b("A", key=["A", "Ae"] + blocks("A", 4))
     lhs = lambda p, m="B": b(m, 15 - p, 143 - p)
 
-    dma("y", "ld0", b("tp")[0], T.tops[:], [], ["tp"], 1500)
-    dma("y", "ld2", b("KI", 0, V0)[0], T.kids[:], [], ["KI"], 4000)
-    dma("y", "ld3", b("A", 0, V0)[0], T.a0[:], [], ["A"], 3900)
-    dma("s", "ld1", b("xb")[0], T.x0[:], [], ["xb"], 2000)
-    dma("s", "ld4", b("thi", p1=8)[0], T.th[:], [], ["thi"], 2000)
+    dma("ld0", b("tp")[0], T.tops[:], [], ["tp"], 4)
+    dma("ld1", b("xb")[0], T.x0[:], [], ["xb"], 32)
+    dma("ld2", b("KI", 0, V0)[0], T.kids[:], [], ["KI"], 512)
+    dma("ld3", b("A", 0, V0)[0], T.a0[:], [], ["A"], 256)
+    dma("ld4", b("thi", p1=8)[0], T.th[:], [], ["thi"], 4)
     fill(b("KI", V0, WIN, key="KIe"), 4095)
     fill(b("C", V0, WIN, key=["Ce"] + blocks("C", 4)), 4095)
     ms(b("A", V0, W, key=blocks("A", 4)), 0.0)
     ms(b("A", W, WIN, key="Ae"), 4096.0)
     ms(b("ones"), 1.0)
-    ms(b("one8"), 1.0)
+    fill(b("one8"), 1)
+    fill(b("W4", key=["W4b", "W4d"]), 0)
     fill(b("AN", 256, 272, key="ANz"), 0)
     fill(b("AN", 0, 128, key="Mb"), 0)
     fill(b("CN", 128, 272, key="CNz"), 4095)
     ms(b("RW", 0, 16, key="RWa"), 0.0)
     ms(b("RW", 144, 160, key="rowM"), 0.0)
-    ms(b("row", 128, 144, key="rowz"), -1.0)
-    ms(b("rr", 0, 16, key="rra"), -1.0)
+    fill(b("row", 128, 144, key="rowz"), -1)
+    fill(b("rr", 15, 144, 128, key=["rra", "r20"]), -1)
     fill(b("d0", key=["d0", "d0b"]), 0)
     fill(b("d1", key=["d1a", "d1b", "d1c", "d1s"]), 256)
     ms(b("B"), 0.0)
-    for j, v in ((0, 1.0), (2, 63.0), (3, 65.0), (4, 128.0), (5, -0.5), (6, 127.0)):
-        (fill if j in (2, 3, 4, 6) else ms)(row(j), v)
+    ms(row(ONE), 1.0)
+    ms(row(RH), -0.5)
+    for j, v in ((R65, 65), (R128, 128), (R127, 127)):
+        fill(row(j), v)
     for nm in ("RM", "RM2"):
         ms(b(nm), 0.0)
-        ms(b(nm, 0, 128, 16), BIG)
-    ms(b("RM2", 1, 128, 16), BIG)
+        ms(b(nm, 0, None, 16), BIG)
+    ms(b("RM2", 1, 64, 16), BIG)
     for nm in ("clv", "clb"):
         fill(b(nm, key=[nm, nm + "t"]), 2 ** 23)
         fill(b(nm, 0, 136, 17), -2 ** 23)
     for k in range(2):
-        fill(b("come%d" % k, 64, 80, key="come%dz" % k), 0)
+        fill(b("come%d" % k, 64, 80, key="come%dz" % k), NONE)
     for k in range(4):
-        fill(b("msg%d" % k, 0, CAP), 0)
+        fill(b("msg%d" % k, 0, CAP), NONE)
     fill(b("coef", 16, 24, key="coefc"), 128)
     fill(b("coef", 40, 48, key="coeff"), 0)
 
     io(b("pin"), [[0, 16]], 0, 1)
     io(b("ci"), [[1, 128]], 0, 0)
-    io(b("ri"), [[1, 16], [16, 8]], 0, 0)
+    io(b("ri"), [[64, 2], [1, 16], [16, 4]], 0, 0)
     cp(b("plist"), b("ri"))
-    cp(JROW, b("ci", p1=1))
-    cp(b("pP"), b("pin", 0, 1))
-    ts(b("I"), b("ci"), b("pP"), OP.is_equal)
+    io(row(JROW), [[1, 128]], 0, 0)
+    asel(b("I"), b("ones", 0, 128), [[-1, 128]], OP.is_equal, 0.0, 0, 1)
     cp(b("iot", 0, 128, key="iot0"), b("ci"))
     for k in range(1, 13):
         act(b("iot", 128 * k, min(WIN, 128 * k + 128), key="iot%d" % k), b("iot", 0, min(128, WIN - 128 * k), key="iot0"), AF.Identity, 128.0 * k)
-    for nm, v in (("nI", -1.0), ("nI2", -2.0), ("I63", 63.0), ("nI63", -63.0), ("nI128", -128.0), ("nI8", -8320.0), ("IM", 256 * M), ("idf", 1.0)):
+    for nm, v in (("nI", -1.0), ("nI2", -2.0), ("I63", 63.0), ("nI128", -128.0), ("nI8", -8320.0), ("idf", 1.0)):
         act(b(nm), b("I"), AF.Copy, 0.0, v)
     ts(b("pa", 0, 2), b("pin", 0, 2), 15, OP.bitwise_and)
     cp(b("pf"), b("pa", 0, 1))
-    ts(b("p128"), b("pa", 0, 1), 128.0, OP.mult)
+    act(b("p64"), b("pf"), AF.Copy, 0.0, 64.0)
+    act(b("p64b"), b("pf"), AF.Identity, 960.0, 64.0)
     ts(b("pc", 0, 2), b("pin", 0, 2), 7, OP.bitwise_and)
     cp(b("r7"), b("pc", 0, 1))
     ts(b("pc", 2, 4, key="pc_"), b("pin", 0, 2), 3, OP.logical_shift_right, 1, OP.bitwise_and)
     cp(b("hi"), b("pc", 2, 3, key="pc_"))
     ts(b("jL"), b("ci", 0, 128, 16), b("pf"), OP.add)
-    act(b("cj"), b("jL"), AF.Identity, 129 * M, -M)
+    act(b("cj"), b("jL"), AF.Identity, -128 * M, -M)
     for s in range(4):
         act(b("nL", 8 * s, 8 * s + 8, key="nL%d" % s), b("jL"), AF.Identity, float(V0 + L * s))
     act(b("coef", 8, 16, key="coefb"), b("jL"), AF.Identity, -256.0)
     act(b("coef", 32, 40, key="coefe"), b("jL"), AF.Identity, -128.0)
     act(b("d1", 1, 16, 2, key="d1a"), b("jL"), AF.Identity, 384.0)
-    ts(b("lend"), b("ci", 0, 128, 16), 15.0, OP.add)
     ts(b("lF"), b("pc", 0, 2), 16.0, OP.mult, 15.0, OP.add)
     ts(b("lz"), b("pc", 0, 2), 17.0, OP.mult, 15.0, OP.add)
     cp(b("lr"), b("pc", 0, 2))
-    ts(b("tmp", 0, 1, key="tmpa"), b("hi"), 8.0, OP.mult, b("r7"), OP.add)
-    ts(b("tmp", 1, 2, key="tmpb"), b("r7"), 8.0, OP.add)
+    act(b("tmp", 0, 1, key="tmpa"), b("hi"), AF.Identity, b("r7"), 8.0)
+    act(b("tmp", 1, 2, key="tmpb"), b("r7"), AF.Identity, 8.0)
     cp(b("lg"), b("tmp", 0, 2, key=["tmpa", "tmpb"]))
     for j, (u, v) in enumerate(((0, 32), (32, 32), (24, 24), (0, 0))):
         act(b("tmp", 4 + j, 5 + j, key="tmp%d" % j), b("hi"), AF.Identity, float(u), float(v - u))
-    ts(b("lfl"), b("tmp", 4, 8, key=["tmp%d" % j for j in range(4)]), b("r7"), OP.add)
-    ts(b("tmp2", 0, 1, key="tmp2a"), b("r7"), 16.0, OP.mult, b("hi"), OP.add)
-    ts(b("lperm"), b("ci", 0, 16, 2), b("tmp2", 0, 1, key="tmp2a"), OP.add)
+    ts(b("lfl"), b("tmp", 4, 8, key=pk("tmp", 0, 4)), b("r7"), OP.add)
+    ts(b("pc", 4, 6, key="pc4"), b("pin", 0, 2), 3, OP.bitwise_and)
+    ts(b("pc", 6, 8, key="pc6"), b("pin", 0, 2), 2, OP.logical_shift_right, 3, OP.bitwise_and)
+    cp(b("tmp2", 12, 13, key="tmp2c"), b("pc", 6, 7, key="pc6"))
+    ts(b("tmp2", 0, 1, key="tmp2a"), b("pc", 4, 5, key="pc4"), 16.0, OP.mult, b("tmp2", 12, 13, key="tmp2c"), OP.add)
+    for h in range(2):
+        ts(b("lperm", 4 * h, 4 * h + 4), b("ci", 64 * h, 64 * h + 16, 4), b("tmp2", 0, 1, key="tmp2a"), OP.add)
     ts(b("tmp3", 0, 10), b("ci", 0, 10), b("pf"), OP.is_gt, b("pf"), OP.add)
     ts(b("tmp2", 2, 12, key="tmp2b"), b("ci", 0, 10), -1.0, OP.add, b("pf"), OP.is_equal)
-    ts(b("tmp2", 2, 12, key="tmp2b"), b("tmp2", 2, 12, key="tmp2b"), 128.0, OP.mult)
+    act(b("tmp2", 2, 12, key="tmp2b"), b("tmp2", 2, 12, key="tmp2b"), AF.Copy, 0.0, 128.0)
     tt(b("tmp3", 0, 10), b("tmp3", 0, 10), b("tmp2", 2, 12, key="tmp2b"), OP.add)
-    ts(b("tmp2", 2, 12, key="tmp2b"), b("ci", 0, 10), 15.0, OP.mult)
-    tt(b("tmp3", 0, 10), b("tmp3", 0, 10), b("tmp2", 2, 12, key="tmp2b"), OP.add)
+    io(b("U4", 0, 10), [[15, 10]], 0, 0)
+    tt(b("tmp3", 0, 10), b("tmp3", 0, 10), b("U4", 0, 10), OP.add)
     ts(b("l17"), b("tmp3", 0, 10), 128.0, OP.min)
-    ts(b("dec", 0, 8), b("pin", 0, 8), 4, OP.logical_shift_right)
-    tt(b("dec", 0, 8), b("dec", 0, 8), b("ci", 0, 8), OP.add)
-    ts(b("dec", 0, 8), b("dec", 0, 8), 1, OP.bitwise_and)
-    ts(b("tmp", 8, 16, key="tmpz"), b("dec", 0, 8), 144.0, OP.mult)
-    tt(b("tmp", 8, 16, key="tmpz"), b("tmp", 8, 16, key="tmpz"), b("jL"), OP.add)
-    cp(b("lsel"), b("tmp", 8, 16, key="tmpz"))
-    raw = parts(P1, True)
+    ts(b("dec", 0, 2), b("pin", 0, 2), 4, OP.logical_shift_right, 1, OP.bitwise_and)
+    ts(b("tmp", 8, 9, key="tmpy"), b("dec", 0, 1), 144.0, OP.mult)
+    act(b("tmp", 9, 10, key="tmpz"), b("tmp", 8, 9, key="tmpy"), AF.Identity, 144.0, -1.0)
+    ts(b("lsel", 0, 8, 2), b("jL", 0, 8, 2), b("tmp", 8, 9, key="tmpy"), OP.add)
+    ts(b("lsel", 1, 8, 2), b("jL", 1, 8, 2), b("tmp", 9, 10, key="tmpz"), OP.add)
+    raw = parts(P1[0], True)
     ts(b("tmp3", 12, 13, key="tmp3c"), b("pf"), float(raw[0]), OP.is_ge)
     ts(b("tmp3", 11, 12, key="tmp3b"), b("pf"), float(raw[-1]), OP.is_le, b("tmp3", 12, 13, key="tmp3c"), OP.mult)
     ts(b("tmp2", 2, 10, key="tmp2b"), b("jL"), -128.0, OP.add, b("tmp3", 11, 12, key="tmp3b"), OP.mult)
@@ -381,24 +445,22 @@ def rank_program(g, core, T, topo):
     act(b("B2"), b("B"), AF.Copy, 0.0, 2.0)
     act(b("nB"), b("B"), AF.Copy, 0.0, -1.0)
     act(b("lo"), b("bones"), AF.Copy, 0.0, -M / 128)
-    ts(b("lt"), b("ci"), b("pP"), OP.is_gt)
-    tt(b("lt"), b("lt"), b("lo"), OP.mult)
-    act(b("sh"), b("I"), AF.Copy, 0.0, M)
-    tt(b("ld"), b("lt"), b("sh"), OP.add)
+    asel(b("lt"), b("lo"), [[1, 128]], OP.is_gt, 0.0, 0, -1)
+    asel(b("ld"), b("lt"), [[1, 128]], OP.not_equal, M, 0, -1)
+    asel(b("lp"), b("lt"), [[1, 128]], OP.not_equal, 256 * M, 0, -1)
     act(b("nl8"), b("ld"), AF.Copy, 0.0, -8320.0 / M)
-    ts(b("pQ"), b("pin", 0, 1), -1.0, OP.add)
-    ts(b("pw"), b("ci"), b("pQ"), OP.is_equal, 1.0 / 128, OP.mult)
-    tt(b("pw"), b("pw"), b("bones"), OP.mult)
-    tt(b("dm"), b("I"), b("pw"), OP.subtract)
-    ts(b("nr2", 512, 640, 1, 2, key="jr2"), b("ci", p1=2), b("p128", p1=2), OP.add)
-    ts(b("sh", p1=2), b("ones", 0, 128, 1, 2), b("pf", p1=2), OP.mult)
+    act(b("pw"), b("bones"), AF.Copy, 0.0, -1.0 / 128)
+    asel(b("w3"), b("pw"), [[-1, 128]], OP.is_equal, 0.0, -1, 1)
+    asel(b("dm"), b("w3"), [[-1, 128]], OP.not_equal, 1.0, 0, 1)
+    io(b("nr2", 512, 640, 1, 2, key="jr2"), [[1, 128]], 0, 128)
+    act(b("sh", p1=2), b("ones", 0, 128, 1, 2), AF.Copy, 0.0, b("pf", p1=2))
     for s in range(4):
         act(b("nr2", 128 * s, 128 * s + 128, 1, 2, key="n%d" % s), b("sh", p1=2), AF.Identity, -72.0 - s, 145.0 + 2 * s)
     ts(b("hx"), b("ci"), 15, OP.bitwise_and)
     ts(b("tab", 0, 128), b("hx"), b("pf"), OP.is_equal, 65.0, OP.mult)
-    ms(b("tab", 128, 144, key="tabz"), 65.0)
+    fill(b("tab", 128, 144, key="tabz"), 65)
     act(b("hv"), b("tab", 0, 128), AF.Relu, float(2 ** 26), -float(2 ** 26))
-    ts(b("emc"), b("hv"), 127.0, OP.max)
+    act(b("emc"), b("hv"), AF.Identity, 127.0)
     act(b("E", 0, 144, key="E0"), ind(b("tab", key=["tab", "tabz"]), b("l17", 0, 9)), AF.Relu, float(2 ** 20), -float(2 ** 20))
     act(b("cnt0"), b("E", 0, 136, key="E0"), AF.Copy, 0.0, -1.0)
     act(b("cnt0", 16, 136, 17), b("jL"), AF.Copy)
@@ -415,25 +477,19 @@ def rank_program(g, core, T, topo):
     act(b("lim"), b("thx", 15, 128, 16), AF.Copy)
     act(b("lim1"), b("thx", 15, 128, 16), AF.Identity, 1.0)
 
-    def x_forms(src, s):
-        if s == 2:
-            cp(b("xb"), src)
+    def x_forms(share):
         act(b("xP"), ind(b("xb"), b("lperm")), AF.Copy)
         for k in range(16):
             o = b("xrep", k, 2048, 16, key="xr%d" % k)
-            if k % 2:
+            if k % share:
                 act(o, b("xP"), AF.Copy)
             else:
                 cp(o, b("xP"))
         act(b("xd"), ind(b("AN", key=["Mb", "xb", "ANz"]), b("lxd")), AF.Copy)
         act(b("xm"), b("xb"), AF.Identity, -MAGIC)
-        act(b("xp"), b("xb"), AF.Identity, 256.0)
+        act(b("xn"), b("xb"), AF.Copy, 0.0, -1.0)
 
-    XR = ["xr%d" % k for k in range(16)]
-    pk = lambda nm, p0, n: ["%s%d" % (nm, p) for p in range(p0, p0 + n)]
-
-    def children(out, nodes):
-        ts(b(out), ind(nodes, b("lperm")), float(E1), OP.min)
+    KB = ("pb0", "pb1")
 
     def rows(out, s, nodes):
         if s == 0:
@@ -441,50 +497,48 @@ def rank_program(g, core, T, topo):
         else:
             act(out, ind(Cw(s), nodes), AF.Copy)
 
-    def lst(name, p0, n):
-        return b(name, 8 * p0, 8 * (p0 + n))
+    def lst(name, h, p0, n):
+        return b(name, 64 * h + 4 * p0, 64 * h + 4 * (p0 + n), key=name + str(h))
 
-    def sums(bank, p0, n, m="B", of="Dab"):
+    def piece(name, h, p0, n):
+        return b(name, 1024 * h + 64 * p0, 1024 * h + 64 * (p0 + n), key=pk("xr", 0, 16) if name == "xrep" else pk(name, 16 * h + p0, n))
+
+    def sums(h, o0, p0, n, m="B", of="Dab"):
         for p in range(p0, p0 + n):
-            add(b(bank, 0, 128), lhs(p, m), b(of, 128 * p, 128 * p + 128, key="%s%d" % (of, p)))
+            add(b(KB[h], o0, o0 + 64), lhs(p, m), piece(of, h, p, 1))
 
-    def sweep(pieces, lists, into, keys):
+    def sweep(pieces, h, lists, into, o0):
         p0 = 0
         for n, bank in pieces:
-            c0, c1 = 128 * p0, 128 * (p0 + n)
-            d, x = b(into, c0, c1, key=pk(into, p0, n)), b("xrep", c0, c1, key=XR)
+            d, x = piece(into, h, p0, n), piece("xrep", h, p0, n)
             if bank:
-                act(d, ind(Aw, lst(lists, p0, n)), AF.Copy)
-                mms(b(bank, 0, c1 - c0), [(b("nI"), x), (b("I"), d)])
-                d = b(bank, 0, c1 - c0)
+                act(d, ind(Aw, lst(lists, h, p0, n)), AF.Copy)
+                mms(b(bank, 0, 64 * n), [(b("nI"), x), (b("I"), d)])
+                d = b(bank, 0, 64 * n)
             else:
-                tt(d, ind(Aw, lst(lists, p0, n)), x, OP.subtract)
-            act(b("Dab", c0, c1, key=pk("Dab", p0, n)), d, AF.Abs)
-            sums(keys, p0, n)
+                tt(d, ind(Aw, lst(lists, h, p0, n)), x, OP.subtract)
+            act(piece("Dab", h, p0, n), d, AF.Abs)
+            sums(h, o0, p0, n)
             p0 += n
 
-    def sweep_arrived():
+    def sweep_arrived(h):
         p0 = 0
-        for n, bank in P1X:
-            c0, c1 = 128 * p0, 128 * (p0 + n)
-            a, o, l = b("ag", c0, c1, key=pk("ag", p0, n)), b("Dab", c0, c1, key=pk("Dab", p0, n)), b("plist", 8 * p0, 8 * (p0 + n))
+        for n, bank in P1X[h]:
+            a, o, l = piece("ag", h, p0, n), piece("Dab", h, p0, n), b("plist", 64 * h + 4 * p0, 64 * h + 4 * (p0 + n))
             if bank:
-                x = b("D", c0, c1, key=pk("D", p0, n))
+                x = piece("D", h, p0, n)
                 act(x, ind(b("xb"), l), AF.Copy)
-                mms(b(bank, 0, c1 - c0), [(b("I"), a), (b("nI"), x)])
-                act(o, b(bank, 0, c1 - c0), AF.Abs)
-                sums("pb0", p0, n)
+                mms(b(bank, 0, 64 * n), [(b("I"), a), (b("nI"), x)])
+                act(o, b(bank, 0, 64 * n), AF.Abs)
+                sums(h, 0, p0, n)
             else:
-                tt(o, ind(b("xi"), l), a, OP.max)
-                sums("pb0", p0, n, "nB", "ag")
-                sums("pb0", p0, n, "B2")
+                tt(o, ind(b("xb"), l), a, OP.max)
+                sums(h, 0, p0, n, "nB", "ag")
+                sums(h, 0, p0, n, "B2")
             p0 += n
-        ps = parts(P1X, False)
-        for p in ps:
-            mm(b("pb2", 168, 176), lhs(p), b("xb", p, 128, 16), p == ps[0], p == ps[-1])
 
-    def firsts(lists, node, on, bank, cl, z):
-        act(b("row", 0, 128), ind(b("iot", key=["iot%d" % k for k in range(13)]), lists), AF.Copy)
+    def firsts(lists, node, on, bank, cl, z, top=WIN):
+        act(b("row", 0, 128), ind(b("iot", 0, top, key=pk("iot", 0, -(-top // 128))), lists), AF.Copy)
         act(b("r17"), ind(b("row", key=["row", "rowz"]), b("l17", 0, 9)), AF.Copy)
         begin(b(bank, 0, 136), b("I"), b("cnt0"))
         for c in range(8):
@@ -495,20 +549,21 @@ def rank_program(g, core, T, topo):
                 add(b(bank, 17 * c + 17, 136), b("lo"), b("E", e0 + 17 * c + 17, e0 + 136, key="E%d" % c))
         scan(b(z), b(cl, key=[cl, cl + "t"]), b(bank, 0, 136), OP.min, OP.max)
 
-    def prefix(o0, f):
-        mm(b("pb2", o0, o0 + 8), b("ld"), f(0, 8), True, False)
-        for d in range(1, 8):
-            mm(b("pb2", o0 + d, o0 + 8), b("lo"), f(0, 8 - d), False, False)
-        mm(b("pb2", o0, o0 + 8), b("IM"), f(0, 8), False, True)
+    def lower(o0, f):
+        scan(b("cum"), b("one8"), f, OP.mult, OP.add)
+        add(b("pb2", o0 + 1, o0 + 8), b("lo"), b("cum", 0, 7))
 
     def send(s):
         h = hops(T, topo, rank, s)
         m = "msg%d" % s
-        fl = "fl%d" % (s % ST)
-        prefix(176, lambda a, z: b(fl, 8 + a, 8 + z))
-        tt(b("pz"), b("pb2", 176, 184), b("cj"), OP.max)
-        ts(b("posu"), b("pz"), -1.0 / M, OP.mult, 257.0, OP.add)
-        scatter(b(m), b("posu"), b("xp"))
+        f, o = b("fl%d" % (s % ST), 8, 16), b("pb2", 176, 184)
+        begin(o, b("I"), b("cj"))
+        add(o, b("lt"), f)
+        lower(176, f)
+        tt(b("fw"), f, b("cj"), OP.mult)
+        add(o, b("nI"), b("fw"))
+        ts(b("posu"), o, -1.0 / M, OP.mult)
+        scatter(b(m), b("posu"), b("xn"))
         n = engines_of(topo, core, h[1])
         rid, pid = topo.addr(h[1], core)
         if len(h) == 3:
@@ -516,14 +571,14 @@ def rank_program(g, core, T, topo):
         else:
             to, sem = T["come%d" % (s // ST)][:, CAP * (s % ST):CAP * (s % ST) + CAP], T.sem["in%d" % s]
         op("g", lambda e: e.remote_dma(to, T[m][:, 0:CAP], sem, T.sem["ls%d" % s], pid, rid, emask(topo, core, h[1], n)),
-           [m], ["come%d_%d" % (s // ST, s % ST)], 120, 3500, "remote%d" % s)
+           [m], ["come%d_%d" % (s // ST, s % ST)], 120, TRIP[s], "remote%d" % s)
 
     def front(s):
         t = s % ST
         vu = b("tu") if t == 0 else b("lu", 8, 16)
         vf = (lambda a, z: b("topf", a, z)) if t == 0 else (lambda a, z: b("s2", 17 + 2 * a, 17 + 2 * z, 2))
         rows(b("cvf"), s, vu)
-        children("cvu", b("cvf"))
+        ts(b("cvu", key=pk("cvu", 0, 2)), ind(b("cvf"), b("lperm")), float(E1), OP.min)
         mm(b("pb2", 0, 160), b("dm"), b("RW", 0, 160, key=["RWa", "cvf", "rowM"]))
         turn(b("tr", 0, 128, key="tra"), b("pb2", 16, 144))
         turn(b("tr", 128, 288, key="trb"), b("pb2", 0, 160))
@@ -531,20 +586,17 @@ def rank_program(g, core, T, topo):
         act(b("emp"), b("cvf"), AF.Relu, -4094.0)
         for p in range(16):
             mm(b("pb2", 160, 168), lhs(p), b("emp", p, 128, 16), p == 0, p == 15)
-        act(b("rB", 0, 8, key="rBa"), b("pb2", 160, 168), AF.Copy, 0.0, BIG / 128)
-        act(b("rB", 8, 16, key="rBb"), b("pb2", 160, 168), AF.Relu, BIG, -BIG / 128)
+        act(b("W4", 8, 16, key="W4b"), b("pb2", 160, 168), AF.Copy, 0.0, BIG / 128)
+        act(b("W4", 24, 32, key="W4d"), b("pb2", 160, 168), AF.Relu, BIG, -BIG / 128)
         nrow = (b("nr2", 128 * s, 128 * s + 128, 1, 2, key="n%d" % s), b("nr2", 512, 640, 1, 2, key="jr2"))
         mms(b("pb3", 144, 272), [nrow, (b("nl8"), b("emp"))])
         tt(b("RW", 272, 400, key="rowN"), b("cvf"), b("pb3", 144, 272), OP.min)
         if s != 2:
             act(b("clv", 16, 136, 17, key="clvt"), vf(0, 8), AF.Identity, 128.0)
-            firsts(vu, lambda c: vf(c, c + 1), lambda c: b("one8" if t == 0 else "nonr", c, c + 1), "pb3", "clv", "zv")
+            firsts(vu, lambda c: vf(c, c + 1), lambda c: b("one8" if t == 0 else "nonr", c, c + 1), "pb3", "clv", "zv", V0 + L * s)
             cp(b("uvu%d" % t), b("zv", 16, 136, 17))
             act(b("acB%d" % t), ind(b("zv"), b("lz")), AF.Relu, 0.0, BIG / M)
             act(b("nac%d" % t), b("acB%d" % t, 0, 8), AF.Identity, BIG, -1.0)
-        tt(b("W4", 16, 24, key="W4c"), b("lim1"), b("nac%d" % t), OP.max)
-        tt(b("W4", 8, 16, key="W4b"), b("W4", 16, 24, key="W4c"), b("rB", 0, 8, key="rBa"), OP.max)
-        tt(b("W4", 24, 32, key="W4d"), b("W4", 16, 24, key="W4c"), b("rB", 8, 16, key="rBb"), OP.max)
         tt(b("coef", 24, 32, key="coefd"), b("nL", 8 * s, 8 * s + 8, key="nL%d" % s), vf(0, 8), OP.subtract)
         act(b("d1", 17, 32, 2, key="d1b"), vf(0, 8), AF.Copy)
         return nrow
@@ -552,83 +604,108 @@ def rank_program(g, core, T, topo):
     def step(s, nrow):
         t = s % ST
         n0 = V0 + L * s
-        v0 = b("d1", 17, 32, 2, key="d1b")
-        begin(b("pb0", 0, 128), ONE, JROW)
+        bf = lambda a, z: b("pay", 15 + 16 * a, 16 * z, 16, key=["pay0", "pay1"])
+        for h in range(2):
+            K1 = b(KB[h], 0, 64)
+            begin(K1, row(ONE), row(JROW, 64 * h, 64 * h + 64))
+            if s == 2:
+                sweep_arrived(h)
+            else:
+                sweep(P1[h], h, "cvu", "D", 0)
+            r0 = 16 + 128 * h
+            r = b("rr", r0, r0 + 64, key="r1%d" % h)
+            half = lambda nm: b(nm, 64 * h, 64 * h + 64, key=nm + str(h))
+            scan(r, b("RM", 0, 64), K1, OP.max, OP.min)
+            tt(half("e"), r, K1, OP.not_equal)
+            scan(half("pay"), half("e"), b("dl", 64 * h, 64 * h + 64), OP.mult, OP.add)
+            bu = b("bu", 4 * h, 4 * h + 4, key="bu%d" % h)
+            ts(bu, b("pay", 64 * h + 15, 64 * h + 64, 16, key="pay%d" % h), float(E1), OP.min)
+            rows(half("dvf"), s, bu)
+            ts(half("dvu"), ind(half("dvf"), b("lperm", 0, 4)), float(E1), OP.min)
+            tt(half("cand"), b("rr", r0 - 1, r0 + 63, key=["r1%d" % h, "r20" if h else "rra"]), K1, OP.max)
+            scan(b("rr", r0 + 64, r0 + 128, key="r2%d" % h), b("RM2"), half("cand"), OP.max, OP.min)
+            act(b("mbt", 4 * h, 4 * h + 4, key="mb%d" % h), b("rr", r0 + 15, r0 + 64, 16, key="r1%d" % h), AF.Copy)
+        mb = b("mbt", key=["mb0", "mb1"])
         if s == 2:
-            sweep_arrived()
-        else:
-            sweep(P1, "cvu", "D", "pb0")
-        r = b("rr", 16, 144, key="r1")
-        rs = b("rr", 15, 143, key=["r1", "rra"])
-        scan(r, b("RM"), b("pb0", 0, 128), OP.max, OP.min)
-        scan(b("r0"), b("RM"), b("pb0", 0, 128), OP.max, OP.min)
-        tt(b("e"), ind(b("r0"), b("lend")), rs, OP.is_equal)
-        scan(b("pay"), b("e"), b("dl"), OP.mult, OP.add)
-        bf = lambda a, z: b("pay", 15 + 16 * a, 16 * z, 16)
-        ts(b("bu"), bf(0, 8), float(E1), OP.min)
-        rows(b("dvf"), s, b("bu"))
-        children("dvu", b("dvf"))
-        tt(b("cand"), rs, b("pb0", 0, 128), OP.max)
-        scan(b("rr", 144, 272, key="r2"), b("RM2"), b("cand"), OP.max, OP.min)
-        cp(b("dec"), b("rr", 31, 272, 16, key=["r1", "r2"]))
+            ps = parts(P1X[0], False)
+            for p in ps:
+                mm(b("pb2", 168, 176), lhs(p), b("xb", p, 128, 16), p == ps[0], p == ps[-1])
+            tt(b("mbx"), mb, b("pb2", 168, 176), OP.subtract)
+            mb = b("mbx")
+        cp(b("dec"), b("rr", 31, 272, 16, key=["r10", "r11", "r20", "r21"]))
         ts(b("dk"), b("dec"), 127, OP.bitwise_and)
-        ts(b("du"), b("dk"), b("p128"), OP.add)
+        ts(b("du", 0, 8, key="du0"), b("dk", 0, 8), b("p64"), OP.add)
+        ts(b("du", 8, 16, key="du1"), b("dk", 8, 16), b("p64b"), OP.add)
         cp(b("ku"), b("dk"))
         bare = "ag" if s == 2 else "D"
-        act(b("dd"), ind(b(bare, key=pk(bare, 0, 16)), b("du")), AF.Copy)
+        act(b("dd"), ind(b(bare, key=pk(bare, 0, 32)), b("du", key=["du0", "du1"])), AF.Copy)
         act(b("oh"), ind(b("tab", 0, 128), b("ku")), AF.Copy)
-        db, dq, ohb, ohq = b("dd", 0, 128), b("dd", 128, 256), b("oh", 0, 128), b("oh", 128, 256)
+        db, dq, ohb, ohq = ("dd", 0), ("dd", 64), ("oh", 0), ("oh", 64)
+
+        def mmh(bank, o0, whole, halves):
+            if whole:
+                begin(b(bank, o0, o0 + 128), *whole[0])
+                for l, r in whole[1:]:
+                    add(b(bank, o0, o0 + 128), l, r)
+            for h in range(2):
+                pairs = [(l, b(nm, 128 * h + c0, 128 * h + c0 + 64)) for l, (nm, c0) in halves]
+                o = b(bank, o0 + 64 * h, o0 + 64 * h + 64)
+                if whole:
+                    for l, r in pairs:
+                        add(o, l, r)
+                else:
+                    mms(o, pairs)
+
         xd = b("xb" if s == 2 else "xd")
-        mms(b("pb6", 0, 128), [(ONE, RH), (b("nI2"), xd), (b("I"), db), (b("I"), dq)])
+        mmh("pb6", 0, [(row(ONE), row(RH)), (b("nI2"), xd)], [(b("I"), db), (b("I"), dq)])
         act(b("pb6", 128, 256), b("pb6", 0, 128), AF.Identity, MAGIC, 0.5)
         act(b("absM"), b("pb6", 128, 256), AF.Abs, -MAGIC)
         tt(b("AN", 0, 128, key="Mb"), b("xm"), b("pb6", 128, 256), OP.add)
-        mms(b("pb4", 256, 384), [(b("I"), b("emc")), (b("bones"), b("absM"))])
-        scan(b("es"), b("RM"), b("pb4", 256, 384), OP.max, OP.min)
-        mms(b("pb4", 384, 512), [(b("nI"), xd), (b("I"), db)])
-        act(b("cl", 0, 128, key="cla"), b("pb4", 384, 512), AF.Relu, -4.0)
-        act(b("cl", 128, 256, key="clz"), b("pb4", 384, 512), AF.Relu, -4.0, -1.0)
+        mms(b("pb6", 384, 512), [(b("I"), b("emc")), (b("bones"), b("absM"))])
+        scan(b("es"), b("RM"), b("pb6", 384, 512), OP.max, OP.min)
+        mmh("pb2", 384, [(b("nI"), xd)], [(b("I"), db)])
+        act(b("cl", 0, 128, key="cla"), b("pb2", 384, 512), AF.Relu, -4.0)
+        act(b("cl", 128, 256, key="clz"), b("pb2", 384, 512), AF.Relu, -4.0, -1.0)
         mms(b("pb6", 256, 384), [(b("I"), b("xb")), (b("I"), b("cl", 0, 128, key="cla")), (b("nI"), b("cl", 128, 256, key="clz"))])
         act(b("hv"), b("pb6", 256, 384), AF.Copy)
-        begin(b("pb1", 0, 128), ONE, R127)
-        sweep(P2, "dvu", "D" if s == 2 else "ag", "pb1")
-        mb = b("rr", 31, 144, 16, key="r1")
-        if s == 2:
-            tt(b("mbx"), mb, b("pb2", 168, 176), OP.subtract)
-            mb = b("mbx")
-        tt(b("W4", 0, 8, key="W4a"), mb, b("nac%d" % t), OP.max)
+        for h in range(2):
+            begin(b(KB[h], 64, 128), row(ONE), row(R127, 0, 64))
+            sweep(P2[h], h, "dvu", "D" if s == 2 else "ag", 64)
         tt(b("df"), mb, b("lim"), OP.subtract)
         act(b("G2", 0, 8, key="G2a"), b("df"), AF.Relu, 0.0, BIG)
         act(b("G2", 8, 16, key="G2b"), b("df"), AF.Relu, BIG, -BIG)
-        tt(b("UU"), ind(b("G2", key=["G2a", "G2b"]), b("lg")), b("W4", key=["W4a", "W4b", "W4c", "W4d"]), OP.max)
+        tt(b("G4"), ind(b("G2", key=["G2a", "G2b"]), b("lg")), b("W4", key=["W4b", "W4d"]), OP.max)
         tt(b("U1"), mb, b("lim1"), OP.min)
+        tt(b("Uac"), b("U1"), b("nac%d" % t), OP.max)
+        tt(b("UU"), ind(b("Uac"), b("lr")), b("G4"), OP.max)
         tt(b("U4"), ind(b("U1"), b("lr")), b("acB%d" % t), OP.min)
-        tt(b("coef", 0, 8, key="coefa"), bf(0, 8), v0, OP.subtract)
+        tt(b("coef", 0, 8, key="coefa"), bf(0, 8), b("d1", 17, 32, 2, key="d1b"), OP.subtract)
         act(b("clb", 16, 136, 17, key="clbt"), bf(0, 8), AF.Identity, 128.0)
         tt(b("FL", 0, 32), ind(b("es"), b("lF")), b("UU"), OP.is_ge)
         tt(b("FL", 32, 40, key="am"), b("es", 15, 128, 16), b("U4", 0, 8), OP.is_lt)
-        tt(b("Tt4"), ind(b("es"), b("lF")), b("U4"), OP.min)
+        tt(b("TT", 0, 32, key=["Tt", "THh"]), ind(b("es"), b("lF")), b("U4"), OP.min)
         act(b("nfl"), b("FL", 0, 32), AF.Identity, BIG, -BIG)
-        tt(b("TH"), b("U4"), b("nfl"), OP.max)
+        tt(b("TT", 24, 56, key=["THh", "TH"]), b("U4"), b("nfl"), OP.max)
         tt(b("prod", 8, 56), ind(b("FL", key=["FL", "am"]), b("lfl", 0, 3)), b("coef", key=["coef" + k for k in "abcdef"]), OP.mult)
         act(b("prod", 0, 8, key="proda"), b("FL", 16, 24), AF.Identity, -384.0, 256.0)
         tt(b("d0", 1, 48, 2, key="d0b"), b("prod", 0, 24, key=["prod", "proda"]), b("prod", 24, 48), OP.add)
-        mms(b("pb5", 0, 128), [(b("I63"), ohb)])
-        mms(b("pb5", 128, 256), [(b("I63"), ohb), (b("I63"), ohq)])
-        mms(b("pb5", 256, 384), [nrow, (b("nI128"), ohb)])
-        mms(b("pb5", 384, 512), [(R63, R65), (b("nI63"), ohb), (b("nI63"), ohq)])
-        mms(b("pb3", 272, 400), [(R128, R65), (b("nI8"), b("emp")), (b("nI128"), ohb), (b("idf"), b("dvf"))])
+        mmh("pb5", 0, [], [(b("I63"), ohb)])
+        mmh("pb5", 128, [], [(b("I63"), ohb), (b("I63"), ohq)])
+        mmh("pb5", 256, [nrow], [(b("nI128"), ohb)])
+        act(b("pb5", 384, 512), b("pb5", 128, 256), AF.Identity, 4095.0, -1.0)
+        mmh("pb3", 272, [(row(R128), row(R65)), (b("nI8"), b("emp")), (b("idf"), b("dvf", key=["dvf0", "dvf1"]))], [(b("nI128"), ohb)])
         tt(b("w3"), b("cvf"), b("pb5", 0, 128), OP.max)
         tt(b("w4"), b("cvf"), b("pb5", 128, 256), OP.max)
         tt(b("CN", 0, 128), b("cvf"), b("pb5", 384, 512), OP.max)
         tt(b("RW", 144, 272, key="rowM"), b("w4"), b("pb5", 256, 384), OP.min)
         tt(b("RW", 400, 528, key="rsp"), b("w3"), b("pb3", 272, 400), OP.min)
         fl = "fl%d" % t
-        scan(b("fs"), b("RM"), b("pb1", 0, 128), OP.max, OP.min)
-        tt(b("hf"), b("fs", 15, 128, 16), b("TH", 0, 8), OP.is_ge)
-        tt(b(fl, 8, 24), ind(b("fs"), b("lF", 0, 1)), b("TH", 8, 24), OP.is_ge)
-        tt(b("d1", 0, 64, 2, key="d1s"), ind(b("fs"), b("lF")), b("Tt4"), OP.is_ge)
-        scan(b("s2"), b("d0", 0, 48, key=["d0", "d0b"]), b("d1", 0, 48, key=["d1a", "d1b", "d1c", "d1s"]), OP.mult, OP.add)
+        for h in range(2):
+            scan(b("fs", 64 * h, 64 * h + 64, key="fs%d" % h), b("RM", 0, 64), b(KB[h], 64, 128), OP.max, OP.min)
+        fs = b("fs", key=["fs0", "fs1"])
+        tt(b("d1", 0, 64, 2, key="d1s"), ind(fs, b("lF")), b("TT", 0, 32, key=["Tt", "THh"]), OP.is_ge)
+        tt(b(fl, 8, 24), ind(fs, b("lF", 0, 1)), b("TT", 32, 48, key="TH"), OP.is_ge)
+        scan(b("s2"), b("d0", key=["d0", "d0b"]), b("d1", 0, 48, key=["d1a", "d1b", "d1c", "d1s"]), OP.mult, OP.add)
         cp(b("lu"), b("s2", 1, 48, 2))
         if t == 0:
             act(b("nonr"), b(fl, 16, 24), AF.Identity, 1.0, -1.0)
@@ -636,7 +713,7 @@ def rank_program(g, core, T, topo):
         scatter(b("CW", 0, 128 + n0, key=["C"] + blocks("C", s)), b("uvu%d" % t), b("rpre"))
         act(b("C", n0, n0 + L, key="Cb%d" % s), ind(b("CN", key=["CN", "CNz"]), b("lu", 16, 24)), AF.Copy)
         act(b("A", n0, n0 + L, key="Ab%d" % s), ind(b("AN", key=["Mb", "xb", "ANz"]), b("lu", 16, 24)), AF.Copy)
-        firsts(b("bu"), lambda c: bf(c, c + 1), lambda c: b("hf", c, c + 1), "pb4", "clb", "zb")
+        firsts(b("bu", key=["bu0", "bu1"]), lambda c: bf(c, c + 1), lambda c: b("d1", 48 + 2 * c, 49 + 2 * c, key="d1s"), "pb7", "clb", "zb")
         cp(b("oAu"), b("zb", 16, 136, 17))
         scatter(b("AW", 0, 128 + n0, key=["A"] + blocks("A", s)), b("oAu"), b("hv"))
         send(s)
@@ -644,41 +721,43 @@ def rank_program(g, core, T, topo):
     def round_end(s):
         cm = "come%d" % (s // ST)
         tt(b("rest2"), b("fl0", 16, 24), b("fl1", 16, 24), OP.add)
-        prefix(192, lambda a, z: b("rest2", a, z))
-        act(b("nrs"), b("pb2", 192, 200), AF.Identity, 257.0, -1.0 / M)
+        begin(b("pb2", 192, 200), b("lp"), b("rest2"))
+        lower(192, b("rest2"))
+        act(b("nrs"), b("pb2", 192, 200), AF.Identity, 256.0, -1.0 / M)
         act(b("absM"), ind(Aw, b("lu", 8, 16)), AF.Copy)
         mms(b("pb6", 0, 128), [(b("nI"), b("xb")), (b("I"), b("absM"))])
         act(b("ad"), b("pb6", 0, 128), AF.Abs)
         first = b(cm, 0, CAP, key=cm + "_0")
-        op("s", lambda e: e.activation(b("msk")[0], first[0], AF.Sign, accum_out=b("n0")[0]), first[1], ["msk", "n0"], 90)
-        act(b("cd"), b("n0"), AF.Identity, float(CAP), -1.0)
+        op("s", lambda e: e.activation(b("msk")[0], first[0], AF.Sign, bias=NONE / 2, scale=-1.0, accum_out=b("na")[0]),
+           first[1], ["msk", "na"], 90)
+        act(b("n0"), b("na"), AF.Identity, CAP / 2, 0.5)
+        act(b("cd"), b("na"), AF.Identity, CAP / 2, -0.5)
         ts(b("ge"), b("nrs"), b("n0"), OP.is_ge, b("cd"), OP.mult)
         tt(b("idx"), b("nrs"), b("ge"), OP.add)
         ts(b("iu"), b("idx"), 64.0, OP.min)
-        tt(b("hx"), ind(b(cm, key=[cm + "_0", cm + "_1", cm + "z"]), b("iu")), b("ad"), OP.max)
-        ts(b("xi"), b("hx"), 255, OP.bitwise_and)
+        tt(b("hz"), ind(b(cm, key=[cm + "_0", cm + "_1", cm + "z"]), b("iu")), b("ad"), OP.min)
+        act(b("xb"), b("hz"), AF.Abs)
 
-    x_forms(b("xb"), 0)
+    x_forms(2)
     nrow = front(0)
     for s in range(4):
         step(s, nrow)
         if s == 3:
-            dma("y", "ld5", T.yc[:], b("C", 0, W)[0], ["C"] + blocks("C", 4), ["yc"], 5000)
-            dma("s", "ld6", T.ya[:], b("A", 0, W)[0], ["A"] + blocks("A", 4), ["ya"], 3500)
+            dma("ld5", T.yc[:], b("C", 0, W)[0], ["C"] + blocks("C", 4), ["yc"], 768)
+            dma("ld6", T.ya[:], b("A", 0, W)[0], ["A"] + blocks("A", 4), ["ya"], 384)
         if s % ST == 1:
             round_end(s)
         if s < 3:
             nrow = front(s + 1)
         if s == 1:
             for j in range(8):
-                o, a = b("ag", 256 * j, 256 * j + 256, key=pk("ag", 2 * j, 2)), ind(Aw, lst("cvu", 2 * j, 2))
-                if j % 2:
+                o, a = piece("ag", j // 4, 4 * (j % 4), 4), ind(Aw, lst("cvu", j // 4, 4 * (j % 4), 4))
+                if j % 3:
                     act(o, a, AF.Copy)
                 else:
                     cp(o, a)
-            x_forms(b("xi"), 2)
-    cp(b("xb"), b("xi"))
-    dma("y", "ld7", T.yx[:], b("xb")[0], ["xb"], ["yx"], 1500)
+            x_forms(4)
+    dma("ld7", T.yx[:], b("xb")[0], ["xb"], ["yx"], 32)
 
     if "o" not in ORDER:
         ORDER["o"] = order_calls(ops)

@@ -7,15 +7,25 @@ WIN = W + 8
 BIG = float(2 ** 30)
 MAGIC = float(3 * 2 ** 22)
 NONE = 1000
-M = 2048.0
+M = float(2 ** 22)
+UNIT = 2.0 ** -21
+KEY = 256 * UNIT
+FAR = 2048.0
+NH = 2
+HC, HW = 8 // NH, 128 // NH
 P1 = [[(4, None), (4, bank), (5, None), (3, None)] for bank in ("pb7", "pb4")]
 P1X = [[(5, None), (2, bank), (5, None), (4, None)] for bank in ("pb7", "pb4")]
 P2 = P1
-ROUNDS, TRIES, SLACK = 6, (5000, 3000, 2000), 60.0
+AGQ = "vssvssvs"
+ROUNDS, TRIES, SLACK = 6, (1400,) * 14, 60.0
 CYCLE, GAT, SCA = 0.83, 1.5, 3.2
 START, KIB = 1000.0, 3.9
 TRIP = (10000, 3900, 7000, 3900)
-WAKE = 220.0
+WAKE = 235.0
+
+COSTS = ((0.83, 1.5, 3.2, 235.0, 0.5), (1.2, 1.55, 3.6, 250.0, 0.36))
+
+CHOICE, BAR, GAIN = 3, 20, 200.0
 
 SLOT = {}
 SIZE = {"F": 0, "B": 0, "I": 0, "U": 0}
@@ -27,21 +37,31 @@ def _s(kind, **kw):
         SIZE[kind] += (w + 15) // 16 * 16
 
 
-_s("B", AW=128 + WIN, xrep=2048, D=2048, Dab=2048, ag=2048, AN=272, xP=128, xd=128, xn=128, hz=128, nr2=640, ones=144, B=144, B2=144, nB=144, pw=128,
-   bones=128, lo=128, lt=128, ld=128, lp=128, nl8=128, I=128, nI=128, nI2=128, I63=128, nI128=128, nI8=128, sh=128, cr=1024,
-   cnt0=136, emc=128, tab=144, emp=128, oh=256, dd=256, cl=256, absM=128, hv=128, E=1088, fl0=32, fl1=32, rest2=8, cum=8, cj=8, fw=8, msk=32)
-_s("F", CW=128 + WIN, iot=WIN, RW=544, CN=272, idf=128, dm=128, RM=128, RM2=64, tr=288, dl=128, rr=272, e=128, cand=128, pay=128,
-   row=144, r17=144, clv=136, clb=136, zv=136, zb=136, w3=128, w4=128, rpre=128, dvf=128, es=128, fs=128, xm=128,
-   ad=128, thf=128, thx=128, lim=8, lim1=8, jL=8, topf=8, nL=32, acB0=32, acB1=32, nac0=8, nac1=8, W4=32, G2=16, G4=32,
-   UU=32, U1=8, Uac=8, U4=32, TT=56, FL=40, nfl=32, coef=48, prod=56, d0=48, d1=64, s2=48, df=8, mbt=8, mbx=8, nonr=8, one8=8,
-   nrs=8, ge=8, idx=8, na=1, n0=1, cd=1, r7=1, hi=1, p64=1, p64b=1, pf=1, pG=1, tmp=16, tmp2=16, tmp3=16)
+_s("B", AW=128 + WIN, xrep=2048, D=2048, Dab=2048, ag=2048, AN=512, xP=128, xd=128, xn=128, hz=128, nr2=640, ones=144, B=144, B2=144, nB=144, pw=128,
+   bones=128, lo=128, lt=128, ld=128, lp=128, nl8=128, I=128, nI=128, hI=128, nhI=128, I63=128, nI63=128, I128=128, I256=128, nI128=128, nI8=128,
+   sh=128, cr=1280, cnt0=128, emc=128, tab=128, emp=128, oh=256, ab=128, dq=128, cl=128, absM=128, E0=1024, E1=1024, fl0=32, fl1=32, rest2=8, cum=8,
+   cj=8, fw=8, msk=32)
+_s("F", CW=128 + WIN, iot=WIN, RW=544, CN=512, idf=128, dm=128, RM=128, RM2=128, RN=128, RF=128, NF=32, RZ=128, tr=288, dl=128, RX=640, e=128, cand=128, pay=128,
+   row0=128, row1=128, RY0=136, RY1=136, zv=136, zb=136, w3=128, rpre=128, dvf=128, fs=128, rm=128, xm=128,
+   ad=128, thf=128, thx=128, lim4=32, jL=8, topf=8, nL=32, LA0=32, LA1=32, U4=32, TT=64, FL=32, nfl=32, coef=24, prod=32, d0=32, d1=64, s2=32,
+   cvp=128, dvp=128, cB=8, cB2=8, uv=8, ub=8, nonr=8, one8=8,
+   nrs=8, ge=8, idx=8, na=1, n0=1, cd=1, r7=1, pH=2, pf=1, pG=1, tmp=16, tmp2=16, tmp3=16)
 _s("I", KI=WIN, tp=8, thi=128, pin=16, pa=16, pc=16, ci=128, ri=128, dec=16, dk=16, hx=128, xi=128)
-_s("U", tu=8, cvu=128, dvu=128, bu=8, du=16, ku=16, uvu0=8, uvu1=8, lu=24, oAu=8, posu=8, iu=8,
-   plist=128, lperm=8, l17=10, lsel=8, lF=2, lr=2, lz=2, lg=2, lfl=4, lxd=8)
+_s("U", tu=8, cvu=128, dvu=128, rowu0=128, rowu1=128, bu=8, du=8, ku=16, uvu0=8, uvu1=8, lu=16, oAu=8, posu=8, iu=8,
+   plist=128, lperm=8, lsel=8, lF=2, lz=2, lxd=8)
 SLOT["C"] = ("arF", SLOT["CW"][1] + 128, WIN)
 SLOT["A"] = ("arB", SLOT["AW"][1] + 128, WIN)
 SLOT["cvf"] = ("arF", SLOT["RW"][1] + 16, 128)
-SLOT["xb"] = ("arB", SLOT["AN"][1] + 128, 128)
+SLOT["xb"] = ("arB", SLOT["AN"][1] + 256, 128)
+for _k, _n in enumerate(("r2", "r1", "lim", "es", "no")):
+    SLOT[_n] = ("arF", SLOT["RX"][1] + 128 * _k, 128)
+ROWU, CLS, MBS = (2, 2), False, False
+STAG = (1, 0, 1, 1)
+NFV = True
+IOTG = 8
+D3 = True
+CVS, RMT = (False, False), False
+XQ = ("vsvsvsvsvsvsvsvs", "vsssvsssvsssvsss")
 
 SCRATCH = {"arF": ("sbuf", [128, SIZE["F"]], "float32"), "arB": ("sbuf", [128, SIZE["B"]], "bfloat16"),
            "arI": ("sbuf", [128, SIZE["I"]], "int32"), "arU": ("sbuf", [128, SIZE["U"]], "uint16")}
@@ -52,6 +72,9 @@ for _k in range(4):
     SCRATCH["rl%d" % _k] = ("sbuf", [128, 32], "bfloat16")
 for _k in range(2):
     SCRATCH["come%d" % _k] = ("sbuf", [128, 80], "bfloat16")
+    SCRATCH["r3%d" % _k] = ("sbuf", [128, 8, 17], "uint16")
+    SCRATCH["e4%d" % _k] = ("sbuf", [128, 8, 8, 17], "bfloat16")
+SCRATCH["c3"] = ("sbuf", [128, 8, 17], "bfloat16")
 SEMAPHORES = (["qv", "qs", "qt", "qg"] + ["in%d" % k for k in range(4)] + ["rr%d" % k for k in range(4)] + ["ls%d" % k for k in range(4)]
               + ["ld%d" % k for k in range(8)])
 ORDER = {}
@@ -125,6 +148,8 @@ def order_calls(ops):
                 wr[k] = i
                 rd[k] = []
                 adds[k] = []
+        for j in o.get("after", []):
+            d.setdefault(j, 0.0)
         d.pop(i, None)
         pre.append(d)
     post = [{} for _ in range(n)]
@@ -165,51 +190,122 @@ def order_calls(ops):
         if best is None or max(end) < best[0]:
             best = (max(end), start)
         way = place(sorted(range(n), key=lambda i: (-end[i], -i)), post, True)[1]
-    need = [list(d.items()) for d in pre]
-    time, lag, queue = [o["c"] for o in ops], [o["lag"] for o in ops], [o["q"] for o in ops]
+    lag, queue = [o["lag"] for o in ops], [o["q"] for o in ops]
+    costs = [([o["cs"][k] for o in ops], [[(j, m[3] if w else 0.0) for j, w in d.items()] for d in pre], m[4]) for k, m in enumerate(COSTS)]
 
-    def run(order):
-        end, why, free = [0.0] * n, [-1] * n, {q: (0.0, 0) for q in queue}
-        for i in order:
-            t, y = free[queue[i]]
-            y = -2 - y if t else -1
-            for j, w in need[i]:
-                if end[j] + w >= t:
-                    t, y = end[j] + w, j
-            free[queue[i]], end[i], why[i] = (t + time[i], i), t + time[i] + lag[i], y
-        return max(end), end, why
+    def run(order, a=0, old=None):
+        before, total, found = {}, 0.0, []
+        for i in reversed(order[:a]):
+            if queue[i] not in before:
+                before[queue[i]] = i
+                if len(before) == 5:
+                    break
+        for k, (time, need, weight) in enumerate(costs):
+            end, why = (list(old[k][0]), list(old[k][1])) if a else ([0.0] * n, [-1] * n)
+            free = {q: (end[before[q]] - lag[before[q]], before[q]) if q in before else (0.0, 0) for q in "vstgy"}
+            for i in order[a:]:
+                t, y = free[queue[i]]
+                y = -2 - y if t else -1
+                for j, w in need[i]:
+                    if end[j] + w >= t:
+                        t, y = end[j] + w, j
+                t += time[i]
+                free[queue[i]], end[i], why[i] = (t, i), t + lag[i], y
+            total += weight * max(end)
+            found.append((end, why))
+        return total, found
+
+    gives = [[[(j, m[3] if w else 0.0) for j, w in d.items()] for d in post] for m in COSTS]
+
+    def tails(order):
+        found = []
+        for (time, need, weight), give in zip(costs, gives):
+            rest, behind = [0.0] * n, dict.fromkeys("vstgy", 0.0)
+            for i in reversed(order):
+                t = 0.0
+                for j, w in give[i]:
+                    if rest[j] + w > t:
+                        t = rest[j] + w
+                t += lag[i]
+                if behind[queue[i]] > t:
+                    t = behind[queue[i]]
+                behind[queue[i]] = rest[i] = t + time[i]
+            found.append(rest)
+        return found
+
+    def through(order, a, z, part, found, rests, at):
+        kinds, before, after, total = {queue[i] for i in part}, {}, {}, 0.0
+        for places, into in ((range(a - 1, -1, -1), before), (range(z + 1, n), after)):
+            for m in places:
+                q = queue[order[m]]
+                if q in kinds and q not in into:
+                    into[q] = order[m]
+                    if len(into) == len(kinds):
+                        break
+        for (time, need, weight), give, (old, why), rest in zip(costs, gives, found, rests):
+            end, far = {}, max(old) - GAIN
+            free = {q: old[before[q]] - lag[before[q]] if q in before else 0.0 for q in kinds}
+            for i in part:
+                t = free[queue[i]]
+                for j, w in need[i]:
+                    y = end.get(j, old[j]) + w
+                    if y > t:
+                        t = y
+                free[queue[i]] = t = t + time[i]
+                end[i] = t = t + lag[i]
+                if t > far:
+                    far = t
+                for j, w in give[i]:
+                    if at[j] > z and t + w + rest[j] > far:
+                        far = t + w + rest[j]
+            for q in after:
+                far = max(far, free[q] + rest[after[q]])
+            total += weight * far
+        return total
 
     def exchange(order, tries, seed):
-        last, end, why = run(order)
-        good = (last, order, end)
-        for _ in range(tries):
-            seed = (seed * 1103515245 + 12345) % 2 ** 31
-            i, pairs = end.index(last), []
-            while i >= 0:
-                if why[i] <= -2:
-                    pairs.append((-2 - why[i], i))
-                i = why[i] if why[i] >= -1 else -2 - why[i]
-            u, v = pairs[(seed >> 8) % len(pairs)]
-            a, z, early = order.index(u), order.index(v), seed >> 5 & 1
-            for _ in range((0, 0, 0, 1, 2, 4)[(seed >> 20) % 6]):
-                if early:
-                    a = max([m for m in range(max(0, a - 60), a) if queue[order[m]] == queue[u]] or [a])
-                else:
-                    z = min([m for m in range(z + 1, min(n, z + 60)) if queue[order[m]] == queue[u]] or [z])
-            part, tied = order[a:z + 1], {v if early else u}
-            for x in (reversed(part) if early else part):
-                if early and x in tied:
-                    tied.update(pre[x])
-                elif not early and any(j in tied for j in pre[x]):
-                    tied.add(x)
-            if order[a if early else z] in tied:
-                continue
-            new = order[:a] + [x for x in part if (x in tied) == early] + [x for x in part if (x in tied) != early] + order[z + 1:]
-            now = run(new)
-            if now[0] <= last + SLACK * (seed >> 3 & 3) / 3 * (seed >> 12 & 3) / 3:
-                order, (last, end, why) = new, now
+        last, found = run(order)
+        good, barred, rest = (last, order, found[0][0]), {}, None
+        for turn in range(tries):
+            if rest is None:
+                rest, pairs, at = tails(order), [], {i: m for m, i in enumerate(order)}
+                for end, why in found:
+                    i = end.index(max(end))
+                    while i >= 0:
+                        if why[i] <= -2:
+                            pairs.append((-2 - why[i], i))
+                        i = why[i] if why[i] >= -1 else -2 - why[i]
+            pick = None
+            for _ in range(CHOICE):
+                seed = (seed * 1103515245 + 12345) % 2 ** 31
+                u, v = pairs[(seed >> 8) % len(pairs)]
+                if barred.get((u, v), -1) > turn:
+                    continue
+                a, z, early = at[u], at[v], seed >> 5 & 1
+                for _ in range((0, 0, 0, 1, 2, 4)[(seed >> 20) % 6]):
+                    if early:
+                        a = max([m for m in range(max(0, a - 40), a) if queue[order[m]] == queue[u]] or [a])
+                    else:
+                        z = min([m for m in range(z + 1, min(n, z + 40)) if queue[order[m]] == queue[u]] or [z])
+                part, tied = order[a:z + 1], {v if early else u}
+                for x in (reversed(part) if early else part):
+                    if early and x in tied:
+                        tied.update(pre[x])
+                    elif not early and any(j in tied for j in pre[x]):
+                        tied.add(x)
+                if order[a if early else z] in tied:
+                    continue
+                part = [x for x in part if (x in tied) == early] + [x for x in part if (x in tied) != early]
+                guess = through(order, a, z, part, found, rest, at)
+                if pick is None or guess < pick[0]:
+                    pick = (guess, a, z, part, u, v)
+            if pick and pick[0] <= last + SLACK * (seed >> 3 & 3) / 3 * (seed >> 12 & 3) / 3:
+                guess, a, z, part, u, v = pick
+                order = order[:a] + part + order[z + 1:]
+                last, found = run(order, a, found)
+                barred[(v, u)], rest = turn + BAR + (seed >> 9 & 7), None
                 if last < good[0]:
-                    good = (last, order, end)
+                    good = (last, order, found[0][0])
         return good
 
     order = sorted(range(n), key=lambda i: (best[1][i], i))
@@ -217,8 +313,9 @@ def order_calls(ops):
         last, order, end = exchange(order, tries, k + 1)
         way = place(sorted(range(n), key=lambda i: (-end[i], -i)), post, True)[1]
         start, end = place(sorted(range(n), key=lambda i: (-way[i], i)), pre, False)
-        if max(end) < last:
-            order = sorted(range(n), key=lambda i: (start[i], i))
+        other = sorted(range(n), key=lambda i: (start[i], i))
+        if run(other)[0] < last:
+            order = other
     return order
 
 
@@ -233,10 +330,12 @@ def rank_program(g, core, T, topo):
         relay(g, core, T, topo)
         return
     eng = {"v": g.vector, "s": g.scalar, "t": g.tensor, "g": g, "y": g.sync}
-    ops = []
+    ops, picks = [], [0, 0]
 
     def op(q, call, R, Wk, c, lag=0.0, dma=None, adds=None):
-        ops.append({"q": q, "call": call, "R": R, "W": Wk, "c": c * CYCLE, "lag": lag, "dma": dma, "adds": adds})
+        cs = [c * CYCLE if dma else (c + (m[1] - GAT) * picks[0] + (m[2] - SCA) * picks[1]) * m[0] for m in COSTS]
+        ops.append({"q": q, "call": call, "R": R, "W": Wk, "c": c * CYCLE, "cs": cs, "pk": list(picks), "lag": lag, "dma": dma, "adds": adds})
+        picks[:] = [0, 0]
 
     def dma(sem, out, in_, R, Wk, kib):
         op("y", lambda e: e.dma_start(out, in_), R, Wk, 60 + kib * KIB / CYCLE, START, sem)
@@ -261,6 +360,7 @@ def rank_program(g, core, T, topo):
 
     def cyc(o, a, f=1.0):
         if a[3] == "ind":
+            picks[0] = a[2]
             return 70 + GAT * a[2]
         return max(64, a[2] * (f / 2 if o[3] in ("arB", "arU") and a[3] in ("arB", "arU") and f == 1.0 else f))
 
@@ -276,8 +376,14 @@ def rank_program(g, core, T, topo):
     def cp(o, a):
         op("v", lambda e: e.tensor_copy(o[0], a[0]), ks(a), ks(o), cyc(o, a))
 
-    def scatter(win, off, a):
-        op("v", lambda e: e.tensor_copy(win[0].indirect(off[0]), a[0]), ks(a, off), ks(win), 60 + SCA * a[2])
+    def scatter(win, off, a, c=None):
+        picks[1] = a[2]
+        if c is None:
+            op("v", lambda e: e.tensor_copy(win[0].indirect(off[0]), a[0]), ks(a, off), ks(win), 60 + SCA * a[2])
+        elif len(c) == 2:
+            op("v", lambda e: e.tensor_scalar(win[0].indirect(off[0]), a[0], c[0], c[1], OP.mult, OP.add), ks(a, off), ks(win), 60 + SCA * a[2])
+        else:
+            op("v", lambda e: e.tensor_tensor(win[0].indirect(off[0]), a[0], c[0], OP.add), ks(a, c, off), ks(win), 60 + SCA * a[2])
 
     def ms(o, v):
         op("v", lambda e: e.memset(o[0], v), [], ks(o), cyc(o, o))
@@ -309,6 +415,11 @@ def rank_program(g, core, T, topo):
             return e.matmul(o[0], l[0], r[0], False, left[k] == 0)
         op("t", call, ks(l, r), ks(o), max(min(64, l[2]), r[2]) * (4 if l[3] == "arF" else 1), adds=k)
 
+    def close(o, l, r):
+        k = (o[1][0], opened[o[1][0]])
+        left[k] += 1
+        mm(o, l, r, False, True)
+
     def mms(o, pairs):
         if len(pairs) == 1:
             mm(o, *pairs[0])
@@ -332,10 +443,10 @@ def rank_program(g, core, T, topo):
     def row(j, c0=0, c1=128):
         return b("cr", 128 * j + c0, 128 * j + c1, 1, 1, key="cr%d" % j)
 
-    ONE, JROW, R65, R128, RH, R127 = range(6)
+    ONE, JROW, R65, R128, RH, R160, RMG, RU = range(8)
     blocks = lambda t, n: ["%sb%d" % (t, k) for k in range(n)]
     pk = lambda nm, p0, n: ["%s%d" % (nm, p) for p in range(p0, p0 + n)]
-    Cw = lambda s: b("KI", key=["KI", "KIe"]) if s == 0 else b("C", key=["C", "Ce"] + blocks("C", 4))
+    Cw = lambda s: b("KI", 0, V0) if s == 0 else b("C", key=["C", "Ce"] + blocks("C", 4) + pk("Ck", 0, 4))
     Aw = b("A", key=["A", "Ae"] + blocks("A", 4))
     lhs = lambda p, m="B": b(m, 15 - p, 143 - p)
 
@@ -344,89 +455,71 @@ def rank_program(g, core, T, topo):
     dma("ld2", b("KI", 0, V0)[0], T.kids[:], [], ["KI"], 512)
     dma("ld3", b("A", 0, V0)[0], T.a0[:], [], ["A"], 256)
     dma("ld4", b("thi", p1=8)[0], T.th[:], [], ["thi"], 4)
-    fill(b("KI", V0, WIN, key="KIe"), 4095)
     fill(b("C", V0, WIN, key=["Ce"] + blocks("C", 4)), 4095)
     ms(b("A", V0, W, key=blocks("A", 4)), 0.0)
-    ms(b("A", W, WIN, key="Ae"), 4096.0)
+    ms(b("A", W, WIN, key="Ae"), FAR)
     ms(b("ones"), 1.0)
     fill(b("one8"), 1)
-    fill(b("W4", key=["W4b", "W4d"]), 0)
-    fill(b("AN", 256, 272, key="ANz"), 0)
-    fill(b("AN", 0, 128, key="Mb"), 0)
-    fill(b("CN", 128, 272, key="CNz"), 4095)
+    ms(b("AN", 0, 256, key=["ANz", "Mb"]), 0.0)
+    ms(b("AN", 384, 512, key="ANy"), 0.0)
+    fill(b("CN", 0, 128, key="CNz"), 4095)
+    fill(b("CN", 256, 512, key="CNy"), 4095)
     ms(b("RW", 0, 16, key="RWa"), 0.0)
     ms(b("RW", 144, 160, key="rowM"), 0.0)
-    fill(b("row", 128, 144, key="rowz"), -1)
-    fill(b("rr", 15, 144, 128, key=["rra", "r20"]), -1)
+    fill(b("cand", 0, 128, HW, key="candz"), 0)
     fill(b("d0", key=["d0", "d0b"]), 0)
-    fill(b("d1", key=["d1a", "d1b", "d1c", "d1s"]), 256)
     ms(b("B"), 0.0)
     ms(row(ONE), 1.0)
-    ms(row(RH), -0.5)
-    for j, v in ((R65, 65), (R128, 128), (R127, 127)):
-        fill(row(j), v)
-    for nm in ("RM", "RM2"):
-        ms(b(nm), 0.0)
-        ms(b(nm, 0, None, 16), BIG)
-    ms(b("RM2", 1, 64, 16), BIG)
-    for nm in ("clv", "clb"):
-        fill(b(nm, key=[nm, nm + "t"]), 2 ** 23)
-        fill(b(nm, 0, 136, 17), -2 ** 23)
+    ms(row(RH), -0.25)
+    for j, v in ((R65, 65), (R128, 128), (R160, 160), (RMG, MAGIC), (RU, UNIT)):
+        ms(row(j), float(v))
+    for nm, n, v in (("RM", 128, BIG), ("RM2", HW, BIG), ("RF", HW, 0.75)):
+        ms(b(nm, 0, n), 0.0)
+        ms(b(nm, 0, n, 16), v)
+    ms(b("RM2", 1, HW, 16), BIG)
+    fill(b("RN", 0, HW), 6)
+    fill(b("RN", 0, HW, 16), 0)
+    if not D3:
+        fill(b("RZ"), 2 ** 23)
     for k in range(2):
         fill(b("come%d" % k, 64, 80, key="come%dz" % k), NONE)
     for k in range(4):
         fill(b("msg%d" % k, 0, CAP), NONE)
-    fill(b("coef", 16, 24, key="coefc"), 128)
-    fill(b("coef", 40, 48, key="coeff"), 0)
 
     io(b("pin"), [[0, 16]], 0, 1)
     io(b("ci"), [[1, 128]], 0, 0)
-    io(b("ri"), [[64, 2], [1, 16], [16, 4]], 0, 0)
+    io(b("ri"), [[HW, NH], [1, 16], [16, HC]], 0, 0)
     cp(b("plist"), b("ri"))
     io(row(JROW), [[1, 128]], 0, 0)
     asel(b("I"), b("ones", 0, 128), [[-1, 128]], OP.is_equal, 0.0, 0, 1)
     cp(b("iot", 0, 128, key="iot0"), b("ci"))
-    for k in range(1, 13):
+    if IOTG < 13:
+        io(b("iot", 128 * IOTG, WIN, key=pk("iot", IOTG, 13 - IOTG)), [[1, WIN - 128 * IOTG]], 128 * IOTG, 0)
+    for k in range(1, IOTG):
         act(b("iot", 128 * k, min(WIN, 128 * k + 128), key="iot%d" % k), b("iot", 0, min(128, WIN - 128 * k), key="iot0"), AF.Identity, 128.0 * k)
-    for nm, v in (("nI", -1.0), ("nI2", -2.0), ("I63", 63.0), ("nI128", -128.0), ("nI8", -8320.0), ("idf", 1.0)):
+    for nm, v in (("nI", -1.0), ("hI", 0.5), ("nhI", -0.5), ("I63", 63.0), ("nI63", -63.0), ("I128", 128.0), ("I256", 256.0), ("nI128", -128.0),
+                  ("nI8", -8320.0), ("idf", 1.0)):
         act(b(nm), b("I"), AF.Copy, 0.0, v)
     ts(b("pa", 0, 2), b("pin", 0, 2), 15, OP.bitwise_and)
     cp(b("pf"), b("pa", 0, 1))
-    act(b("p64"), b("pf"), AF.Copy, 0.0, 64.0)
-    act(b("p64b"), b("pf"), AF.Identity, 960.0, 64.0)
+    for h in range(NH):
+        act(b("pH", h, h + 1, key="pH%d" % h), b("pf"), AF.Identity, 15.0 * HW * h, float(HW))
     ts(b("pc", 0, 2), b("pin", 0, 2), 7, OP.bitwise_and)
-    cp(b("r7"), b("pc", 0, 1))
-    ts(b("pc", 2, 4, key="pc_"), b("pin", 0, 2), 3, OP.logical_shift_right, 1, OP.bitwise_and)
-    cp(b("hi"), b("pc", 2, 3, key="pc_"))
     ts(b("jL"), b("ci", 0, 128, 16), b("pf"), OP.add)
     act(b("cj"), b("jL"), AF.Identity, -128 * M, -M)
     for s in range(4):
         act(b("nL", 8 * s, 8 * s + 8, key="nL%d" % s), b("jL"), AF.Identity, float(V0 + L * s))
-    act(b("coef", 8, 16, key="coefb"), b("jL"), AF.Identity, -256.0)
-    act(b("coef", 32, 40, key="coefe"), b("jL"), AF.Identity, -128.0)
-    act(b("d1", 1, 16, 2, key="d1a"), b("jL"), AF.Identity, 384.0)
+    fill(b("d1", key=["d1a", "d1b", "d1s"]), 0)
+    act(b("d1", 17, 32, 2, key="d1a"), b("jL"), AF.Identity, 384.0)
+    if not D3:
+        act(b("RZ", 0, 128, 16), b("jL"), AF.Identity, -1.0, -1.0)
     ts(b("lF"), b("pc", 0, 2), 16.0, OP.mult, 15.0, OP.add)
-    ts(b("lz"), b("pc", 0, 2), 17.0, OP.mult, 15.0, OP.add)
-    cp(b("lr"), b("pc", 0, 2))
-    act(b("tmp", 0, 1, key="tmpa"), b("hi"), AF.Identity, b("r7"), 8.0)
-    act(b("tmp", 1, 2, key="tmpb"), b("r7"), AF.Identity, 8.0)
-    cp(b("lg"), b("tmp", 0, 2, key=["tmpa", "tmpb"]))
-    for j, (u, v) in enumerate(((0, 32), (32, 32), (24, 24), (0, 0))):
-        act(b("tmp", 4 + j, 5 + j, key="tmp%d" % j), b("hi"), AF.Identity, float(u), float(v - u))
-    ts(b("lfl"), b("tmp", 4, 8, key=pk("tmp", 0, 4)), b("r7"), OP.add)
-    ts(b("pc", 4, 6, key="pc4"), b("pin", 0, 2), 3, OP.bitwise_and)
-    ts(b("pc", 6, 8, key="pc6"), b("pin", 0, 2), 2, OP.logical_shift_right, 3, OP.bitwise_and)
+    ts(b("pc", 4, 6, key="pc4"), b("pin", 0, 2), HC - 1, OP.bitwise_and)
+    ts(b("pc", 6, 8, key="pc6"), b("pin", 0, 2), HC.bit_length() - 1, OP.logical_shift_right, 16 // HC - 1, OP.bitwise_and)
     cp(b("tmp2", 12, 13, key="tmp2c"), b("pc", 6, 7, key="pc6"))
     ts(b("tmp2", 0, 1, key="tmp2a"), b("pc", 4, 5, key="pc4"), 16.0, OP.mult, b("tmp2", 12, 13, key="tmp2c"), OP.add)
-    for h in range(2):
-        ts(b("lperm", 4 * h, 4 * h + 4), b("ci", 64 * h, 64 * h + 16, 4), b("tmp2", 0, 1, key="tmp2a"), OP.add)
-    ts(b("tmp3", 0, 10), b("ci", 0, 10), b("pf"), OP.is_gt, b("pf"), OP.add)
-    ts(b("tmp2", 2, 12, key="tmp2b"), b("ci", 0, 10), -1.0, OP.add, b("pf"), OP.is_equal)
-    act(b("tmp2", 2, 12, key="tmp2b"), b("tmp2", 2, 12, key="tmp2b"), AF.Copy, 0.0, 128.0)
-    tt(b("tmp3", 0, 10), b("tmp3", 0, 10), b("tmp2", 2, 12, key="tmp2b"), OP.add)
-    io(b("U4", 0, 10), [[15, 10]], 0, 0)
-    tt(b("tmp3", 0, 10), b("tmp3", 0, 10), b("U4", 0, 10), OP.add)
-    ts(b("l17"), b("tmp3", 0, 10), 128.0, OP.min)
+    for h in range(NH):
+        ts(b("lperm", HC * h, HC * h + HC), b("ci", HW * h, HW * h + 16, 16 // HC), b("tmp2", 0, 1, key="tmp2a"), OP.add)
     ts(b("dec", 0, 2), b("pin", 0, 2), 4, OP.logical_shift_right, 1, OP.bitwise_and)
     ts(b("tmp", 8, 9, key="tmpy"), b("dec", 0, 1), 144.0, OP.mult)
     act(b("tmp", 9, 10, key="tmpz"), b("tmp", 8, 9, key="tmpy"), AF.Identity, 144.0, -1.0)
@@ -435,60 +528,69 @@ def rank_program(g, core, T, topo):
     raw = parts(P1[0], True)
     ts(b("tmp3", 12, 13, key="tmp3c"), b("pf"), float(raw[0]), OP.is_ge)
     ts(b("tmp3", 11, 12, key="tmp3b"), b("pf"), float(raw[-1]), OP.is_le, b("tmp3", 12, 13, key="tmp3c"), OP.mult)
-    ts(b("tmp2", 2, 10, key="tmp2b"), b("jL"), -128.0, OP.add, b("tmp3", 11, 12, key="tmp3b"), OP.mult)
-    ts(b("lxd"), b("tmp2", 2, 10, key="tmp2b"), 256.0, OP.add)
+    ts(b("lxd"), b("jL"), 256.0, OP.add, b("tmp3", 11, 12, key="tmp3b"), OP.mult)
     ts(b("pa", 2, 4, key="pa_"), b("pin", 0, 2), 4, OP.logical_shift_right)
     cp(b("pG"), b("pa", 2, 3, key="pa_"))
     ts(b("xi"), b("ci"), 4, OP.logical_shift_right)
-    ts(b("bones"), b("xi"), b("pG"), OP.is_equal, 128.0, OP.mult)
+    ts(b("bones"), b("xi"), b("pG"), OP.is_equal, KEY, OP.mult)
     cp(b("B", 15, 143, 16), b("bones", 0, 128, 16))
     act(b("B2"), b("B"), AF.Copy, 0.0, 2.0)
     act(b("nB"), b("B"), AF.Copy, 0.0, -1.0)
-    act(b("lo"), b("bones"), AF.Copy, 0.0, -M / 128)
+    act(b("lo"), b("bones"), AF.Copy, 0.0, -M / KEY)
     asel(b("lt"), b("lo"), [[1, 128]], OP.is_gt, 0.0, 0, -1)
     asel(b("ld"), b("lt"), [[1, 128]], OP.not_equal, M, 0, -1)
     asel(b("lp"), b("lt"), [[1, 128]], OP.not_equal, 256 * M, 0, -1)
-    act(b("nl8"), b("ld"), AF.Copy, 0.0, -8320.0 / M)
-    act(b("pw"), b("bones"), AF.Copy, 0.0, -1.0 / 128)
+    act(b("nl8"), b("lt"), AF.Copy, 0.0, -8320.0 / M)
+    act(b("pw"), b("bones"), AF.Copy, 0.0, -1.0 / KEY)
     asel(b("w3"), b("pw"), [[-1, 128]], OP.is_equal, 0.0, -1, 1)
     asel(b("dm"), b("w3"), [[-1, 128]], OP.not_equal, 1.0, 0, 1)
     io(b("nr2", 512, 640, 1, 2, key="jr2"), [[1, 128]], 0, 128)
     act(b("sh", p1=2), b("ones", 0, 128, 1, 2), AF.Copy, 0.0, b("pf", p1=2))
     for s in range(4):
-        act(b("nr2", 128 * s, 128 * s + 128, 1, 2, key="n%d" % s), b("sh", p1=2), AF.Identity, -72.0 - s, 145.0 + 2 * s)
+        act(b("nr2", 128 * s, 128 * s + 128, 1, 2, key="n%d" % s), b("sh", p1=2), AF.Identity, -7.0 - s, 15.0 + 2 * s)
     ts(b("hx"), b("ci"), 15, OP.bitwise_and)
     ts(b("tab", 0, 128), b("hx"), b("pf"), OP.is_equal, 65.0, OP.mult)
-    fill(b("tab", 128, 144, key="tabz"), 65)
-    act(b("hv"), b("tab", 0, 128), AF.Relu, float(2 ** 26), -float(2 ** 26))
-    act(b("emc"), b("hv"), AF.Identity, 127.0)
-    act(b("E", 0, 144, key="E0"), ind(b("tab", key=["tab", "tabz"]), b("l17", 0, 9)), AF.Relu, float(2 ** 20), -float(2 ** 20))
-    act(b("cnt0"), b("E", 0, 136, key="E0"), AF.Copy, 0.0, -1.0)
-    act(b("cnt0", 16, 136, 17), b("jL"), AF.Copy)
+    act(b("cl"), b("tab", 0, 128), AF.Relu, float(2 ** 26), -float(2 ** 26))
+    act(b("emc"), b("cl"), AF.Identity, 128 * UNIT)
+    if D3:
+        act((T.c3[:, :, 0:16], ["cnt0"], 128, "arB"), b("cl"), AF.Identity, -M / 2, -1.0)
+        act((T.c3[:, :, 16], ["cnt0"], 8, "arB"), b("jL"), AF.Copy)
+        ts(b("lz"), b("pc", 0, 2), 17.0, OP.mult, 15.0, OP.add)
+        for k in range(2):
+            ms((T["r3%d" % k][:, :, 16], ["rowu%dz" % k], 8, "arU"), 65535)
+            fill(b("RY%d" % k, key=["RY%d" % k, "RY%dt" % k]), 2 ** 23)
+            fill(b("RY%d" % k, 0, 136, 17), -2 ** 23)
+    else:
+        act(b("cnt0"), b("cl"), AF.Identity, -M / 2, -1.0)
     cp(b("tu"), b("tp"))
     cp(b("topf"), b("tp"))
     for h in range(4):
-        cp(b("C", 256 * h, 256 * h + 256), b("KI", 256 * h, 256 * h + 256))
+        cp(b("C", 256 * h, 256 * h + 256, key="Ck%d" % h), b("KI", 256 * h, 256 * h + 256))
     cp(b("thf", p1=8), b("thi", p1=8))
     asel(b("thx", p1=8), b("ones", 0, 128, 1, 8), [[1, 128]], OP.is_ge, 0.0, 0, -16)
     asel(b("es", p1=8), b("thx", p1=8), [[-1, 128]], OP.is_ge, 0.0, 15, 16)
-    act(b("es", p1=8), b("es", p1=8), AF.Copy, 0.0, 128.0)
+    act(b("es", p1=8), b("es", p1=8), AF.Copy, 0.0, KEY)
     mms(b("pb6", 384, 512), [(b("I"), b("emc")), (b("es", p1=8), b("thf", p1=8))])
     scan(b("thx"), b("RM"), b("pb6", 384, 512), OP.max, OP.min)
-    act(b("lim"), b("thx", 15, 128, 16), AF.Copy)
-    act(b("lim1"), b("thx", 15, 128, 16), AF.Identity, 1.0)
+    act(b("lim"), b("thx"), AF.Identity, 64 * UNIT)
+    act(b("lim4"), ind(b("lim"), b("lF")), AF.Copy)
 
     def x_forms(share):
         act(b("xP"), ind(b("xb"), b("lperm")), AF.Copy)
         for k in range(16):
             o = b("xrep", k, 2048, 16, key="xr%d" % k)
-            if k % share:
+            if share[k] == "s":
                 act(o, b("xP"), AF.Copy)
+            elif share[k] == "g":
+                asel(o, b("xP"), [[0, 128]], OP.is_ge, 0.0, 0, 0)
             else:
                 cp(o, b("xP"))
-        act(b("xd"), ind(b("AN", key=["Mb", "xb", "ANz"]), b("lxd")), AF.Copy)
-        act(b("xm"), b("xb"), AF.Identity, -MAGIC)
+        act(b("xd"), ind(b("AN", 0, 384, key=["Mb", "xb", "ANz"]), b("lxd")), AF.Copy)
+        if not MBS:
+            act(b("xm"), b("xb"), AF.Identity, -MAGIC)
         act(b("xn"), b("xb"), AF.Copy, 0.0, -1.0)
 
+    KB2 = ("pb0", "pb1") if NH == 2 else ("pb1",)
     KB = ("pb0", "pb1")
 
     def rows(out, s, nodes):
@@ -498,14 +600,21 @@ def rank_program(g, core, T, topo):
             act(out, ind(Cw(s), nodes), AF.Copy)
 
     def lst(name, h, p0, n):
-        return b(name, 64 * h + 4 * p0, 64 * h + 4 * (p0 + n), key=name + str(h))
+        return b(name, HW * h + HC * p0, HW * h + HC * (p0 + n), key=name + str(h))
 
     def piece(name, h, p0, n):
-        return b(name, 1024 * h + 64 * p0, 1024 * h + 64 * (p0 + n), key=pk("xr", 0, 16) if name == "xrep" else pk(name, 16 * h + p0, n))
+        return b(name, HW * (16 * h + p0), HW * (16 * h + p0 + n), key=pk("xr", 0, 16) if name == "xrep" else pk(name, 16 * h + p0, n))
+
+    turns = {}
+
+    def inturn(line, on):
+        if on and line in turns:
+            ops[-1]["after"] = [turns[line]]
+        turns[line] = len(ops) - 1
 
     def sums(h, o0, p0, n, m="B", of="Dab"):
         for p in range(p0, p0 + n):
-            add(b(KB[h], o0, o0 + 64), lhs(p, m), piece(of, h, p, 1))
+            add(b((KB2 if o0 else KB)[h], o0, o0 + HW), lhs(p, m), piece(of, h, p, 1))
 
     def sweep(pieces, h, lists, into, o0):
         p0 = 0
@@ -513,41 +622,71 @@ def rank_program(g, core, T, topo):
             d, x = piece(into, h, p0, n), piece("xrep", h, p0, n)
             if bank:
                 act(d, ind(Aw, lst(lists, h, p0, n)), AF.Copy)
-                mms(b(bank, 0, 64 * n), [(b("nI"), x), (b("I"), d)])
-                d = b(bank, 0, 64 * n)
+                inturn("sg", STAG[1])
+                mms(b(bank, 0, HW * n), [(b("nI"), x), (b("I"), d)])
+                d = b(bank, 0, HW * n)
             else:
                 tt(d, ind(Aw, lst(lists, h, p0, n)), x, OP.subtract)
+                inturn("vg", STAG[0])
             act(piece("Dab", h, p0, n), d, AF.Abs)
+            inturn("sa", STAG[2])
             sums(h, o0, p0, n)
             p0 += n
 
     def sweep_arrived(h):
         p0 = 0
         for n, bank in P1X[h]:
-            a, o, l = piece("ag", h, p0, n), piece("Dab", h, p0, n), b("plist", 64 * h + 4 * p0, 64 * h + 4 * (p0 + n))
+            a, o, l = piece("ag", h, p0, n), piece("Dab", h, p0, n), b("plist", HW * h + HC * p0, HW * h + HC * (p0 + n))
             if bank:
                 x = piece("D", h, p0, n)
                 act(x, ind(b("xb"), l), AF.Copy)
-                mms(b(bank, 0, 64 * n), [(b("I"), a), (b("nI"), x)])
-                act(o, b(bank, 0, 64 * n), AF.Abs)
+                mms(b(bank, 0, HW * n), [(b("I"), a), (b("nI"), x)])
+                act(o, b(bank, 0, HW * n), AF.Abs)
                 sums(h, 0, p0, n)
             else:
                 tt(o, ind(b("xb"), l), a, OP.max)
+                inturn("vg", STAG[3])
                 sums(h, 0, p0, n, "nB", "ag")
                 sums(h, 0, p0, n, "B2")
             p0 += n
 
-    def firsts(lists, node, on, bank, cl, z, top=WIN):
-        act(b("row", 0, 128), ind(b("iot", 0, top, key=pk("iot", 0, -(-top // 128))), lists), AF.Copy)
-        act(b("r17"), ind(b("row", key=["row", "rowz"]), b("l17", 0, 9)), AF.Copy)
-        begin(b(bank, 0, 136), b("I"), b("cnt0"))
+    def firsts(lists, node, on, bank, z, u, out, top=WIN):
+        nodes = ind(b("iot", 0, top, key=pk("iot", 0, -(-top // 128))), lists)
+        k = int(z == "zb")
+        rw, E = ("rowu" if ROWU[k] else "row") + str(k), "E" + str(k)
+        if D3:
+            R3, E4, rz = T["r3%d" % k], T["e4%d" % k], "RY%d" % k
+            act(b("row" + str(k)), nodes, AF.Copy)
+            cp((R3[:, :, 0:16], [rw], 128, "arU"), b("row" + str(k)))
+            act(b(rz, 16, 136, 17, key=rz + "t"), node(0, 8), AF.Identity, 128.0)
+            begin(b(bank, 0, 136), b("I"), (T.c3[:], ["cnt0"], 136, "arB"))
+            for c in range(8):
+                key = E + str(c)
+                ts((E4[:, c, 0:8 - c, :], [key], 136 - 17 * c, "arB"), (R3[:, c:8, :], [rw, rw + "z"], 136 - 17 * c, "arU"), node(c, c + 1),
+                   OP.is_equal, on(c), OP.mult)
+                if c < 7:
+                    add(b(bank, 17 * c + 17, 136), b("lo"), (E4[:, c, 1:8 - c, :], [key], 119 - 17 * c, "arB"))
+            add(b(bank, 0, 136), b("ld"), (E4[:, :, 0, :], pk(E, 0, 8), 136, "arB"))
+            scan(b(z), b(rz, key=[rz, rz + "t"]), b(bank, 0, 136), OP.min, OP.max)
+            cp(b(out), b(z, 16, 136, 17))
+            return
+        if ROWU[k] == 2:
+            act(b("row" + str(k)), nodes, AF.Copy)
+            cp(b(rw), b("row" + str(k)))
+        elif ROWU[k]:
+            cp(b(rw), nodes)
+        else:
+            act(b(rw), nodes, AF.Copy)
+        begin(b(bank, 0, 128), b("I"), b("cnt0"))
         for c in range(8):
-            e0 = 136 * c
-            ts(b("E", e0 + 17 * c, e0 + 136, key="E%d" % c), b("r17", 17 * c, 136), node(c), OP.is_equal, on(c), OP.mult)
-            add(b(bank, 17 * c, 17 * c + 17), b("ld"), b("E", e0 + 17 * c, e0 + 17 * c + 17, key="E%d" % c))
+            e0, key = 128 * c, E + str(c)
+            ts(b(E, e0 + 16 * c, e0 + 128, key=key), b(rw, 16 * c, 128), node(c, c + 1), OP.is_equal, on(c), OP.mult)
+            add(b(bank, 16 * c, 16 * c + 16), b("ld"), b(E, e0 + 16 * c, e0 + 16 * c + 16, key=key))
             if c < 7:
-                add(b(bank, 17 * c + 17, 136), b("lo"), b("E", e0 + 17 * c + 17, e0 + 136, key="E%d" % c))
-        scan(b(z), b(cl, key=[cl, cl + "t"]), b(bank, 0, 136), OP.min, OP.max)
+                add(b(bank, 16 * c + 16, 128), b("lo"), b(E, e0 + 16 * c + 16, e0 + 128, key=key))
+        scan(b(z, 0, 128), b("RZ"), b(bank, 0, 128), OP.min, OP.max)
+        tt(b(u), b(z, 15, 128, 16), node(0, 8), OP.min)
+        ts(b(out), b(u), 128.0, OP.add)
 
     def lower(o0, f):
         scan(b("cum"), b("one8"), f, OP.mult, OP.add)
@@ -556,7 +695,7 @@ def rank_program(g, core, T, topo):
     def send(s):
         h = hops(T, topo, rank, s)
         m = "msg%d" % s
-        f, o = b("fl%d" % (s % ST), 8, 16), b("pb2", 176, 184)
+        f, o = b("fl%d" % (s % ST), 0, 8), b("pb2", 176, 184)
         begin(o, b("I"), b("cj"))
         add(o, b("lt"), f)
         lower(176, f)
@@ -575,156 +714,157 @@ def rank_program(g, core, T, topo):
 
     def front(s):
         t = s % ST
-        vu = b("tu") if t == 0 else b("lu", 8, 16)
-        vf = (lambda a, z: b("topf", a, z)) if t == 0 else (lambda a, z: b("s2", 17 + 2 * a, 17 + 2 * z, 2))
+        vu = b("tu") if t == 0 else b("lu", 0, 8)
+        vf = (lambda a, z: b("topf", a, z)) if t == 0 else (lambda a, z: b("s2", 1 + 2 * a, 1 + 2 * z, 2))
         rows(b("cvf"), s, vu)
-        ts(b("cvu", key=pk("cvu", 0, 2)), ind(b("cvf"), b("lperm")), float(E1), OP.min)
+        if CVS[0]:
+            act(b("cvp"), ind(b("cvf"), b("lperm")), AF.Copy)
+            ts(b("cvu", key=pk("cvu", 0, NH)), b("cvp"), float(E1), OP.min)
+        else:
+            ts(b("cvu", key=pk("cvu", 0, NH)), ind(b("cvf"), b("lperm")), float(E1), OP.min)
         mm(b("pb2", 0, 160), b("dm"), b("RW", 0, 160, key=["RWa", "cvf", "rowM"]))
         turn(b("tr", 0, 128, key="tra"), b("pb2", 16, 144))
         turn(b("tr", 128, 288, key="trb"), b("pb2", 0, 160))
         act(b("dl"), ind(b("tr", key=["tra", "trb"]), b("lsel")), AF.Copy)
         act(b("emp"), b("cvf"), AF.Relu, -4094.0)
-        for p in range(16):
-            mm(b("pb2", 160, 168), lhs(p), b("emp", p, 128, 16), p == 0, p == 15)
-        act(b("W4", 8, 16, key="W4b"), b("pb2", 160, 168), AF.Copy, 0.0, BIG / 128)
-        act(b("W4", 24, 32, key="W4d"), b("pb2", 160, 168), AF.Relu, BIG, -BIG / 128)
+        if RMT:
+            for p in range(16):
+                mm(b("pb2", 160, 168), lhs(p), b("emp", p, 128, 16), p == 0, p == 15)
+            act(b("cB"), b("pb2", 160, 168), AF.Sign)
+            act(b("coef", 8, 16, key="coefb"), b("cB"), AF.Copy, 0.0, 256.0)
+            act(b("cB2"), b("cB"), AF.Copy, 0.0, 4 * M)
+            tt(b("no", 15, 128, 16), b("lim", 15, 128, 16), b("cB2"), OP.max)
         nrow = (b("nr2", 128 * s, 128 * s + 128, 1, 2, key="n%d" % s), b("nr2", 512, 640, 1, 2, key="jr2"))
         mms(b("pb3", 144, 272), [nrow, (b("nl8"), b("emp"))])
         tt(b("RW", 272, 400, key="rowN"), b("cvf"), b("pb3", 144, 272), OP.min)
         if s != 2:
-            act(b("clv", 16, 136, 17, key="clvt"), vf(0, 8), AF.Identity, 128.0)
-            firsts(vu, lambda c: vf(c, c + 1), lambda c: b("one8" if t == 0 else "nonr", c, c + 1), "pb3", "clv", "zv", V0 + L * s)
-            cp(b("uvu%d" % t), b("zv", 16, 136, 17))
-            act(b("acB%d" % t), ind(b("zv"), b("lz")), AF.Relu, 0.0, BIG / M)
-            act(b("nac%d" % t), b("acB%d" % t, 0, 8), AF.Identity, BIG, -1.0)
-        tt(b("coef", 24, 32, key="coefd"), b("nL", 8 * s, 8 * s + 8, key="nL%d" % s), vf(0, 8), OP.subtract)
-        act(b("d1", 17, 32, 2, key="d1b"), vf(0, 8), AF.Copy)
+            firsts(vu, vf, lambda c: b("one8" if t == 0 else "nonr", c, c + 1), "pb3", "zv", "uv", "uvu%d" % t, V0 + L * s)
+            tt(b("LA%d" % t), ind(b("zv", 0, 136 if D3 else 128), b("lz" if D3 else "lF")), b("lim4"), OP.min)
+        tt(b("coef", 16, 24, key="coefc"), b("nL", 8 * s, 8 * s + 8, key="nL%d" % s), vf(0, 8), OP.subtract)
+        act(b("d1", 1, 16, 2, key="d1b"), vf(0, 8), AF.Copy)
         return nrow
 
     def step(s, nrow):
         t = s % ST
         n0 = V0 + L * s
         bf = lambda a, z: b("pay", 15 + 16 * a, 16 * z, 16, key=["pay0", "pay1"])
-        for h in range(2):
-            K1 = b(KB[h], 0, 64)
-            begin(K1, row(ONE), row(JROW, 64 * h, 64 * h + 64))
+        for h in range(NH):
+            K1 = b(KB[h], 0, HW)
+            begin(K1, row(RU), row(JROW, HW * h, HW * h + HW))
             if s == 2:
                 sweep_arrived(h)
             else:
                 sweep(P1[h], h, "cvu", "D", 0)
-            r0 = 16 + 128 * h
-            r = b("rr", r0, r0 + 64, key="r1%d" % h)
-            half = lambda nm: b(nm, 64 * h, 64 * h + 64, key=nm + str(h))
-            scan(r, b("RM", 0, 64), K1, OP.max, OP.min)
+            half = lambda nm, a=0, z=HW: b(nm, HW * h + a, HW * h + z, key=nm + str(h))
+            r = half("r1")
+            scan(r, b("RM", 0, HW), K1, OP.max, OP.min)
             tt(half("e"), r, K1, OP.not_equal)
-            scan(half("pay"), half("e"), b("dl", 64 * h, 64 * h + 64), OP.mult, OP.add)
-            bu = b("bu", 4 * h, 4 * h + 4, key="bu%d" % h)
-            ts(bu, b("pay", 64 * h + 15, 64 * h + 64, 16, key="pay%d" % h), float(E1), OP.min)
-            rows(half("dvf"), s, bu)
-            ts(half("dvu"), ind(half("dvf"), b("lperm", 0, 4)), float(E1), OP.min)
-            tt(half("cand"), b("rr", r0 - 1, r0 + 63, key=["r1%d" % h, "r20" if h else "rra"]), K1, OP.max)
-            scan(b("rr", r0 + 64, r0 + 128, key="r2%d" % h), b("RM2"), half("cand"), OP.max, OP.min)
-            act(b("mbt", 4 * h, 4 * h + 4, key="mb%d" % h), b("rr", r0 + 15, r0 + 64, 16, key="r1%d" % h), AF.Copy)
-        mb = b("mbt", key=["mb0", "mb1"])
+            scan(half("pay"), half("e"), b("dl", HW * h, HW * h + HW), OP.mult, OP.add)
+            bu = b("bu", HC * h, HC * h + HC, key="bu%d" % h)
+            ts(bu, b("pay", HW * h + 15, HW * h + HW, 16, key="pay%d" % h), float(E1), OP.min)
+            rows(half("dvf"), 1, bu)
+            if CVS[1]:
+                act(half("dvp"), ind(half("dvf"), b("lperm", 0, HC)), AF.Copy)
+                ts(half("dvu"), half("dvp"), float(E1), OP.min)
+            else:
+                ts(half("dvu"), ind(half("dvf"), b("lperm", 0, HC)), float(E1), OP.min)
+            tt(half("cand", 1, HW), half("r1", 0, HW - 1), b(KB[h], 1, HW), OP.max)
+            scan(half("r2"), b("RM2", 0, HW), b("cand", HW * h, HW * h + HW, key=["cand%d" % h, "candz"]), OP.max, OP.min)
+            if not RMT:
+                scan(half("rm"), b("RN", 0, HW), K1, OP.min, OP.max)
+        r1 = ["r10", "r11"]
+        ts(b("dec"), b("RX", 15, 256, 16, key=r1 + ["r20", "r21"]), 1 / UNIT, OP.mult)
         if s == 2:
             ps = parts(P1X[0], False)
             for p in ps:
                 mm(b("pb2", 168, 176), lhs(p), b("xb", p, 128, 16), p == ps[0], p == ps[-1])
-            tt(b("mbx"), mb, b("pb2", 168, 176), OP.subtract)
-            mb = b("mbx")
-        cp(b("dec"), b("rr", 31, 272, 16, key=["r10", "r11", "r20", "r21"]))
+            tt(b("r1", 15, 128, 16, key=r1), b("r1", 15, 128, 16, key=r1), b("pb2", 168, 176), OP.subtract)
         ts(b("dk"), b("dec"), 127, OP.bitwise_and)
-        ts(b("du", 0, 8, key="du0"), b("dk", 0, 8), b("p64"), OP.add)
-        ts(b("du", 8, 16, key="du1"), b("dk", 8, 16), b("p64b"), OP.add)
+        for h in range(NH):
+            ts(b("du", HC * h, HC * h + HC, key="du%d" % h), b("dk", HC * h, HC * h + HC), b("pH", h, h + 1, key="pH%d" % h), OP.add)
         cp(b("ku"), b("dk"))
         bare = "ag" if s == 2 else "D"
-        act(b("dd"), ind(b(bare, key=pk(bare, 0, 32)), b("du", key=["du0", "du1"])), AF.Copy)
-        act(b("oh"), ind(b("tab", 0, 128), b("ku")), AF.Copy)
-        db, dq, ohb, ohq = ("dd", 0), ("dd", 64), ("oh", 0), ("oh", 64)
-
-        def mmh(bank, o0, whole, halves):
-            if whole:
-                begin(b(bank, o0, o0 + 128), *whole[0])
-                for l, r in whole[1:]:
-                    add(b(bank, o0, o0 + 128), l, r)
-            for h in range(2):
-                pairs = [(l, b(nm, 128 * h + c0, 128 * h + c0 + 64)) for l, (nm, c0) in halves]
-                o = b(bank, o0 + 64 * h, o0 + 64 * h + 64)
-                if whole:
-                    for l, r in pairs:
-                        add(o, l, r)
-                else:
-                    mms(o, pairs)
-
-        xd = b("xb" if s == 2 else "xd")
-        mmh("pb6", 0, [(row(ONE), row(RH)), (b("nI2"), xd)], [(b("I"), db), (b("I"), dq)])
-        act(b("pb6", 128, 256), b("pb6", 0, 128), AF.Identity, MAGIC, 0.5)
-        act(b("absM"), b("pb6", 128, 256), AF.Abs, -MAGIC)
-        tt(b("AN", 0, 128, key="Mb"), b("xm"), b("pb6", 128, 256), OP.add)
+        bu = b("bu", key=["bu0", "bu1"])
+        act(b("ab"), ind(Aw, bu), AF.Copy)
+        act(b("dq"), ind(b(bare, key=pk(bare, 0, 32)), b("du", key=["du0", "du1"])), AF.Copy)
+        oq, nb = b("oh", 0, 128, key="oq"), b("oh", 128, 256, key="nb")
+        act(oq, ind(b("tab"), b("ku", 0, 8)), AF.Copy)
+        act(nb, ind(b("tab"), b("ku", 8, 16)), AF.Identity, 65.0, -1.0)
+        o = b("pb6", 0, 128)
+        begin(o, row(ONE), row(RH))
+        for l, r in [("hI", "ab"), ("hI", "dq")] + ([("nI", "xb")] if s == 2 else [("nhI", "xb"), ("nhI", "xd")]):
+            add(o, b(l), b(r))
+        close(o, row(ONE), row(RMG))
+        act(b("absM"), o, AF.Abs, -MAGIC)
         mms(b("pb6", 384, 512), [(b("I"), b("emc")), (b("bones"), b("absM"))])
         scan(b("es"), b("RM"), b("pb6", 384, 512), OP.max, OP.min)
-        mmh("pb2", 384, [(b("nI"), xd)], [(b("I"), db)])
-        act(b("cl", 0, 128, key="cla"), b("pb2", 384, 512), AF.Relu, -4.0)
-        act(b("cl", 128, 256, key="clz"), b("pb2", 384, 512), AF.Relu, -4.0, -1.0)
-        mms(b("pb6", 256, 384), [(b("I"), b("xb")), (b("I"), b("cl", 0, 128, key="cla")), (b("nI"), b("cl", 128, 256, key="clz"))])
-        act(b("hv"), b("pb6", 256, 384), AF.Copy)
-        for h in range(2):
-            begin(b(KB[h], 64, 128), row(ONE), row(R127, 0, 64))
-            sweep(P2[h], h, "dvu", "D" if s == 2 else "ag", 64)
-        tt(b("df"), mb, b("lim"), OP.subtract)
-        act(b("G2", 0, 8, key="G2a"), b("df"), AF.Relu, 0.0, BIG)
-        act(b("G2", 8, 16, key="G2b"), b("df"), AF.Relu, BIG, -BIG)
-        tt(b("G4"), ind(b("G2", key=["G2a", "G2b"]), b("lg")), b("W4", key=["W4b", "W4d"]), OP.max)
-        tt(b("U1"), mb, b("lim1"), OP.min)
-        tt(b("Uac"), b("U1"), b("nac%d" % t), OP.max)
-        tt(b("UU"), ind(b("Uac"), b("lr")), b("G4"), OP.max)
-        tt(b("U4"), ind(b("U1"), b("lr")), b("acB%d" % t), OP.min)
-        tt(b("coef", 0, 8, key="coefa"), bf(0, 8), b("d1", 17, 32, 2, key="d1b"), OP.subtract)
-        act(b("clb", 16, 136, 17, key="clbt"), bf(0, 8), AF.Identity, 128.0)
-        tt(b("FL", 0, 32), ind(b("es"), b("lF")), b("UU"), OP.is_ge)
-        tt(b("FL", 32, 40, key="am"), b("es", 15, 128, 16), b("U4", 0, 8), OP.is_lt)
-        tt(b("TT", 0, 32, key=["Tt", "THh"]), ind(b("es"), b("lF")), b("U4"), OP.min)
-        act(b("nfl"), b("FL", 0, 32), AF.Identity, BIG, -BIG)
-        tt(b("TT", 24, 56, key=["THh", "TH"]), b("U4"), b("nfl"), OP.max)
-        tt(b("prod", 8, 56), ind(b("FL", key=["FL", "am"]), b("lfl", 0, 3)), b("coef", key=["coef" + k for k in "abcdef"]), OP.mult)
-        act(b("prod", 0, 8, key="proda"), b("FL", 16, 24), AF.Identity, -384.0, 256.0)
-        tt(b("d0", 1, 48, 2, key="d0b"), b("prod", 0, 24, key=["prod", "proda"]), b("prod", 24, 48), OP.add)
-        mmh("pb5", 0, [], [(b("I63"), ohb)])
-        mmh("pb5", 128, [], [(b("I63"), ohb), (b("I63"), ohq)])
-        mmh("pb5", 256, [nrow], [(b("nI128"), ohb)])
-        act(b("pb5", 384, 512), b("pb5", 128, 256), AF.Identity, 4095.0, -1.0)
-        mmh("pb3", 272, [(row(R128), row(R65)), (b("nI8"), b("emp")), (b("idf"), b("dvf", key=["dvf0", "dvf1"]))], [(b("nI128"), ohb)])
+        if MBS:
+            o = b("pb6", 128, 256)
+            begin(o, row(ONE), row(RH))
+            for l, r in [("hI", "ab"), ("hI", "dq")] + ([] if s == 2 else [("hI", "xb"), ("nhI", "xd")]):
+                add(o, b(l), b(r))
+            close(o, row(ONE), row(RMG))
+            act(b("AN", 128, 256, key="Mb"), o, AF.Identity, -MAGIC)
+        else:
+            tt(b("AN", 128, 256, key="Mb"), b("xm"), o, OP.add)
+        mms(b("pb2", 384, 512), [(b("I"), b("xb")), (b("nI"), b("ab"))])
+        if CLS:
+            act(b("cl"), b("pb2", 384, 512), AF.Relu, 4.0)
+            act(b("cl"), b("cl"), AF.Relu, 8.0, -1.0)
+            act(b("cl"), b("cl"), AF.Identity, 4.0, -1.0)
+        else:
+            ts(b("cl"), b("pb2", 384, 512), -4.0, OP.max, 4.0, OP.min)
+        for h in range(NH):
+            begin(b(KB2[h], HW, 2 * HW), row(RU), row(R160, 0, HW))
+            sweep(P2[h], h, "dvu", "D" if s == 2 else "ag", HW)
+        if not RMT:
+            ts(b("cB"), b("rm", 15, 128, 16, key=["rm0", "rm1"]), 2.0, OP.is_ge, 8.0, OP.mult)
+            tt(b("no", 15, 128, 16), b("lim", 15, 128, 16), b("cB"), OP.max)
+            act(b("coef", 8, 16, key="coefb"), b("cB"), AF.Copy, 0.0, 32.0)
+        tt(b("coef", 0, 8, key="coefa"), bf(0, 8), b("d1", 1, 16, 2, key="d1b"), OP.subtract)
+        tt(b("U4"), ind(b("r1", key=r1), b("lF")), b("LA%d" % t), OP.min)
+        tt(b("TT", 0, 32, key="Tt"), ind(b("es"), b("lF")), b("U4"), OP.min)
+        tt(b("FL"), b("RX", 143, 640, 16, key=r1 + ["lim", "es", "no"]), b("TT", 0, 32, key="Tt"), OP.is_equal)
+        if NFV:
+            tt(b("nfl"), b("RX", 143, 640, 16, key=r1 + ["lim", "es", "no"]), b("TT", 0, 32, key="Tt"), OP.not_equal)
+        else:
+            act(b("nfl"), b("FL"), AF.Identity, 1.0, -1.0)
+        tt(b("TT", 32, 64, key="TH"), b("TT", 0, 32, key="Tt"), b("nfl"), OP.max)
+        tt(b("prod", 0, 24), b("FL", 0, 24), b("coef", key=["coefa", "coefb", "coefc"]), OP.mult)
+        act(b("prod", 24, 32, key="proda"), b("FL", 16, 24), AF.Identity, -384.0, 128.0)
+        tt(b("d0", 1, 32, 2, key="d0b"), b("prod", 0, 16), b("prod", 16, 32, key=["prod", "proda"]), OP.add)
+        mms(b("pb5", 0, 128), [(row(R128), row(R65)), (b("nI128"), nb)])
+        mms(b("pb5", 128, 256), [(b("I63"), nb), (b("nI63"), oq)])
+        mms(b("pb5", 256, 384), [nrow, (b("nI128"), nb), (b("I256"), oq)])
+        mms(b("pb3", 272, 400), [(b("nI8"), b("emp")), (b("idf"), b("dvf", key=["dvf0", "dvf1"])), (b("I128"), nb)])
         tt(b("w3"), b("cvf"), b("pb5", 0, 128), OP.max)
-        tt(b("w4"), b("cvf"), b("pb5", 128, 256), OP.max)
-        tt(b("CN", 0, 128), b("cvf"), b("pb5", 384, 512), OP.max)
-        tt(b("RW", 144, 272, key="rowM"), b("w4"), b("pb5", 256, 384), OP.min)
+        tt(b("CN", 128, 256), b("cvf"), b("pb5", 128, 256), OP.max)
+        tt(b("RW", 144, 272, key="rowM"), b("cvf"), b("pb5", 256, 384), OP.max)
         tt(b("RW", 400, 528, key="rsp"), b("w3"), b("pb3", 272, 400), OP.min)
-        fl = "fl%d" % t
-        for h in range(2):
-            scan(b("fs", 64 * h, 64 * h + 64, key="fs%d" % h), b("RM", 0, 64), b(KB[h], 64, 128), OP.max, OP.min)
-        fs = b("fs", key=["fs0", "fs1"])
-        tt(b("d1", 0, 64, 2, key="d1s"), ind(fs, b("lF")), b("TT", 0, 32, key=["Tt", "THh"]), OP.is_ge)
-        tt(b(fl, 8, 24), ind(fs, b("lF", 0, 1)), b("TT", 32, 48, key="TH"), OP.is_ge)
-        scan(b("s2"), b("d0", key=["d0", "d0b"]), b("d1", 0, 48, key=["d1a", "d1b", "d1c", "d1s"]), OP.mult, OP.add)
-        cp(b("lu"), b("s2", 1, 48, 2))
+        for h in range(NH):
+            scan(b("fs", HW * h, HW * h + HW, key="fs%d" % h), b("RF", 0, HW), b(KB2[h], HW, 2 * HW), OP.max, OP.min)
+        fs = ["fs0", "fs1"]
+        tt(b("d1", 0, 64, 2, key="d1s"), ind(b("fs", key=fs), b("lF")), b("TT", 16, 48, key=["Tt", "TH"]), OP.is_gt)
+        tt(b("fl%d" % t, 0, 8), b("fs", 15, 128, 16, key=fs), b("TT", 56, 64, key="TH"), OP.is_gt)
+        scan(b("s2"), b("d0", key=["d0", "d0b"]), b("d1", 0, 32, key=["d1a", "d1b", "d1s"]), OP.mult, OP.add)
+        cp(b("lu"), b("s2", 1, 32, 2))
         if t == 0:
-            act(b("nonr"), b(fl, 16, 24), AF.Identity, 1.0, -1.0)
-        act(b("rpre"), ind(b("RW", 16, 528, key=["cvf", "rowM", "rowN", "rsp"]), b("lu", 0, 8)), AF.Copy)
-        scatter(b("CW", 0, 128 + n0, key=["C"] + blocks("C", s)), b("uvu%d" % t), b("rpre"))
-        act(b("C", n0, n0 + L, key="Cb%d" % s), ind(b("CN", key=["CN", "CNz"]), b("lu", 16, 24)), AF.Copy)
-        act(b("A", n0, n0 + L, key="Ab%d" % s), ind(b("AN", key=["Mb", "xb", "ANz"]), b("lu", 16, 24)), AF.Copy)
-        firsts(b("bu", key=["bu0", "bu1"]), lambda c: bf(c, c + 1), lambda c: b("d1", 48 + 2 * c, 49 + 2 * c, key="d1s"), "pb7", "clb", "zb")
-        cp(b("oAu"), b("zb", 16, 136, 17))
-        scatter(b("AW", 0, 128 + n0, key=["A"] + blocks("A", s)), b("oAu"), b("hv"))
+            act(b("nonr"), b("d1", 48, 64, 2, key="d1s"), AF.Identity, 1.0, -1.0)
+        act(b("rpre"), ind(b("RW", 16, 528, key=["cvf", "rowM", "rowN", "rsp"]), b("lu", 8, 16)), AF.Relu, 4095.0, -1.0)
+        scatter(b("CW", 0, 128 + n0, key=["C"] + blocks("C", s) + pk("Ck", 0, 4)), b("uvu%d" % t), b("rpre"), (-1.0, 4095.0))
+        act(b("C", n0, n0 + L, key="Cb%d" % s), ind(b("CN", key=["CN", "CNz", "CNy"]), b("lu", 8, 16)), AF.Copy)
+        act(b("A", n0, n0 + L, key="Ab%d" % s), ind(b("AN", key=["Mb", "xb", "ANz", "ANy"]), b("lu", 8, 16)), AF.Copy)
+        firsts(bu, bf, lambda c: b("d1", 32 + 2 * c, 33 + 2 * c, key="d1s"), "pb7", "zb", "ub", "oAu")
+        scatter(b("AW", 0, 128 + n0, key=["A"] + blocks("A", s)), b("oAu"), b("ab"), b("cl"))
         send(s)
 
     def round_end(s):
         cm = "come%d" % (s // ST)
-        tt(b("rest2"), b("fl0", 16, 24), b("fl1", 16, 24), OP.add)
+        tt(b("rest2"), b("d1", 48, 64, 2, key="d1s"), b("nonr"), OP.is_ge)
         begin(b("pb2", 192, 200), b("lp"), b("rest2"))
         lower(192, b("rest2"))
         act(b("nrs"), b("pb2", 192, 200), AF.Identity, 256.0, -1.0 / M)
-        act(b("absM"), ind(Aw, b("lu", 8, 16)), AF.Copy)
+        act(b("absM"), ind(Aw, b("lu", 0, 8)), AF.Copy)
         mms(b("pb6", 0, 128), [(b("nI"), b("xb")), (b("I"), b("absM"))])
         act(b("ad"), b("pb6", 0, 128), AF.Abs)
         first = b(cm, 0, CAP, key=cm + "_0")
@@ -738,7 +878,7 @@ def rank_program(g, core, T, topo):
         tt(b("hz"), ind(b(cm, key=[cm + "_0", cm + "_1", cm + "z"]), b("iu")), b("ad"), OP.min)
         act(b("xb"), b("hz"), AF.Abs)
 
-    x_forms(2)
+    x_forms(XQ[0])
     nrow = front(0)
     for s in range(4):
         step(s, nrow)
@@ -750,13 +890,14 @@ def rank_program(g, core, T, topo):
         if s < 3:
             nrow = front(s + 1)
         if s == 1:
-            for j in range(8):
-                o, a = piece("ag", j // 4, 4 * (j % 4), 4), ind(Aw, lst("cvu", j // 4, 4 * (j % 4), 4))
-                if j % 3:
+            for j in range(len(AGQ)):
+                n = 16 * NH // len(AGQ)
+                o, a = piece("ag", j * n // 16, j * n % 16, n), ind(Aw, lst("cvu", j * n // 16, j * n % 16, n))
+                if AGQ[j] == "s":
                     act(o, a, AF.Copy)
                 else:
                     cp(o, a)
-            x_forms(4)
+            x_forms(XQ[1])
     dma("ld7", T.yx[:], b("xb")[0], ["xb"], ["yx"], 32)
 
     if "o" not in ORDER:

@@ -2,30 +2,27 @@ from concourse.mybir import AluOpType as OP, ActivationFunctionType as AF
 
 V0, L, ST, RO, CAP, NR = 1024, 128, 2, 2, 32, 8
 W = V0 + RO * ST * L
-E1 = W
-WIN = W + 8
 BIG = float(2 ** 30)
 MAGIC = float(3 * 2 ** 22)
 NONE = 1000
-M = float(2 ** 22)
-UNIT = 2.0 ** -21
-KEY = 256 * UNIT
-FAR = 2048.0
+M = float(2 ** 12)
+UNIT = 2.0 ** -24
+KEY = 128 * UNIT
+STEP = 33
+FAR = 1024.0
 NH = 2
 HC, HW = 8 // NH, 128 // NH
-P1 = [[(4, None), (4, bank), (5, None), (3, None)] for bank in ("pb7", "pb4")]
-P1X = [[(5, None), (2, bank), (5, None), (4, None)] for bank in ("pb7", "pb4")]
-P2 = P1
+P1 = [[(4, None), (5, None), (4, bank), (3, None)] for bank in ("pb7", "pb4")]
+P1X = P1
+P2 = [[(3, None), (3, None), (7, "pb7"), (3, None)], [(5, None), (5, None), (4, None), (2, None)]]
 AGQ = "vssvssvs"
-ROUNDS, TRIES, SLACK = 6, (1400,) * 14, 60.0
+ROUNDS, TRIES, SLACK = 6, ((80, 1000), (110, 1000), (60, 800), (150, 1200)) * 5, 800.0
 CYCLE, GAT, SCA = 0.83, 1.5, 3.2
 START, KIB = 1000.0, 3.9
 TRIP = (10000, 3900, 7000, 3900)
 WAKE = 235.0
-
-COSTS = ((0.83, 1.5, 3.2, 235.0, 0.5), (1.2, 1.55, 3.6, 250.0, 0.36))
-
-CHOICE, BAR, GAIN = 3, 20, 200.0
+COSTS = ((0.86, 1.2, 2.4, 290.0, 0.36), (0.92, 1.75, 4.0, 215.0, 0.34), (1.18, 1.4, 3.6, 250.0, 0.3))
+CHOICE, BAR, GAIN = 3, 8, 600.0
 
 SLOT = {}
 SIZE = {"F": 0, "B": 0, "I": 0, "U": 0}
@@ -37,31 +34,34 @@ def _s(kind, **kw):
         SIZE[kind] += (w + 15) // 16 * 16
 
 
-_s("B", AW=128 + WIN, xrep=2048, D=2048, Dab=2048, ag=2048, AN=512, xP=128, xd=128, xn=128, hz=128, nr2=640, ones=144, B=144, B2=144, nB=144, pw=128,
-   bones=128, lo=128, lt=128, ld=128, lp=128, nl8=128, I=128, nI=128, hI=128, nhI=128, I63=128, nI63=128, I128=128, I256=128, nI128=128, nI8=128,
-   sh=128, cr=1280, cnt0=128, emc=128, tab=128, emp=128, oh=256, ab=128, dq=128, cl=128, absM=128, E0=1024, E1=1024, fl0=32, fl1=32, rest2=8, cum=8,
-   cj=8, fw=8, msk=32)
-_s("F", CW=128 + WIN, iot=WIN, RW=544, CN=512, idf=128, dm=128, RM=128, RM2=128, RN=128, RF=128, NF=32, RZ=128, tr=288, dl=128, RX=640, e=128, cand=128, pay=128,
-   row0=128, row1=128, RY0=136, RY1=136, zv=136, zb=136, w3=128, rpre=128, dvf=128, fs=128, rm=128, xm=128,
-   ad=128, thf=128, thx=128, lim4=32, jL=8, topf=8, nL=32, LA0=32, LA1=32, U4=32, TT=64, FL=32, nfl=32, coef=24, prod=32, d0=32, d1=64, s2=32,
-   cvp=128, dvp=128, cB=8, cB2=8, uv=8, ub=8, nonr=8, one8=8,
-   nrs=8, ge=8, idx=8, na=1, n0=1, cd=1, r7=1, pH=2, pf=1, pG=1, tmp=16, tmp2=16, tmp3=16)
-_s("I", KI=WIN, tp=8, thi=128, pin=16, pa=16, pc=16, ci=128, ri=128, dec=16, dk=16, hx=128, xi=128)
-_s("U", tu=8, cvu=128, dvu=128, rowu0=128, rowu1=128, bu=8, du=8, ku=16, uvu0=8, uvu1=8, lu=16, oAu=8, posu=8, iu=8,
-   plist=128, lperm=8, lsel=8, lF=2, lz=2, lxd=8)
-SLOT["C"] = ("arF", SLOT["CW"][1] + 128, WIN)
-SLOT["A"] = ("arB", SLOT["AW"][1] + 128, WIN)
+_s("B", AW=128 + W, xrep=2048, D=2048, Dab=2048, ag=2048, AN=512, xP=128, xn=144, hz=128, nr2=640, ones=144, B=144, B2=144, nB=144,
+   bones=128, lo=128, lt=128, ld=128, lp=128, nl8=128, I=128, nI=128, hI=128, I63=128, nI63=128, cr=384, kl=128, kr=128, emc=128, tab=1024,
+   oq=128, nb=128, ab=128, dq=128, cl=128, cl0=128, bx=128, absM=128, av=128, fl1=32, far0=256, far1=256, rest2=8, cum=8, cj=8, fw=8,
+   msk=128, frow=128, crow=128)
+_s("F", CW=128 + W, iot=W, RW=544, CN=512, dm=128, RM=128, tr=288, dl=128, RX=576, es=128, e=128, pay=128, row0=128, row1=128, RY0=136, RY1=136,
+   zv=136, zb=136, w3=128, rpre=128, dvf=128, mf=128, xm=128, ad=128, thf=128, thx=128, lim4=32, jL=8, topf=8, nL=32, LA0=32, LA1=32,
+   BD=128, nfl=32, fg=64, d1=64, s2=64, fl0=32, neg0=8, neg1=8, nonr=8, room=16, one8=8, nrs=8, ge=8, idx=8, na=1, n0=1, cd=1, pH=1, pf=1,
+   pG=1, inv=2, tmp=16, tmp2=16)
+_s("I", KI=V0, tp=8, thi=128, pin=16, pa=16, pc=16, ci=128, ri=128, dec=16, dk=16, hx=128, xi=128)
+_s("U", tu=8, cvu=128, dvu=128, bu=8, du=16, uvu0=8, uvu1=8, lu=16, oAu=8, posu=8, iu=8, fu=8, ivu=2, plist=128, lperm=8, lsel=8, lF=2, lG=4, lz=2)
+SLOT["C"] = ("arF", SLOT["CW"][1] + 128, W)
+SLOT["A"] = ("arB", SLOT["AW"][1] + 128, W)
 SLOT["cvf"] = ("arF", SLOT["RW"][1] + 16, 128)
 SLOT["xb"] = ("arB", SLOT["AN"][1] + 256, 128)
-for _k, _n in enumerate(("r2", "r1", "lim", "es", "no")):
-    SLOT[_n] = ("arF", SLOT["RX"][1] + 128 * _k, 128)
-ROWU, CLS, MBS = (2, 2), False, False
+for _n, _o, _w in (("r2", 0, 256), ("r1", 64, 128), ("lim", 448, 128)):
+    SLOT[_n] = ("arF", SLOT["RX"][1] + _o, _w)
+DQ = "ssss"
+EB = "pb4"
+MB, RB = ("pb6", "pb6"), (("pb5", "pb3"), ("pb5", "pb3"))
+ES = (8, 4)
+GQ = "gg"
+SPLIT = (1, 1, 1, 0, 1, 0, 0)
 STAG = (1, 0, 1, 1)
-NFV = True
-IOTG = 8
-D3 = True
-CVS, RMT = (False, False), False
-XQ = ("vsvsvsvsvsvsvsvs", "vsssvsssvsssvsss")
+IOTQ = "sssssssgggg"
+XQ = ("vsvsvsvsvsvsvsvs", "gsgvgsgsgsgvgsgs")
+PULL = (1, 0, 1, 0)
+CKQ = "gggg"
+JOIN, SEED = 3, 5
 
 SCRATCH = {"arF": ("sbuf", [128, SIZE["F"]], "float32"), "arB": ("sbuf", [128, SIZE["B"]], "bfloat16"),
            "arI": ("sbuf", [128, SIZE["I"]], "int32"), "arU": ("sbuf", [128, SIZE["U"]], "uint16")}
@@ -74,9 +74,10 @@ for _k in range(2):
     SCRATCH["come%d" % _k] = ("sbuf", [128, 80], "bfloat16")
     SCRATCH["r3%d" % _k] = ("sbuf", [128, 8, 17], "uint16")
     SCRATCH["e4%d" % _k] = ("sbuf", [128, 8, 8, 17], "bfloat16")
-SCRATCH["c3"] = ("sbuf", [128, 8, 17], "bfloat16")
+SCRATCH["c3"] = SCRATCH["em3"] = ("sbuf", [128, 8, 17], "bfloat16")
+SCRATCH["xd"] = ("sbuf", [128, 8, 16], "bfloat16")
 SEMAPHORES = (["qv", "qs", "qt", "qg"] + ["in%d" % k for k in range(4)] + ["rr%d" % k for k in range(4)] + ["ls%d" % k for k in range(4)]
-              + ["ld%d" % k for k in range(8)])
+              + ["ld%d" % k for k in range(9)])
 ORDER = {}
 
 
@@ -193,88 +194,119 @@ def order_calls(ops):
     lag, queue = [o["lag"] for o in ops], [o["q"] for o in ops]
     costs = [([o["cs"][k] for o in ops], [[(j, m[3] if w else 0.0) for j, w in d.items()] for d in pre], m[4]) for k, m in enumerate(COSTS)]
 
-    def run(order, a=0, old=None):
-        before, total, found = {}, 0.0, []
-        for i in reversed(order[:a]):
-            if queue[i] not in before:
-                before[queue[i]] = i
-                if len(before) == 5:
-                    break
-        for k, (time, need, weight) in enumerate(costs):
-            end, why = (list(old[k][0]), list(old[k][1])) if a else ([0.0] * n, [-1] * n)
-            free = {q: (end[before[q]] - lag[before[q]], before[q]) if q in before else (0.0, 0) for q in "vstgy"}
-            for i in order[a:]:
-                t, y = free[queue[i]]
-                y = -2 - y if t else -1
-                for j, w in need[i]:
-                    if end[j] + w >= t:
-                        t, y = end[j] + w, j
-                t += time[i]
-                free[queue[i]], end[i], why[i] = (t, i), t + lag[i], y
-            total += weight * max(end)
-            found.append((end, why))
-        return total, found
-
     gives = [[[(j, m[3] if w else 0.0) for j, w in d.items()] for d in post] for m in COSTS]
+    sets = range(len(COSTS))
 
-    def tails(order):
-        found = []
-        for (time, need, weight), give in zip(costs, gives):
-            rest, behind = [0.0] * n, dict.fromkeys("vstgy", 0.0)
-            for i in reversed(order):
+    def ends(part, a, end, why, free):
+        total, far = 0.0, []
+        for k in sets:
+            time, need, weight = costs[k]
+            e, y0, f = end[k], why[k], dict(free[k])
+            for i in part[:a]:
+                f[queue[i]] = i
+            f = {q: (e[i] - lag[i], i) if i >= 0 else (0.0, -1) for q, i in f.items()}
+            for i in part[a:]:
+                t, y = f[queue[i]]
+                y = -2 - y
+                for j, w in need[i]:
+                    if e[j] + w >= t:
+                        t, y = e[j] + w, j
+                t += time[i]
+                f[queue[i]], e[i], y0[i] = (t, i), t + lag[i], y
+            far.append(f)
+        return far
+
+    def rests(part, rest, behind):
+        for k in sets:
+            time, give, r, q0 = costs[k][0], gives[k], rest[k], dict(behind[k])
+            for i in reversed(part):
                 t = 0.0
                 for j, w in give[i]:
-                    if rest[j] + w > t:
-                        t = rest[j] + w
+                    if r[j] + w > t:
+                        t = r[j] + w
                 t += lag[i]
-                if behind[queue[i]] > t:
-                    t = behind[queue[i]]
-                behind[queue[i]] = rest[i] = t + time[i]
-            found.append(rest)
-        return found
+                if q0[queue[i]] > t:
+                    t = q0[queue[i]]
+                q0[queue[i]] = r[i] = t + time[i]
 
-    def through(order, a, z, part, found, rests, at):
-        kinds, before, after, total = {queue[i] for i in part}, {}, {}, 0.0
-        for places, into in ((range(a - 1, -1, -1), before), (range(z + 1, n), after)):
-            for m in places:
-                q = queue[order[m]]
-                if q in kinds and q not in into:
-                    into[q] = order[m]
-                    if len(into) == len(kinds):
-                        break
-        for (time, need, weight), give, (old, why), rest in zip(costs, gives, found, rests):
-            end, far = {}, max(old) - GAIN
-            free = {q: old[before[q]] - lag[before[q]] if q in before else 0.0 for q in kinds}
-            for i in part:
-                t = free[queue[i]]
-                for j, w in need[i]:
-                    y = end.get(j, old[j]) + w
-                    if y > t:
-                        t = y
-                free[queue[i]] = t = t + time[i]
-                end[i] = t = t + lag[i]
-                if t > far:
-                    far = t
-                for j, w in give[i]:
-                    if at[j] > z and t + w + rest[j] > far:
-                        far = t + w + rest[j]
-            for q in after:
-                far = max(far, free[q] + rest[after[q]])
-            total += weight * far
-        return total
+    def better(order, lo, hi, tries, seed):
+        end, why, rest = ([[0.0] * n for _ in sets] for _ in range(3))
+        part, none = order[lo:hi], dict.fromkeys("vstgy", -1)
+        ends(order[:lo], 0, end, why, [none for _ in sets])
+        rests(order[hi:], rest, [dict.fromkeys("vstgy", 0.0) for _ in sets])
+        first, at = dict(none), [-1] * n
+        for i in order[:lo]:
+            first[queue[i]] = i
+        behind = [dict.fromkeys("vstgy", 0.0) for _ in sets]
+        for i in reversed(order[hi:]):
+            at[i] = n
+            for k in sets:
+                behind[k][queue[i]] = rest[k][i]
+        out = [[max([w + rest[k][j] for j, w in gives[k][i] if at[j] == n] + [0.0]) if at[i] < n else 0.0 for i in range(n)] for k in sets]
+        size = len(part)
 
-    def exchange(order, tries, seed):
-        last, found = run(order)
-        good, barred, rest = (last, order, found[0][0]), {}, None
+        def value(a):
+            free, total, tops = ends(part, a, end, why, [first for _ in sets]), 0.0, []
+            for k in sets:
+                e, o = end[k], out[k]
+                top = max([(e[i] + o[i], i) for i in part] + [(t + behind[k][q], i) for q, (t, i) in free[k].items()])
+                total += costs[k][2] * top[0]
+                tops.append(top)
+            return total, tops
+
+        def through(a, z, new):
+            kinds, before, after, total = {queue[i] for i in new}, {}, {}, 0.0
+            for places, into in ((range(a - 1, -1, -1), before), (range(z + 1, size), after)):
+                for m in places:
+                    q = queue[part[m]]
+                    if q in kinds and q not in into:
+                        into[q] = part[m]
+                        if len(into) == len(kinds):
+                            break
+            for k in sets:
+                time, need, weight = costs[k]
+                old, r, give, e, far = end[k], rest[k], gives[k], {}, tops[k][0] - GAIN
+                free = {}
+                for q in kinds:
+                    i = before.get(q, first[q])
+                    free[q] = old[i] - lag[i] if i >= 0 else 0.0
+                for i in new:
+                    t = free[queue[i]]
+                    for j, w in need[i]:
+                        y = e.get(j, old[j]) + w
+                        if y > t:
+                            t = y
+                    free[queue[i]] = t = t + time[i]
+                    e[i] = t = t + lag[i]
+                    if t > far:
+                        far = t
+                    for j, w in give[i]:
+                        if at[j] > z and t + w + r[j] > far:
+                            far = t + w + r[j]
+                for q in kinds:
+                    far = max(far, free[q] + (r[after[q]] if q in after else behind[k][q]))
+                total += weight * far
+            return total
+
+        last, tops = value(0)
+        good, barred, pairs = (last, part), {}, None
         for turn in range(tries):
-            if rest is None:
-                rest, pairs, at = tails(order), [], {i: m for m, i in enumerate(order)}
-                for end, why in found:
-                    i = end.index(max(end))
-                    while i >= 0:
-                        if why[i] <= -2:
-                            pairs.append((-2 - why[i], i))
-                        i = why[i] if why[i] >= -1 else -2 - why[i]
+            if pairs is None:
+                rests(part, rest, behind)
+                pairs = []
+                for m, i in enumerate(part):
+                    at[i] = m
+                for k in sets:
+                    i, y0 = tops[k][1], why[k]
+                    while i >= 0 and at[i] >= 0:
+                        j = y0[i]
+                        if j <= -2:
+                            j = -2 - j
+                            if at[j] >= 0:
+                                pairs.append((j, i))
+                        i = j
+                if not pairs:
+                    break
             pick = None
             for _ in range(CHOICE):
                 seed = (seed * 1103515245 + 12345) % 2 ** 31
@@ -284,38 +316,48 @@ def order_calls(ops):
                 a, z, early = at[u], at[v], seed >> 5 & 1
                 for _ in range((0, 0, 0, 1, 2, 4)[(seed >> 20) % 6]):
                     if early:
-                        a = max([m for m in range(max(0, a - 40), a) if queue[order[m]] == queue[u]] or [a])
+                        a = next((m for m in range(a - 1, max(-1, a - 40), -1) if queue[part[m]] == queue[u]), a)
                     else:
-                        z = min([m for m in range(z + 1, min(n, z + 40)) if queue[order[m]] == queue[u]] or [z])
-                part, tied = order[a:z + 1], {v if early else u}
-                for x in (reversed(part) if early else part):
+                        z = next((m for m in range(z + 1, min(size, z + 40)) if queue[part[m]] == queue[u]), z)
+                new, tied = part[a:z + 1], {v if early else u}
+                for x in (reversed(new) if early else new):
                     if early and x in tied:
                         tied.update(pre[x])
                     elif not early and any(j in tied for j in pre[x]):
                         tied.add(x)
-                if order[a if early else z] in tied:
+                if part[a if early else z] in tied:
                     continue
-                part = [x for x in part if (x in tied) == early] + [x for x in part if (x in tied) != early]
-                guess = through(order, a, z, part, found, rest, at)
+                new = [x for x in new if (x in tied) == early] + [x for x in new if (x in tied) != early]
+                guess = through(a, z, new)
                 if pick is None or guess < pick[0]:
-                    pick = (guess, a, z, part, u, v)
+                    pick = (guess, a, z, new, u, v)
             if pick and pick[0] <= last + SLACK * (seed >> 3 & 3) / 3 * (seed >> 12 & 3) / 3:
-                guess, a, z, part, u, v = pick
-                order = order[:a] + part + order[z + 1:]
-                last, found = run(order, a, found)
-                barred[(v, u)], rest = turn + BAR + (seed >> 9 & 7), None
+                guess, a, z, new, u, v = pick
+                part = part[:a] + new + part[z + 1:]
+                last, tops = value(a)
+                barred[(v, u)], pairs = turn + BAR + (seed >> 9 & 7), None
                 if last < good[0]:
-                    good = (last, order, found[0][0])
-        return good
+                    good = (last, part)
+        return order[:lo] + good[1] + order[hi:]
+
+    def timed(order):
+        end, why = ([[0.0] * n for _ in sets] for _ in range(2))
+        ends(order, 0, end, why, [dict.fromkeys("vstgy", -1) for _ in sets])
+        return sum(costs[k][2] * max(end[k]) for k in sets), end[0]
 
     order = sorted(range(n), key=lambda i: (best[1][i], i))
-    for k, tries in enumerate(TRIES):
-        last, order, end = exchange(order, tries, k + 1)
+    for k, (width, tries) in enumerate(TRIES):
+        for lo in range(-width // 2 * (k % 2), n, width):
+            order = better(order, max(0, lo), min(n, lo + width), tries, 97 * k + lo + n + SEED)
+        last, end = timed(order)
+        at = {i: m for m, i in enumerate(order)}
+        order.sort(key=lambda i: (end[i] - lag[i] - costs[0][0][i], at[i]))
         way = place(sorted(range(n), key=lambda i: (-end[i], -i)), post, True)[1]
         start, end = place(sorted(range(n), key=lambda i: (-way[i], i)), pre, False)
         other = sorted(range(n), key=lambda i: (start[i], i))
-        if run(other)[0] < last:
+        if timed(other)[0] < last:
             order = other
+        ORDER.setdefault("log", []).append(round(last))
     return order
 
 
@@ -337,8 +379,12 @@ def rank_program(g, core, T, topo):
         ops.append({"q": q, "call": call, "R": R, "W": Wk, "c": c * CYCLE, "cs": cs, "pk": list(picks), "lag": lag, "dma": dma, "adds": adds})
         picks[:] = [0, 0]
 
-    def dma(sem, out, in_, R, Wk, kib):
-        op("y", lambda e: e.dma_start(out, in_), R, Wk, 60 + kib * KIB / CYCLE, START, sem)
+    def dma(out, in_, R, Wk, kib, q="y"):
+        sem = "ld%d" % len([o for o in ops if (o["dma"] or "")[:2] == "ld"])
+        if q == "y":
+            op("y", lambda e: e.dma_start(out, in_), R, Wk, 60 + kib * KIB / CYCLE, START, sem)
+        else:
+            op(q, lambda e: e.dma_start(out, in_), R, Wk, 60, START + kib * KIB, sem)
 
     def b(name, c0=0, c1=None, st=1, p1=128, key=None):
         if name in SLOT:
@@ -388,8 +434,8 @@ def rank_program(g, core, T, topo):
     def ms(o, v):
         op("v", lambda e: e.memset(o[0], v), [], ks(o), cyc(o, o))
 
-    def scan(o, a, c, f0, f1):
-        op("v", lambda e: e.tensor_tensor_scan(o[0], a[0], c[0], 0.0, f0, f1), ks(a, c), ks(o), cyc(o, a, 1.01))
+    def scan(o, a, c, f0, f1, first=0.0):
+        op("v", lambda e: e.tensor_tensor_scan(o[0], a[0], c[0], first, f0, f1), ks(a, c), ks(o), cyc(o, a, 1.0 if c[3] == "arB" else 1.01))
 
     def turn(o, a):
         op("v", lambda e: e.transpose(o[0], a[0]), ks(a), ks(o), cyc(o, a, 1.01))
@@ -414,6 +460,14 @@ def rank_program(g, core, T, topo):
             left[k] -= 1
             return e.matmul(o[0], l[0], r[0], False, left[k] == 0)
         op("t", call, ks(l, r), ks(o), max(min(64, l[2]), r[2]) * (4 if l[3] == "arF" else 1), adds=k)
+
+    def join(n):
+        part = ops[-n:]
+        del ops[-n:]
+        one = dict(part[0], call=lambda e: [o["call"](e) for o in part], c=sum(o["c"] for o in part), cs=[sum(c) for c in zip(*(o["cs"] for o in part))])
+        for k in "RW":
+            one[k] = list(dict.fromkeys(x for o in part for x in o[k]))
+        ops.append(one)
 
     def close(o, l, r):
         k = (o[1][0], opened[o[1][0]])
@@ -440,162 +494,170 @@ def rank_program(g, core, T, topo):
     def asel(o, a, pat, f, other, base, cm):
         op("g", lambda e: e.affine_select(o[0], a[0], pat, f, other, base, cm), ks(a), ks(o), 200 + 2 * o[2])
 
+    def copy(q, o, a):
+        if q == "s":
+            act(o, a, AF.Copy)
+        elif q == "g":
+            asel(o, a, [[0, o[2]]], OP.is_ge, 0.0, 0, 0)
+        else:
+            cp(o, a)
+
     def row(j, c0=0, c1=128):
         return b("cr", 128 * j + c0, 128 * j + c1, 1, 1, key="cr%d" % j)
 
-    ONE, JROW, R65, R128, RH, R160, RMG, RU = range(8)
+    ONE, RH, RMG = range(3)
     blocks = lambda t, n: ["%sb%d" % (t, k) for k in range(n)]
     pk = lambda nm, p0, n: ["%s%d" % (nm, p) for p in range(p0, p0 + n)]
-    Cw = lambda s: b("KI", 0, V0) if s == 0 else b("C", key=["C", "Ce"] + blocks("C", 4) + pk("Ck", 0, 4))
-    Aw = b("A", key=["A", "Ae"] + blocks("A", 4))
+    Cw = lambda s: b("C", 0, V0 + L * s + 1, key=["C"] + blocks("C", s + 1) + pk("Ck", 0, 4))
+    Aw = lambda s, more=1: b("A", 0, V0 + L * s + more, key=["A"] + blocks("A", s + 1))
     lhs = lambda p, m="B": b(m, 15 - p, 143 - p)
 
-    dma("ld0", b("tp")[0], T.tops[:], [], ["tp"], 4)
-    dma("ld1", b("xb")[0], T.x0[:], [], ["xb"], 32)
-    dma("ld2", b("KI", 0, V0)[0], T.kids[:], [], ["KI"], 512)
-    dma("ld3", b("A", 0, V0)[0], T.a0[:], [], ["A"], 256)
-    dma("ld4", b("thi", p1=8)[0], T.th[:], [], ["thi"], 4)
-    fill(b("C", V0, WIN, key=["Ce"] + blocks("C", 4)), 4095)
-    ms(b("A", V0, W, key=blocks("A", 4)), 0.0)
-    ms(b("A", W, WIN, key="Ae"), FAR)
+    dma(b("xb")[0], T.x0[:], [], ["xb"], 32, DQ[0])
+    dma(b("tp")[0], T.tops[:], [], ["tp"], 4, DQ[1])
+    dma(b("KI", 0, V0)[0], T.kids[:], [], ["KI"], 512 + 36 * (DQ[0] == "s"))
+    dma(b("A", 0, V0)[0], T.a0[:], [], ["A"], 256)
+    dma(b("thi", p1=8)[0], T.th[:], [], ["thi"], 4, DQ[2])
+    ms(b("A", V0, W, L, key=blocks("A", 4)), FAR)
+    fill(b("C", V0, W, L, key=blocks("C", 4)), 4095)
     ms(b("ones"), 1.0)
     fill(b("one8"), 1)
-    ms(b("AN", 0, 256, key=["ANz", "Mb"]), 0.0)
-    ms(b("AN", 384, 512, key="ANy"), 0.0)
+    fill(b("AN", 0, 128, key="ANz"), 0)
+    fill(b("AN", 384, 512, key="ANy"), 0)
     fill(b("CN", 0, 128, key="CNz"), 4095)
     fill(b("CN", 256, 512, key="CNy"), 4095)
-    ms(b("RW", 0, 16, key="RWa"), 0.0)
-    ms(b("RW", 144, 160, key="rowM"), 0.0)
-    fill(b("cand", 0, 128, HW, key="candz"), 0)
-    fill(b("d0", key=["d0", "d0b"]), 0)
     ms(b("B"), 0.0)
     ms(row(ONE), 1.0)
-    ms(row(RH), -0.25)
-    for j, v in ((R65, 65), (R128, 128), (R160, 160), (RMG, MAGIC), (RU, UNIT)):
-        ms(row(j), float(v))
-    for nm, n, v in (("RM", 128, BIG), ("RM2", HW, BIG), ("RF", HW, 0.75)):
-        ms(b(nm, 0, n), 0.0)
-        ms(b(nm, 0, n, 16), v)
-    ms(b("RM2", 1, HW, 16), BIG)
-    fill(b("RN", 0, HW), 6)
-    fill(b("RN", 0, HW, 16), 0)
-    if not D3:
-        fill(b("RZ"), 2 ** 23)
+    ms(row(RH), 1.75)
+    ms(row(RMG), MAGIC)
+    mm(b("pb2", 0, 160), row(ONE), b("cr", 0, 160, 1, 1, key=["cr0", "cr1"]))
+    ms(b("RM"), 0.0)
+    ms(b("RM", 0, 128, 16), BIG)
+    ms((T.em3[:, :, 16], ["empz"], 8, "arB"), 0.0)
     for k in range(2):
         fill(b("come%d" % k, 64, 80, key="come%dz" % k), NONE)
     for k in range(4):
-        fill(b("msg%d" % k, 0, CAP), NONE)
+        if not PULL[k]:
+            fill(b("msg%d" % k, 0, CAP), NONE)
+    high = lambda nm: (T.arB[32:33, SLOT[nm][1]:SLOT[nm][1] + 128], [nm + "h"], 128, "arB")
+    ms(b("kl", p1=32), 0.0)
+    ms(b("kl", p1=1), UNIT)
+    ms(high("kl"), 1 / 256)
+    io(b("kr", p1=64, key=["kr", "krh"]), [[0, NH], [-STEP, HC], [0, 16]], STEP * HC, 0)
+    io(b("kr", 0, HW, p1=1), [[1, HW]], -HW, 0)
+    ms(b("kr", HW, 128, p1=1), 32.0)
+    fill(b("BD", 0, 64, 4, key="BDz"), -1)
+    for k, v in enumerate((256, 128, -256)):
+        fill(b("d1", 32 + k, 64, 4, key="d1k%d" % k), v)
 
     io(b("pin"), [[0, 16]], 0, 1)
-    io(b("ci"), [[1, 128]], 0, 0)
+    io(b("iot", 0, 128, key="iot0"), [[1, 128]], 0, 0)
     io(b("ri"), [[HW, NH], [1, 16], [16, HC]], 0, 0)
     cp(b("plist"), b("ri"))
-    io(row(JROW), [[1, 128]], 0, 0)
     asel(b("I"), b("ones", 0, 128), [[-1, 128]], OP.is_equal, 0.0, 0, 1)
-    cp(b("iot", 0, 128, key="iot0"), b("ci"))
-    if IOTG < 13:
-        io(b("iot", 128 * IOTG, WIN, key=pk("iot", IOTG, 13 - IOTG)), [[1, WIN - 128 * IOTG]], 128 * IOTG, 0)
-    for k in range(1, IOTG):
-        act(b("iot", 128 * k, min(WIN, 128 * k + 128), key="iot%d" % k), b("iot", 0, min(128, WIN - 128 * k), key="iot0"), AF.Identity, 128.0 * k)
-    for nm, v in (("nI", -1.0), ("hI", 0.5), ("nhI", -0.5), ("I63", 63.0), ("nI63", -63.0), ("I128", 128.0), ("I256", 256.0), ("nI128", -128.0),
-                  ("nI8", -8320.0), ("idf", 1.0)):
+    cp(b("ci"), b("iot", 0, 128, key="iot0"))
+    for k in range(1, 12):
+        if IOTQ[k - 1] == "g":
+            io(b("iot", 128 * k, 128 * k + 128, key="iot%d" % k), [[1, 128]], 128 * k, 0)
+        else:
+            act(b("iot", 128 * k, 128 * k + 128, key="iot%d" % k), b("iot", 0, 128, key="iot0"), AF.Identity, 128.0 * k)
+    for nm, v in (("nI", -1.0), ("hI", 0.5), ("I63", 63.0), ("nI63", -63.0)):
         act(b(nm), b("I"), AF.Copy, 0.0, v)
     ts(b("pa", 0, 2), b("pin", 0, 2), 15, OP.bitwise_and)
     cp(b("pf"), b("pa", 0, 1))
-    for h in range(NH):
-        act(b("pH", h, h + 1, key="pH%d" % h), b("pf"), AF.Identity, 15.0 * HW * h, float(HW))
+    act(b("pH"), b("pf"), AF.Copy, 0.0, float(HW))
     ts(b("pc", 0, 2), b("pin", 0, 2), 7, OP.bitwise_and)
     ts(b("jL"), b("ci", 0, 128, 16), b("pf"), OP.add)
     act(b("cj"), b("jL"), AF.Identity, -128 * M, -M)
-    for s in range(4):
-        act(b("nL", 8 * s, 8 * s + 8, key="nL%d" % s), b("jL"), AF.Identity, float(V0 + L * s))
-    fill(b("d1", key=["d1a", "d1b", "d1s"]), 0)
-    act(b("d1", 17, 32, 2, key="d1a"), b("jL"), AF.Identity, 384.0)
-    if not D3:
-        act(b("RZ", 0, 128, 16), b("jL"), AF.Identity, -1.0, -1.0)
+    io(b("nL"), [[16, 32]], V0, 0)
+    ts(b("nL"), b("nL"), b("pf"), OP.add)
+    act(b("d1", 35, 64, 4, key="d1k3"), b("jL"), AF.Identity, 256.0)
+    fill(b("xn", 128, 144, key="xnz"), NONE)
     ts(b("lF"), b("pc", 0, 2), 16.0, OP.mult, 15.0, OP.add)
+    io(b("pc", 8, 12, key="pc8"), [[0, 2], [64, 2]], 15, 0)
     ts(b("pc", 4, 6, key="pc4"), b("pin", 0, 2), HC - 1, OP.bitwise_and)
     ts(b("pc", 6, 8, key="pc6"), b("pin", 0, 2), HC.bit_length() - 1, OP.logical_shift_right, 16 // HC - 1, OP.bitwise_and)
     cp(b("tmp2", 12, 13, key="tmp2c"), b("pc", 6, 7, key="pc6"))
+    act(b("tmp2", 8, 9, key="tmp2b"), b("tmp2", 12, 13, key="tmp2c"), AF.Copy, 0.0, 16.0)
+    ts(b("lG"), b("pc", 8, 12, key="pc8"), b("tmp2", 8, 9, key="tmp2b"), OP.add)
     ts(b("tmp2", 0, 1, key="tmp2a"), b("pc", 4, 5, key="pc4"), 16.0, OP.mult, b("tmp2", 12, 13, key="tmp2c"), OP.add)
     for h in range(NH):
         ts(b("lperm", HC * h, HC * h + HC), b("ci", HW * h, HW * h + 16, 16 // HC), b("tmp2", 0, 1, key="tmp2a"), OP.add)
-    ts(b("dec", 0, 2), b("pin", 0, 2), 4, OP.logical_shift_right, 1, OP.bitwise_and)
-    ts(b("tmp", 8, 9, key="tmpy"), b("dec", 0, 1), 144.0, OP.mult)
+    ts(b("pc", 12, 14, key="pc12"), b("pin", 0, 2), 4, OP.logical_shift_right, 1, OP.bitwise_and)
+    ts(b("tmp", 8, 9, key="tmpy"), b("pc", 12, 13, key="pc12"), 144.0, OP.mult)
     act(b("tmp", 9, 10, key="tmpz"), b("tmp", 8, 9, key="tmpy"), AF.Identity, 144.0, -1.0)
     ts(b("lsel", 0, 8, 2), b("jL", 0, 8, 2), b("tmp", 8, 9, key="tmpy"), OP.add)
     ts(b("lsel", 1, 8, 2), b("jL", 1, 8, 2), b("tmp", 9, 10, key="tmpz"), OP.add)
-    raw = parts(P1[0], True)
-    ts(b("tmp3", 12, 13, key="tmp3c"), b("pf"), float(raw[0]), OP.is_ge)
-    ts(b("tmp3", 11, 12, key="tmp3b"), b("pf"), float(raw[-1]), OP.is_le, b("tmp3", 12, 13, key="tmp3c"), OP.mult)
-    ts(b("lxd"), b("jL"), 256.0, OP.add, b("tmp3", 11, 12, key="tmp3b"), OP.mult)
     ts(b("pa", 2, 4, key="pa_"), b("pin", 0, 2), 4, OP.logical_shift_right)
     cp(b("pG"), b("pa", 2, 3, key="pa_"))
     ts(b("xi"), b("ci"), 4, OP.logical_shift_right)
     ts(b("bones"), b("xi"), b("pG"), OP.is_equal, KEY, OP.mult)
     cp(b("B", 15, 143, 16), b("bones", 0, 128, 16))
+    asel(b("bx"), b("bones"), [[0, 128]], OP.is_ge, 0.0, 0, 0)
+    for p in parts(P1X[0], True):
+        fill(b("bx", p, 128, 16), 0)
     act(b("B2"), b("B"), AF.Copy, 0.0, 2.0)
     act(b("nB"), b("B"), AF.Copy, 0.0, -1.0)
     act(b("lo"), b("bones"), AF.Copy, 0.0, -M / KEY)
     asel(b("lt"), b("lo"), [[1, 128]], OP.is_gt, 0.0, 0, -1)
     asel(b("ld"), b("lt"), [[1, 128]], OP.not_equal, M, 0, -1)
     asel(b("lp"), b("lt"), [[1, 128]], OP.not_equal, 256 * M, 0, -1)
-    act(b("nl8"), b("lt"), AF.Copy, 0.0, -8320.0 / M)
-    act(b("pw"), b("bones"), AF.Copy, 0.0, -1.0 / KEY)
-    asel(b("w3"), b("pw"), [[-1, 128]], OP.is_equal, 0.0, -1, 1)
-    asel(b("dm"), b("w3"), [[-1, 128]], OP.not_equal, 1.0, 0, 1)
+    act(b("nl8"), b("lt"), AF.Copy, 0.0, -128.0 / M)
+    asel(b("row1"), b("lo"), [[-1, 128]], OP.is_equal, 0.0, -1, 1)
+    asel(b("dm"), b("row1"), [[-1, 128]], OP.not_equal, M, 0, 1)
     io(b("nr2", 512, 640, 1, 2, key="jr2"), [[1, 128]], 0, 128)
-    act(b("sh", p1=2), b("ones", 0, 128, 1, 2), AF.Copy, 0.0, b("pf", p1=2))
     for s in range(4):
-        act(b("nr2", 128 * s, 128 * s + 128, 1, 2, key="n%d" % s), b("sh", p1=2), AF.Identity, -7.0 - s, 15.0 + 2 * s)
+        io(b("nr2", 128 * s, 128 * s + 128, 1, 2, key="n%d" % s), [[0, 128]], -7 - s, 15 + 2 * s)
     ts(b("hx"), b("ci"), 15, OP.bitwise_and)
     ts(b("tab", 0, 128), b("hx"), b("pf"), OP.is_equal, 65.0, OP.mult)
-    act(b("cl"), b("tab", 0, 128), AF.Relu, float(2 ** 26), -float(2 ** 26))
-    act(b("emc"), b("cl"), AF.Identity, 128 * UNIT)
-    if D3:
-        act((T.c3[:, :, 0:16], ["cnt0"], 128, "arB"), b("cl"), AF.Identity, -M / 2, -1.0)
-        act((T.c3[:, :, 16], ["cnt0"], 8, "arB"), b("jL"), AF.Copy)
-        ts(b("lz"), b("pc", 0, 2), 17.0, OP.mult, 15.0, OP.add)
-        for k in range(2):
-            ms((T["r3%d" % k][:, :, 16], ["rowu%dz" % k], 8, "arU"), 65535)
-            fill(b("RY%d" % k, key=["RY%d" % k, "RY%dt" % k]), 2 ** 23)
-            fill(b("RY%d" % k, 0, 136, 17), -2 ** 23)
-    else:
-        act(b("cnt0"), b("cl"), AF.Identity, -M / 2, -1.0)
+    act(b("cl0"), b("tab", 0, 128), AF.Relu, float(2 ** 26), -float(2 ** 26))
+    for k in range(2):
+        cp(b("tab", 128 << k, 256 << k, key="tab%d" % (k + 1)), b("tab", 0, 128 << k, key=["tab"] + pk("tab", 1, k)))
+    dma(b("tab", 512, 1024)[0], b("tab", 0, 512)[0], ["tab", "tab1", "tab2"], ["tab3"], 128)
+    mms(b("pb6", 0, 128), [(b("I"), b("cl0")), (high("kl"), high("kr"))])
+    act(b("emc"), b("pb6", 0, 128), AF.Copy)
+    act((T.c3[:, :, 0:16], ["cnt0"], 128, "arB"), b("cl0"), AF.Identity, -M / 2, -1.0)
+    act((T.c3[:, :, 16], ["cnt0"], 8, "arB"), b("jL"), AF.Identity, -128.0)
+    ts(b("lz"), b("pc", 0, 2), 17.0, OP.mult, 15.0, OP.add)
+    for k in range(2):
+        ms((T["r3%d" % k][:, :, 16], ["rowu%dz" % k], 8, "arU"), 65535)
+        if ES[k] < 8:
+            ms((T["e4%d" % k][:, ES[k]:8, :, 16], pk("E%d" % k, ES[k], 8 - ES[k]), 64 - 8 * ES[k], "arB"), 0.0)
+        fill(b("RY%d" % k, key=["RY%d" % k, "RY%dt" % k]), 2 ** 23)
+        fill(b("RY%d" % k, 0, 136, 17), -2 ** 23)
     cp(b("tu"), b("tp"))
     cp(b("topf"), b("tp"))
     for h in range(4):
-        cp(b("C", 256 * h, 256 * h + 256, key="Ck%d" % h), b("KI", 256 * h, 256 * h + 256))
-    cp(b("thf", p1=8), b("thi", p1=8))
+        o, a = b("C", 256 * h, 256 * h + 256, key="Ck%d" % h), b("KI", 256 * h, 256 * h + 256)
+        if CKQ[h] == "g":
+            asel(o, a, [[0, 256]], OP.is_ge, 0.0, 0, 0)
+        else:
+            cp(o, a)
+    ts(b("thf", p1=8), b("thi", p1=8), KEY, OP.mult)
     asel(b("thx", p1=8), b("ones", 0, 128, 1, 8), [[1, 128]], OP.is_ge, 0.0, 0, -16)
-    asel(b("es", p1=8), b("thx", p1=8), [[-1, 128]], OP.is_ge, 0.0, 15, 16)
-    act(b("es", p1=8), b("es", p1=8), AF.Copy, 0.0, KEY)
-    mms(b("pb6", 384, 512), [(b("I"), b("emc")), (b("es", p1=8), b("thf", p1=8))])
+    asel(b("ad", p1=8), b("thx", p1=8), [[-1, 128]], OP.is_ge, 0.0, 15, 16)
+    mms(b("pb6", 384, 512), [(b("I"), b("emc")), (b("ad", p1=8), b("thf", p1=8))])
     scan(b("thx"), b("RM"), b("pb6", 384, 512), OP.max, OP.min)
-    act(b("lim"), b("thx"), AF.Identity, 64 * UNIT)
-    act(b("lim4"), ind(b("lim"), b("lF")), AF.Copy)
+    act(b("lim", 15, 128, 16), b("thx", 15, 128, 16), AF.Identity, 48 * UNIT)
+    act(b("lim4"), ind(b("thx"), b("lF")), AF.Identity, 48 * UNIT)
 
-    def x_forms(share):
-        act(b("xP"), ind(b("xb"), b("lperm")), AF.Copy)
+    def x_forms(share, of):
+        act(b("xP"), ind(b(of), b("lperm")), AF.Abs)
         for k in range(16):
-            o = b("xrep", k, 2048, 16, key="xr%d" % k)
-            if share[k] == "s":
-                act(o, b("xP"), AF.Copy)
-            elif share[k] == "g":
-                asel(o, b("xP"), [[0, 128]], OP.is_ge, 0.0, 0, 0)
-            else:
-                cp(o, b("xP"))
-        act(b("xd"), ind(b("AN", 0, 384, key=["Mb", "xb", "ANz"]), b("lxd")), AF.Copy)
-        if not MBS:
-            act(b("xm"), b("xb"), AF.Identity, -MAGIC)
-        act(b("xn"), b("xb"), AF.Copy, 0.0, -1.0)
+            copy(share[k], b("xrep", k, 2048, 16, key="xr%d" % k), b("xP"))
+        act(b("xm"), b("xb"), AF.Identity, -MAGIC)
+        act(b("xn", 0, 128), b("xb"), AF.Copy, 0.0, -1.0)
+        act((T.xd[:], ["xd"], 128, "arB"), b("xb"), AF.Copy, 0.0, -1.0)
+        for hs in ([0, 1],) if parts(P1[0], True) == parts(P1[1], True) else ([0], [1]):
+            raw = parts(P1[hs[0]], True)
+            if raw:
+                o = (T.xd[:, HC * hs[0]:HC * hs[-1] + HC, raw[0]:raw[-1] + 1], ["xd"], 32, "arB")
+                act(o, o, AF.Copy, 0.0, 2.0)
 
-    KB2 = ("pb0", "pb1") if NH == 2 else ("pb1",)
     KB = ("pb0", "pb1")
 
     def rows(out, s, nodes):
         if s == 0:
-            cp(out, ind(Cw(s), nodes))
+            cp(out, ind(b("KI", 0, V0), nodes))
         else:
             act(out, ind(Cw(s), nodes), AF.Copy)
 
@@ -614,19 +676,22 @@ def rank_program(g, core, T, topo):
 
     def sums(h, o0, p0, n, m="B", of="Dab"):
         for p in range(p0, p0 + n):
-            add(b((KB2 if o0 else KB)[h], o0, o0 + HW), lhs(p, m), piece(of, h, p, 1))
+            add(b(KB[h], o0, o0 + HW), lhs(p, m), piece(of, h, p, 1))
+            if JOIN and (p - p0) % JOIN == JOIN - 1 or p == p0 + n - 1:
+                join((p - p0) % JOIN + 1 if JOIN else 1)
 
-    def sweep(pieces, h, lists, into, o0):
+    def sweep(s, pieces, h, lists, into, o0):
         p0 = 0
         for n, bank in pieces:
             d, x = piece(into, h, p0, n), piece("xrep", h, p0, n)
             if bank:
-                act(d, ind(Aw, lst(lists, h, p0, n)), AF.Copy)
+                act(d, ind(Aw(s), lst(lists, h, p0, n)), AF.Copy)
                 inturn("sg", STAG[1])
-                mms(b(bank, 0, HW * n), [(b("nI"), x), (b("I"), d)])
-                d = b(bank, 0, HW * n)
+                o = HW * (p0 - parts(pieces, True)[0])
+                mms(b(bank, o, o + HW * n), [(b("nI"), x), (b("I"), d)])
+                d = b(bank, o, o + HW * n)
             else:
-                tt(d, ind(Aw, lst(lists, h, p0, n)), x, OP.subtract)
+                tt(d, ind(Aw(s), lst(lists, h, p0, n)), x, OP.subtract)
                 inturn("vg", STAG[0])
             act(piece("Dab", h, p0, n), d, AF.Abs)
             inturn("sa", STAG[2])
@@ -639,7 +704,7 @@ def rank_program(g, core, T, topo):
             a, o, l = piece("ag", h, p0, n), piece("Dab", h, p0, n), b("plist", HW * h + HC * p0, HW * h + HC * (p0 + n))
             if bank:
                 x = piece("D", h, p0, n)
-                act(x, ind(b("xb"), l), AF.Copy)
+                act(x, ind(b("hz"), l), AF.Abs)
                 mms(b(bank, 0, HW * n), [(b("I"), a), (b("nI"), x)])
                 act(o, b(bank, 0, HW * n), AF.Abs)
                 sums(h, 0, p0, n)
@@ -650,43 +715,43 @@ def rank_program(g, core, T, topo):
                 sums(h, 0, p0, n, "B2")
             p0 += n
 
-    def firsts(lists, node, on, bank, z, u, out, top=WIN):
-        nodes = ind(b("iot", 0, top, key=pk("iot", 0, -(-top // 128))), lists)
+    def emp(a, z):
+        return (T.em3[:, a // 16:z // 16, 0:16], ["emp"], z - a, "arB")
+
+    def both(nm):
+        return [nm + "0", nm + "1"]
+
+    def lanes(split):
+        for hs in ([0], [1]) if split else ([0, 1],):
+            a, z = HW * hs[0], HW * hs[-1] + HW
+            own = lambda nm, o=0, key=None, hs=hs, a=a, z=z: b(nm, o + a, o + z, key=[(key or nm) + str(h) for h in hs])
+            yield hs, a, z, own, lambda nm, o=0, key=None, p1=128, a=a, z=z: b(nm, o + a, o + z, p1=p1, key=key)
+
+    def firsts(lists, node, off, on, bank, z, out, top):
         k = int(z == "zb")
-        rw, E = ("rowu" if ROWU[k] else "row") + str(k), "E" + str(k)
-        if D3:
-            R3, E4, rz = T["r3%d" % k], T["e4%d" % k], "RY%d" % k
-            act(b("row" + str(k)), nodes, AF.Copy)
-            cp((R3[:, :, 0:16], [rw], 128, "arU"), b("row" + str(k)))
-            act(b(rz, 16, 136, 17, key=rz + "t"), node(0, 8), AF.Identity, 128.0)
-            begin(b(bank, 0, 136), b("I"), (T.c3[:], ["cnt0"], 136, "arB"))
-            for c in range(8):
-                key = E + str(c)
-                ts((E4[:, c, 0:8 - c, :], [key], 136 - 17 * c, "arB"), (R3[:, c:8, :], [rw, rw + "z"], 136 - 17 * c, "arU"), node(c, c + 1),
-                   OP.is_equal, on(c), OP.mult)
-                if c < 7:
-                    add(b(bank, 17 * c + 17, 136), b("lo"), (E4[:, c, 1:8 - c, :], [key], 119 - 17 * c, "arB"))
-            add(b(bank, 0, 136), b("ld"), (E4[:, :, 0, :], pk(E, 0, 8), 136, "arB"))
-            scan(b(z), b(rz, key=[rz, rz + "t"]), b(bank, 0, 136), OP.min, OP.max)
-            cp(b(out), b(z, 16, 136, 17))
-            return
-        if ROWU[k] == 2:
-            act(b("row" + str(k)), nodes, AF.Copy)
-            cp(b(rw), b("row" + str(k)))
-        elif ROWU[k]:
-            cp(b(rw), nodes)
-        else:
-            act(b(rw), nodes, AF.Copy)
-        begin(b(bank, 0, 128), b("I"), b("cnt0"))
+        rw, E, R3, E4, rz = "rowu" + str(k), "E" + str(k), T["r3%d" % k], T["e4%d" % k], "RY%d" % k
+        act(b("row" + str(k)), ind(b("iot", 0, top, key=pk("iot", 0, -(-top // 128))), lists), AF.Copy)
+        cp((R3[:, :, 0:16], [rw], 128, "arU"), b("row" + str(k)))
+        copy(GQ[0], b(rz, 16, 136, 17, key=rz + "t"), node(0, 8))
+        begin(b(bank, 0, 136), b("I"), (T.c3[:], ["cnt0"], 136, "arB"))
+        if not k:
+            add(b(bank, 0, 136), b("bones"), (T.em3[:], ["emp", "empz"], 136, "arB"))
+        if ES[k] < 8:
+            act(b("neg%d" % k), node(0, 8), AF.Copy, 0.0, -1.0)
         for c in range(8):
-            e0, key = 128 * c, E + str(c)
-            ts(b(E, e0 + 16 * c, e0 + 128, key=key), b(rw, 16 * c, 128), node(c, c + 1), OP.is_equal, on(c), OP.mult)
-            add(b(bank, 16 * c, 16 * c + 16), b("ld"), b(E, e0 + 16 * c, e0 + 16 * c + 16, key=key))
+            key = E + str(c)
+            if c < ES[k]:
+                ts((E4[:, c, 0:8 - c, :], [key], 136 - 17 * c, "arB"), (R3[:, c:8, :], [rw, rw + "z"], 136 - 17 * c, "arU"), node(c, c + 1),
+                   OP.is_equal, off(c), OP.is_gt)
+            else:
+                far = b("far%d" % k, 64 * (c % 4), 64 * (c % 4) + 128 - 16 * c, key="far%d%d" % (k, c))
+                act(far, b("row" + str(k), 16 * c, 128), AF.Abs, b("neg%d" % k, c, c + 1))
+                act((E4[:, c, 0:8 - c, 0:16], [key], 128 - 16 * c, "arB"), far, AF.Relu, on(c), -1.0)
             if c < 7:
-                add(b(bank, 16 * c + 16, 128), b("lo"), b(E, e0 + 16 * c + 16, e0 + 128, key=key))
-        scan(b(z, 0, 128), b("RZ"), b(bank, 0, 128), OP.min, OP.max)
-        tt(b(u), b(z, 15, 128, 16), node(0, 8), OP.min)
-        ts(b(out), b(u), 128.0, OP.add)
+                add(b(bank, 17 * c + 17, 136), b("lo"), (E4[:, c, 1:8 - c, :], [key], 119 - 17 * c, "arB"))
+        add(b(bank, 0, 136), b("ld"), (E4[:, :, 0, :], pk(E, 0, 8), 136, "arB"))
+        scan(b(z), b(rz, key=[rz, rz + "t"]), b(bank, 0, 136), OP.min, OP.max)
+        ts(b(out), b(z, 16, 136, 17), 128.0, OP.add)
 
     def lower(o0, f):
         scan(b("cum"), b("one8"), f, OP.mult, OP.add)
@@ -695,14 +760,24 @@ def rank_program(g, core, T, topo):
     def send(s):
         h = hops(T, topo, rank, s)
         m = "msg%d" % s
-        f, o = b("fl%d" % (s % ST), 0, 8), b("pb2", 176, 184)
-        begin(o, b("I"), b("cj"))
-        add(o, b("lt"), f)
-        lower(176, f)
-        tt(b("fw"), f, b("cj"), OP.mult)
-        add(o, b("nI"), b("fw"))
-        ts(b("posu"), o, -1.0 / M, OP.mult)
-        scatter(b(m), b("posu"), b("xn"))
+        f, o = b("fl%d" % (s % ST), 16, 24), b("pb2", 176, 184)
+        if PULL[s]:
+            cp(b("fu"), f)
+            act(b("frow"), ind(b("iot", 0, 16, key="iot0"), b("fu")), AF.Copy)
+            scan(b("crow"), b("ones", 0, 128), b("frow"), OP.mult, OP.add, -0.5)
+            for k in range(2):
+                op("s", lambda e, k=k: e.activation(b("msk")[0], b("crow")[0], AF.Sign, bias=b("jL", k, k + 1)[0], scale=-1.0,
+                                                    accum_out=b("inv", k, k + 1)[0]), ["crow", "jL"], ["msk", "inv%d" % k], 152)
+            ts(b("ivu"), b("inv", key=["inv0", "inv1"]), 0.5, OP.mult, 64.0, OP.add)
+            act(b(m, 0, CAP), ind(b("xn", key=["xn", "xnz"]), b("ivu")), AF.Copy)
+        else:
+            begin(o, b("I"), b("cj"))
+            add(o, b("lt"), f)
+            lower(176, f)
+            tt(b("fw"), f, b("cj"), OP.mult)
+            add(o, b("nI"), b("fw"))
+            ts(b("posu"), o, -1.0 / M, OP.mult)
+            scatter(b(m), b("posu"), b("xn", 0, 128))
         n = engines_of(topo, core, h[1])
         rid, pid = topo.addr(h[1], core)
         if len(h) == 3:
@@ -712,36 +787,39 @@ def rank_program(g, core, T, topo):
         op("g", lambda e: e.remote_dma(to, T[m][:, 0:CAP], sem, T.sem["ls%d" % s], pid, rid, emask(topo, core, h[1], n)),
            [m], ["come%d_%d" % (s // ST, s % ST)], 120, TRIP[s], "remote%d" % s)
 
+    def nodes(t):
+        return (lambda a, z: b("topf", a, z)) if t == 0 else (lambda a, z: b("s2", 3 + 4 * a, 4 * z, 4))
+
     def front(s):
         t = s % ST
         vu = b("tu") if t == 0 else b("lu", 0, 8)
-        vf = (lambda a, z: b("topf", a, z)) if t == 0 else (lambda a, z: b("s2", 1 + 2 * a, 1 + 2 * z, 2))
-        rows(b("cvf"), s, vu)
-        if CVS[0]:
-            act(b("cvp"), ind(b("cvf"), b("lperm")), AF.Copy)
-            ts(b("cvu", key=pk("cvu", 0, NH)), b("cvp"), float(E1), OP.min)
-        else:
-            ts(b("cvu", key=pk("cvu", 0, NH)), ind(b("cvf"), b("lperm")), float(E1), OP.min)
-        mm(b("pb2", 0, 160), b("dm"), b("RW", 0, 160, key=["RWa", "cvf", "rowM"]))
+        vf = nodes(t)
+        for hs, a, z, own, all_ in lanes(SPLIT[5] and t):
+            rows(own("cvf"), s, b("tu" if t == 0 else "lu", a // 16, z // 16))
+        for hs, a, z, own, all_ in lanes(SPLIT[6] and t):
+            ts(own("cvu"), ind(own("cvf"), b("lperm", 0, (z - a) // 16)), float(V0 + L * s), OP.min)
+        cvf = b("cvf", key=both("cvf"))
+        mm(b("pb2", 16, 144), b("dm"), cvf)
         turn(b("tr", 0, 128, key="tra"), b("pb2", 16, 144))
         turn(b("tr", 128, 288, key="trb"), b("pb2", 0, 160))
-        act(b("dl"), ind(b("tr", key=["tra", "trb"]), b("lsel")), AF.Copy)
-        act(b("emp"), b("cvf"), AF.Relu, -4094.0)
-        if RMT:
-            for p in range(16):
-                mm(b("pb2", 160, 168), lhs(p), b("emp", p, 128, 16), p == 0, p == 15)
-            act(b("cB"), b("pb2", 160, 168), AF.Sign)
-            act(b("coef", 8, 16, key="coefb"), b("cB"), AF.Copy, 0.0, 256.0)
-            act(b("cB2"), b("cB"), AF.Copy, 0.0, 4 * M)
-            tt(b("no", 15, 128, 16), b("lim", 15, 128, 16), b("cB2"), OP.max)
+        act(b("dl"), ind(b("tr", key=["tra", "trb"]), b("lsel")), AF.Copy, 0.0, 1 / M)
+        act(emp(0, 128), cvf, AF.Relu, -65.0 * 4094, 65.0)
         nrow = (b("nr2", 128 * s, 128 * s + 128, 1, 2, key="n%d" % s), b("nr2", 512, 640, 1, 2, key="jr2"))
-        mms(b("pb3", 144, 272), [nrow, (b("nl8"), b("emp"))])
-        tt(b("RW", 272, 400, key="rowN"), b("cvf"), b("pb3", 144, 272), OP.min)
+        mms(b("pb3", 144, 272), [nrow, (b("nl8"), emp(0, 128))])
+        tt(b("RW", 272, 400, key="rowN"), cvf, b("pb3", 144, 272), OP.min)
         if s != 2:
-            firsts(vu, vf, lambda c: b("one8" if t == 0 else "nonr", c, c + 1), "pb3", "zv", "uv", "uvu%d" % t, V0 + L * s)
-            tt(b("LA%d" % t), ind(b("zv", 0, 136 if D3 else 128), b("lz" if D3 else "lF")), b("lim4"), OP.min)
-        tt(b("coef", 16, 24, key="coefc"), b("nL", 8 * s, 8 * s + 8, key="nL%d" % s), vf(0, 8), OP.subtract)
-        act(b("d1", 1, 16, 2, key="d1b"), vf(0, 8), AF.Copy)
+            if t and ES[0] < 8:
+                act(b("nonr"), b("fl0", 24, 32), AF.Identity, 1.0, -1.0)
+            firsts(vu, vf, lambda c: b("fl0", 24 + c, 25 + c) if t else 0.0, lambda c: b("nonr", c, c + 1) if t else 1.0, "pb3", "zv", "uvu%d" % t, V0 + L * s)
+            tt(b("LA%d" % t), ind(b("zv"), b("lz")), b("lim4"), OP.min)
+        else:
+            mms(b("pb3", 0, 136), [(b("I"), (T.c3[:], ["cnt0"], 136, "arB")), (b("bones"), (T.em3[:], ["emp", "empz"], 136, "arB"))])
+            scan(b("zv"), b("RY0", key=["RY0", "RY0t"]), b("pb3", 0, 136), OP.min, OP.max)
+        full = -M / 2 if s == 2 else M / 2
+        act(b("room", 0, 8, key="room0"), b("zv", 15, 136, 17), AF.Relu, 1.0 + M * full, -M)
+        act(b("room", 8, 16, key="room1"), b("zv", 15, 136, 17), AF.Sign, -full)
+        tt(b("d1", 0, 32, 4, key="d1a"), vf(0, 8), b("nL", 8 * s, 8 * s + 8), OP.subtract)
+        act(b("d1", 1, 32, 4, key="d1b"), b("d1", 0, 32, 4, key="d1a"), AF.Copy, 0.0, -1.0)
         return nrow
 
     def step(s, nrow):
@@ -750,125 +828,104 @@ def rank_program(g, core, T, topo):
         bf = lambda a, z: b("pay", 15 + 16 * a, 16 * z, 16, key=["pay0", "pay1"])
         for h in range(NH):
             K1 = b(KB[h], 0, HW)
-            begin(K1, row(RU), row(JROW, HW * h, HW * h + HW))
+            begin(K1, b("kl", p1=33, key=["kl", "klh"]), b("kr", 0, HW, p1=33, key=["kr", "krh"]))
             if s == 2:
                 sweep_arrived(h)
             else:
-                sweep(P1[h], h, "cvu", "D", 0)
+                sweep(s, P1[h], h, "cvu", "D", 0)
             half = lambda nm, a=0, z=HW: b(nm, HW * h + a, HW * h + z, key=nm + str(h))
             r = half("r1")
             scan(r, b("RM", 0, HW), K1, OP.max, OP.min)
             tt(half("e"), r, K1, OP.not_equal)
             scan(half("pay"), half("e"), b("dl", HW * h, HW * h + HW), OP.mult, OP.add)
             bu = b("bu", HC * h, HC * h + HC, key="bu%d" % h)
-            ts(bu, b("pay", HW * h + 15, HW * h + HW, 16, key="pay%d" % h), float(E1), OP.min)
-            rows(half("dvf"), 1, bu)
-            if CVS[1]:
-                act(half("dvp"), ind(half("dvf"), b("lperm", 0, HC)), AF.Copy)
-                ts(half("dvu"), half("dvp"), float(E1), OP.min)
-            else:
-                ts(half("dvu"), ind(half("dvf"), b("lperm", 0, HC)), float(E1), OP.min)
-            tt(half("cand", 1, HW), half("r1", 0, HW - 1), b(KB[h], 1, HW), OP.max)
-            scan(half("r2"), b("RM2", 0, HW), b("cand", HW * h, HW * h + HW, key=["cand%d" % h, "candz"]), OP.max, OP.min)
-            if not RMT:
-                scan(half("rm"), b("RN", 0, HW), K1, OP.min, OP.max)
+            ts(bu, b("pay", HW * h + 15, HW * h + HW, 16, key="pay%d" % h), float(n0), OP.min)
+            act(half("dvf"), ind(Cw(s), bu), AF.Copy)
+            ts(half("dvu"), ind(half("dvf"), b("lperm", 0, HC)), float(n0), OP.min)
+            scan(b("r2", 192 * h + 1, 192 * h + HW, key="r2%d" % h), b(KB[h], 1, HW), half("r1", 0, HW - 1), OP.min, OP.max, BIG)
         r1 = ["r10", "r11"]
-        ts(b("dec"), b("RX", 15, 256, 16, key=r1 + ["r20", "r21"]), 1 / UNIT, OP.mult)
+        bare, bu, tab = "ag" if s == 2 else "D", b("bu", key=["bu0", "bu1"]), b("tab", key=["tab"] + pk("tab", 1, 3))
+        for hs, a, z, own, all_ in lanes(SPLIT[0]):
+            keys = [nm + str(h) for nm in ("r1", "r2") for h in hs]
+            half = lambda nm: b(nm, a // 8, z // 8, key=[nm + str(h) for h in hs])
+            ts(half("dec"), b("RX", 2 * a + 15, 2 * z, 16, key=keys), 1 / UNIT, OP.mult)
+            ts(half("dk"), half("dec"), HW - 1, OP.bitwise_and)
+            ts(half("du"), half("dk"), b("pH"), OP.add)
         if s == 2:
-            ps = parts(P1X[0], False)
-            for p in ps:
-                mm(b("pb2", 168, 176), lhs(p), b("xb", p, 128, 16), p == ps[0], p == ps[-1])
-            tt(b("r1", 15, 128, 16, key=r1), b("r1", 15, 128, 16, key=r1), b("pb2", 168, 176), OP.subtract)
-        ts(b("dk"), b("dec"), 127, OP.bitwise_and)
+            mms(b("pb6", 384, 512), [(b("I"), b("cl0")), (b("bx"), b("xb"))])
+            scan(b("thx"), b("RM"), b("pb6", 384, 512), OP.max, OP.min)
+            tt(b("r1", 15, 128, 16, key=r1), b("r1", 15, 128, 16, key=r1), b("thx", 15, 128, 16), OP.subtract)
+        for hs, a, z, own, all_ in lanes(SPLIT[1]):
+            act(own("ab"), ind(Aw(s), b("bu", a // 16, z // 16, key=["bu%d" % h for h in hs])), AF.Identity, -4.0)
         for h in range(NH):
-            ts(b("du", HC * h, HC * h + HC, key="du%d" % h), b("dk", HC * h, HC * h + HC), b("pH", h, h + 1, key="pH%d" % h), OP.add)
-        cp(b("ku"), b("dk"))
-        bare = "ag" if s == 2 else "D"
-        bu = b("bu", key=["bu0", "bu1"])
-        act(b("ab"), ind(Aw, bu), AF.Copy)
-        act(b("dq"), ind(b(bare, key=pk(bare, 0, 32)), b("du", key=["du0", "du1"])), AF.Copy)
-        oq, nb = b("oh", 0, 128, key="oq"), b("oh", 128, 256, key="nb")
-        act(oq, ind(b("tab"), b("ku", 0, 8)), AF.Copy)
-        act(nb, ind(b("tab"), b("ku", 8, 16)), AF.Identity, 65.0, -1.0)
-        o = b("pb6", 0, 128)
-        begin(o, row(ONE), row(RH))
-        for l, r in [("hI", "ab"), ("hI", "dq")] + ([("nI", "xb")] if s == 2 else [("nhI", "xb"), ("nhI", "xd")]):
-            add(o, b(l), b(r))
-        close(o, row(ONE), row(RMG))
-        act(b("absM"), o, AF.Abs, -MAGIC)
-        mms(b("pb6", 384, 512), [(b("I"), b("emc")), (b("bones"), b("absM"))])
-        scan(b("es"), b("RM"), b("pb6", 384, 512), OP.max, OP.min)
-        if MBS:
-            o = b("pb6", 128, 256)
-            begin(o, row(ONE), row(RH))
-            for l, r in [("hI", "ab"), ("hI", "dq")] + ([] if s == 2 else [("hI", "xb"), ("nhI", "xd")]):
-                add(o, b(l), b(r))
-            close(o, row(ONE), row(RMG))
-            act(b("AN", 128, 256, key="Mb"), o, AF.Identity, -MAGIC)
-        else:
-            tt(b("AN", 128, 256, key="Mb"), b("xm"), o, OP.add)
-        mms(b("pb2", 384, 512), [(b("I"), b("xb")), (b("nI"), b("ab"))])
-        if CLS:
-            act(b("cl"), b("pb2", 384, 512), AF.Relu, 4.0)
-            act(b("cl"), b("cl"), AF.Relu, 8.0, -1.0)
-            act(b("cl"), b("cl"), AF.Identity, 4.0, -1.0)
-        else:
-            ts(b("cl"), b("pb2", 384, 512), -4.0, OP.max, 4.0, OP.min)
+            lq = b("du", 12 * h, 12 * h + HC, key="du%d" % h)
+            act(b("dq", HW * h, HW * h + HW, key="dq%d" % h), ind(piece(bare, h, 0, 16), lq), AF.Copy)
+            act(b("oq", HW * h, HW * h + HW, key="oq%d" % h), ind(tab, lq), AF.Copy, 0.0, 2.0)
+        for hs, a, z, own, all_ in lanes(SPLIT[2]):
+            act(own("nb"), ind(tab, b("du", HC + a // 16, HC + z // 16, key=["du%d" % h for h in hs])), AF.Identity, 65.0, -1.0)
+        for hs, a, z, own, all_ in lanes(SPLIT[3]):
+            o = b(MB[hs[0]], a, z)
+            begin(o, row(ONE), row(RH, a, z))
+            for l, r in [("hI", own("ab")), ("hI", own("dq")), ("nI", all_("xb")) if s == 2 else ("hI", (T.xd[:, a // 16:z // 16, :], ["xd"], z - a, "arB"))]:
+                add(o, b(l), r)
+            close(o, row(ONE), row(RMG, a, z))
+            act(own("absM"), o, AF.Abs, -MAGIC)
+            mms(b(EB, 384 + a, 384 + z), [(b("I"), all_("emc")), (b("bones"), own("absM"))])
+            scan(own("es"), b("RM", a, z), b(EB, 384 + a, 384 + z), OP.max, OP.min)
+            tt(own("AN", 128, "Mb"), all_("xm"), o, OP.add)
+        mms(b("pb2", 384, 512), [(b("I"), b("xb")), (b("nI"), b("ab", key=both("ab")))])
+        act(b("cl"), b("pb2", 384, 512), AF.Relu, 8.0, -1.0)
+        act(b("cl"), b("cl"), AF.Relu, 8.0, -1.0)
         for h in range(NH):
-            begin(b(KB2[h], HW, 2 * HW), row(RU), row(R160, 0, HW))
-            sweep(P2[h], h, "dvu", "D" if s == 2 else "ag", HW)
-        if not RMT:
-            ts(b("cB"), b("rm", 15, 128, 16, key=["rm0", "rm1"]), 2.0, OP.is_ge, 8.0, OP.mult)
-            tt(b("no", 15, 128, 16), b("lim", 15, 128, 16), b("cB"), OP.max)
-            act(b("coef", 8, 16, key="coefb"), b("cB"), AF.Copy, 0.0, 32.0)
-        tt(b("coef", 0, 8, key="coefa"), bf(0, 8), b("d1", 1, 16, 2, key="d1b"), OP.subtract)
-        tt(b("U4"), ind(b("r1", key=r1), b("lF")), b("LA%d" % t), OP.min)
-        tt(b("TT", 0, 32, key="Tt"), ind(b("es"), b("lF")), b("U4"), OP.min)
-        tt(b("FL"), b("RX", 143, 640, 16, key=r1 + ["lim", "es", "no"]), b("TT", 0, 32, key="Tt"), OP.is_equal)
-        if NFV:
-            tt(b("nfl"), b("RX", 143, 640, 16, key=r1 + ["lim", "es", "no"]), b("TT", 0, 32, key="Tt"), OP.not_equal)
-        else:
-            act(b("nfl"), b("FL"), AF.Identity, 1.0, -1.0)
-        tt(b("TT", 32, 64, key="TH"), b("TT", 0, 32, key="Tt"), b("nfl"), OP.max)
-        tt(b("prod", 0, 24), b("FL", 0, 24), b("coef", key=["coefa", "coefb", "coefc"]), OP.mult)
-        act(b("prod", 24, 32, key="proda"), b("FL", 16, 24), AF.Identity, -384.0, 128.0)
-        tt(b("d0", 1, 32, 2, key="d0b"), b("prod", 0, 16), b("prod", 16, 32, key=["prod", "proda"]), OP.add)
-        mms(b("pb5", 0, 128), [(row(R128), row(R65)), (b("nI128"), nb)])
-        mms(b("pb5", 128, 256), [(b("I63"), nb), (b("nI63"), oq)])
-        mms(b("pb5", 256, 384), [nrow, (b("nI128"), nb), (b("I256"), oq)])
-        mms(b("pb3", 272, 400), [(b("nI8"), b("emp")), (b("idf"), b("dvf", key=["dvf0", "dvf1"])), (b("I128"), nb)])
-        tt(b("w3"), b("cvf"), b("pb5", 0, 128), OP.max)
-        tt(b("CN", 128, 256), b("cvf"), b("pb5", 128, 256), OP.max)
-        tt(b("RW", 144, 272, key="rowM"), b("cvf"), b("pb5", 256, 384), OP.max)
-        tt(b("RW", 400, 528, key="rsp"), b("w3"), b("pb3", 272, 400), OP.min)
+            begin(b(KB[h], HW, 2 * HW), b("kl", p1=33, key=["kl", "klh"]), b("kr", HW, 128, p1=33, key=["kr", "krh"]))
+            sweep(s, P2[h], h, "dvu", "D" if s == 2 else "ag", HW)
+        tt(b("RX", 207, 448, 16, key=["ro", "r21"]), b("lim4", 0, 16), b("room", key=["room0", "room1"]), OP.add)
+        tt(b("d1", 2, 32, 4, key="d1c"), nodes(t)(0, 8), bf(0, 8), OP.subtract)
+        copy(GQ[1], b("d1", 3, 32, 4, key="d1d"), bf(0, 8))
+        U = b("BD", 2, 128, 4, key="BDu")
+        tt(U, ind(b("r1", key=r1), b("lF")), b("LA%d" % t), OP.min)
+        tt(b("nfl"), b("RX", 79, 576, 16, key=r1 + ["lim", "ro", "r21"]), U, OP.not_equal)
+        tt(b("BD", 3, 128, 4, key="BDb"), U, b("nfl"), OP.max)
+        act(b("BD", 1, 64, 4, key="BDe"), ind(b("es", key=both("es")), b("lF", 0, 1)), AF.Copy)
+        for hs, a, z, own, all_ in lanes(SPLIT[4]):
+            p5, p3 = (lambda o: b(RB[hs[0]][0], o + a, o + z)), b(RB[hs[0]][1], 272 + a, 272 + z)
+            mms(p5(128), [(b("I63"), own("nb")), (b("nI63"), own("oq"))])
+            mms(p5(256), [(nrow[0], all_("nr2", 512, "jr2", 2)), (b("nI63"), own("nb")), (b("I63"), own("oq"))])
+            mms(p3, [(b("nI63"), emp(a, z)), (b("I63"), own("nb"))])
+            tt(own("CN", 128), own("cvf"), p5(128), OP.max)
+            tt(own("RW", 144, "rowM"), own("cvf"), p5(256), OP.max)
+            tt(own("w3"), own("cvf"), p3, OP.min)
+            tt(p3, own("dvf"), p3, OP.subtract)
+            tt(own("RW", 400, "rsp"), own("w3"), p3, OP.max)
         for h in range(NH):
-            scan(b("fs", HW * h, HW * h + HW, key="fs%d" % h), b("RF", 0, HW), b(KB2[h], HW, 2 * HW), OP.max, OP.min)
-        fs = ["fs0", "fs1"]
-        tt(b("d1", 0, 64, 2, key="d1s"), ind(b("fs", key=fs), b("lF")), b("TT", 16, 48, key=["Tt", "TH"]), OP.is_gt)
-        tt(b("fl%d" % t, 0, 8), b("fs", 15, 128, 16, key=fs), b("TT", 56, 64, key="TH"), OP.is_gt)
-        scan(b("s2"), b("d0", key=["d0", "d0b"]), b("d1", 0, 32, key=["d1a", "d1b", "d1s"]), OP.mult, OP.add)
-        cp(b("lu"), b("s2", 1, 32, 2))
-        if t == 0:
-            act(b("nonr"), b("d1", 48, 64, 2, key="d1s"), AF.Identity, 1.0, -1.0)
-        act(b("rpre"), ind(b("RW", 16, 528, key=["cvf", "rowM", "rowN", "rsp"]), b("lu", 8, 16)), AF.Relu, 4095.0, -1.0)
+            scan(b("mf", HW * h, HW * h + HW, key="mf%d" % h), b("es", HW * h, HW * h + HW, key="es%d" % h), b(KB[h], HW, 2 * HW), OP.min, OP.min, BIG)
+        mf = b("mf", key=["mf0", "mf1"])
+        tt(b("fg"), ind(mf, b("lG")), b("BD", 0, 64, key=["BDz", "BDe", "BDu", "BDb"]), OP.is_lt)
+        if ES[1] < 8:
+            tt(b("fl%d" % t), ind(mf, b("lF")), b("BD", 3, 128, 4, key="BDb"), OP.is_gt)
+        else:
+            tt(b("fl%d" % t, 16, 32), ind(mf, b("lF", 0, 1)), b("BD", 67, 128, 4, key="BDb"), OP.is_gt)
+        scan(b("s2"), b("fg"), b("d1", key=["d1a", "d1b", "d1c", "d1d"] + pk("d1k", 0, 4)), OP.mult, OP.add)
+        cp(b("lu"), b("s2", 3, 64, 4))
+        act(b("rpre"), ind(b("RW", 16, 528, key=["rowN"] + both("cvf") + both("rowM") + both("rsp")), b("lu", 8, 16)), AF.Relu, 4095.0, -1.0)
         scatter(b("CW", 0, 128 + n0, key=["C"] + blocks("C", s) + pk("Ck", 0, 4)), b("uvu%d" % t), b("rpre"), (-1.0, 4095.0))
-        act(b("C", n0, n0 + L, key="Cb%d" % s), ind(b("CN", key=["CN", "CNz", "CNy"]), b("lu", 8, 16)), AF.Copy)
-        act(b("A", n0, n0 + L, key="Ab%d" % s), ind(b("AN", key=["Mb", "xb", "ANz", "ANy"]), b("lu", 8, 16)), AF.Copy)
-        firsts(bu, bf, lambda c: b("d1", 32 + 2 * c, 33 + 2 * c, key="d1s"), "pb7", "zb", "ub", "oAu")
-        scatter(b("AW", 0, 128 + n0, key=["A"] + blocks("A", s)), b("oAu"), b("ab"), b("cl"))
+        act(b("C", n0, n0 + L, key="Cb%d" % s), ind(b("CN", key=both("CN") + ["CNz", "CNy"]), b("lu", 8, 16)), AF.Copy)
+        act(b("A", n0, n0 + L, key="Ab%d" % s), ind(b("AN", key=both("Mb") + ["xb", "ANz", "ANy"]), b("lu", 8, 16)), AF.Copy)
+        firsts(bu, bf, lambda c: b("fg", 3 + 4 * c, 4 + 4 * c), lambda c: b("fl%d" % t, c, c + 1), "pb7", "zb", "oAu", n0 + 1)
+        scatter(b("AW", 0, 128 + n0, key=["A"] + blocks("A", s)), b("oAu"), b("ab", key=both("ab")), b("cl"))
         send(s)
 
     def round_end(s):
         cm = "come%d" % (s // ST)
-        tt(b("rest2"), b("d1", 48, 64, 2, key="d1s"), b("nonr"), OP.is_ge)
+        tt(b("rest2"), b("fl0", 24, 32), b("fl1", 24, 32), OP.max)
         begin(b("pb2", 192, 200), b("lp"), b("rest2"))
         lower(192, b("rest2"))
         act(b("nrs"), b("pb2", 192, 200), AF.Identity, 256.0, -1.0 / M)
-        act(b("absM"), ind(Aw, b("lu", 0, 8)), AF.Copy)
-        mms(b("pb6", 0, 128), [(b("nI"), b("xb")), (b("I"), b("absM"))])
+        act(b("av"), ind(Aw(s, L), b("lu", 0, 8)), AF.Copy)
+        mms(b("pb6", 0, 128), [(b("nI"), b("xb")), (b("I"), b("av"))])
         act(b("ad"), b("pb6", 0, 128), AF.Abs)
         first = b(cm, 0, CAP, key=cm + "_0")
-        op("s", lambda e: e.activation(b("msk")[0], first[0], AF.Sign, bias=NONE / 2, scale=-1.0, accum_out=b("na")[0]),
+        op("s", lambda e: e.activation(b("msk", 0, CAP)[0], first[0], AF.Sign, bias=NONE / 2, scale=-1.0, accum_out=b("na")[0]),
            first[1], ["msk", "na"], 90)
         act(b("n0"), b("na"), AF.Identity, CAP / 2, 0.5)
         act(b("cd"), b("na"), AF.Identity, CAP / 2, -0.5)
@@ -878,13 +935,13 @@ def rank_program(g, core, T, topo):
         tt(b("hz"), ind(b(cm, key=[cm + "_0", cm + "_1", cm + "z"]), b("iu")), b("ad"), OP.min)
         act(b("xb"), b("hz"), AF.Abs)
 
-    x_forms(XQ[0])
+    x_forms(XQ[0], "xb")
     nrow = front(0)
     for s in range(4):
         step(s, nrow)
         if s == 3:
-            dma("ld5", T.yc[:], b("C", 0, W)[0], ["C"] + blocks("C", 4), ["yc"], 768)
-            dma("ld6", T.ya[:], b("A", 0, W)[0], ["A"] + blocks("A", 4), ["ya"], 384)
+            dma(T.yc[:], b("C", 0, W)[0], ["C"] + blocks("C", 4), ["yc"], 768)
+            dma(T.ya[:], b("A", 0, W)[0], ["A"] + blocks("A", 4), ["ya"], 384)
         if s % ST == 1:
             round_end(s)
         if s < 3:
@@ -892,13 +949,13 @@ def rank_program(g, core, T, topo):
         if s == 1:
             for j in range(len(AGQ)):
                 n = 16 * NH // len(AGQ)
-                o, a = piece("ag", j * n // 16, j * n % 16, n), ind(Aw, lst("cvu", j * n // 16, j * n % 16, n))
+                o, a = piece("ag", j * n // 16, j * n % 16, n), ind(Aw(s + 1), lst("cvu", j * n // 16, j * n % 16, n))
                 if AGQ[j] == "s":
                     act(o, a, AF.Copy)
                 else:
                     cp(o, a)
-            x_forms(XQ[1])
-    dma("ld7", T.yx[:], b("xb")[0], ["xb"], ["yx"], 32)
+            x_forms(XQ[1], "hz")
+    dma(T.yx[:], b("xb")[0], ["xb"], ["yx"], 32, DQ[3])
 
     if "o" not in ORDER:
         ORDER["o"] = order_calls(ops)
@@ -940,8 +997,10 @@ def rank_program(g, core, T, topo):
         q, kind = o["q"], o["dma"]
         if kind is None:
             need(q, o["R"], o["W"])
-            cnt[own[q]] += 1
-            o["call"](eng[q]).then_inc(T.sem[own[q]], 1)
+            made = o["call"](eng[q])
+            for one in made if isinstance(made, list) else [made]:
+                cnt[own[q]] += 1
+                one.then_inc(T.sem[own[q]], 1)
             note(q, own[q], cnt[own[q]], know[q], o["R"], o["W"])
         elif kind[:6] == "remote":
             s = int(kind[6:])

from concourse.mybir import AluOpType as OP, ActivationFunctionType as AF

V0, L, ST, RO, CAP, NR = 1024, 128, 2, 2, 32, 8
W = V0 + RO * ST * L
BIG = float(2 ** 30)
MAGIC = float(3 * 2 ** 22)
NONE = 1000
M = float(2 ** 12)
UNIT = 2.0 ** -24
KEY = 128 * UNIT
STEP = 33
FAR = 1024.0
NH = 2
HC, HW = 8 // NH, 128 // NH
P1 = [[(4, None), (5, None), (4, bank), (3, None)] for bank in ("pb7", "pb4")]
P1X = P1
P2 = [[(3, None), (3, None), (7, "pb7"), (3, None)], [(5, None), (5, None), (4, None), (2, None)]]
AGQ = "vssvssvs"
ROUNDS, TRIES, SLACK = 6, ((80, 1000), (110, 1000), (60, 800), (150, 1200)) * 5, 800.0
CYCLE, GAT, SCA = 0.83, 1.5, 3.2
START, KIB = 1000.0, 3.9
TRIP = (10000, 3900, 7000, 3900)
WAKE = 235.0
COSTS = ((0.86, 1.2, 2.4, 290.0, 0.36), (0.92, 1.75, 4.0, 215.0, 0.34), (1.18, 1.4, 3.6, 250.0, 0.3))
CHOICE, BAR, GAIN = 3, 8, 600.0

SLOT = {}
SIZE = {"F": 0, "B": 0, "I": 0, "U": 0}


def _s(kind, **kw):
    for n, w in kw.items():
        SLOT[n] = ("ar" + kind, SIZE[kind], w)
        SIZE[kind] += (w + 15) // 16 * 16


_s("B", AW=128 + W, xrep=2048, D=2048, Dab=2048, ag=2048, AN=512, xP=128, xn=144, hz=128, nr2=640, ones=144, B=144, B2=144, nB=144,
   bones=128, lo=128, lt=128, ld=128, lp=128, nl8=128, I=128, nI=128, hI=128, I63=128, nI63=128, cr=384, kl=128, kr=128, emc=128, tab=1024,
   oq=128, nb=128, ab=128, dq=128, cl=128, cl0=128, bx=128, absM=128, av=128, fl1=32, far0=256, far1=256, rest2=8, cum=8, cj=8, fw=8,
   msk=128, frow=128, crow=128)
_s("F", CW=128 + W, iot=W, RW=544, CN=512, dm=128, RM=128, tr=288, dl=128, RX=576, es=128, e=128, pay=128, row0=128, row1=128, RY0=136, RY1=136,
   zv=136, zb=136, w3=128, rpre=128, dvf=128, mf=128, xm=128, ad=128, thf=128, thx=128, lim4=32, jL=8, topf=8, nL=32, LA0=32, LA1=32,
   BD=128, nfl=32, fg=64, d1=64, s2=64, fl0=32, neg0=8, neg1=8, nonr=8, room=16, one8=8, nrs=8, ge=8, idx=8, na=1, n0=1, cd=1, pH=1, pf=1,
   pG=1, inv=2, tmp=16, tmp2=16)
_s("I", KI=V0, tp=8, thi=128, pin=16, pa=16, pc=16, ci=128, ri=128, dec=16, dk=16, hx=128, xi=128)
_s("U", tu=8, cvu=128, dvu=128, bu=8, du=16, uvu0=8, uvu1=8, lu=16, oAu=8, posu=8, iu=8, fu=8, ivu=2, plist=128, lperm=8, lsel=8, lF=2, lG=4, lz=2)
SLOT["C"] = ("arF", SLOT["CW"][1] + 128, W)
SLOT["A"] = ("arB", SLOT["AW"][1] + 128, W)
SLOT["cvf"] = ("arF", SLOT["RW"][1] + 16, 128)
SLOT["xb"] = ("arB", SLOT["AN"][1] + 256, 128)
for _n, _o, _w in (("r2", 0, 256), ("r1", 64, 128), ("lim", 448, 128)):
    SLOT[_n] = ("arF", SLOT["RX"][1] + _o, _w)
DQ = "ssss"
EB = "pb4"
MB, RB = ("pb6", "pb6"), (("pb5", "pb3"), ("pb5", "pb3"))
ES = (8, 4)
GQ = "gg"
SPLIT = (1, 1, 1, 0, 1, 0, 0)
STAG = (1, 0, 1, 1)
IOTQ = "sssssssgggg"
XQ = ("vsvsvsvsvsvsvsvs", "gsgvgsgsgsgvgsgs")
PULL = (1, 0, 1, 0)
CKQ = "gggg"
JOIN, SEED = 3, 5

SCRATCH = {"arF": ("sbuf", [128, SIZE["F"]], "float32"), "arB": ("sbuf", [128, SIZE["B"]], "bfloat16"),
           "arI": ("sbuf", [128, SIZE["I"]], "int32"), "arU": ("sbuf", [128, SIZE["U"]], "uint16")}
for _k in range(8):
    SCRATCH["pb%d" % _k] = ("psum", [128, 512], "float32")
for _k in range(4):
    SCRATCH["msg%d" % _k] = ("sbuf", [128, 384], "bfloat16")
    SCRATCH["rl%d" % _k] = ("sbuf", [128, 32], "bfloat16")
for _k in range(2):
    SCRATCH["come%d" % _k] = ("sbuf", [128, 80], "bfloat16")
    SCRATCH["r3%d" % _k] = ("sbuf", [128, 8, 17], "uint16")
    SCRATCH["e4%d" % _k] = ("sbuf", [128, 8, 8, 17], "bfloat16")
SCRATCH["c3"] = SCRATCH["em3"] = ("sbuf", [128, 8, 17], "bfloat16")
SCRATCH["xd"] = ("sbuf", [128, 8, 16], "bfloat16")
SEMAPHORES = (["qv", "qs", "qt", "qg"] + ["in%d" % k for k in range(4)] + ["rr%d" % k for k in range(4)] + ["ls%d" % k for k in range(4)]
              + ["ld%d" % k for k in range(9)])
ORDER = {}


def emask(topo, src, dst, n):
    m = 0
    for e in topo.engines(src, dst)[:n]:
        m |= 1 << e
    return m


NE_ON, NE_OFF = 16, 8


def hops(T, topo, rank, s):
    src, dst = T.cores[rank], T.cores[(rank + 1 + s % (NR - 1)) % NR]
    if s > 0 and topo.may_write(src, dst):
        return [src, dst]
    ways = [c for c in topo.cores_of(src) if c != src and all(topo.may_write(c, d) for d in T.cores if d not in topo.cores_of(src))]
    ways.sort(key=lambda c: topo.die(c) != topo.die(src))
    return [src, ways[0], dst]


def engines_of(topo, a, b):
    return NE_ON if b in topo.cores_of(a) else NE_OFF


def relay(g, core, T, topo):
    for s in range(ST * RO):
        for rank in range(NR):
            h = hops(T, topo, rank, s)
            if len(h) == 3 and h[1] == core:
                n = engines_of(topo, h[1], h[2])
                g.wait_ge(T.sem["rr%d" % s], engines_of(topo, h[0], core))
                rid, pid = topo.addr(h[2], core)
                g.remote_dma(T["come%d" % (s // ST)][:, CAP * (s % ST):CAP * (s % ST) + CAP], T["rl%d" % s][:, 0:CAP], T.sem["in%d" % s],
                             T.sem["ls%d" % s], pid, rid, emask(topo, core, h[2], n))
    for s in range(ST * RO):
        for rank in range(NR):
            h = hops(T, topo, rank, s)
            if len(h) == 3 and h[1] == core:
                g.wait_ge(T.sem["ls%d" % s], engines_of(topo, h[1], h[2]))


def order_calls(ops):
    n = len(ops)
    wr, rd, pre, adds = {}, {}, [], {}
    for i, o in enumerate(ops):
        d = {}
        for k in o["R"] + o["W"]:
            if not o["adds"]:
                for j in adds.get(k, []):
                    d[j] = 0.0 if o["q"] == "t" else WAKE
        if o["adds"]:
            adds.setdefault(o["W"][0], []).append(i)
        for k in o["R"]:
            if k in wr:
                d[wr[k]] = WAKE
            if k[:2] == "pb":
                for j in rd.get(k, []):
                    d[j] = max(d.get(j, 0.0), WAKE if ops[j]["q"] != o["q"] else 0.0)
        for k in o["W"]:
            for j in rd.get(k, []) + ([wr[k]] if k in wr else []):
                near = ops[j]["q"] == o["q"] == "t" and j == wr.get(k)
                d[j] = max(d.get(j, 0.0), 0.0 if near else WAKE)
        for k in o["R"]:
            rd.setdefault(k, []).append(i)
        for k in o["W"]:
            if not o["adds"]:
                wr[k] = i
                rd[k] = []
                adds[k] = []
        for j in o.get("after", []):
            d.setdefault(j, 0.0)
        d.pop(i, None)
        pre.append(d)
    post = [{} for _ in range(n)]
    for i in range(n):
        for j, w in pre[i].items():
            post[j][i] = w

    def place(rank, before, back):
        busy, start, end = {}, [0.0] * n, [0.0] * n
        for i in rank:
            c, lag, row = ops[i]["c"], ops[i]["lag"], busy.setdefault(ops[i]["q"], [])
            t = max([end[j] + w for j, w in before[i].items()] + [0.0]) + (lag if back else 0.0)
            at = len(row)
            for m, (a, z) in enumerate(row):
                if z <= t:
                    continue
                if t + c <= a:
                    at = m
                    break
                t = z
            row.insert(at, (t, t + c))
            start[i], end[i] = t, t + c + (0.0 if back else lag)
        return start, end

    way, behind = [0.0] * n, {}
    for i in range(n - 1, -1, -1):
        k = ops[i]["adds"]
        if k:
            way[i] = max(way[i], behind.get(k, 0.0))
        way[i] += ops[i]["c"] + ops[i]["lag"]
        behind[k] = way[i]
        for j, w in pre[i].items():
            way[j] = max(way[j], way[i] + w)
    ORDER["dag"] = (ops, pre, post, list(way))
    best = None
    for _ in range(ROUNDS):
        start, end = place(sorted(range(n), key=lambda i: (-way[i], i)), pre, False)
        if best is None or max(end) < best[0]:
            best = (max(end), start)
        way = place(sorted(range(n), key=lambda i: (-end[i], -i)), post, True)[1]
    lag, queue = [o["lag"] for o in ops], [o["q"] for o in ops]
    costs = [([o["cs"][k] for o in ops], [[(j, m[3] if w else 0.0) for j, w in d.items()] for d in pre], m[4]) for k, m in enumerate(COSTS)]

    gives = [[[(j, m[3] if w else 0.0) for j, w in d.items()] for d in post] for m in COSTS]
    sets = range(len(COSTS))

    def ends(part, a, end, why, free):
        total, far = 0.0, []
        for k in sets:
            time, need, weight = costs[k]
            e, y0, f = end[k], why[k], dict(free[k])
            for i in part[:a]:
                f[queue[i]] = i
            f = {q: (e[i] - lag[i], i) if i >= 0 else (0.0, -1) for q, i in f.items()}
            for i in part[a:]:
                t, y = f[queue[i]]
                y = -2 - y
                for j, w in need[i]:
                    if e[j] + w >= t:
                        t, y = e[j] + w, j
                t += time[i]
                f[queue[i]], e[i], y0[i] = (t, i), t + lag[i], y
            far.append(f)
        return far

    def rests(part, rest, behind):
        for k in sets:
            time, give, r, q0 = costs[k][0], gives[k], rest[k], dict(behind[k])
            for i in reversed(part):
                t = 0.0
                for j, w in give[i]:
                    if r[j] + w > t:
                        t = r[j] + w
                t += lag[i]
                if q0[queue[i]] > t:
                    t = q0[queue[i]]
                q0[queue[i]] = r[i] = t + time[i]

    def better(order, lo, hi, tries, seed):
        end, why, rest = ([[0.0] * n for _ in sets] for _ in range(3))
        part, none = order[lo:hi], dict.fromkeys("vstgy", -1)
        ends(order[:lo], 0, end, why, [none for _ in sets])
        rests(order[hi:], rest, [dict.fromkeys("vstgy", 0.0) for _ in sets])
        first, at = dict(none), [-1] * n
        for i in order[:lo]:
            first[queue[i]] = i
        behind = [dict.fromkeys("vstgy", 0.0) for _ in sets]
        for i in reversed(order[hi:]):
            at[i] = n
            for k in sets:
                behind[k][queue[i]] = rest[k][i]
        out = [[max([w + rest[k][j] for j, w in gives[k][i] if at[j] == n] + [0.0]) if at[i] < n else 0.0 for i in range(n)] for k in sets]
        size = len(part)

        def value(a):
            free, total, tops = ends(part, a, end, why, [first for _ in sets]), 0.0, []
            for k in sets:
                e, o = end[k], out[k]
                top = max([(e[i] + o[i], i) for i in part] + [(t + behind[k][q], i) for q, (t, i) in free[k].items()])
                total += costs[k][2] * top[0]
                tops.append(top)
            return total, tops

        def through(a, z, new):
            kinds, before, after, total = {queue[i] for i in new}, {}, {}, 0.0
            for places, into in ((range(a - 1, -1, -1), before), (range(z + 1, size), after)):
                for m in places:
                    q = queue[part[m]]
                    if q in kinds and q not in into:
                        into[q] = part[m]
                        if len(into) == len(kinds):
                            break
            for k in sets:
                time, need, weight = costs[k]
                old, r, give, e, far = end[k], rest[k], gives[k], {}, tops[k][0] - GAIN
                free = {}
                for q in kinds:
                    i = before.get(q, first[q])
                    free[q] = old[i] - lag[i] if i >= 0 else 0.0
                for i in new:
                    t = free[queue[i]]
                    for j, w in need[i]:
                        y = e.get(j, old[j]) + w
                        if y > t:
                            t = y
                    free[queue[i]] = t = t + time[i]
                    e[i] = t = t + lag[i]
                    if t > far:
                        far = t
                    for j, w in give[i]:
                        if at[j] > z and t + w + r[j] > far:
                            far = t + w + r[j]
                for q in kinds:
                    far = max(far, free[q] + (r[after[q]] if q in after else behind[k][q]))
                total += weight * far
            return total

        last, tops = value(0)
        good, barred, pairs = (last, part), {}, None
        for turn in range(tries):
            if pairs is None:
                rests(part, rest, behind)
                pairs = []
                for m, i in enumerate(part):
                    at[i] = m
                for k in sets:
                    i, y0 = tops[k][1], why[k]
                    while i >= 0 and at[i] >= 0:
                        j = y0[i]
                        if j <= -2:
                            j = -2 - j
                            if at[j] >= 0:
                                pairs.append((j, i))
                        i = j
                if not pairs:
                    break
            pick = None
            for _ in range(CHOICE):
                seed = (seed * 1103515245 + 12345) % 2 ** 31
                u, v = pairs[(seed >> 8) % len(pairs)]
                if barred.get((u, v), -1) > turn:
                    continue
                a, z, early = at[u], at[v], seed >> 5 & 1
                for _ in range((0, 0, 0, 1, 2, 4)[(seed >> 20) % 6]):
                    if early:
                        a = next((m for m in range(a - 1, max(-1, a - 40), -1) if queue[part[m]] == queue[u]), a)
                    else:
                        z = next((m for m in range(z + 1, min(size, z + 40)) if queue[part[m]] == queue[u]), z)
                new, tied = part[a:z + 1], {v if early else u}
                for x in (reversed(new) if early else new):
                    if early and x in tied:
                        tied.update(pre[x])
                    elif not early and any(j in tied for j in pre[x]):
                        tied.add(x)
                if part[a if early else z] in tied:
                    continue
                new = [x for x in new if (x in tied) == early] + [x for x in new if (x in tied) != early]
                guess = through(a, z, new)
                if pick is None or guess < pick[0]:
                    pick = (guess, a, z, new, u, v)
            if pick and pick[0] <= last + SLACK * (seed >> 3 & 3) / 3 * (seed >> 12 & 3) / 3:
                guess, a, z, new, u, v = pick
                part = part[:a] + new + part[z + 1:]
                last, tops = value(a)
                barred[(v, u)], pairs = turn + BAR + (seed >> 9 & 7), None
                if last < good[0]:
                    good = (last, part)
        return order[:lo] + good[1] + order[hi:]

    def timed(order):
        end, why = ([[0.0] * n for _ in sets] for _ in range(2))
        ends(order, 0, end, why, [dict.fromkeys("vstgy", -1) for _ in sets])
        return sum(costs[k][2] * max(end[k]) for k in sets), end[0]

    order = sorted(range(n), key=lambda i: (best[1][i], i))
    for k, (width, tries) in enumerate(TRIES):
        for lo in range(-width // 2 * (k % 2), n, width):
            order = better(order, max(0, lo), min(n, lo + width), tries, 97 * k + lo + n + SEED)
        last, end = timed(order)
        at = {i: m for m, i in enumerate(order)}
        order.sort(key=lambda i: (end[i] - lag[i] - costs[0][0][i], at[i]))
        way = place(sorted(range(n), key=lambda i: (-end[i], -i)), post, True)[1]
        start, end = place(sorted(range(n), key=lambda i: (-way[i], i)), pre, False)
        other = sorted(range(n), key=lambda i: (start[i], i))
        if timed(other)[0] < last:
            order = other
        ORDER.setdefault("log", []).append(round(last))
    return order


def parts(pieces, scalar):
    return [p for j, (n, bank) in enumerate(pieces) if bool(bank) == scalar
            for p in range(sum(q[0] for q in pieces[:j]), sum(q[0] for q in pieces[:j + 1]))]


def rank_program(g, core, T, topo):
    rank = T.rank_of(core)
    if rank is None:
        relay(g, core, T, topo)
        return
    eng = {"v": g.vector, "s": g.scalar, "t": g.tensor, "g": g, "y": g.sync}
    ops, picks = [], [0, 0]

    def op(q, call, R, Wk, c, lag=0.0, dma=None, adds=None):
        cs = [c * CYCLE if dma else (c + (m[1] - GAT) * picks[0] + (m[2] - SCA) * picks[1]) * m[0] for m in COSTS]
        ops.append({"q": q, "call": call, "R": R, "W": Wk, "c": c * CYCLE, "cs": cs, "pk": list(picks), "lag": lag, "dma": dma, "adds": adds})
        picks[:] = [0, 0]

    def dma(out, in_, R, Wk, kib, q="y"):
        sem = "ld%d" % len([o for o in ops if (o["dma"] or "")[:2] == "ld"])
        if q == "y":
            op("y", lambda e: e.dma_start(out, in_), R, Wk, 60 + kib * KIB / CYCLE, START, sem)
        else:
            op(q, lambda e: e.dma_start(out, in_), R, Wk, 60, START + kib * KIB, sem)

    def b(name, c0=0, c1=None, st=1, p1=128, key=None):
        if name in SLOT:
            buf, o, w = SLOT[name]
        else:
            buf, o, w = name, 0, SCRATCH[name][1][1]
        c1 = w if c1 is None else c1
        a = T[buf][0:p1, o + c0:o + c1:st] if st != 1 else T[buf][0:p1, o + c0:o + c1]
        return (a, key if isinstance(key, list) else [key or name], (c1 - c0 + st - 1) // st, buf[:3])

    def ind(win, off):
        return (win[0].indirect(off[0]), win[1] + off[1], 16 * off[2], "ind")

    def ks(*refs):
        return [k for r in refs if isinstance(r, tuple) for k in r[1]]

    def ap(x):
        return x[0] if isinstance(x, tuple) else x

    def cyc(o, a, f=1.0):
        if a[3] == "ind":
            picks[0] = a[2]
            return 70 + GAT * a[2]
        return max(64, a[2] * (f / 2 if o[3] in ("arB", "arU") and a[3] in ("arB", "arU") and f == 1.0 else f))

    def tt(o, a, c, f):
        op("v", lambda e: e.tensor_tensor(o[0], a[0], c[0], f), ks(a, c), ks(o), cyc(o, a, 1.01 if "p" in (a[3][0], c[3][0]) else 2))

    def ts(o, a, s1, f0, s2=None, f1=None):
        if f1 is None:
            op("v", lambda e: e.tensor_scalar(o[0], a[0], ap(s1), None, f0), ks(a, s1), ks(o), cyc(o, a))
        else:
            op("v", lambda e: e.tensor_scalar(o[0], a[0], ap(s1), ap(s2), f0, f1), ks(a, s1, s2), ks(o), cyc(o, a))

    def cp(o, a):
        op("v", lambda e: e.tensor_copy(o[0], a[0]), ks(a), ks(o), cyc(o, a))

    def scatter(win, off, a, c=None):
        picks[1] = a[2]
        if c is None:
            op("v", lambda e: e.tensor_copy(win[0].indirect(off[0]), a[0]), ks(a, off), ks(win), 60 + SCA * a[2])
        elif len(c) == 2:
            op("v", lambda e: e.tensor_scalar(win[0].indirect(off[0]), a[0], c[0], c[1], OP.mult, OP.add), ks(a, off), ks(win), 60 + SCA * a[2])
        else:
            op("v", lambda e: e.tensor_tensor(win[0].indirect(off[0]), a[0], c[0], OP.add), ks(a, c, off), ks(win), 60 + SCA * a[2])

    def ms(o, v):
        op("v", lambda e: e.memset(o[0], v), [], ks(o), cyc(o, o))

    def scan(o, a, c, f0, f1, first=0.0):
        op("v", lambda e: e.tensor_tensor_scan(o[0], a[0], c[0], first, f0, f1), ks(a, c), ks(o), cyc(o, a, 1.0 if c[3] == "arB" else 1.01))

    def turn(o, a):
        op("v", lambda e: e.transpose(o[0], a[0]), ks(a), ks(o), cyc(o, a, 1.01))

    def act(o, a, f, bias=0.0, scale=1.0):
        op("s", lambda e: e.activation(o[0], a[0], f, bias=ap(bias), scale=ap(scale)), ks(a, scale, bias), ks(o), cyc(o, a, 1.01))

    def mm(o, l, r, start=True, stop=True):
        op("t", lambda e: e.matmul(o[0], l[0], r[0], start, stop), ks(l, r), ks(o), max(min(64, l[2]), r[2]) * (4 if l[3] == "arF" else 1))

    left, opened = {}, {}

    def begin(o, l, r):
        opened[o[1][0]] = len(ops)
        mm(o, l, r, True, False)

    def add(o, l, r):
        k = (o[1][0], opened[o[1][0]])
        left[k] = left.get(k, 0) + 1

        def call(e):
            left[k] -= 1
            return e.matmul(o[0], l[0], r[0], False, left[k] == 0)
        op("t", call, ks(l, r), ks(o), max(min(64, l[2]), r[2]) * (4 if l[3] == "arF" else 1), adds=k)

    def join(n):
        part = ops[-n:]
        del ops[-n:]
        one = dict(part[0], call=lambda e: [o["call"](e) for o in part], c=sum(o["c"] for o in part), cs=[sum(c) for c in zip(*(o["cs"] for o in part))])
        for k in "RW":
            one[k] = list(dict.fromkeys(x for o in part for x in o[k]))
        ops.append(one)

    def close(o, l, r):
        k = (o[1][0], opened[o[1][0]])
        left[k] += 1
        mm(o, l, r, False, True)

    def mms(o, pairs):
        if len(pairs) == 1:
            mm(o, *pairs[0])
        else:
            begin(o, *pairs[0])
            for l, r in pairs[1:]:
                add(o, l, r)

    def io(o, pat, base, cm):
        if o[3] == "arI":
            op("g", lambda e: e.iota(o[0], pat, base, cm), [], ks(o), 160 + 2 * o[2])
        else:
            op("g", lambda e: e.iota(o[0], pat, base, cm, allow_small_or_imprecise_dtypes=True), [], ks(o), 160 + 2 * o[2])

    def fill(o, v):
        io(o, [[0, o[2]]], int(v), 0)

    def asel(o, a, pat, f, other, base, cm):
        op("g", lambda e: e.affine_select(o[0], a[0], pat, f, other, base, cm), ks(a), ks(o), 200 + 2 * o[2])

    def copy(q, o, a):
        if q == "s":
            act(o, a, AF.Copy)
        elif q == "g":
            asel(o, a, [[0, o[2]]], OP.is_ge, 0.0, 0, 0)
        else:
            cp(o, a)

    def row(j, c0=0, c1=128):
        return b("cr", 128 * j + c0, 128 * j + c1, 1, 1, key="cr%d" % j)

    ONE, RH, RMG = range(3)
    blocks = lambda t, n: ["%sb%d" % (t, k) for k in range(n)]
    pk = lambda nm, p0, n: ["%s%d" % (nm, p) for p in range(p0, p0 + n)]
    Cw = lambda s: b("C", 0, V0 + L * s + 1, key=["C"] + blocks("C", s + 1) + pk("Ck", 0, 4))
    Aw = lambda s, more=1: b("A", 0, V0 + L * s + more, key=["A"] + blocks("A", s + 1))
    lhs = lambda p, m="B": b(m, 15 - p, 143 - p)

    dma(b("xb")[0], T.x0[:], [], ["xb"], 32, DQ[0])
    dma(b("tp")[0], T.tops[:], [], ["tp"], 4, DQ[1])
    dma(b("KI", 0, V0)[0], T.kids[:], [], ["KI"], 512 + 36 * (DQ[0] == "s"))
    dma(b("A", 0, V0)[0], T.a0[:], [], ["A"], 256)
    dma(b("thi", p1=8)[0], T.th[:], [], ["thi"], 4, DQ[2])
    ms(b("A", V0, W, L, key=blocks("A", 4)), FAR)
    fill(b("C", V0, W, L, key=blocks("C", 4)), 4095)
    ms(b("ones"), 1.0)
    fill(b("one8"), 1)
    fill(b("AN", 0, 128, key="ANz"), 0)
    fill(b("AN", 384, 512, key="ANy"), 0)
    fill(b("CN", 0, 128, key="CNz"), 4095)
    fill(b("CN", 256, 512, key="CNy"), 4095)
    ms(b("B"), 0.0)
    ms(row(ONE), 1.0)
    ms(row(RH), 1.75)
    ms(row(RMG), MAGIC)
    mm(b("pb2", 0, 160), row(ONE), b("cr", 0, 160, 1, 1, key=["cr0", "cr1"]))
    ms(b("RM"), 0.0)
    ms(b("RM", 0, 128, 16), BIG)
    ms((T.em3[:, :, 16], ["empz"], 8, "arB"), 0.0)
    for k in range(2):
        fill(b("come%d" % k, 64, 80, key="come%dz" % k), NONE)
    for k in range(4):
        if not PULL[k]:
            fill(b("msg%d" % k, 0, CAP), NONE)
    high = lambda nm: (T.arB[32:33, SLOT[nm][1]:SLOT[nm][1] + 128], [nm + "h"], 128, "arB")
    ms(b("kl", p1=32), 0.0)
    ms(b("kl", p1=1), UNIT)
    ms(high("kl"), 1 / 256)
    io(b("kr", p1=64, key=["kr", "krh"]), [[0, NH], [-STEP, HC], [0, 16]], STEP * HC, 0)
    io(b("kr", 0, HW, p1=1), [[1, HW]], -HW, 0)
    ms(b("kr", HW, 128, p1=1), 32.0)
    fill(b("BD", 0, 64, 4, key="BDz"), -1)
    for k, v in enumerate((256, 128, -256)):
        fill(b("d1", 32 + k, 64, 4, key="d1k%d" % k), v)

    io(b("pin"), [[0, 16]], 0, 1)
    io(b("iot", 0, 128, key="iot0"), [[1, 128]], 0, 0)
    io(b("ri"), [[HW, NH], [1, 16], [16, HC]], 0, 0)
    cp(b("plist"), b("ri"))
    asel(b("I"), b("ones", 0, 128), [[-1, 128]], OP.is_equal, 0.0, 0, 1)
    cp(b("ci"), b("iot", 0, 128, key="iot0"))
    for k in range(1, 12):
        if IOTQ[k - 1] == "g":
            io(b("iot", 128 * k, 128 * k + 128, key="iot%d" % k), [[1, 128]], 128 * k, 0)
        else:
            act(b("iot", 128 * k, 128 * k + 128, key="iot%d" % k), b("iot", 0, 128, key="iot0"), AF.Identity, 128.0 * k)
    for nm, v in (("nI", -1.0), ("hI", 0.5), ("I63", 63.0), ("nI63", -63.0)):
        act(b(nm), b("I"), AF.Copy, 0.0, v)
    ts(b("pa", 0, 2), b("pin", 0, 2), 15, OP.bitwise_and)
    cp(b("pf"), b("pa", 0, 1))
    act(b("pH"), b("pf"), AF.Copy, 0.0, float(HW))
    ts(b("pc", 0, 2), b("pin", 0, 2), 7, OP.bitwise_and)
    ts(b("jL"), b("ci", 0, 128, 16), b("pf"), OP.add)
    act(b("cj"), b("jL"), AF.Identity, -128 * M, -M)
    io(b("nL"), [[16, 32]], V0, 0)
    ts(b("nL"), b("nL"), b("pf"), OP.add)
    act(b("d1", 35, 64, 4, key="d1k3"), b("jL"), AF.Identity, 256.0)
    fill(b("xn", 128, 144, key="xnz"), NONE)
    ts(b("lF"), b("pc", 0, 2), 16.0, OP.mult, 15.0, OP.add)
    io(b("pc", 8, 12, key="pc8"), [[0, 2], [64, 2]], 15, 0)
    ts(b("pc", 4, 6, key="pc4"), b("pin", 0, 2), HC - 1, OP.bitwise_and)
    ts(b("pc", 6, 8, key="pc6"), b("pin", 0, 2), HC.bit_length() - 1, OP.logical_shift_right, 16 // HC - 1, OP.bitwise_and)
    cp(b("tmp2", 12, 13, key="tmp2c"), b("pc", 6, 7, key="pc6"))
    act(b("tmp2", 8, 9, key="tmp2b"), b("tmp2", 12, 13, key="tmp2c"), AF.Copy, 0.0, 16.0)
    ts(b("lG"), b("pc", 8, 12, key="pc8"), b("tmp2", 8, 9, key="tmp2b"), OP.add)
    ts(b("tmp2", 0, 1, key="tmp2a"), b("pc", 4, 5, key="pc4"), 16.0, OP.mult, b("tmp2", 12, 13, key="tmp2c"), OP.add)
    for h in range(NH):
        ts(b("lperm", HC * h, HC * h + HC), b("ci", HW * h, HW * h + 16, 16 // HC), b("tmp2", 0, 1, key="tmp2a"), OP.add)
    ts(b("pc", 12, 14, key="pc12"), b("pin", 0, 2), 4, OP.logical_shift_right, 1, OP.bitwise_and)
    ts(b("tmp", 8, 9, key="tmpy"), b("pc", 12, 13, key="pc12"), 144.0, OP.mult)
    act(b("tmp", 9, 10, key="tmpz"), b("tmp", 8, 9, key="tmpy"), AF.Identity, 144.0, -1.0)
    ts(b("lsel", 0, 8, 2), b("jL", 0, 8, 2), b("tmp", 8, 9, key="tmpy"), OP.add)
    ts(b("lsel", 1, 8, 2), b("jL", 1, 8, 2), b("tmp", 9, 10, key="tmpz"), OP.add)
    ts(b("pa", 2, 4, key="pa_"), b("pin", 0, 2), 4, OP.logical_shift_right)
    cp(b("pG"), b("pa", 2, 3, key="pa_"))
    ts(b("xi"), b("ci"), 4, OP.logical_shift_right)
    ts(b("bones"), b("xi"), b("pG"), OP.is_equal, KEY, OP.mult)
    cp(b("B", 15, 143, 16), b("bones", 0, 128, 16))
    asel(b("bx"), b("bones"), [[0, 128]], OP.is_ge, 0.0, 0, 0)
    for p in parts(P1X[0], True):
        fill(b("bx", p, 128, 16), 0)
    act(b("B2"), b("B"), AF.Copy, 0.0, 2.0)
    act(b("nB"), b("B"), AF.Copy, 0.0, -1.0)
    act(b("lo"), b("bones"), AF.Copy, 0.0, -M / KEY)
    asel(b("lt"), b("lo"), [[1, 128]], OP.is_gt, 0.0, 0, -1)
    asel(b("ld"), b("lt"), [[1, 128]], OP.not_equal, M, 0, -1)
    asel(b("lp"), b("lt"), [[1, 128]], OP.not_equal, 256 * M, 0, -1)
    act(b("nl8"), b("lt"), AF.Copy, 0.0, -128.0 / M)
    asel(b("row1"), b("lo"), [[-1, 128]], OP.is_equal, 0.0, -1, 1)
    asel(b("dm"), b("row1"), [[-1, 128]], OP.not_equal, M, 0, 1)
    io(b("nr2", 512, 640, 1, 2, key="jr2"), [[1, 128]], 0, 128)
    for s in range(4):
        io(b("nr2", 128 * s, 128 * s + 128, 1, 2, key="n%d" % s), [[0, 128]], -7 - s, 15 + 2 * s)
    ts(b("hx"), b("ci"), 15, OP.bitwise_and)
    ts(b("tab", 0, 128), b("hx"), b("pf"), OP.is_equal, 65.0, OP.mult)
    act(b("cl0"), b("tab", 0, 128), AF.Relu, float(2 ** 26), -float(2 ** 26))
    for k in range(2):
        cp(b("tab", 128 << k, 256 << k, key="tab%d" % (k + 1)), b("tab", 0, 128 << k, key=["tab"] + pk("tab", 1, k)))
    dma(b("tab", 512, 1024)[0], b("tab", 0, 512)[0], ["tab", "tab1", "tab2"], ["tab3"], 128)
    mms(b("pb6", 0, 128), [(b("I"), b("cl0")), (high("kl"), high("kr"))])
    act(b("emc"), b("pb6", 0, 128), AF.Copy)
    act((T.c3[:, :, 0:16], ["cnt0"], 128, "arB"), b("cl0"), AF.Identity, -M / 2, -1.0)
    act((T.c3[:, :, 16], ["cnt0"], 8, "arB"), b("jL"), AF.Identity, -128.0)
    ts(b("lz"), b("pc", 0, 2), 17.0, OP.mult, 15.0, OP.add)
    for k in range(2):
        ms((T["r3%d" % k][:, :, 16], ["rowu%dz" % k], 8, "arU"), 65535)
        if ES[k] < 8:
            ms((T["e4%d" % k][:, ES[k]:8, :, 16], pk("E%d" % k, ES[k], 8 - ES[k]), 64 - 8 * ES[k], "arB"), 0.0)
        fill(b("RY%d" % k, key=["RY%d" % k, "RY%dt" % k]), 2 ** 23)
        fill(b("RY%d" % k, 0, 136, 17), -2 ** 23)
    cp(b("tu"), b("tp"))
    cp(b("topf"), b("tp"))
    for h in range(4):
        o, a = b("C", 256 * h, 256 * h + 256, key="Ck%d" % h), b("KI", 256 * h, 256 * h + 256)
        if CKQ[h] == "g":
            asel(o, a, [[0, 256]], OP.is_ge, 0.0, 0, 0)
        else:
            cp(o, a)
    ts(b("thf", p1=8), b("thi", p1=8), KEY, OP.mult)
    asel(b("thx", p1=8), b("ones", 0, 128, 1, 8), [[1, 128]], OP.is_ge, 0.0, 0, -16)
    asel(b("ad", p1=8), b("thx", p1=8), [[-1, 128]], OP.is_ge, 0.0, 15, 16)
    mms(b("pb6", 384, 512), [(b("I"), b("emc")), (b("ad", p1=8), b("thf", p1=8))])
    scan(b("thx"), b("RM"), b("pb6", 384, 512), OP.max, OP.min)
    act(b("lim", 15, 128, 16), b("thx", 15, 128, 16), AF.Identity, 48 * UNIT)
    act(b("lim4"), ind(b("thx"), b("lF")), AF.Identity, 48 * UNIT)

    def x_forms(share, of):
        act(b("xP"), ind(b(of), b("lperm")), AF.Abs)
        for k in range(16):
            copy(share[k], b("xrep", k, 2048, 16, key="xr%d" % k), b("xP"))
        act(b("xm"), b("xb"), AF.Identity, -MAGIC)
        act(b("xn", 0, 128), b("xb"), AF.Copy, 0.0, -1.0)
        act((T.xd[:], ["xd"], 128, "arB"), b("xb"), AF.Copy, 0.0, -1.0)
        for hs in ([0, 1],) if parts(P1[0], True) == parts(P1[1], True) else ([0], [1]):
            raw = parts(P1[hs[0]], True)
            if raw:
                o = (T.xd[:, HC * hs[0]:HC * hs[-1] + HC, raw[0]:raw[-1] + 1], ["xd"], 32, "arB")
                act(o, o, AF.Copy, 0.0, 2.0)

    KB = ("pb0", "pb1")

    def rows(out, s, nodes):
        if s == 0:
            cp(out, ind(b("KI", 0, V0), nodes))
        else:
            act(out, ind(Cw(s), nodes), AF.Copy)

    def lst(name, h, p0, n):
        return b(name, HW * h + HC * p0, HW * h + HC * (p0 + n), key=name + str(h))

    def piece(name, h, p0, n):
        return b(name, HW * (16 * h + p0), HW * (16 * h + p0 + n), key=pk("xr", 0, 16) if name == "xrep" else pk(name, 16 * h + p0, n))

    turns = {}

    def inturn(line, on):
        if on and line in turns:
            ops[-1]["after"] = [turns[line]]
        turns[line] = len(ops) - 1

    def sums(h, o0, p0, n, m="B", of="Dab"):
        for p in range(p0, p0 + n):
            add(b(KB[h], o0, o0 + HW), lhs(p, m), piece(of, h, p, 1))
            if JOIN and (p - p0) % JOIN == JOIN - 1 or p == p0 + n - 1:
                join((p - p0) % JOIN + 1 if JOIN else 1)

    def sweep(s, pieces, h, lists, into, o0):
        p0 = 0
        for n, bank in pieces:
            d, x = piece(into, h, p0, n), piece("xrep", h, p0, n)
            if bank:
                act(d, ind(Aw(s), lst(lists, h, p0, n)), AF.Copy)
                inturn("sg", STAG[1])
                o = HW * (p0 - parts(pieces, True)[0])
                mms(b(bank, o, o + HW * n), [(b("nI"), x), (b("I"), d)])
                d = b(bank, o, o + HW * n)
            else:
                tt(d, ind(Aw(s), lst(lists, h, p0, n)), x, OP.subtract)
                inturn("vg", STAG[0])
            act(piece("Dab", h, p0, n), d, AF.Abs)
            inturn("sa", STAG[2])
            sums(h, o0, p0, n)
            p0 += n

    def sweep_arrived(h):
        p0 = 0
        for n, bank in P1X[h]:
            a, o, l = piece("ag", h, p0, n), piece("Dab", h, p0, n), b("plist", HW * h + HC * p0, HW * h + HC * (p0 + n))
            if bank:
                x = piece("D", h, p0, n)
                act(x, ind(b("hz"), l), AF.Abs)
                mms(b(bank, 0, HW * n), [(b("I"), a), (b("nI"), x)])
                act(o, b(bank, 0, HW * n), AF.Abs)
                sums(h, 0, p0, n)
            else:
                tt(o, ind(b("xb"), l), a, OP.max)
                inturn("vg", STAG[3])
                sums(h, 0, p0, n, "nB", "ag")
                sums(h, 0, p0, n, "B2")
            p0 += n

    def emp(a, z):
        return (T.em3[:, a // 16:z // 16, 0:16], ["emp"], z - a, "arB")

    def both(nm):
        return [nm + "0", nm + "1"]

    def lanes(split):
        for hs in ([0], [1]) if split else ([0, 1],):
            a, z = HW * hs[0], HW * hs[-1] + HW
            own = lambda nm, o=0, key=None, hs=hs, a=a, z=z: b(nm, o + a, o + z, key=[(key or nm) + str(h) for h in hs])
            yield hs, a, z, own, lambda nm, o=0, key=None, p1=128, a=a, z=z: b(nm, o + a, o + z, p1=p1, key=key)

    def firsts(lists, node, off, on, bank, z, out, top):
        k = int(z == "zb")
        rw, E, R3, E4, rz = "rowu" + str(k), "E" + str(k), T["r3%d" % k], T["e4%d" % k], "RY%d" % k
        act(b("row" + str(k)), ind(b("iot", 0, top, key=pk("iot", 0, -(-top // 128))), lists), AF.Copy)
        cp((R3[:, :, 0:16], [rw], 128, "arU"), b("row" + str(k)))
        copy(GQ[0], b(rz, 16, 136, 17, key=rz + "t"), node(0, 8))
        begin(b(bank, 0, 136), b("I"), (T.c3[:], ["cnt0"], 136, "arB"))
        if not k:
            add(b(bank, 0, 136), b("bones"), (T.em3[:], ["emp", "empz"], 136, "arB"))
        if ES[k] < 8:
            act(b("neg%d" % k), node(0, 8), AF.Copy, 0.0, -1.0)
        for c in range(8):
            key = E + str(c)
            if c < ES[k]:
                ts((E4[:, c, 0:8 - c, :], [key], 136 - 17 * c, "arB"), (R3[:, c:8, :], [rw, rw + "z"], 136 - 17 * c, "arU"), node(c, c + 1),
                   OP.is_equal, off(c), OP.is_gt)
            else:
                far = b("far%d" % k, 64 * (c % 4), 64 * (c % 4) + 128 - 16 * c, key="far%d%d" % (k, c))
                act(far, b("row" + str(k), 16 * c, 128), AF.Abs, b("neg%d" % k, c, c + 1))
                act((E4[:, c, 0:8 - c, 0:16], [key], 128 - 16 * c, "arB"), far, AF.Relu, on(c), -1.0)
            if c < 7:
                add(b(bank, 17 * c + 17, 136), b("lo"), (E4[:, c, 1:8 - c, :], [key], 119 - 17 * c, "arB"))
        add(b(bank, 0, 136), b("ld"), (E4[:, :, 0, :], pk(E, 0, 8), 136, "arB"))
        scan(b(z), b(rz, key=[rz, rz + "t"]), b(bank, 0, 136), OP.min, OP.max)
        ts(b(out), b(z, 16, 136, 17), 128.0, OP.add)

    def lower(o0, f):
        scan(b("cum"), b("one8"), f, OP.mult, OP.add)
        add(b("pb2", o0 + 1, o0 + 8), b("lo"), b("cum", 0, 7))

    def send(s):
        h = hops(T, topo, rank, s)
        m = "msg%d" % s
        f, o = b("fl%d" % (s % ST), 16, 24), b("pb2", 176, 184)
        if PULL[s]:
            cp(b("fu"), f)
            act(b("frow"), ind(b("iot", 0, 16, key="iot0"), b("fu")), AF.Copy)
            scan(b("crow"), b("ones", 0, 128), b("frow"), OP.mult, OP.add, -0.5)
            for k in range(2):
                op("s", lambda e, k=k: e.activation(b("msk")[0], b("crow")[0], AF.Sign, bias=b("jL", k, k + 1)[0], scale=-1.0,
                                                    accum_out=b("inv", k, k + 1)[0]), ["crow", "jL"], ["msk", "inv%d" % k], 152)
            ts(b("ivu"), b("inv", key=["inv0", "inv1"]), 0.5, OP.mult, 64.0, OP.add)
            act(b(m, 0, CAP), ind(b("xn", key=["xn", "xnz"]), b("ivu")), AF.Copy)
        else:
            begin(o, b("I"), b("cj"))
            add(o, b("lt"), f)
            lower(176, f)
            tt(b("fw"), f, b("cj"), OP.mult)
            add(o, b("nI"), b("fw"))
            ts(b("posu"), o, -1.0 / M, OP.mult)
            scatter(b(m), b("posu"), b("xn", 0, 128))
        n = engines_of(topo, core, h[1])
        rid, pid = topo.addr(h[1], core)
        if len(h) == 3:
            to, sem = T["rl%d" % s][:, 0:CAP], T.sem["rr%d" % s]
        else:
            to, sem = T["come%d" % (s // ST)][:, CAP * (s % ST):CAP * (s % ST) + CAP], T.sem["in%d" % s]
        op("g", lambda e: e.remote_dma(to, T[m][:, 0:CAP], sem, T.sem["ls%d" % s], pid, rid, emask(topo, core, h[1], n)),
           [m], ["come%d_%d" % (s // ST, s % ST)], 120, TRIP[s], "remote%d" % s)

    def nodes(t):
        return (lambda a, z: b("topf", a, z)) if t == 0 else (lambda a, z: b("s2", 3 + 4 * a, 4 * z, 4))

    def front(s):
        t = s % ST
        vu = b("tu") if t == 0 else b("lu", 0, 8)
        vf = nodes(t)
        for hs, a, z, own, all_ in lanes(SPLIT[5] and t):
            rows(own("cvf"), s, b("tu" if t == 0 else "lu", a // 16, z // 16))
        for hs, a, z, own, all_ in lanes(SPLIT[6] and t):
            ts(own("cvu"), ind(own("cvf"), b("lperm", 0, (z - a) // 16)), float(V0 + L * s), OP.min)
        cvf = b("cvf", key=both("cvf"))
        mm(b("pb2", 16, 144), b("dm"), cvf)
        turn(b("tr", 0, 128, key="tra"), b("pb2", 16, 144))
        turn(b("tr", 128, 288, key="trb"), b("pb2", 0, 160))
        act(b("dl"), ind(b("tr", key=["tra", "trb"]), b("lsel")), AF.Copy, 0.0, 1 / M)
        act(emp(0, 128), cvf, AF.Relu, -65.0 * 4094, 65.0)
        nrow = (b("nr2", 128 * s, 128 * s + 128, 1, 2, key="n%d" % s), b("nr2", 512, 640, 1, 2, key="jr2"))
        mms(b("pb3", 144, 272), [nrow, (b("nl8"), emp(0, 128))])
        tt(b("RW", 272, 400, key="rowN"), cvf, b("pb3", 144, 272), OP.min)
        if s != 2:
            if t and ES[0] < 8:
                act(b("nonr"), b("fl0", 24, 32), AF.Identity, 1.0, -1.0)
            firsts(vu, vf, lambda c: b("fl0", 24 + c, 25 + c) if t else 0.0, lambda c: b("nonr", c, c + 1) if t else 1.0, "pb3", "zv", "uvu%d" % t, V0 + L * s)
            tt(b("LA%d" % t), ind(b("zv"), b("lz")), b("lim4"), OP.min)
        else:
            mms(b("pb3", 0, 136), [(b("I"), (T.c3[:], ["cnt0"], 136, "arB")), (b("bones"), (T.em3[:], ["emp", "empz"], 136, "arB"))])
            scan(b("zv"), b("RY0", key=["RY0", "RY0t"]), b("pb3", 0, 136), OP.min, OP.max)
        full = -M / 2 if s == 2 else M / 2
        act(b("room", 0, 8, key="room0"), b("zv", 15, 136, 17), AF.Relu, 1.0 + M * full, -M)
        act(b("room", 8, 16, key="room1"), b("zv", 15, 136, 17), AF.Sign, -full)
        tt(b("d1", 0, 32, 4, key="d1a"), vf(0, 8), b("nL", 8 * s, 8 * s + 8), OP.subtract)
        act(b("d1", 1, 32, 4, key="d1b"), b("d1", 0, 32, 4, key="d1a"), AF.Copy, 0.0, -1.0)
        return nrow

    def step(s, nrow):
        t = s % ST
        n0 = V0 + L * s
        bf = lambda a, z: b("pay", 15 + 16 * a, 16 * z, 16, key=["pay0", "pay1"])
        for h in range(NH):
            K1 = b(KB[h], 0, HW)
            begin(K1, b("kl", p1=33, key=["kl", "klh"]), b("kr", 0, HW, p1=33, key=["kr", "krh"]))
            if s == 2:
                sweep_arrived(h)
            else:
                sweep(s, P1[h], h, "cvu", "D", 0)
            half = lambda nm, a=0, z=HW: b(nm, HW * h + a, HW * h + z, key=nm + str(h))
            r = half("r1")
            scan(r, b("RM", 0, HW), K1, OP.max, OP.min)
            tt(half("e"), r, K1, OP.not_equal)
            scan(half("pay"), half("e"), b("dl", HW * h, HW * h + HW), OP.mult, OP.add)
            bu = b("bu", HC * h, HC * h + HC, key="bu%d" % h)
            ts(bu, b("pay", HW * h + 15, HW * h + HW, 16, key="pay%d" % h), float(n0), OP.min)
            act(half("dvf"), ind(Cw(s), bu), AF.Copy)
            ts(half("dvu"), ind(half("dvf"), b("lperm", 0, HC)), float(n0), OP.min)
            scan(b("r2", 192 * h + 1, 192 * h + HW, key="r2%d" % h), b(KB[h], 1, HW), half("r1", 0, HW - 1), OP.min, OP.max, BIG)
        r1 = ["r10", "r11"]
        bare, bu, tab = "ag" if s == 2 else "D", b("bu", key=["bu0", "bu1"]), b("tab", key=["tab"] + pk("tab", 1, 3))
        for hs, a, z, own, all_ in lanes(SPLIT[0]):
            keys = [nm + str(h) for nm in ("r1", "r2") for h in hs]
            half = lambda nm: b(nm, a // 8, z // 8, key=[nm + str(h) for h in hs])
            ts(half("dec"), b("RX", 2 * a + 15, 2 * z, 16, key=keys), 1 / UNIT, OP.mult)
            ts(half("dk"), half("dec"), HW - 1, OP.bitwise_and)
            ts(half("du"), half("dk"), b("pH"), OP.add)
        if s == 2:
            mms(b("pb6", 384, 512), [(b("I"), b("cl0")), (b("bx"), b("xb"))])
            scan(b("thx"), b("RM"), b("pb6", 384, 512), OP.max, OP.min)
            tt(b("r1", 15, 128, 16, key=r1), b("r1", 15, 128, 16, key=r1), b("thx", 15, 128, 16), OP.subtract)
        for hs, a, z, own, all_ in lanes(SPLIT[1]):
            act(own("ab"), ind(Aw(s), b("bu", a // 16, z // 16, key=["bu%d" % h for h in hs])), AF.Identity, -4.0)
        for h in range(NH):
            lq = b("du", 12 * h, 12 * h + HC, key="du%d" % h)
            act(b("dq", HW * h, HW * h + HW, key="dq%d" % h), ind(piece(bare, h, 0, 16), lq), AF.Copy)
            act(b("oq", HW * h, HW * h + HW, key="oq%d" % h), ind(tab, lq), AF.Copy, 0.0, 2.0)
        for hs, a, z, own, all_ in lanes(SPLIT[2]):
            act(own("nb"), ind(tab, b("du", HC + a // 16, HC + z // 16, key=["du%d" % h for h in hs])), AF.Identity, 65.0, -1.0)
        for hs, a, z, own, all_ in lanes(SPLIT[3]):
            o = b(MB[hs[0]], a, z)
            begin(o, row(ONE), row(RH, a, z))
            for l, r in [("hI", own("ab")), ("hI", own("dq")), ("nI", all_("xb")) if s == 2 else ("hI", (T.xd[:, a // 16:z // 16, :], ["xd"], z - a, "arB"))]:
                add(o, b(l), r)
            close(o, row(ONE), row(RMG, a, z))
            act(own("absM"), o, AF.Abs, -MAGIC)
            mms(b(EB, 384 + a, 384 + z), [(b("I"), all_("emc")), (b("bones"), own("absM"))])
            scan(own("es"), b("RM", a, z), b(EB, 384 + a, 384 + z), OP.max, OP.min)
            tt(own("AN", 128, "Mb"), all_("xm"), o, OP.add)
        mms(b("pb2", 384, 512), [(b("I"), b("xb")), (b("nI"), b("ab", key=both("ab")))])
        act(b("cl"), b("pb2", 384, 512), AF.Relu, 8.0, -1.0)
        act(b("cl"), b("cl"), AF.Relu, 8.0, -1.0)
        for h in range(NH):
            begin(b(KB[h], HW, 2 * HW), b("kl", p1=33, key=["kl", "klh"]), b("kr", HW, 128, p1=33, key=["kr", "krh"]))
            sweep(s, P2[h], h, "dvu", "D" if s == 2 else "ag", HW)
        tt(b("RX", 207, 448, 16, key=["ro", "r21"]), b("lim4", 0, 16), b("room", key=["room0", "room1"]), OP.add)
        tt(b("d1", 2, 32, 4, key="d1c"), nodes(t)(0, 8), bf(0, 8), OP.subtract)
        copy(GQ[1], b("d1", 3, 32, 4, key="d1d"), bf(0, 8))
        U = b("BD", 2, 128, 4, key="BDu")
        tt(U, ind(b("r1", key=r1), b("lF")), b("LA%d" % t), OP.min)
        tt(b("nfl"), b("RX", 79, 576, 16, key=r1 + ["lim", "ro", "r21"]), U, OP.not_equal)
        tt(b("BD", 3, 128, 4, key="BDb"), U, b("nfl"), OP.max)
        act(b("BD", 1, 64, 4, key="BDe"), ind(b("es", key=both("es")), b("lF", 0, 1)), AF.Copy)
        for hs, a, z, own, all_ in lanes(SPLIT[4]):
            p5, p3 = (lambda o: b(RB[hs[0]][0], o + a, o + z)), b(RB[hs[0]][1], 272 + a, 272 + z)
            mms(p5(128), [(b("I63"), own("nb")), (b("nI63"), own("oq"))])
            mms(p5(256), [(nrow[0], all_("nr2", 512, "jr2", 2)), (b("nI63"), own("nb")), (b("I63"), own("oq"))])
            mms(p3, [(b("nI63"), emp(a, z)), (b("I63"), own("nb"))])
            tt(own("CN", 128), own("cvf"), p5(128), OP.max)
            tt(own("RW", 144, "rowM"), own("cvf"), p5(256), OP.max)
            tt(own("w3"), own("cvf"), p3, OP.min)
            tt(p3, own("dvf"), p3, OP.subtract)
            tt(own("RW", 400, "rsp"), own("w3"), p3, OP.max)
        for h in range(NH):
            scan(b("mf", HW * h, HW * h + HW, key="mf%d" % h), b("es", HW * h, HW * h + HW, key="es%d" % h), b(KB[h], HW, 2 * HW), OP.min, OP.min, BIG)
        mf = b("mf", key=["mf0", "mf1"])
        tt(b("fg"), ind(mf, b("lG")), b("BD", 0, 64, key=["BDz", "BDe", "BDu", "BDb"]), OP.is_lt)
        if ES[1] < 8:
            tt(b("fl%d" % t), ind(mf, b("lF")), b("BD", 3, 128, 4, key="BDb"), OP.is_gt)
        else:
            tt(b("fl%d" % t, 16, 32), ind(mf, b("lF", 0, 1)), b("BD", 67, 128, 4, key="BDb"), OP.is_gt)
        scan(b("s2"), b("fg"), b("d1", key=["d1a", "d1b", "d1c", "d1d"] + pk("d1k", 0, 4)), OP.mult, OP.add)
        cp(b("lu"), b("s2", 3, 64, 4))
        act(b("rpre"), ind(b("RW", 16, 528, key=["rowN"] + both("cvf") + both("rowM") + both("rsp")), b("lu", 8, 16)), AF.Relu, 4095.0, -1.0)
        scatter(b("CW", 0, 128 + n0, key=["C"] + blocks("C", s) + pk("Ck", 0, 4)), b("uvu%d" % t), b("rpre"), (-1.0, 4095.0))
        act(b("C", n0, n0 + L, key="Cb%d" % s), ind(b("CN", key=both("CN") + ["CNz", "CNy"]), b("lu", 8, 16)), AF.Copy)
        act(b("A", n0, n0 + L, key="Ab%d" % s), ind(b("AN", key=both("Mb") + ["xb", "ANz", "ANy"]), b("lu", 8, 16)), AF.Copy)
        firsts(bu, bf, lambda c: b("fg", 3 + 4 * c, 4 + 4 * c), lambda c: b("fl%d" % t, c, c + 1), "pb7", "zb", "oAu", n0 + 1)
        scatter(b("AW", 0, 128 + n0, key=["A"] + blocks("A", s)), b("oAu"), b("ab", key=both("ab")), b("cl"))
        send(s)

    def round_end(s):
        cm = "come%d" % (s // ST)
        tt(b("rest2"), b("fl0", 24, 32), b("fl1", 24, 32), OP.max)
        begin(b("pb2", 192, 200), b("lp"), b("rest2"))
        lower(192, b("rest2"))
        act(b("nrs"), b("pb2", 192, 200), AF.Identity, 256.0, -1.0 / M)
        act(b("av"), ind(Aw(s, L), b("lu", 0, 8)), AF.Copy)
        mms(b("pb6", 0, 128), [(b("nI"), b("xb")), (b("I"), b("av"))])
        act(b("ad"), b("pb6", 0, 128), AF.Abs)
        first = b(cm, 0, CAP, key=cm + "_0")
        op("s", lambda e: e.activation(b("msk", 0, CAP)[0], first[0], AF.Sign, bias=NONE / 2, scale=-1.0, accum_out=b("na")[0]),
           first[1], ["msk", "na"], 90)
        act(b("n0"), b("na"), AF.Identity, CAP / 2, 0.5)
        act(b("cd"), b("na"), AF.Identity, CAP / 2, -0.5)
        ts(b("ge"), b("nrs"), b("n0"), OP.is_ge, b("cd"), OP.mult)
        tt(b("idx"), b("nrs"), b("ge"), OP.add)
        ts(b("iu"), b("idx"), 64.0, OP.min)
        tt(b("hz"), ind(b(cm, key=[cm + "_0", cm + "_1", cm + "z"]), b("iu")), b("ad"), OP.min)
        act(b("xb"), b("hz"), AF.Abs)

    x_forms(XQ[0], "xb")
    nrow = front(0)
    for s in range(4):
        step(s, nrow)
        if s == 3:
            dma(T.yc[:], b("C", 0, W)[0], ["C"] + blocks("C", 4), ["yc"], 768)
            dma(T.ya[:], b("A", 0, W)[0], ["A"] + blocks("A", 4), ["ya"], 384)
        if s % ST == 1:
            round_end(s)
        if s < 3:
            nrow = front(s + 1)
        if s == 1:
            for j in range(len(AGQ)):
                n = 16 * NH // len(AGQ)
                o, a = piece("ag", j * n // 16, j * n % 16, n), ind(Aw(s + 1), lst("cvu", j * n // 16, j * n % 16, n))
                if AGQ[j] == "s":
                    act(o, a, AF.Copy)
                else:
                    cp(o, a)
            x_forms(XQ[1], "hz")
    dma(T.yx[:], b("xb")[0], ["xb"], ["yx"], 32, DQ[3])

    if "o" not in ORDER:
        ORDER["o"] = order_calls(ops)
    own = {"v": "qv", "s": "qs", "t": "qt", "g": "qg"}
    cnt = {"qv": 0, "qs": 0, "qt": 0, "qg": 0}
    know = {q: {} for q in eng}
    wr, rd = {}, {}

    def need(q, R, Wk):
        deps = []
        for k in R:
            if k in wr:
                deps.append(wr[k])
            if k[:2] == "pb":
                deps += [d for d in rd.get(k, []) if d[0] != q]
        for k in Wk:
            if k in wr and (wr[k][0] != q or q != "t"):
                deps.append(wr[k])
            deps += rd.get(k, [])
        for d in sorted(deps, key=lambda d: -d[2]):
            if know[q].get(d[1], 0) < d[2]:
                eng[q].wait_ge(T.sem[d[1]], d[2])
                for n, v in d[3].items():
                    know[q][n] = max(know[q].get(n, 0), v)

    def note(tag, sem, val, snap, R, Wk):
        snap = dict(snap)
        snap[sem] = val
        d = (tag, sem, val, snap)
        for k in R:
            rd.setdefault(k, []).append(d)
            rd[k] = [e for e in rd[k] if e is d or e[0] != tag or e[1] != sem]
        for k in Wk:
            wr[k] = d
            rd[k] = []

    for i in ORDER["o"]:
        o = ops[i]
        q, kind = o["q"], o["dma"]
        if kind is None:
            need(q, o["R"], o["W"])
            made = o["call"](eng[q])
            for one in made if isinstance(made, list) else [made]:
                cnt[own[q]] += 1
                one.then_inc(T.sem[own[q]], 1)
            note(q, own[q], cnt[own[q]], know[q], o["R"], o["W"])
        elif kind[:6] == "remote":
            s = int(kind[6:])
            need(q, o["R"], [])
            o["call"](g)
            h = hops(T, topo, (rank - 1 - s % (NR - 1)) % NR, s)
            n = engines_of(topo, h[-2], h[-1])
            wr[o["W"][0]] = ("remote", "in%d" % s, n, {"in%d" % s: n})
            cnt["in%d" % s] = n
        else:
            need(q, o["R"], o["W"])
            o["call"](eng[q]).then_inc(T.sem[kind], 16)
            cnt[kind] = 16
            note("dma" + kind, kind, 16, know[q], o["R"], o["W"])
    for n in sorted(cnt):
        if cnt[n] and know["g"].get(n, 0) < cnt[n]:
            g.wait_ge(T.sem[n], cnt[n])
    for s in range(4):
        g.wait_ge(T.sem["ls%d" % s], engines_of(topo, core, hops(T, topo, rank, s)[1]))
